import numpy as np
import ml_dtypes


def mxq(x, axis, fmt="e4m3"):
    dtype, down = {"e4m3": (ml_dtypes.float8_e4m3fn, 7), "e5m2": (ml_dtypes.float8_e5m2, 14)}[fmt]
    v = np.moveaxis(np.asarray(x, np.float32).astype(ml_dtypes.bfloat16).astype(np.float64), axis, -1)
    blocks = v.reshape(v.shape[:-1] + (-1, 32))
    amax = np.abs(blocks).max(-1, keepdims=True)
    byte = np.maximum(np.where(amax > 0, np.frexp(amax)[1] - 1 + 127, 0) - down, 1)
    scale = np.exp2(byte - 127.0)
    codes = (blocks / scale).astype(np.float32).astype(dtype).astype(np.float64)
    return np.moveaxis((codes * scale).reshape(v.shape), -1, axis)


WIDE = False


def mx_kscale(k):
    if not WIDE:
        return np.ones(k)
    levels = np.array([10, -10, 5, -5, 0])
    if k % 512:
        return np.exp2(np.random.permutation(np.resize(levels, k // 32))).repeat(32)
    a = np.empty((k // 512, 16))
    for p in range(k // 512):
        a[p, :8] = np.random.permutation(np.resize(levels, 8))
        for g in range(8):
            far = levels[np.abs(levels - a[p, g]) >= 10]
            a[p, g + 8] = far[np.random.randint(len(far))]
    return np.exp2(a.ravel()).repeat(32)


def f64(x):
    return np.asarray(x).astype(np.float64)


def striped(idx):
    return np.tile(idx.reshape(-1, 16).T, (8, 1)).astype(np.uint16)


def unstriped(offs):
    return offs[:16].T.reshape(-1).astype(np.int64)


E2M1 = np.array([0.0, 0.5, 1.0, 1.5, 2.0, 3.0, 4.0, 6.0, -0.0, -0.5, -1.0, -1.5, -2.0, -3.0, -4.0, -6.0])


def pack_weight(w, fmt):
    k, n = w.shape
    w = f64(np.asarray(w, np.float32).astype(ml_dtypes.bfloat16)).reshape(k // 32, 32, n)
    amax = np.abs(w).max(1)
    if fmt == "e4m3":
        byte = np.frexp(amax)[1] - 1 + 127 - 7
    else:
        mant, ex = np.frexp(amax / 6.0)
        byte = np.where(mant > 0.5, ex, ex - 1) + 127
    byte = np.clip(np.where(amax > 0, byte, 1), 1, 254)
    scaled = (w * np.exp2(127.0 - byte)[:, None, :]).reshape(k, n).astype(np.float32)
    by_word = np.ascontiguousarray(scaled.reshape(k // 512, 128, 4, n).transpose(0, 1, 3, 2))
    if fmt == "e4m3":
        words = by_word.astype(ml_dtypes.float8_e4m3fn).view(np.uint8)
    else:
        c = by_word.astype(ml_dtypes.float4_e2m1fn).view(np.uint8) & 0xF
        words = (c[..., 0::2] | (c[..., 1::2] << 4)).reshape(k // 512, 128, 2 * n)
    return np.ascontiguousarray(words), np.ascontiguousarray(byte.astype(np.uint8).reshape(k // 512, 16, n))


def unpack_weight(words, scales, fmt):
    g, _, n = scales.shape
    words = np.ascontiguousarray(words).reshape(g, 128, n, -1)
    if fmt == "e4m3":
        vals = words.view(ml_dtypes.float8_e4m3fn).astype(np.float64)
    else:
        nib = np.empty((g, 128, n, 4), np.uint8)
        nib[..., 0::2] = words & 0xF
        nib[..., 1::2] = words >> 4
        vals = E2M1[nib]
    vals = vals * np.repeat(np.exp2(scales.astype(np.float64) - 127.0), 8, axis=1)[..., None]
    return vals.transpose(0, 1, 3, 2).reshape(g * 512, n)


def gelu(v):
    return 0.5 * v * (1.0 + np.tanh(np.sqrt(2.0 / np.pi) * (v + 0.044715 * v**3)))


def bf(x):
    return np.asarray(x, np.float32).astype(ml_dtypes.bfloat16)

def planes(Y):
    n, m = Y.shape
    b = f64(bf(Y)).reshape(n // 32, 32, m)
    amax = np.abs(b).max(1)
    byte = np.clip(np.where(amax > 0, np.frexp(amax)[1] - 1 + 127 - 7, 1), 1, 254)
    codes = (b * np.exp2(127.0 - byte)[:, None, :]).reshape(n, m).astype(np.float32).astype(ml_dtypes.float8_e4m3fn).view(np.uint8)
    words = codes.reshape(n // 512, 128, 4, m).transpose(0, 1, 3, 2)
    return np.ascontiguousarray(words), np.ascontiguousarray(byte.astype(np.uint8).reshape(n // 512, 16, m))


K, T, S, P, H, N = 512, 4096, 1024, 512, 1024, 1024


def setup_inputs():
    n = np.random.standard_normal
    s = mx_kscale(K)[:, None]
    u = mx_kscale(H)[:, None]
    tab_words, tab_scales = pack_weight(n((K, T)) * s, "e4m3")
    offs = striped(np.random.permutation(T)[:S])
    pos1 = striped(np.random.permutation(S)[:P])
    pos2 = striped(np.random.permutation(S)[:P])
    w1 = (n((K, H)) / np.sqrt(K) / s).astype(np.float32)
    w2_words, w2_scales = pack_weight(n((K, H)) / np.sqrt(K) / s, "e2m1")
    w3_words, w3_scales = pack_weight(n((K, H)) / np.sqrt(K) / s, "e4m3")
    rel = (np.exp(0.3 * n(H)) * u[:, 0]).astype(np.float32)
    w4 = (1.5 * n((H, N)) / np.sqrt(H) * np.exp(0.8 * n(N))[None, :] / u).astype(np.float32)
    return dict(tab_words=tab_words, tab_scales=tab_scales, offs=offs, pos1=pos1, pos2=pos2,
                w1=w1, w2_words=w2_words, w2_scales=w2_scales,
                w3_words=w3_words, w3_scales=w3_scales, rel=rel, w4=w4)


def reference(tab_words, tab_scales, offs, pos1, pos2, w1, w2_words, w2_scales,
              w3_words, w3_scales, rel, w4):
    v = unpack_weight(tab_words, tab_scales, "e4m3")[:, unstriped(offs)]
    w2 = unpack_weight(w2_words, w2_scales, "e2m1")
    w3 = unpack_weight(w3_words, w3_scales, "e4m3")
    h = mxq(f64(w1), 0, "e4m3").T @ v
    q = w2.T @ v
    r = w3.T @ v
    a = h[:, unstriped(pos1)]
    b = h[:, unstriped(pos2)]
    m = a * b * f64(rel)[:, None]
    d = q[:, unstriped(pos1)] - r[:, unstriped(pos2)]
    gate = 1.0 / (1.0 + np.exp(-d))
    z = m * gate
    y = mxq(f64(w4), 0, "e4m3").T @ mxq(z, 0, "e4m3")
    words, scales = planes(y)
    return y, words, scales

@@ -1,0 +1,301 @@
+from contextlib import ExitStack
+
+import concourse.mybir as mybir
+from concourse.masks import make_identity
+
+K, T, S, PAIRS, H, N = 512, 4096, 1024, 512, 1024, 1024
+FLOPS = 3 * 2 * K * H * S + 2 * H * N * PAIRS
+
+F32 = mybir.dt.float32
+BF16 = mybir.dt.bfloat16
+I32 = mybir.dt.int32
+U32 = mybir.dt.uint32
+U16 = mybir.dt.uint16
+U8 = mybir.dt.uint8
+FP8X4 = mybir.dt.float8_e4m3fn_x4
+FP4X4 = mybir.dt.float4_e2m1fn_x4
+MULT = mybir.AluOpType.mult
+COPY = mybir.ActivationFunctionType.Copy
+SIGMOID = mybir.ActivationFunctionType.Sigmoid
+
+P = 128
+PACK = 4
+GROUP = P * PACK
+BANK = 512
+LIST_ROWS = 16
+PIECES = ((512,), (256, 128, 128))
+ACC = 4
+DIFF = 1
+OUTB = 4
+PICK_BUFS = 6
+LAG = 2
+W4_ON_SCALAR = ((1, 0), (1, 1))
+RQ_BUFS = 3
+GATED_BUFS = 2
+Z_BUFS = 2
+WARM = True
+RAW_SLOTS = (0, 1, 0, 0, 1, 2)
+Z_ON_SCALAR = ("z00", "z01")
+Y_ON_SCALAR = (0, 1)
+ORDER = "r0 w0 r1 w1 r2 s0 h00 r3 s1 x00 r4 s2 h01 r5 s3 x01 r6 s4 r7 s5 g01 g00 s6 g02 g03 h02 s7 h03 p00 h10 h11 h12 h13 g13 g12 g11 g10 x10 x11 z00 p10 z10 p11 z11 y0 p12 z12 y1 y2"
+
+
+def tile_list_triple_pair_rerank_kernel(
+    tc, tab_words, tab_scales, offs, pos1, pos2, w1, w2_words, w2_scales, w3_words, w3_scales, rel, w4,
+    out_0, out_1, out_2,
+):
+    nc = tc.nc
+    with ExitStack() as ctx:
+        keep = ctx.enter_context(tc.tile_pool(name="keep", bufs=1))
+        ring = ctx.enter_context(tc.tile_pool(name="ring", bufs=2))
+        raws = ctx.enter_context(tc.tile_pool(name="raws", bufs=1))
+        psum = ctx.enter_context(tc.psum_pool(name="psum", bufs=1))
+
+        def ring_of(pool, count, shape, dtype, name):
+            tiles = [pool.tile(shape, dtype, name="%s%d" % (name, k), align_bytes=64) for k in range(count)]
+            return list(tiles)
+
+        def take(tiles):
+            tiles.append(tiles.pop(0))
+            return tiles[-1]
+
+        banks = [psum.tile([P, BANK], F32, name="bank%d" % k) for k in range(8)]
+        acc_banks = list(banks[:ACC])
+        diff_banks = list(banks[ACC : ACC + DIFF])
+        back_banks = list(banks[ACC + DIFF :])
+        out_banks = list(banks[8 - OUTB :])
+        r_tiles = ring_of(keep, RQ_BUFS, [P, S], F32, "r_neg")
+        q_tiles = ring_of(keep, RQ_BUFS, [P, S], F32, "q")
+        picks = ring_of(keep, PICK_BUFS, [P, PAIRS], F32, "pick")
+        z_tiles = ring_of(keep, Z_BUFS, [P, PACK * max(PIECES[0] + PIECES[1])], F32, "z32_")
+        z_wovens = ring_of(keep, 2, [P, PACK * max(PIECES[0] + PIECES[1])], BF16, "z_woven")
+        dealts = ring_of(keep, 2, [P, PACK * GROUP], BF16, "dealt")
+
+        offs_sb = keep.tile([P, S // LIST_ROWS], U16, name="offs_sb")
+        pos1_sb = keep.tile([P, PAIRS // LIST_ROWS], U16, name="pos1_sb")
+        pos2_sb = keep.tile([P, PAIRS // LIST_ROWS], U16, name="pos2_sb")
+        tab_w = raws.tile([P, T], U32, name="tab_w", align_bytes=64, offset=12288)
+        tab_s = raws.tile([P, T], U8, name="tab_s", align_bytes=64, offset=7168)
+        w2_w = keep.tile([P, 2 * H], U8, name="w2_w", align_bytes=64)
+        w3_w = keep.tile([P, H], U32, name="w3_w", align_bytes=64)
+        w2_s = keep.tile([P, H], U8, name="w2_s", align_bytes=64)
+        w3_s = keep.tile([P, H], U8, name="w3_s", align_bytes=64)
+        rel_sb = keep.tile([P, 2, PACK], F32, name="rel_sb")
+        ident = keep.tile([P, P], F32, name="ident")
+
+        def load_scales(queues, plane, rows):
+            for quad in range(4):
+                queues[quad].dma_start(
+                    out=plane[32 * quad : 32 * quad + 4, :].bitcast(I32),
+                    in_=rows[0, 4 * quad : 4 * quad + 4, :].bitcast(I32),
+                )
+
+        for plane in (tab_s, w3_s, w2_s):
+            nc.vector.memset(plane[:].bitcast(I32), 0)
+        load_scales([nc.scalar] * 4, tab_s, tab_scales)
+        nc.sync.dma_start(offs_sb[:], offs)
+        nc.sync.dma_start(pos2_sb[:], pos2)
+        nc.sync.dma_start(pos1_sb[:], pos1)
+        nc.sync.dma_start(out=tab_w[:].bitcast(I32), in_=tab_words[0].rearrange("p t i -> p (t i)").bitcast(I32))
+        nc.sync.dma_start(out=w3_w[:].bitcast(I32), in_=w3_words[0].rearrange("p e i -> p (e i)").bitcast(I32))
+        load_scales([nc.scalar, nc.gpsimd, nc.gpsimd, nc.gpsimd], w3_s, w3_scales)
+        nc.sync.dma_start(out=w2_w[:].bitcast(I32), in_=w2_words[0].bitcast(I32))
+        load_scales([nc.scalar] * 4, w2_s, w2_scales)
+
+        def load_weight(w, k_group, col_group):
+            raw = take(raw_halves)
+            rows = w[GROUP * k_group : GROUP * (k_group + 1), GROUP * col_group : GROUP * (col_group + 1)]
+            nc.sync.dma_start(out=raw, in_=rows.rearrange("(p j) c -> p j c", j=PACK))
+            return raw
+
+        def quantise_weight(w, k_group, col_group, name, on_scalar):
+            raw = load_weight(w, k_group, col_group)
+            dealt = take(dealts)
+            dst = dealt[:].rearrange("p (t m j) -> p m t j", t=PACK, j=PACK)
+            src = raw.rearrange("p j (m t) -> p m t j", t=PACK)
+            if on_scalar:
+                nc.scalar.copy(out=dst, in_=src)
+            else:
+                nc.vector.tensor_copy(out=dst, in_=src)
+            codes = keep.tile([P, GROUP], U32, name=name + "_codes", align_bytes=64)
+            scales = keep.tile([P, GROUP], U8, name=name + "_scales", align_bytes=64)
+            nc.vector.quantize_mx(out=codes[:].bitcast(FP8X4), scales=scales[:], in_=dealt[:])
+            return codes, scales
+
+        make_identity(nc, ident[:])
+        if WARM:
+            warm = keep.tile([P, 1], F32, name="warm")
+            nc.scalar.activation(out=warm[:], in_=ident[:, 0:1], func=SIGMOID)
+        nc.gpsimd.dma_start(out=rel_sb[:], in_=rel.rearrange("(g p t) -> p g t", g=2, t=PACK))
+        v_s = keep.tile([P, S], U8, name="v_s", align_bytes=64)
+        nc.vector.tensor_copy(v_s[:], tab_s[:].indirect(offs_sb[:]))
+        v_w = raws.tile([P, S], U32, name="v_w", align_bytes=64, offset=8192)
+        for half in range(2):
+            cols = slice(half * BANK // LIST_ROWS, (half + 1) * BANK // LIST_ROWS)
+            nc.vector.tensor_copy(v_w[:, half * BANK : (half + 1) * BANK], tab_w[:].indirect(offs_sb[:, cols]))
+        raw_tiles = [
+            raws.tile([P, PACK, GROUP], F32, name="raw%d" % k, align_bytes=64, offset=(0, 12288, 20480)[k]) for k in range(3)
+        ]
+        raw_halves = list([raw_tiles[k][:] for k in RAW_SLOTS])
+
+        def first_stage(dst, codes, scales, negate):
+            for half in range(2):
+                cols = slice(half * BANK, (half + 1) * BANK)
+                acc = take(acc_banks)
+                nc.tensor.matmul_mx(
+                    out=acc[:], lhsT=codes, lhsT_scale=scales,
+                    rhs=v_w[:, cols].bitcast(FP8X4), rhs_scale=v_s[:, cols], start=True, stop=True,
+                )
+                if negate:
+                    nc.scalar.activation(out=dst[:, cols], in_=acc[:], func=COPY, scale=-1.0)
+                else:
+                    nc.scalar.copy(out=dst[:, cols], in_=acc[:])
+
+        picked = {}
+
+        def pick_r_q(a):
+            cols = slice(P * a, P * (a + 1))
+            r_neg = take(r_tiles)
+            first_stage(r_neg, w3_w[:, cols].bitcast(FP8X4), w3_s[:, cols], True)
+            q = take(q_tiles)
+            first_stage(q, w2_w[:, 2 * P * a : 2 * P * (a + 1)].bitcast(FP4X4), w2_s[:, cols], False)
+            r_tail = take(picks)
+            nc.vector.tensor_copy(r_tail[:], r_neg[:].indirect(pos2_sb[:]))
+            q_head = take(picks)
+            nc.vector.tensor_copy(q_head[:], q[:].indirect(pos1_sb[:]))
+            picked[a] = (q_head, r_tail)
+
+        gate_t = [keep.tile([P, PACK, PACK, P], F32, name="gate_t%d" % g) for g in range(2)]
+
+        def sigmoid_of_difference(a):
+            diff = take(diff_banks)
+            for block in range(PAIRS // P):
+                cols = slice(P * block, P * (block + 1))
+                for first, part in zip((True, False), picked[a]):
+                    nc.tensor.matmul(
+                        diff[:, cols], lhsT=part[:, cols], rhs=ident[:], is_transpose=True, start=first, stop=not first
+                    )
+            g, local = divmod(a, PACK)
+            nc.scalar.activation(
+                out=gate_t[g][:, :, :, 32 * local : 32 * (local + 1)],
+                in_=diff[:].rearrange("p (b m t) -> p b t m", b=PACK, t=PACK),
+                func=SIGMOID,
+            )
+
+        gate = {}
+        h = {}
+
+        def turn_gate(g, t):
+            back = take(back_banks)
+            for block in range(PAIRS // P):
+                nc.tensor.transpose(back[:, P * block : P * (block + 1)], gate_t[g][:, block, t, :], ident[:])
+            gate[g, t] = keep.tile([P, PAIRS], F32, name="gate%d%d" % (g, t))
+            nc.scalar.activation(out=gate[g, t][:], in_=back[:], func=COPY, scale=rel_sb[:, g, t : t + 1])
+
+        def make_h(g, t):
+            codes, scales = w1_q[g]
+            cols = slice(P * t, P * (t + 1))
+            h[g, t] = keep.tile([P, S], F32, name="h%d%d" % (g, t))
+            first_stage(h[g, t], codes[:, cols].bitcast(FP8X4), scales[:, cols], False)
+
+        def pick_h(g, slots, z32, lo, hi):
+            lists = slice(lo // LIST_ROWS, hi // LIST_ROWS)
+            gated = {}
+            for t in slots:
+                gated[t] = take(picks)[:, : hi - lo]
+                nc.vector.tensor_tensor(gated[t], h[g, t][:].indirect(pos1_sb[:, lists]), gate[g, t][:, lo:hi], MULT)
+            for t in slots:
+                nc.vector.tensor_tensor(z32[:, t, :], h[g, t][:].indirect(pos2_sb[:, lists]), gated[t], MULT)
+
+        z_q = {}
+
+        def quantise_z(g, z32, lo, hi, on_scalar):
+            width = hi - lo
+            woven = take(z_wovens)[:, : width * PACK]
+            dst = woven.rearrange("p (c i t) -> p c t i", i=4, t=PACK)
+            src = z32.rearrange("p t (c i) -> p c t i", i=4)
+            if on_scalar:
+                nc.scalar.copy(out=dst, in_=src)
+            else:
+                nc.vector.tensor_copy(out=dst, in_=src)
+            codes = keep.tile([P, width], U32, name="z_codes%d_%d" % (g, lo), align_bytes=64)
+            scales = keep.tile([P, width], U8, name="z_scales%d_%d" % (g, lo), align_bytes=64)
+            nc.vector.quantize_mx(out=codes[:].bitcast(FP8X4), scales=scales[:], in_=woven)
+            for col in range(lo, hi, P):
+                z_q[g, col] = (codes[:, col - lo : col - lo + P].bitcast(FP8X4), scales[:, col - lo : col - lo + P])
+
+        y_scales = keep.tile([P, 2 * PAIRS], U8, name="y_scales", align_bytes=64)
+
+        def second_stage(lo, hi, weave_on_scalar):
+            width = hi - lo
+            y_codes = ring.tile([P, 2 * width], U32, name="y_codes", align_bytes=64, bufs=3)
+            for g in range(2):
+                y32 = ring.tile([P, PACK, width], F32, name="y32", bufs=4)
+                woven = ring.tile([P, width * PACK], BF16, name="y_woven", align_bytes=64, bufs=4)
+                for col in range(lo, hi, P):
+                    acc = take(out_banks)[:].rearrange("p (t m) -> p t m", t=PACK)
+                    for t in range(PACK):
+                        cols = slice(P * t, P * (t + 1))
+                        for a in range(2):
+                            codes, scales = w4_q[a, g]
+                            nc.tensor.matmul_mx(
+                                out=acc[:, t, :], lhsT=codes[:, cols].bitcast(FP8X4), lhsT_scale=scales[:, cols],
+                                rhs=z_q[a, col][0], rhs_scale=z_q[a, col][1], start=(a == 0), stop=(a == 1),
+                            )
+                    local = col - lo
+                    dst = woven[:, PACK * local : PACK * (local + P)].rearrange("p (m t) -> p m t", t=PACK)
+                    if weave_on_scalar:
+                        nc.scalar.copy(out=dst, in_=acc.rearrange("p t m -> p m t"))
+                    else:
+                        nc.vector.tensor_copy(out=dst, in_=acc.rearrange("p t m -> p m t"))
+                    nc.scalar.copy(out=y32[:, :, local : local + P], in_=acc)
+                rows = out_0[GROUP * g : GROUP * (g + 1), lo:hi].rearrange("(p t) i -> p t i", t=PACK)
+                nc.sync.dma_start(out=rows, in_=y32[:])
+                nc.vector.quantize_mx(
+                    out=y_codes[:, g * width : (g + 1) * width].bitcast(FP8X4), scales=y_scales[:, PAIRS * g + lo : PAIRS * g + hi], in_=woven[:]
+                )
+            words = out_1.rearrange("g p m t -> p g (m t)").bitcast(I32)
+            nc.sync.dma_start(out=words[:, :, lo:hi], in_=y_codes[:].bitcast(I32).rearrange("p (g m) -> p g m", g=2))
+
+        w1_q = {}
+        w4_q = {}
+        def w4_part(a, g):
+            w4_q[a, g] = quantise_weight(w4, a, g, "w4_%d%d" % (a, g), (a, g) in W4_ON_SCALAR)
+
+        z_of = {}
+
+        def products(g, lo, hi):
+            z32 = take(z_tiles)[:, : PACK * (hi - lo)].rearrange("p (t i) -> p t i", t=PACK)
+            pick_h(g, (0, 1), z32, lo, hi)
+            pick_h(g, (2, 3), z32, lo, hi)
+            z_of[g, lo] = z32
+
+        for step in ORDER.split():
+            kind, num = step[0], [int(c) for c in step[1:]]
+            if kind == "r":
+                pick_r_q(num[0])
+            elif kind == "s":
+                sigmoid_of_difference(num[0])
+            elif kind == "w":
+                w1_q[num[0]] = quantise_weight(w1, 0, num[0], "w1_%d" % num[0], False)
+            elif kind == "x":
+                w4_part(num[0], num[1])
+            elif kind == "h":
+                make_h(num[0], num[1])
+            elif kind == "g":
+                turn_gate(num[0], num[1])
+            elif kind == "p":
+                lo = sum(PIECES[num[0]][: num[1]])
+                products(num[0], lo, lo + PIECES[num[0]][num[1]])
+            elif kind == "z":
+                lo = sum(PIECES[num[0]][: num[1]])
+                quantise_z(num[0], z_of[num[0], lo], lo, lo + PIECES[num[0]][num[1]], step in Z_ON_SCALAR)
+            elif kind == "y":
+                lo = sum(PIECES[1][: num[0]])
+                second_stage(lo, lo + PIECES[1][num[0]], num[0] in Y_ON_SCALAR)
+        planes = y_scales[:].bitcast(I32).rearrange("p (g m) -> p g m", g=2)
+        for quad in range(4):
+            nc.sync.dma_start(
+                out=out_2[:, 4 * quad : 4 * quad + 4, :].rearrange("g r m -> r g m").bitcast(I32),
+                in_=planes[32 * quad : 32 * quad + 4, :, :],
+            )

@@ -1,7 +1,6 @@
 from contextlib import ExitStack
 
 import concourse.mybir as mybir
-from concourse.masks import make_identity
 
 K, T, S, PAIRS, H, N = 512, 4096, 1024, 512, 1024, 1024
 FLOPS = 3 * 2 * K * H * S + 2 * H * N * PAIRS
@@ -15,6 +14,7 @@ U8 = mybir.dt.uint8
 FP8X4 = mybir.dt.float8_e4m3fn_x4
 FP4X4 = mybir.dt.float4_e2m1fn_x4
 MULT = mybir.AluOpType.mult
+SUBTRACT = mybir.AluOpType.subtract
 COPY = mybir.ActivationFunctionType.Copy
 SIGMOID = mybir.ActivationFunctionType.Sigmoid
 
@@ -23,21 +23,18 @@ PACK = 4
 GROUP = P * PACK
 BANK = 512
 LIST_ROWS = 16
-PIECES = ((512,), (256, 128, 128))
-ACC = 4
-DIFF = 1
-OUTB = 4
-PICK_BUFS = 6
-LAG = 2
-W4_ON_SCALAR = ((1, 0), (1, 1))
+PIECES = ((256, 128, 128), (256, 128, 128))
+ACC = 8
+PICK_BUFS = 2
+TAIL_BUFS = 3
+W4_ON_SCALAR = ((0,1),(1,0),(1,1))
 RQ_BUFS = 3
-GATED_BUFS = 2
 Z_BUFS = 2
 WARM = True
-RAW_SLOTS = (0, 1, 0, 0, 1, 2)
-Z_ON_SCALAR = ("z00", "z01")
+RAW_SLOTS = (0,1,0,2,1,0)
+Z_ON_SCALAR = ("z00","z01")
 Y_ON_SCALAR = (0, 1)
-ORDER = "r0 w0 r1 w1 r2 s0 h00 r3 s1 x00 r4 s2 h01 r5 s3 x01 r6 s4 r7 s5 g01 g00 s6 g02 g03 h02 s7 h03 p00 h10 h11 h12 h13 g13 g12 g11 g10 x10 x11 z00 p10 z10 p11 z11 y0 p12 z12 y1 y2"
+ORDER = "r0 r1 q0 w0 r2 q1 r3 h001 s0 q2 e0 w1 r4 s1 q3 e1 r5 h023 s2 q4 e2 x00 r6 s3 q5 e3 p00 r7 s4 q6 e4 h101 s5 q7 e5 s6 h123 e6 s7 e7 z00 x01 x10 x11 p10 z10 p01 z01 a0 y0 p11 z11 p02 z02 a1 y1 a2 p12 z12 y2"
 
 
 def tile_list_triple_pair_rerank_kernel(
@@ -61,12 +58,11 @@ def tile_list_triple_pair_rerank_kernel(
 
         banks = [psum.tile([P, BANK], F32, name="bank%d" % k) for k in range(8)]
         acc_banks = list(banks[:ACC])
-        diff_banks = list(banks[ACC : ACC + DIFF])
-        back_banks = list(banks[ACC + DIFF :])
-        out_banks = list(banks[8 - OUTB :])
         r_tiles = ring_of(keep, RQ_BUFS, [P, S], F32, "r_neg")
         q_tiles = ring_of(keep, RQ_BUFS, [P, S], F32, "q")
         picks = ring_of(keep, PICK_BUFS, [P, PAIRS], F32, "pick")
+        gateds = ring_of(keep, 2, [P, PAIRS], F32, "gated")
+        tails = ring_of(keep, TAIL_BUFS, [P, PAIRS], F32, "tail")
         z_tiles = ring_of(keep, Z_BUFS, [P, PACK * max(PIECES[0] + PIECES[1])], F32, "z32_")
         z_wovens = ring_of(keep, 2, [P, PACK * max(PIECES[0] + PIECES[1])], BF16, "z_woven")
         dealts = ring_of(keep, 2, [P, PACK * GROUP], BF16, "dealt")
@@ -76,31 +72,43 @@ def tile_list_triple_pair_rerank_kernel(
         pos2_sb = keep.tile([P, PAIRS // LIST_ROWS], U16, name="pos2_sb")
         tab_w = raws.tile([P, T], U32, name="tab_w", align_bytes=64, offset=12288)
         tab_s = raws.tile([P, T], U8, name="tab_s", align_bytes=64, offset=7168)
+        w2_in = keep.tile([P, 2 * H], U8, name="w2_in", align_bytes=64)
+        w3_in = keep.tile([P, H], I32, name="w3_in", align_bytes=64)
+        ws_in = keep.tile([P, H], U8, name="ws_in", align_bytes=64)
         w2_w = keep.tile([P, 2 * H], U8, name="w2_w", align_bytes=64)
-        w3_w = keep.tile([P, H], U32, name="w3_w", align_bytes=64)
-        w2_s = keep.tile([P, H], U8, name="w2_s", align_bytes=64)
-        w3_s = keep.tile([P, H], U8, name="w3_s", align_bytes=64)
+        w3_w = keep.tile([P, H], I32, name="w3_w", align_bytes=64)
+        w_s = keep.tile([P, H], U8, name="w_s", align_bytes=64)
         rel_sb = keep.tile([P, 2, PACK], F32, name="rel_sb")
-        ident = keep.tile([P, P], F32, name="ident")
 
-        def load_scales(queues, plane, rows):
+        def load_scales(queues, plane, first_row, rows):
             for quad in range(4):
                 queues[quad].dma_start(
-                    out=plane[32 * quad : 32 * quad + 4, :].bitcast(I32),
+                    out=plane[32 * quad + first_row : 32 * quad + first_row + 4, :].bitcast(I32),
                     in_=rows[0, 4 * quad : 4 * quad + 4, :].bitcast(I32),
                 )
 
-        for plane in (tab_s, w3_s, w2_s):
+        for plane in (tab_s, ws_in):
             nc.vector.memset(plane[:].bitcast(I32), 0)
-        load_scales([nc.scalar] * 4, tab_s, tab_scales)
+        load_scales([nc.scalar] * 4, tab_s, 0, tab_scales)
         nc.sync.dma_start(offs_sb[:], offs)
         nc.sync.dma_start(pos2_sb[:], pos2)
         nc.sync.dma_start(pos1_sb[:], pos1)
+        nc.sync.dma_start(out=w3_in[:], in_=w3_words[0].rearrange("p e i -> p (e i)").bitcast(I32))
+        nc.sync.dma_start(out=w2_in[:].bitcast(I32), in_=w2_words[0].bitcast(I32))
         nc.sync.dma_start(out=tab_w[:].bitcast(I32), in_=tab_words[0].rearrange("p t i -> p (t i)").bitcast(I32))
-        nc.sync.dma_start(out=w3_w[:].bitcast(I32), in_=w3_words[0].rearrange("p e i -> p (e i)").bitcast(I32))
-        load_scales([nc.scalar, nc.gpsimd, nc.gpsimd, nc.gpsimd], w3_s, w3_scales)
-        nc.sync.dma_start(out=w2_w[:].bitcast(I32), in_=w2_words[0].bitcast(I32))
-        load_scales([nc.scalar] * 4, w2_s, w2_scales)
+        load_scales([nc.scalar, nc.scalar, nc.scalar, nc.gpsimd], ws_in, 4, w3_scales)
+        load_scales([nc.gpsimd] * 4, ws_in, 0, w2_scales)
+        nc.gpsimd.dma_start(out=rel_sb[:], in_=rel.rearrange("(g p t) -> p g t", g=2, t=PACK))
+        nc.vector.tensor_copy(
+            out=w3_w[:].rearrange("p (g t m) -> p g m t", g=2, t=PACK), in_=w3_in[:].rearrange("p (g m t) -> p g m t", g=2, t=PACK)
+        )
+        nc.vector.tensor_copy(
+            out=w2_w[:].rearrange("p (g t m b) -> p g m t b", g=2, t=PACK, b=2),
+            in_=w2_in[:].rearrange("p (g m t b) -> p g m t b", g=2, t=PACK, b=2),
+        )
+        nc.vector.tensor_copy(
+            out=w_s[:].rearrange("p (g t m) -> p g m t", g=2, t=PACK), in_=ws_in[:].rearrange("p (g m t) -> p g m t", g=2, t=PACK)
+        )
 
         def load_weight(w, k_group, col_group):
             raw = take(raw_halves)
@@ -122,11 +130,9 @@ def tile_list_triple_pair_rerank_kernel(
             nc.vector.quantize_mx(out=codes[:].bitcast(FP8X4), scales=scales[:], in_=dealt[:])
             return codes, scales
 
-        make_identity(nc, ident[:])
         if WARM:
             warm = keep.tile([P, 1], F32, name="warm")
-            nc.scalar.activation(out=warm[:], in_=ident[:, 0:1], func=SIGMOID)
-        nc.gpsimd.dma_start(out=rel_sb[:], in_=rel.rearrange("(g p t) -> p g t", g=2, t=PACK))
+            nc.scalar.activation(out=warm[:], in_=rel_sb[:, 0, 0:1], func=SIGMOID)
         v_s = keep.tile([P, S], U8, name="v_s", align_bytes=64)
         nc.vector.tensor_copy(v_s[:], tab_s[:].indirect(offs_sb[:]))
         v_w = raws.tile([P, S], U32, name="v_w", align_bytes=64, offset=8192)
@@ -138,71 +144,63 @@ def tile_list_triple_pair_rerank_kernel(
         ]
         raw_halves = list([raw_tiles[k][:] for k in RAW_SLOTS])
 
-        def first_stage(dst, codes, scales, negate):
-            for half in range(2):
+        def first_stage(jobs, halves=(0, 1)):
+            for half in halves:
                 cols = slice(half * BANK, (half + 1) * BANK)
-                acc = take(acc_banks)
-                nc.tensor.matmul_mx(
-                    out=acc[:], lhsT=codes, lhsT_scale=scales,
-                    rhs=v_w[:, cols].bitcast(FP8X4), rhs_scale=v_s[:, cols], start=True, stop=True,
-                )
-                if negate:
-                    nc.scalar.activation(out=dst[:, cols], in_=acc[:], func=COPY, scale=-1.0)
-                else:
+                for dst, codes, scales in jobs:
+                    acc = take(acc_banks)
+                    nc.tensor.matmul_mx(
+                        out=acc[:], lhsT=codes, lhsT_scale=scales,
+                        rhs=v_w[:, cols].bitcast(FP8X4), rhs_scale=v_s[:, cols], start=True, stop=True,
+                    )
                     nc.scalar.copy(out=dst[:, cols], in_=acc[:])
 
-        picked = {}
-
-        def pick_r_q(a):
-            cols = slice(P * a, P * (a + 1))
-            r_neg = take(r_tiles)
-            first_stage(r_neg, w3_w[:, cols].bitcast(FP8X4), w3_s[:, cols], True)
-            q = take(q_tiles)
-            first_stage(q, w2_w[:, 2 * P * a : 2 * P * (a + 1)].bitcast(FP4X4), w2_s[:, cols], False)
-            r_tail = take(picks)
-            nc.vector.tensor_copy(r_tail[:], r_neg[:].indirect(pos2_sb[:]))
-            q_head = take(picks)
-            nc.vector.tensor_copy(q_head[:], q[:].indirect(pos1_sb[:]))
-            picked[a] = (q_head, r_tail)
-
-        gate_t = [keep.tile([P, PACK, PACK, P], F32, name="gate_t%d" % g) for g in range(2)]
-
-        def sigmoid_of_difference(a):
-            diff = take(diff_banks)
-            for block in range(PAIRS // P):
-                cols = slice(P * block, P * (block + 1))
-                for first, part in zip((True, False), picked[a]):
-                    nc.tensor.matmul(
-                        diff[:, cols], lhsT=part[:, cols], rhs=ident[:], is_transpose=True, start=first, stop=not first
-                    )
-            g, local = divmod(a, PACK)
-            nc.scalar.activation(
-                out=gate_t[g][:, :, :, 32 * local : 32 * (local + 1)],
-                in_=diff[:].rearrange("p (b m t) -> p b t m", b=PACK, t=PACK),
-                func=SIGMOID,
-            )
-
+        r_tail = {}
+        diff = {}
         gate = {}
         h = {}
 
-        def turn_gate(g, t):
-            back = take(back_banks)
-            for block in range(PAIRS // P):
-                nc.tensor.transpose(back[:, P * block : P * (block + 1)], gate_t[g][:, block, t, :], ident[:])
-            gate[g, t] = keep.tile([P, PAIRS], F32, name="gate%d%d" % (g, t))
-            nc.scalar.activation(out=gate[g, t][:], in_=back[:], func=COPY, scale=rel_sb[:, g, t : t + 1])
+        def pick_r(a):
+            cols = slice(P * a, P * (a + 1))
+            r = take(r_tiles)
+            first_stage([(r, w3_w[:, cols].bitcast(FP8X4), w_s[4:P, cols])])
+            r_tail[a] = take(tails)
+            nc.vector.tensor_copy(r_tail[a][:], r[:].indirect(pos2_sb[:]))
 
-        def make_h(g, t):
+        q_of = {}
+
+        def pick_q(a, halves):
+            if 0 in halves:
+                q_of[a] = take(q_tiles)
+            q = q_of[a]
+            first_stage([(q, w2_w[:, 2 * P * a : 2 * P * (a + 1)].bitcast(FP4X4), w_s[:, P * a : P * (a + 1)])], halves)
+            if 1 in halves:
+                diff[a] = take(picks)
+                nc.vector.tensor_tensor(diff[a][:], q[:].indirect(pos1_sb[:]), r_tail[a][:], SUBTRACT)
+
+        def sigmoid_of_difference(a):
+            g, t = divmod(a, PACK)
+            gate[g, t] = keep.tile([P, PAIRS], F32, name="gate%d%d" % (g, t))
+            nc.scalar.activation(out=gate[g, t][:], in_=diff[a][:], func=SIGMOID)
+
+        def weigh_gate(a):
+            g, t = divmod(a, PACK)
+            nc.scalar.activation(out=gate[g, t][:], in_=gate[g, t][:], func=COPY, scale=rel_sb[:, g, t : t + 1])
+
+        def make_h(g, slots):
             codes, scales = w1_q[g]
-            cols = slice(P * t, P * (t + 1))
-            h[g, t] = keep.tile([P, S], F32, name="h%d%d" % (g, t))
-            first_stage(h[g, t], codes[:, cols].bitcast(FP8X4), scales[:, cols], False)
+            jobs = []
+            for t in slots:
+                cols = slice(P * t, P * (t + 1))
+                h[g, t] = keep.tile([P, S], F32, name="h%d%d" % (g, t))
+                jobs.append((h[g, t], codes[:, cols].bitcast(FP8X4), scales[:, cols]))
+            first_stage(jobs)
 
         def pick_h(g, slots, z32, lo, hi):
             lists = slice(lo // LIST_ROWS, hi // LIST_ROWS)
             gated = {}
             for t in slots:
-                gated[t] = take(picks)[:, : hi - lo]
+                gated[t] = take(gateds)[:, : hi - lo]
                 nc.vector.tensor_tensor(gated[t], h[g, t][:].indirect(pos1_sb[:, lists]), gate[g, t][:, lo:hi], MULT)
             for t in slots:
                 nc.vector.tensor_tensor(z32[:, t, :], h[g, t][:].indirect(pos2_sb[:, lists]), gated[t], MULT)
@@ -226,6 +224,18 @@ def tile_list_triple_pair_rerank_kernel(
 
         y_scales = keep.tile([P, 2 * PAIRS], U8, name="y_scales", align_bytes=64)
 
+        def second_passes(a, g, col):
+            acc = banks[2 * (col // P) + g][:].rearrange("p (t m) -> p t m", t=PACK)
+            codes, scales = w4_q[a, g]
+            for t in range(PACK):
+                cols = slice(P * t, P * (t + 1))
+                nc.tensor.matmul_mx(
+                    out=acc[:, t, :], lhsT=codes[:, cols].bitcast(FP8X4), lhsT_scale=scales[:, cols],
+                    rhs=z_q[a, col][0], rhs_scale=z_q[a, col][1],
+                    start=(a == 0 and t == 0), stop=(a == 1 and t == PACK - 1),
+                )
+            return acc
+
         def second_stage(lo, hi, weave_on_scalar):
             width = hi - lo
             y_codes = ring.tile([P, 2 * width], U32, name="y_codes", align_bytes=64, bufs=3)
@@ -233,15 +243,7 @@ def tile_list_triple_pair_rerank_kernel(
                 y32 = ring.tile([P, PACK, width], F32, name="y32", bufs=4)
                 woven = ring.tile([P, width * PACK], BF16, name="y_woven", align_bytes=64, bufs=4)
                 for col in range(lo, hi, P):
-                    acc = take(out_banks)[:].rearrange("p (t m) -> p t m", t=PACK)
-                    for t in range(PACK):
-                        cols = slice(P * t, P * (t + 1))
-                        for a in range(2):
-                            codes, scales = w4_q[a, g]
-                            nc.tensor.matmul_mx(
-                                out=acc[:, t, :], lhsT=codes[:, cols].bitcast(FP8X4), lhsT_scale=scales[:, cols],
-                                rhs=z_q[a, col][0], rhs_scale=z_q[a, col][1], start=(a == 0), stop=(a == 1),
-                            )
+                    acc = second_passes(1, g, col)
                     local = col - lo
                     dst = woven[:, PACK * local : PACK * (local + P)].rearrange("p (m t) -> p m t", t=PACK)
                     if weave_on_scalar:
@@ -255,7 +257,7 @@ def tile_list_triple_pair_rerank_kernel(
                     out=y_codes[:, g * width : (g + 1) * width].bitcast(FP8X4), scales=y_scales[:, PAIRS * g + lo : PAIRS * g + hi], in_=woven[:]
                 )
             words = out_1.rearrange("g p m t -> p g (m t)").bitcast(I32)
-            nc.sync.dma_start(out=words[:, :, lo:hi], in_=y_codes[:].bitcast(I32).rearrange("p (g m) -> p g m", g=2))
+            (nc.sync if hi == PAIRS else nc.gpsimd).dma_start(out=words[:, :, lo:hi], in_=y_codes[:].bitcast(I32).rearrange("p (g m) -> p g m", g=2))
 
         w1_q = {}
         w4_q = {}
@@ -263,6 +265,7 @@ def tile_list_triple_pair_rerank_kernel(
             w4_q[a, g] = quantise_weight(w4, a, g, "w4_%d%d" % (a, g), (a, g) in W4_ON_SCALAR)
 
         z_of = {}
+        gated0 = {}
 
         def products(g, lo, hi):
             z32 = take(z_tiles)[:, : PACK * (hi - lo)].rearrange("p (t i) -> p t i", t=PACK)
@@ -273,7 +276,23 @@ def tile_list_triple_pair_rerank_kernel(
         for step in ORDER.split():
             kind, num = step[0], [int(c) for c in step[1:]]
             if kind == "r":
-                pick_r_q(num[0])
+                pick_r(num[0])
+            elif kind == "q":
+                pick_q(num[0], num[1:] or [0, 1])
+            elif kind == "t":
+                gated0[num[0]] = take(gateds)
+                nc.vector.tensor_tensor(gated0[num[0]][:], h[0, num[0]][:].indirect(pos1_sb[:]), gate[0, num[0]][:], MULT)
+            elif kind == "u":
+                if num[0] == 0:
+                    z_of[0, 0] = take(z_tiles)[:].rearrange("p (t i) -> p t i", t=PACK)
+                nc.vector.tensor_tensor(z_of[0, 0][:, num[0], :], h[0, num[0]][:].indirect(pos2_sb[:]), gated0[num[0]][:], MULT)
+            elif kind == "e":
+                weigh_gate(num[0])
+            elif kind == "a":
+                lo = sum(PIECES[1][: num[0]])
+                for g in range(2):
+                    for col in range(lo, lo + PIECES[1][num[0]], P):
+                        second_passes(0, g, col)
             elif kind == "s":
                 sigmoid_of_difference(num[0])
             elif kind == "w":
@@ -281,9 +300,7 @@ def tile_list_triple_pair_rerank_kernel(
             elif kind == "x":
                 w4_part(num[0], num[1])
             elif kind == "h":
-                make_h(num[0], num[1])
-            elif kind == "g":
-                turn_gate(num[0], num[1])
+                make_h(num[0], num[1:])
             elif kind == "p":
                 lo = sum(PIECES[num[0]][: num[1]])
                 products(num[0], lo, lo + PIECES[num[0]][num[1]])
@@ -295,7 +312,7 @@ def tile_list_triple_pair_rerank_kernel(
                 second_stage(lo, lo + PIECES[1][num[0]], num[0] in Y_ON_SCALAR)
         planes = y_scales[:].bitcast(I32).rearrange("p (g m) -> p g m", g=2)
         for quad in range(4):
-            nc.sync.dma_start(
+            (nc.sync if quad < 2 else nc.scalar).dma_start(
                 out=out_2[:, 4 * quad : 4 * quad + 4, :].rearrange("g r m -> r g m").bitcast(I32),
                 in_=planes[32 * quad : 32 * quad + 4, :, :],
             )

@@ -21,20 +21,27 @@ SIGMOID = mybir.ActivationFunctionType.Sigmoid
 P = 128
 PACK = 4
 GROUP = P * PACK
+GROUPS = 2
+TILES = H // P
 BANK = 512
+BANKS = 8
 LIST_ROWS = 16
-PIECES = ((256, 128, 128), (256, 128, 128))
-ACC = 8
-PICK_BUFS = 2
-TAIL_BUFS = 3
-W4_ON_SCALAR = ((0,1),(1,0),(1,1))
-RQ_BUFS = 3
-Z_BUFS = 2
-WARM = True
-RAW_SLOTS = (0,1,0,2,1,0)
-Z_ON_SCALAR = ("z00","z01")
-Y_ON_SCALAR = (0, 1)
-ORDER = "r0 r1 q0 w0 r2 q1 r3 h001 s0 q2 e0 w1 r4 s1 q3 e1 r5 h023 s2 q4 e2 x00 r6 s3 q5 e3 p00 r7 s4 q6 e4 h101 s5 q7 e5 s6 h123 e6 s7 e7 z00 x01 x10 x11 p10 z10 p01 z01 a0 y0 p11 z11 p02 z02 a1 y1 a2 p12 z12 y2"
+LINE = 4
+ALIGN = 64
+
+PIECES = (256, 128, 128)
+GATE_LAG = 2
+BLOCKS_ON_VECTOR = 3
+ROW_DEPTH = 3
+TAIL_DEPTH = 3
+PAIR_DEPTH = 2
+
+STAGE_BYTES = PACK * GROUP * 4
+AT_STAGE_0 = 0
+AT_V_WORDS = STAGE_BYTES
+AT_TAB_SCALES = AT_V_WORDS - T // 4
+AT_TAB_WORDS = AT_V_WORDS + 4 * S
+AT_STAGE_1 = AT_TAB_WORDS
 
 
 def tile_list_triple_pair_rerank_kernel(
@@ -44,275 +51,266 @@ def tile_list_triple_pair_rerank_kernel(
     nc = tc.nc
     with ExitStack() as ctx:
         keep = ctx.enter_context(tc.tile_pool(name="keep", bufs=1))
-        ring = ctx.enter_context(tc.tile_pool(name="ring", bufs=2))
-        raws = ctx.enter_context(tc.tile_pool(name="raws", bufs=1))
+        results = ctx.enter_context(tc.tile_pool(name="results", bufs=4))
+        shared = ctx.enter_context(tc.tile_pool(name="shared", bufs=1))
         psum = ctx.enter_context(tc.psum_pool(name="psum", bufs=1))
 
-        def ring_of(pool, count, shape, dtype, name):
-            tiles = [pool.tile(shape, dtype, name="%s%d" % (name, k), align_bytes=64) for k in range(count)]
-            return list(tiles)
+        def ring_of(depth, columns, dtype, name):
+            return [keep.tile([P, columns], dtype, name="%s%d" % (name, k), align_bytes=ALIGN) for k in range(depth)]
 
-        def take(tiles):
-            tiles.append(tiles.pop(0))
-            return tiles[-1]
+        def take(ring):
+            ring.append(ring.pop(0))
+            return ring[-1]
 
-        banks = [psum.tile([P, BANK], F32, name="bank%d" % k) for k in range(8)]
-        acc_banks = list(banks[:ACC])
-        r_tiles = ring_of(keep, RQ_BUFS, [P, S], F32, "r_neg")
-        q_tiles = ring_of(keep, RQ_BUFS, [P, S], F32, "q")
-        picks = ring_of(keep, PICK_BUFS, [P, PAIRS], F32, "pick")
-        gateds = ring_of(keep, 2, [P, PAIRS], F32, "gated")
-        tails = ring_of(keep, TAIL_BUFS, [P, PAIRS], F32, "tail")
-        z_tiles = ring_of(keep, Z_BUFS, [P, PACK * max(PIECES[0] + PIECES[1])], F32, "z32_")
-        z_wovens = ring_of(keep, 2, [P, PACK * max(PIECES[0] + PIECES[1])], BF16, "z_woven")
-        dealts = ring_of(keep, 2, [P, PACK * GROUP], BF16, "dealt")
+        banks = [psum.tile([P, BANK], F32, name="bank%d" % k) for k in range(BANKS)]
+        bank_ring = list(banks)
+        r_ring = ring_of(ROW_DEPTH, S, F32, "r")
+        q_ring = ring_of(ROW_DEPTH, S, F32, "q")
+        diff_ring = ring_of(PAIR_DEPTH, PAIRS, F32, "diff")
+        gated_ring = ring_of(PAIR_DEPTH, PAIRS, F32, "gated")
+        tail_ring = ring_of(TAIL_DEPTH, PAIRS, F32, "r_tail")
+        z_ring = ring_of(PAIR_DEPTH, PACK * PAIRS, F32, "z")
+        z_woven_ring = ring_of(PAIR_DEPTH, PACK * PAIRS, BF16, "z_woven")
+        dealt_ring = ring_of(PAIR_DEPTH, PACK * GROUP, BF16, "dealt")
 
         offs_sb = keep.tile([P, S // LIST_ROWS], U16, name="offs_sb")
         pos1_sb = keep.tile([P, PAIRS // LIST_ROWS], U16, name="pos1_sb")
         pos2_sb = keep.tile([P, PAIRS // LIST_ROWS], U16, name="pos2_sb")
-        tab_w = raws.tile([P, T], U32, name="tab_w", align_bytes=64, offset=12288)
-        tab_s = raws.tile([P, T], U8, name="tab_s", align_bytes=64, offset=7168)
-        w2_in = keep.tile([P, 2 * H], U8, name="w2_in", align_bytes=64)
-        w3_in = keep.tile([P, H], I32, name="w3_in", align_bytes=64)
-        ws_in = keep.tile([P, H], U8, name="ws_in", align_bytes=64)
-        w2_w = keep.tile([P, 2 * H], U8, name="w2_w", align_bytes=64)
-        w3_w = keep.tile([P, H], I32, name="w3_w", align_bytes=64)
-        w_s = keep.tile([P, H], U8, name="w_s", align_bytes=64)
-        rel_sb = keep.tile([P, 2, PACK], F32, name="rel_sb")
+        tab_w = shared.tile([P, T], U32, name="tab_w", align_bytes=ALIGN, offset=AT_TAB_WORDS)
+        tab_s = shared.tile([P, T], U8, name="tab_s", align_bytes=ALIGN, offset=AT_TAB_SCALES)
+        w2_in = keep.tile([P, 2 * H], U8, name="w2_in", align_bytes=ALIGN)
+        w3_in = keep.tile([P, H], I32, name="w3_in", align_bytes=ALIGN)
+        s3_in = keep.tile([P, H], U8, name="s3_in", align_bytes=ALIGN)
+        s2_in = keep.tile([P, H], U8, name="s2_in", align_bytes=ALIGN)
+        w2_w = keep.tile([P, 2 * H], U8, name="w2_w", align_bytes=ALIGN)
+        w3_w = keep.tile([P, H], I32, name="w3_w", align_bytes=ALIGN)
+        w3_s = keep.tile([P, H], U8, name="w3_s", align_bytes=ALIGN)
+        w2_s = keep.tile([P, H], U8, name="w2_s", align_bytes=ALIGN)
+        rel_sb = keep.tile([P, GROUPS, PACK], F32, name="rel_sb")
 
-        def load_scales(queues, plane, first_row, rows):
-            for quad in range(4):
-                queues[quad].dma_start(
-                    out=plane[32 * quad + first_row : 32 * quad + first_row + 4, :].bitcast(I32),
-                    in_=rows[0, 4 * quad : 4 * quad + 4, :].bitcast(I32),
+        def load_scales(queues, plane, rows):
+            for u, queue in enumerate(queues):
+                queue.dma_start(
+                    out=plane[32 * u : 32 * u + 4, :].bitcast(I32), in_=rows[0, 4 * u : 4 * u + 4, :].bitcast(I32)
                 )
 
-        for plane in (tab_s, ws_in):
+        for plane in (tab_s, s3_in, s2_in):
             nc.vector.memset(plane[:].bitcast(I32), 0)
-        load_scales([nc.scalar] * 4, tab_s, 0, tab_scales)
+        load_scales([nc.scalar] * 4, tab_s, tab_scales)
         nc.sync.dma_start(offs_sb[:], offs)
         nc.sync.dma_start(pos2_sb[:], pos2)
         nc.sync.dma_start(pos1_sb[:], pos1)
         nc.sync.dma_start(out=w3_in[:], in_=w3_words[0].rearrange("p e i -> p (e i)").bitcast(I32))
         nc.sync.dma_start(out=w2_in[:].bitcast(I32), in_=w2_words[0].bitcast(I32))
         nc.sync.dma_start(out=tab_w[:].bitcast(I32), in_=tab_words[0].rearrange("p t i -> p (t i)").bitcast(I32))
-        load_scales([nc.scalar, nc.scalar, nc.scalar, nc.gpsimd], ws_in, 4, w3_scales)
-        load_scales([nc.gpsimd] * 4, ws_in, 0, w2_scales)
-        nc.gpsimd.dma_start(out=rel_sb[:], in_=rel.rearrange("(g p t) -> p g t", g=2, t=PACK))
-        nc.vector.tensor_copy(
-            out=w3_w[:].rearrange("p (g t m) -> p g m t", g=2, t=PACK), in_=w3_in[:].rearrange("p (g m t) -> p g m t", g=2, t=PACK)
-        )
-        nc.vector.tensor_copy(
-            out=w2_w[:].rearrange("p (g t m b) -> p g m t b", g=2, t=PACK, b=2),
-            in_=w2_in[:].rearrange("p (g m t b) -> p g m t b", g=2, t=PACK, b=2),
-        )
-        nc.vector.tensor_copy(
-            out=w_s[:].rearrange("p (g t m) -> p g m t", g=2, t=PACK), in_=ws_in[:].rearrange("p (g m t) -> p g m t", g=2, t=PACK)
-        )
+        load_scales([nc.scalar] * 3 + [nc.gpsimd], s3_in, w3_scales)
+        load_scales([nc.scalar] * 4, s2_in, w2_scales)
+        nc.gpsimd.dma_start(out=rel_sb[:], in_=rel.rearrange("(g p t) -> p g t", g=GROUPS, t=PACK))
 
-        def load_weight(w, k_group, col_group):
-            raw = take(raw_halves)
-            rows = w[GROUP * k_group : GROUP * (k_group + 1), GROUP * col_group : GROUP * (col_group + 1)]
-            nc.sync.dma_start(out=raw, in_=rows.rearrange("(p j) c -> p j c", j=PACK))
-            return raw
+        def deal_columns(dst, src):
+            nc.vector.tensor_copy(
+                out=dst[:].rearrange("p (g t m) -> p g m t", g=GROUPS, t=PACK),
+                in_=src[:].rearrange("p (g m t) -> p g m t", g=GROUPS, t=PACK),
+            )
 
-        def quantise_weight(w, k_group, col_group, name, on_scalar):
-            raw = load_weight(w, k_group, col_group)
-            dealt = take(dealts)
-            dst = dealt[:].rearrange("p (t m j) -> p m t j", t=PACK, j=PACK)
-            src = raw.rearrange("p j (m t) -> p m t j", t=PACK)
-            if on_scalar:
-                nc.scalar.copy(out=dst, in_=src)
+        deal_columns(w3_w, w3_in)
+        nc.vector.tensor_copy(
+            out=w2_w[:].rearrange("p (g t m b) -> p g m t b", g=GROUPS, t=PACK, b=2),
+            in_=w2_in[:].rearrange("p (g m t b) -> p g m t b", g=GROUPS, t=PACK, b=2),
+        )
+        deal_columns(w3_s, s3_in)
+        deal_columns(w2_s, s2_in)
+
+        v_s = keep.tile([P, S], U8, name="v_s", align_bytes=ALIGN)
+        nc.vector.tensor_copy(v_s[:], tab_s[:].indirect(offs_sb[:]))
+        v_w = shared.tile([P, S], U32, name="v_w", align_bytes=ALIGN, offset=AT_V_WORDS)
+        for lo in range(0, S, BANK):
+            entries = offs_sb[:, lo // LIST_ROWS : (lo + BANK) // LIST_ROWS]
+            nc.vector.tensor_copy(v_w[:, lo : lo + BANK], tab_w[:].indirect(entries))
+        stage_ring = [
+            shared.tile([P, PACK, GROUP], F32, name="stage%d" % k, align_bytes=ALIGN, offset=at)
+            for k, at in enumerate((AT_STAGE_0, AT_STAGE_1))
+        ]
+
+        def copy_on(on_vector, out, in_):
+            if on_vector:
+                nc.vector.tensor_copy(out=out, in_=in_)
             else:
-                nc.vector.tensor_copy(out=dst, in_=src)
-            codes = keep.tile([P, GROUP], U32, name=name + "_codes", align_bytes=64)
-            scales = keep.tile([P, GROUP], U8, name=name + "_scales", align_bytes=64)
-            nc.vector.quantize_mx(out=codes[:].bitcast(FP8X4), scales=scales[:], in_=dealt[:])
+                nc.scalar.copy(out=out, in_=in_)
+
+        def quantised(width, name, woven):
+            codes = keep.tile([P, width], U32, name=name + "_codes", align_bytes=ALIGN)
+            scales = keep.tile([P, width], U8, name=name + "_scales", align_bytes=ALIGN)
+            nc.vector.quantize_mx(out=codes[:].bitcast(FP8X4), scales=scales[:], in_=woven)
             return codes, scales
 
-        if WARM:
-            warm = keep.tile([P, 1], F32, name="warm")
-            nc.scalar.activation(out=warm[:], in_=rel_sb[:, 0, 0:1], func=SIGMOID)
-        v_s = keep.tile([P, S], U8, name="v_s", align_bytes=64)
-        nc.vector.tensor_copy(v_s[:], tab_s[:].indirect(offs_sb[:]))
-        v_w = raws.tile([P, S], U32, name="v_w", align_bytes=64, offset=8192)
-        for half in range(2):
-            cols = slice(half * BANK // LIST_ROWS, (half + 1) * BANK // LIST_ROWS)
-            nc.vector.tensor_copy(v_w[:, half * BANK : (half + 1) * BANK], tab_w[:].indirect(offs_sb[:, cols]))
-        raw_tiles = [
-            raws.tile([P, PACK, GROUP], F32, name="raw%d" % k, align_bytes=64, offset=(0, 12288, 20480)[k]) for k in range(3)
-        ]
-        raw_halves = list([raw_tiles[k][:] for k in RAW_SLOTS])
+        weight_blocks = [("w1", w1, 0, g) for g in range(GROUPS)]
+        weight_blocks = weight_blocks + [("w4", w4, a, g) for a in range(GROUPS) for g in range(GROUPS)]
+        weight_q = {}
 
-        def first_stage(jobs, halves=(0, 1)):
-            for half in halves:
-                cols = slice(half * BANK, (half + 1) * BANK)
-                for dst, codes, scales in jobs:
-                    acc = take(acc_banks)
+        def quantise_weight_block(number):
+            name, w, row_group, col_group = weight_blocks[number]
+            stage = take(stage_ring)
+            rows = w[GROUP * row_group : GROUP * (row_group + 1), GROUP * col_group : GROUP * (col_group + 1)]
+            nc.sync.dma_start(out=stage[:], in_=rows.rearrange("(p j) c -> p j c", j=PACK))
+            dealt = take(dealt_ring)
+            copy_on(
+                number < BLOCKS_ON_VECTOR,
+                dealt[:].rearrange("p (t m j) -> p m j t", t=PACK, j=PACK),
+                stage[:].rearrange("p j (m t) -> p m j t", t=PACK),
+            )
+            weight_q[name, row_group, col_group] = quantised(GROUP, "%s_%d%d" % (name, row_group, col_group), dealt[:])
+
+        def first_stage(jobs):
+            for lo in range(0, S, BANK):
+                for rows, codes, scales in jobs:
+                    acc = take(bank_ring)
                     nc.tensor.matmul_mx(
                         out=acc[:], lhsT=codes, lhsT_scale=scales,
-                        rhs=v_w[:, cols].bitcast(FP8X4), rhs_scale=v_s[:, cols], start=True, stop=True,
+                        rhs=v_w[:, lo : lo + BANK].bitcast(FP8X4), rhs_scale=v_s[:, lo : lo + BANK],
+                        start=True, stop=True,
                     )
-                    nc.scalar.copy(out=dst[:, cols], in_=acc[:])
+                    nc.scalar.copy(out=rows[:, lo : lo + BANK], in_=acc[:])
 
-        r_tail = {}
-        diff = {}
-        gate = {}
-        h = {}
+        r_tail, diff, gate, h = {}, {}, {}, {}
 
         def pick_r(a):
-            cols = slice(P * a, P * (a + 1))
-            r = take(r_tiles)
-            first_stage([(r, w3_w[:, cols].bitcast(FP8X4), w_s[4:P, cols])])
-            r_tail[a] = take(tails)
+            r = take(r_ring)
+            first_stage([(r, w3_w[:, P * a : P * (a + 1)].bitcast(FP8X4), w3_s[:, P * a : P * (a + 1)])])
+            r_tail[a] = take(tail_ring)
             nc.vector.tensor_copy(r_tail[a][:], r[:].indirect(pos2_sb[:]))
 
-        q_of = {}
+        def pick_q_less_r(a):
+            q = take(q_ring)
+            first_stage([(q, w2_w[:, 2 * P * a : 2 * P * (a + 1)].bitcast(FP4X4), w2_s[:, P * a : P * (a + 1)])])
+            diff[a] = take(diff_ring)
+            nc.vector.tensor_tensor(diff[a][:], q[:].indirect(pos1_sb[:]), r_tail[a][:], SUBTRACT)
 
-        def pick_q(a, halves):
-            if 0 in halves:
-                q_of[a] = take(q_tiles)
-            q = q_of[a]
-            first_stage([(q, w2_w[:, 2 * P * a : 2 * P * (a + 1)].bitcast(FP4X4), w_s[:, P * a : P * (a + 1)])], halves)
-            if 1 in halves:
-                diff[a] = take(picks)
-                nc.vector.tensor_tensor(diff[a][:], q[:].indirect(pos1_sb[:]), r_tail[a][:], SUBTRACT)
-
-        def sigmoid_of_difference(a):
-            g, t = divmod(a, PACK)
-            gate[g, t] = keep.tile([P, PAIRS], F32, name="gate%d%d" % (g, t))
-            nc.scalar.activation(out=gate[g, t][:], in_=diff[a][:], func=SIGMOID)
+        def sigmoid_of_diff(a):
+            gate[a] = keep.tile([P, PAIRS], F32, name="gate%d" % a)
+            nc.scalar.activation(out=gate[a][:], in_=diff[a][:], func=SIGMOID)
 
         def weigh_gate(a):
             g, t = divmod(a, PACK)
-            nc.scalar.activation(out=gate[g, t][:], in_=gate[g, t][:], func=COPY, scale=rel_sb[:, g, t : t + 1])
+            nc.scalar.activation(out=gate[a][:], in_=gate[a][:], func=COPY, scale=rel_sb[:, g, t : t + 1])
 
-        def make_h(g, slots):
-            codes, scales = w1_q[g]
+        def make_h_pair(first):
             jobs = []
-            for t in slots:
-                cols = slice(P * t, P * (t + 1))
-                h[g, t] = keep.tile([P, S], F32, name="h%d%d" % (g, t))
-                jobs.append((h[g, t], codes[:, cols].bitcast(FP8X4), scales[:, cols]))
+            for a in (first, first + 1):
+                g, t = divmod(a, PACK)
+                codes, scales = weight_q["w1", 0, g]
+                h[a] = keep.tile([P, S], F32, name="h%d" % a)
+                jobs.append((h[a], codes[:, P * t : P * (t + 1)].bitcast(FP8X4), scales[:, P * t : P * (t + 1)]))
             first_stage(jobs)
 
-        def pick_h(g, slots, z32, lo, hi):
-            lists = slice(lo // LIST_ROWS, hi // LIST_ROWS)
-            gated = {}
-            for t in slots:
-                gated[t] = take(gateds)[:, : hi - lo]
-                nc.vector.tensor_tensor(gated[t], h[g, t][:].indirect(pos1_sb[:, lists]), gate[g, t][:, lo:hi], MULT)
-            for t in slots:
-                nc.vector.tensor_tensor(z32[:, t, :], h[g, t][:].indirect(pos2_sb[:, lists]), gated[t], MULT)
+        def products(g, lo, hi):
+            z = take(z_ring)[:, : PACK * (hi - lo)].rearrange("p (t i) -> p t i", t=PACK)
+            entries = slice(lo // LIST_ROWS, hi // LIST_ROWS)
+            for pair in ((0, 1), (2, 3)):
+                gated = {}
+                for t in pair:
+                    a = PACK * g + t
+                    gated[t] = take(gated_ring)[:, : hi - lo]
+                    nc.vector.tensor_tensor(gated[t], h[a][:].indirect(pos1_sb[:, entries]), gate[a][:, lo:hi], MULT)
+                for t in pair:
+                    nc.vector.tensor_tensor(z[:, t, :], h[PACK * g + t][:].indirect(pos2_sb[:, entries]), gated[t], MULT)
+            return z
 
         z_q = {}
 
-        def quantise_z(g, z32, lo, hi, on_scalar):
-            width = hi - lo
-            woven = take(z_wovens)[:, : width * PACK]
-            dst = woven.rearrange("p (c i t) -> p c t i", i=4, t=PACK)
-            src = z32.rearrange("p t (c i) -> p c t i", i=4)
-            if on_scalar:
-                nc.scalar.copy(out=dst, in_=src)
-            else:
-                nc.vector.tensor_copy(out=dst, in_=src)
-            codes = keep.tile([P, width], U32, name="z_codes%d_%d" % (g, lo), align_bytes=64)
-            scales = keep.tile([P, width], U8, name="z_scales%d_%d" % (g, lo), align_bytes=64)
-            nc.vector.quantize_mx(out=codes[:].bitcast(FP8X4), scales=scales[:], in_=woven)
+        def quantise_z(g, z, lo, hi, on_vector):
+            woven = take(z_woven_ring)[:, : PACK * (hi - lo)]
+            copy_on(
+                on_vector,
+                woven.rearrange("p (c i t) -> p c t i", i=LINE, t=PACK),
+                z.rearrange("p t (c i) -> p c t i", i=LINE),
+            )
+            codes, scales = quantised(hi - lo, "z%d_%d" % (g, lo), woven)
             for col in range(lo, hi, P):
                 z_q[g, col] = (codes[:, col - lo : col - lo + P].bitcast(FP8X4), scales[:, col - lo : col - lo + P])
 
-        y_scales = keep.tile([P, 2 * PAIRS], U8, name="y_scales", align_bytes=64)
-
         def second_passes(a, g, col):
-            acc = banks[2 * (col // P) + g][:].rearrange("p (t m) -> p t m", t=PACK)
-            codes, scales = w4_q[a, g]
+            acc = banks[GROUPS * (col // P) + g][:].rearrange("p (t i) -> p t i", t=PACK)
+            codes, scales = weight_q["w4", a, g]
             for t in range(PACK):
-                cols = slice(P * t, P * (t + 1))
                 nc.tensor.matmul_mx(
-                    out=acc[:, t, :], lhsT=codes[:, cols].bitcast(FP8X4), lhsT_scale=scales[:, cols],
+                    out=acc[:, t, :],
+                    lhsT=codes[:, P * t : P * (t + 1)].bitcast(FP8X4), lhsT_scale=scales[:, P * t : P * (t + 1)],
                     rhs=z_q[a, col][0], rhs_scale=z_q[a, col][1],
-                    start=(a == 0 and t == 0), stop=(a == 1 and t == PACK - 1),
+                    start=(a == 0 and t == 0), stop=(a == GROUPS - 1 and t == PACK - 1),
                 )
             return acc
 
-        def second_stage(lo, hi, weave_on_scalar):
+        def open_sums(lo, hi):
+            for g in range(GROUPS):
+                for col in range(lo, hi, P):
+                    second_passes(0, g, col)
+
+        y_scales = keep.tile([P, GROUPS * PAIRS], U8, name="y_scales", align_bytes=ALIGN)
+
+        def finish(lo, hi):
             width = hi - lo
-            y_codes = ring.tile([P, 2 * width], U32, name="y_codes", align_bytes=64, bufs=3)
-            for g in range(2):
-                y32 = ring.tile([P, PACK, width], F32, name="y32", bufs=4)
-                woven = ring.tile([P, width * PACK], BF16, name="y_woven", align_bytes=64, bufs=4)
+            last = hi == PAIRS
+            y_codes = results.tile([P, GROUPS * width], U32, name="y_codes", align_bytes=ALIGN, bufs=len(PIECES))
+            for g in range(GROUPS):
+                y = results.tile([P, PACK, width], F32, name="y")
+                woven = results.tile([P, PACK * width], BF16, name="y_woven", align_bytes=ALIGN)
                 for col in range(lo, hi, P):
                     acc = second_passes(1, g, col)
-                    local = col - lo
-                    dst = woven[:, PACK * local : PACK * (local + P)].rearrange("p (m t) -> p m t", t=PACK)
-                    if weave_on_scalar:
-                        nc.scalar.copy(out=dst, in_=acc.rearrange("p t m -> p m t"))
-                    else:
-                        nc.vector.tensor_copy(out=dst, in_=acc.rearrange("p t m -> p m t"))
-                    nc.scalar.copy(out=y32[:, :, local : local + P], in_=acc)
+                    at = col - lo
+                    copy_on(
+                        last,
+                        woven[:, PACK * at : PACK * (at + P)].rearrange("p (i t) -> p i t", t=PACK),
+                        acc.rearrange("p t i -> p i t"),
+                    )
+                    nc.scalar.copy(out=y[:, :, at : at + P], in_=acc)
                 rows = out_0[GROUP * g : GROUP * (g + 1), lo:hi].rearrange("(p t) i -> p t i", t=PACK)
-                nc.sync.dma_start(out=rows, in_=y32[:])
+                (nc.sync if lo == 0 else nc.scalar).dma_start(out=rows, in_=y[:])
                 nc.vector.quantize_mx(
-                    out=y_codes[:, g * width : (g + 1) * width].bitcast(FP8X4), scales=y_scales[:, PAIRS * g + lo : PAIRS * g + hi], in_=woven[:]
+                    out=y_codes[:, g * width : (g + 1) * width].bitcast(FP8X4),
+                    scales=y_scales[:, PAIRS * g + lo : PAIRS * g + hi],
+                    in_=woven[:],
                 )
             words = out_1.rearrange("g p m t -> p g (m t)").bitcast(I32)
-            (nc.sync if hi == PAIRS else nc.gpsimd).dma_start(out=words[:, :, lo:hi], in_=y_codes[:].bitcast(I32).rearrange("p (g m) -> p g m", g=2))
+            (nc.sync if last else nc.gpsimd).dma_start(
+                out=words[:, :, lo:hi], in_=y_codes[:].bitcast(I32).rearrange("p (g m) -> p g m", g=GROUPS)
+            )
 
-        w1_q = {}
-        w4_q = {}
-        def w4_part(a, g):
-            w4_q[a, g] = quantise_weight(w4, a, g, "w4_%d%d" % (a, g), (a, g) in W4_ON_SCALAR)
+        pick_r(0)
+        for step in range(TILES + GATE_LAG):
+            behind = step - GATE_LAG
+            if step + 1 < TILES:
+                pick_r(step + 1)
+            if behind >= 0 and behind % 2 == 0:
+                make_h_pair(behind)
+            if behind >= 0:
+                sigmoid_of_diff(behind)
+            if step < TILES:
+                pick_q_less_r(step)
+            if behind >= 0 and behind % 2 == 1:
+                weigh_gate(behind)
+                weigh_gate(behind - 1)
+            if behind == PACK - 1:
+                z_first = products(0, 0, PAIRS)
+            if behind == TILES - 1:
+                quantise_z(0, z_first, 0, PAIRS, False)
+            if step == 0 or step % 2 == 1:
+                quantise_weight_block((step + 1) // 2)
 
-        z_of = {}
-        gated0 = {}
+        edges = [sum(PIECES[:k]) for k in range(len(PIECES) + 1)]
+        spans = list(zip(edges[:-1], edges[1:]))
+        for number, (lo, hi) in enumerate(spans):
+            quantise_z(1, products(1, lo, hi), lo, hi, True)
+            if number == 1:
+                open_sums(*spans[0])
+                finish(*spans[0])
+                open_sums(spans[1][0], PAIRS)
+        for lo, hi in spans[1:]:
+            finish(lo, hi)
 
-        def products(g, lo, hi):
-            z32 = take(z_tiles)[:, : PACK * (hi - lo)].rearrange("p (t i) -> p t i", t=PACK)
-            pick_h(g, (0, 1), z32, lo, hi)
-            pick_h(g, (2, 3), z32, lo, hi)
-            z_of[g, lo] = z32
-
-        for step in ORDER.split():
-            kind, num = step[0], [int(c) for c in step[1:]]
-            if kind == "r":
-                pick_r(num[0])
-            elif kind == "q":
-                pick_q(num[0], num[1:] or [0, 1])
-            elif kind == "t":
-                gated0[num[0]] = take(gateds)
-                nc.vector.tensor_tensor(gated0[num[0]][:], h[0, num[0]][:].indirect(pos1_sb[:]), gate[0, num[0]][:], MULT)
-            elif kind == "u":
-                if num[0] == 0:
-                    z_of[0, 0] = take(z_tiles)[:].rearrange("p (t i) -> p t i", t=PACK)
-                nc.vector.tensor_tensor(z_of[0, 0][:, num[0], :], h[0, num[0]][:].indirect(pos2_sb[:]), gated0[num[0]][:], MULT)
-            elif kind == "e":
-                weigh_gate(num[0])
-            elif kind == "a":
-                lo = sum(PIECES[1][: num[0]])
-                for g in range(2):
-                    for col in range(lo, lo + PIECES[1][num[0]], P):
-                        second_passes(0, g, col)
-            elif kind == "s":
-                sigmoid_of_difference(num[0])
-            elif kind == "w":
-                w1_q[num[0]] = quantise_weight(w1, 0, num[0], "w1_%d" % num[0], False)
-            elif kind == "x":
-                w4_part(num[0], num[1])
-            elif kind == "h":
-                make_h(num[0], num[1:])
-            elif kind == "p":
-                lo = sum(PIECES[num[0]][: num[1]])
-                products(num[0], lo, lo + PIECES[num[0]][num[1]])
-            elif kind == "z":
-                lo = sum(PIECES[num[0]][: num[1]])
-                quantise_z(num[0], z_of[num[0], lo], lo, lo + PIECES[num[0]][num[1]], step in Z_ON_SCALAR)
-            elif kind == "y":
-                lo = sum(PIECES[1][: num[0]])
-                second_stage(lo, lo + PIECES[1][num[0]], num[0] in Y_ON_SCALAR)
-        planes = y_scales[:].bitcast(I32).rearrange("p (g m) -> p g m", g=2)
-        for quad in range(4):
-            (nc.sync if quad < 2 else nc.scalar).dma_start(
-                out=out_2[:, 4 * quad : 4 * quad + 4, :].rearrange("g r m -> r g m").bitcast(I32),
-                in_=planes[32 * quad : 32 * quad + 4, :, :],
+        plane_rows = y_scales[:].bitcast(I32).rearrange("p (g m) -> p g m", g=GROUPS)
+        for u in range(4):
+            nc.sync.dma_start(
+                out=out_2[:, 4 * u : 4 * u + 4, :].rearrange("g r m -> r g m").bitcast(I32),
+                in_=plane_rows[32 * u : 32 * u + 4, :, :],
             )

@@ -96,16 +96,16 @@ def tile_list_triple_pair_rerank_kernel(
 
         for plane in (tab_s, s3_in, s2_in):
             nc.vector.memset(plane[:].bitcast(I32), 0)
-        load_scales([nc.scalar] * 4, tab_s, tab_scales)
+        load_scales([nc.scalar, nc.sync] * 2, tab_s, tab_scales)
         nc.sync.dma_start(offs_sb[:], offs)
         nc.sync.dma_start(pos2_sb[:], pos2)
         nc.sync.dma_start(pos1_sb[:], pos1)
         nc.sync.dma_start(out=w3_in[:], in_=w3_words[0].rearrange("p e i -> p (e i)").bitcast(I32))
-        nc.sync.dma_start(out=w2_in[:].bitcast(I32), in_=w2_words[0].bitcast(I32))
-        nc.sync.dma_start(out=tab_w[:].bitcast(I32), in_=tab_words[0].rearrange("p t i -> p (t i)").bitcast(I32))
-        load_scales([nc.scalar] * 3 + [nc.gpsimd], s3_in, w3_scales)
-        load_scales([nc.scalar] * 4, s2_in, w2_scales)
         nc.gpsimd.dma_start(out=rel_sb[:], in_=rel.rearrange("(g p t) -> p g t", g=GROUPS, t=PACK))
+        nc.gpsimd.dma_start(out=tab_w[:].bitcast(I32), in_=tab_words[0].rearrange("p t i -> p (t i)").bitcast(I32))
+        load_scales([nc.scalar, nc.sync] * 2, s3_in, w3_scales)
+        nc.gpsimd.dma_start(out=w2_in[:].bitcast(I32), in_=w2_words[0].bitcast(I32))
+        load_scales([nc.scalar, nc.sync] * 2, s2_in, w2_scales)
 
         def deal_columns(dst, src):
             nc.vector.tensor_copy(
@@ -114,12 +114,7 @@ def tile_list_triple_pair_rerank_kernel(
             )
 
         deal_columns(w3_w, w3_in)
-        nc.vector.tensor_copy(
-            out=w2_w[:].rearrange("p (g t m b) -> p g m t b", g=GROUPS, t=PACK, b=2),
-            in_=w2_in[:].rearrange("p (g m t b) -> p g m t b", g=GROUPS, t=PACK, b=2),
-        )
         deal_columns(w3_s, s3_in)
-        deal_columns(w2_s, s2_in)
 
         v_s = keep.tile([P, S], U8, name="v_s", align_bytes=ALIGN)
         nc.vector.tensor_copy(v_s[:], tab_s[:].indirect(offs_sb[:]))
@@ -127,6 +122,8 @@ def tile_list_triple_pair_rerank_kernel(
         for lo in range(0, S, BANK):
             entries = offs_sb[:, lo // LIST_ROWS : (lo + BANK) // LIST_ROWS]
             nc.vector.tensor_copy(v_w[:, lo : lo + BANK], tab_w[:].indirect(entries))
+        deal_columns(w2_w[:].bitcast(U16), w2_in[:].bitcast(U16))
+        deal_columns(w2_s, s2_in)
         stage_ring = [
             shared.tile([P, PACK, GROUP], F32, name="stage%d" % k, align_bytes=ALIGN, offset=at)
             for k, at in enumerate((AT_STAGE_0, AT_STAGE_1))
@@ -156,8 +153,8 @@ def tile_list_triple_pair_rerank_kernel(
             dealt = take(dealt_ring)
             copy_on(
                 number < BLOCKS_ON_VECTOR,
-                dealt[:].rearrange("p (t m j) -> p m j t", t=PACK, j=PACK),
-                stage[:].rearrange("p j (m t) -> p m j t", t=PACK),
+                dealt[:].rearrange("p (t m j) -> p m t j", t=PACK, j=PACK),
+                stage[:].rearrange("p j (m t) -> p m t j", t=PACK),
             )
             weight_q[name, row_group, col_group] = quantised(GROUP, "%s_%d%d" % (name, row_group, col_group), dealt[:])
 
@@ -248,10 +245,11 @@ def tile_list_triple_pair_rerank_kernel(
 
         y_scales = keep.tile([P, GROUPS * PAIRS], U8, name="y_scales", align_bytes=ALIGN)
 
+        y_codes = keep.tile([P, GROUPS * PAIRS], U32, name="y_codes", align_bytes=ALIGN)
+
         def finish(lo, hi):
             width = hi - lo
             last = hi == PAIRS
-            y_codes = results.tile([P, GROUPS * width], U32, name="y_codes", align_bytes=ALIGN, bufs=len(PIECES))
             for g in range(GROUPS):
                 y = results.tile([P, PACK, width], F32, name="y")
                 woven = results.tile([P, PACK * width], BF16, name="y_woven", align_bytes=ALIGN)
@@ -267,14 +265,15 @@ def tile_list_triple_pair_rerank_kernel(
                 rows = out_0[GROUP * g : GROUP * (g + 1), lo:hi].rearrange("(p t) i -> p t i", t=PACK)
                 (nc.sync if lo == 0 else nc.scalar).dma_start(out=rows, in_=y[:])
                 nc.vector.quantize_mx(
-                    out=y_codes[:, g * width : (g + 1) * width].bitcast(FP8X4),
+                    out=y_codes[:, PAIRS * g + lo : PAIRS * g + hi].bitcast(FP8X4),
                     scales=y_scales[:, PAIRS * g + lo : PAIRS * g + hi],
                     in_=woven[:],
                 )
+
+        def store_codes(queue, lo, hi):
             words = out_1.rearrange("g p m t -> p g (m t)").bitcast(I32)
-            (nc.sync if last else nc.gpsimd).dma_start(
-                out=words[:, :, lo:hi], in_=y_codes[:].bitcast(I32).rearrange("p (g m) -> p g m", g=GROUPS)
-            )
+            codes = y_codes[:].bitcast(I32).rearrange("p (g m) -> p g m", g=GROUPS)
+            queue.dma_start(out=words[:, :, lo:hi], in_=codes[:, :, lo:hi])
 
         pick_r(0)
         for step in range(TILES + GATE_LAG):
@@ -304,9 +303,11 @@ def tile_list_triple_pair_rerank_kernel(
             if number == 1:
                 open_sums(*spans[0])
                 finish(*spans[0])
+                store_codes(nc.gpsimd, *spans[0])
                 open_sums(spans[1][0], PAIRS)
         for lo, hi in spans[1:]:
             finish(lo, hi)
+        store_codes(nc.sync, spans[1][0], PAIRS)
 
         plane_rows = y_scales[:].bitcast(I32).rearrange("p (g m) -> p g m", g=GROUPS)
         for u in range(4):

@@ -31,16 +31,16 @@ ALIGN = 64
 
 PIECES = (256, 128, 128)
 GATE_LAG = 2
-BLOCKS_ON_VECTOR = 3
+BLOCKS_ON_VECTOR = 4
 ROW_DEPTH = 3
 TAIL_DEPTH = 3
 PAIR_DEPTH = 2
+RESULT_DEPTH = 4
 
-STAGE_BYTES = PACK * GROUP * 4
-AT_STAGE_0 = 0
-AT_V_WORDS = STAGE_BYTES
-AT_TAB_SCALES = AT_V_WORDS - T // 4
-AT_TAB_WORDS = AT_V_WORDS + 4 * S
+AT_TAB_SCALES = 0
+AT_V_WORDS = 0
+AT_TAB_WORDS = 4 * S
+AT_STAGE_0 = AT_TAB_WORDS + 4 * T
 AT_STAGE_1 = AT_TAB_WORDS
 
 
@@ -51,7 +51,7 @@ def tile_list_triple_pair_rerank_kernel(
     nc = tc.nc
     with ExitStack() as ctx:
         keep = ctx.enter_context(tc.tile_pool(name="keep", bufs=1))
-        results = ctx.enter_context(tc.tile_pool(name="results", bufs=4))
+        results = ctx.enter_context(tc.tile_pool(name="results", bufs=RESULT_DEPTH))
         shared = ctx.enter_context(tc.tile_pool(name="shared", bufs=1))
         psum = ctx.enter_context(tc.psum_pool(name="psum", bufs=1))
 
@@ -89,23 +89,25 @@ def tile_list_triple_pair_rerank_kernel(
         rel_sb = keep.tile([P, GROUPS, PACK], F32, name="rel_sb")
 
         def load_scales(queues, plane, rows):
-            for u, queue in enumerate(queues):
+            for quad, queue in enumerate(queues):
                 queue.dma_start(
-                    out=plane[32 * u : 32 * u + 4, :].bitcast(I32), in_=rows[0, 4 * u : 4 * u + 4, :].bitcast(I32)
+                    out=plane[32 * quad : 32 * quad + 4, :].bitcast(I32),
+                    in_=rows[0, 4 * quad : 4 * quad + 4, :].bitcast(I32),
                 )
 
-        for plane in (tab_s, s3_in, s2_in):
-            nc.vector.memset(plane[:].bitcast(I32), 0)
+        nc.vector.memset(tab_s[:].bitcast(I32), 0)
+        for plane in (s3_in, s2_in):
+            nc.gpsimd.memset(plane[:].bitcast(I32), 0)
         load_scales([nc.scalar, nc.sync] * 2, tab_s, tab_scales)
         nc.sync.dma_start(offs_sb[:], offs)
         nc.sync.dma_start(pos2_sb[:], pos2)
         nc.sync.dma_start(pos1_sb[:], pos1)
-        nc.sync.dma_start(out=w3_in[:], in_=w3_words[0].rearrange("p e i -> p (e i)").bitcast(I32))
-        nc.gpsimd.dma_start(out=rel_sb[:], in_=rel.rearrange("(g p t) -> p g t", g=GROUPS, t=PACK))
-        nc.gpsimd.dma_start(out=tab_w[:].bitcast(I32), in_=tab_words[0].rearrange("p t i -> p (t i)").bitcast(I32))
+        nc.sync.dma_start(out=w3_in[:], in_=w3_words[0].rearrange("p c t -> p (c t)").bitcast(I32))
+        nc.gpsimd.dma_start(out=tab_w[:].bitcast(I32), in_=tab_words[0].rearrange("p e t -> p (e t)").bitcast(I32))
         load_scales([nc.scalar, nc.sync] * 2, s3_in, w3_scales)
         nc.gpsimd.dma_start(out=w2_in[:].bitcast(I32), in_=w2_words[0].bitcast(I32))
         load_scales([nc.scalar, nc.sync] * 2, s2_in, w2_scales)
+        nc.gpsimd.dma_start(out=rel_sb[:], in_=rel.rearrange("(g p t) -> p g t", g=GROUPS, t=PACK))
 
         def deal_columns(dst, src):
             nc.vector.tensor_copy(
@@ -118,10 +120,11 @@ def tile_list_triple_pair_rerank_kernel(
 
         v_s = keep.tile([P, S], U8, name="v_s", align_bytes=ALIGN)
         nc.vector.tensor_copy(v_s[:], tab_s[:].indirect(offs_sb[:]))
-        v_w = shared.tile([P, S], U32, name="v_w", align_bytes=ALIGN, offset=AT_V_WORDS)
+        v_w = {}
         for lo in range(0, S, BANK):
+            v_w[lo] = shared.tile([P, BANK], U32, name="v_w%d" % lo, align_bytes=ALIGN, offset=AT_V_WORDS + 4 * lo)
             entries = offs_sb[:, lo // LIST_ROWS : (lo + BANK) // LIST_ROWS]
-            nc.vector.tensor_copy(v_w[:, lo : lo + BANK], tab_w[:].indirect(entries))
+            nc.vector.tensor_copy(v_w[lo][:], tab_w[:].indirect(entries))
         deal_columns(w2_w[:].bitcast(U16), w2_in[:].bitcast(U16))
         deal_columns(w2_s, s2_in)
         stage_ring = [
@@ -142,7 +145,7 @@ def tile_list_triple_pair_rerank_kernel(
             return codes, scales
 
         weight_blocks = [("w1", w1, 0, g) for g in range(GROUPS)]
-        weight_blocks = weight_blocks + [("w4", w4, a, g) for a in range(GROUPS) for g in range(GROUPS)]
+        weight_blocks = weight_blocks + [("w4", w4, c_group, g) for c_group in range(GROUPS) for g in range(GROUPS)]
         weight_q = {}
 
         def quantise_weight_block(number):
@@ -164,7 +167,7 @@ def tile_list_triple_pair_rerank_kernel(
                     acc = take(bank_ring)
                     nc.tensor.matmul_mx(
                         out=acc[:], lhsT=codes, lhsT_scale=scales,
-                        rhs=v_w[:, lo : lo + BANK].bitcast(FP8X4), rhs_scale=v_s[:, lo : lo + BANK],
+                        rhs=v_w[lo][:].bitcast(FP8X4), rhs_scale=v_s[:, lo : lo + BANK],
                         start=True, stop=True,
                     )
                     nc.scalar.copy(out=rows[:, lo : lo + BANK], in_=acc[:])
@@ -219,22 +222,22 @@ def tile_list_triple_pair_rerank_kernel(
             woven = take(z_woven_ring)[:, : PACK * (hi - lo)]
             copy_on(
                 on_vector,
-                woven.rearrange("p (c i t) -> p c t i", i=LINE, t=PACK),
-                z.rearrange("p t (c i) -> p c t i", i=LINE),
+                woven.rearrange("p (run i t) -> p run t i", i=LINE, t=PACK),
+                z.rearrange("p t (run i) -> p run t i", i=LINE),
             )
             codes, scales = quantised(hi - lo, "z%d_%d" % (g, lo), woven)
             for col in range(lo, hi, P):
                 z_q[g, col] = (codes[:, col - lo : col - lo + P].bitcast(FP8X4), scales[:, col - lo : col - lo + P])
 
-        def second_passes(a, g, col):
+        def second_passes(c_group, g, col):
             acc = banks[GROUPS * (col // P) + g][:].rearrange("p (t i) -> p t i", t=PACK)
-            codes, scales = weight_q["w4", a, g]
+            codes, scales = weight_q["w4", c_group, g]
             for t in range(PACK):
                 nc.tensor.matmul_mx(
                     out=acc[:, t, :],
                     lhsT=codes[:, P * t : P * (t + 1)].bitcast(FP8X4), lhsT_scale=scales[:, P * t : P * (t + 1)],
-                    rhs=z_q[a, col][0], rhs_scale=z_q[a, col][1],
-                    start=(a == 0 and t == 0), stop=(a == GROUPS - 1 and t == PACK - 1),
+                    rhs=z_q[c_group, col][0], rhs_scale=z_q[c_group, col][1],
+                    start=(c_group == 0 and t == 0), stop=(c_group == GROUPS - 1 and t == PACK - 1),
                 )
             return acc
 
@@ -244,7 +247,6 @@ def tile_list_triple_pair_rerank_kernel(
                     second_passes(0, g, col)
 
         y_scales = keep.tile([P, GROUPS * PAIRS], U8, name="y_scales", align_bytes=ALIGN)
-
         y_codes = keep.tile([P, GROUPS * PAIRS], U32, name="y_codes", align_bytes=ALIGN)
 
         def finish(lo, hi):
@@ -271,8 +273,8 @@ def tile_list_triple_pair_rerank_kernel(
                 )
 
         def store_codes(queue, lo, hi):
-            words = out_1.rearrange("g p m t -> p g (m t)").bitcast(I32)
-            codes = y_codes[:].bitcast(I32).rearrange("p (g m) -> p g m", g=GROUPS)
+            words = out_1.rearrange("g p i t -> p g (i t)").bitcast(I32)
+            codes = y_codes[:].bitcast(I32).rearrange("p (g i) -> p g i", g=GROUPS)
             queue.dma_start(out=words[:, :, lo:hi], in_=codes[:, :, lo:hi])
 
         pick_r(0)
@@ -309,9 +311,9 @@ def tile_list_triple_pair_rerank_kernel(
             finish(lo, hi)
         store_codes(nc.sync, spans[1][0], PAIRS)
 
-        plane_rows = y_scales[:].bitcast(I32).rearrange("p (g m) -> p g m", g=GROUPS)
-        for u in range(4):
+        plane_rows = y_scales[:].bitcast(I32).rearrange("p (g i) -> p g i", g=GROUPS)
+        for quad in range(4):
             nc.sync.dma_start(
-                out=out_2[:, 4 * u : 4 * u + 4, :].rearrange("g r m -> r g m").bitcast(I32),
-                in_=plane_rows[32 * u : 32 * u + 4, :, :],
+                out=out_2[:, 4 * quad : 4 * quad + 4, :].rearrange("g row i -> row g i").bitcast(I32),
+                in_=plane_rows[32 * quad : 32 * quad + 4, :, :],
             )

@@ -15,7 +15,6 @@ FP8X4 = mybir.dt.float8_e4m3fn_x4
 FP4X4 = mybir.dt.float4_e2m1fn_x4
 MULT = mybir.AluOpType.mult
 SUBTRACT = mybir.AluOpType.subtract
-COPY = mybir.ActivationFunctionType.Copy
 SIGMOID = mybir.ActivationFunctionType.Sigmoid
 
 P = 128
@@ -30,18 +29,32 @@ LINE = 4
 ALIGN = 64
 
 PIECES = (256, 128, 128)
-GATE_LAG = 2
-BLOCKS_ON_VECTOR = 4
-ROW_DEPTH = 3
-TAIL_DEPTH = 3
+FIRST_PRODUCTS = 3
+BLOCK_STEPS = (0, 4)
+ROW_DEPTH = 4
+HEAD_DEPTH = 3
+DIFF_DEPTH = 3
 PAIR_DEPTH = 2
+DEALT_DEPTH = 4
 RESULT_DEPTH = 4
 
-AT_TAB_SCALES = 0
-AT_V_WORDS = 0
-AT_TAB_WORDS = 4 * S
-AT_STAGE_0 = AT_TAB_WORDS + 4 * T
-AT_STAGE_1 = AT_TAB_WORDS
+STAGE_BYTES = 4 * PACK * GROUP
+AT_STAGE_FIRST = 0
+AT_S2_IN = STAGE_BYTES - ALIGN
+AT_S3_DEALT = AT_S2_IN + H
+AT_TAB_WORDS = AT_S3_DEALT + H - ALIGN
+AT_STAGES = (AT_STAGE_FIRST, AT_TAB_WORDS + ALIGN, AT_TAB_WORDS + ALIGN + STAGE_BYTES)
+AT_W3_IN = AT_STAGES[2] + STAGE_BYTES
+AT_TAB_SCALES = AT_W3_IN + 4 * H - ALIGN
+AT_V_LOW = AT_W3_IN + 4 * H
+AT_W2_DEALT = AT_TAB_SCALES + T - ALIGN
+AT_W2_IN = AT_W2_DEALT + 2 * H
+AT_V_HIGH = AT_W2_IN + 2 * H - ALIGN
+AT_DEALT = AT_V_HIGH + 4 * BANK
+DEALT_BYTES = 2 * PACK * GROUP
+AT_Y_WOVEN = AT_DEALT + DEALT_DEPTH * DEALT_BYTES
+Y_WOVEN_BYTES = 2 * PACK * PIECES[0]
+AT_Z_PIECE = (AT_Y_WOVEN + GROUPS * Y_WOVEN_BYTES, AT_DEALT + DEALT_BYTES, AT_Y_WOVEN)
 
 
 def tile_list_triple_pair_rerank_kernel(
@@ -66,26 +79,25 @@ def tile_list_triple_pair_rerank_kernel(
         bank_ring = list(banks)
         r_ring = ring_of(ROW_DEPTH, S, F32, "r")
         q_ring = ring_of(ROW_DEPTH, S, F32, "q")
-        diff_ring = ring_of(PAIR_DEPTH, PAIRS, F32, "diff")
+        diff_ring = ring_of(DIFF_DEPTH, 2 * PAIRS, F32, "diff")
         gated_ring = ring_of(PAIR_DEPTH, PAIRS, F32, "gated")
-        tail_ring = ring_of(TAIL_DEPTH, PAIRS, F32, "r_tail")
-        z_ring = ring_of(PAIR_DEPTH, PACK * PAIRS, F32, "z")
+        head_ring = ring_of(HEAD_DEPTH, PAIRS, F32, "q_head")
         z_woven_ring = ring_of(PAIR_DEPTH, PACK * PAIRS, BF16, "z_woven")
-        dealt_ring = ring_of(PAIR_DEPTH, PACK * GROUP, BF16, "dealt")
+        dealt_ring = [
+            shared.tile([P, PACK * GROUP], BF16, name="dealt%d" % k, align_bytes=ALIGN, offset=AT_DEALT + k * DEALT_BYTES)
+            for k in range(DEALT_DEPTH)
+        ]
 
         offs_sb = keep.tile([P, S // LIST_ROWS], U16, name="offs_sb")
         pos1_sb = keep.tile([P, PAIRS // LIST_ROWS], U16, name="pos1_sb")
         pos2_sb = keep.tile([P, PAIRS // LIST_ROWS], U16, name="pos2_sb")
         tab_w = shared.tile([P, T], U32, name="tab_w", align_bytes=ALIGN, offset=AT_TAB_WORDS)
         tab_s = shared.tile([P, T], U8, name="tab_s", align_bytes=ALIGN, offset=AT_TAB_SCALES)
-        w2_in = keep.tile([P, 2 * H], U8, name="w2_in", align_bytes=ALIGN)
-        w3_in = keep.tile([P, H], I32, name="w3_in", align_bytes=ALIGN)
+        w2_in = shared.tile([P, 2 * H], U8, name="w2_in", align_bytes=ALIGN, offset=AT_W2_IN)
         s3_in = keep.tile([P, H], U8, name="s3_in", align_bytes=ALIGN)
-        s2_in = keep.tile([P, H], U8, name="s2_in", align_bytes=ALIGN)
-        w2_w = keep.tile([P, 2 * H], U8, name="w2_w", align_bytes=ALIGN)
-        w3_w = keep.tile([P, H], I32, name="w3_w", align_bytes=ALIGN)
-        w3_s = keep.tile([P, H], U8, name="w3_s", align_bytes=ALIGN)
+        s2_in = shared.tile([P, H], U8, name="s2_in", align_bytes=ALIGN, offset=AT_S2_IN)
         w2_s = keep.tile([P, H], U8, name="w2_s", align_bytes=ALIGN)
+        w3_w = keep.tile([P, H], I32, name="w3_w", align_bytes=ALIGN)
         rel_sb = keep.tile([P, GROUPS, PACK], F32, name="rel_sb")
 
         def load_scales(queues, plane, rows):
@@ -96,40 +108,46 @@ def tile_list_triple_pair_rerank_kernel(
                 )
 
         nc.vector.memset(tab_s[:].bitcast(I32), 0)
-        for plane in (s3_in, s2_in):
-            nc.gpsimd.memset(plane[:].bitcast(I32), 0)
-        load_scales([nc.scalar, nc.sync] * 2, tab_s, tab_scales)
+        nc.vector.memset(s3_in[:].bitcast(I32), 0)
+        nc.gpsimd.memset(s2_in[:].bitcast(I32), 0)
         nc.sync.dma_start(offs_sb[:], offs)
-        nc.sync.dma_start(pos2_sb[:], pos2)
         nc.sync.dma_start(pos1_sb[:], pos1)
-        nc.sync.dma_start(out=w3_in[:], in_=w3_words[0].rearrange("p c t -> p (c t)").bitcast(I32))
-        nc.gpsimd.dma_start(out=tab_w[:].bitcast(I32), in_=tab_words[0].rearrange("p e t -> p (e t)").bitcast(I32))
-        load_scales([nc.scalar, nc.sync] * 2, s3_in, w3_scales)
-        nc.gpsimd.dma_start(out=w2_in[:].bitcast(I32), in_=w2_words[0].bitcast(I32))
-        load_scales([nc.scalar, nc.sync] * 2, s2_in, w2_scales)
+        nc.sync.dma_start(pos2_sb[:], pos2)
+        nc.sync.dma_start(out=tab_w[:].bitcast(I32), in_=tab_words[0].rearrange("p e t -> p (e t)").bitcast(I32))
+        nc.sync.dma_start(out=w2_in[:].bitcast(I32), in_=w2_words[0].bitcast(I32))
+        load_scales([nc.scalar] * 4, tab_s, tab_scales)
+        load_scales([nc.scalar] * 4, s3_in, w3_scales)
+        load_scales([nc.gpsimd] * 4, s2_in, w2_scales)
         nc.gpsimd.dma_start(out=rel_sb[:], in_=rel.rearrange("(g p t) -> p g t", g=GROUPS, t=PACK))
 
-        def deal_columns(dst, src):
+        def deal_columns(dst, src, walk):
             nc.vector.tensor_copy(
-                out=dst[:].rearrange("p (g t m) -> p g m t", g=GROUPS, t=PACK),
-                in_=src[:].rearrange("p (g m t) -> p g m t", g=GROUPS, t=PACK),
+                out=dst[:].rearrange("p (g t m) -> p " + walk, g=GROUPS, t=PACK),
+                in_=src[:].rearrange("p (g m t) -> p " + walk, g=GROUPS, t=PACK),
             )
-
-        deal_columns(w3_w, w3_in)
-        deal_columns(w3_s, s3_in)
 
         v_s = keep.tile([P, S], U8, name="v_s", align_bytes=ALIGN)
         nc.vector.tensor_copy(v_s[:], tab_s[:].indirect(offs_sb[:]))
+        deal_columns(w2_s, s2_in, "g t m")
+        w3_in = shared.tile([P, H], I32, name="w3_in", align_bytes=ALIGN, offset=AT_W3_IN)
+        nc.sync.dma_start(out=w3_in[:], in_=w3_words[0].rearrange("p c t -> p (c t)").bitcast(I32))
         v_w = {}
-        for lo in range(0, S, BANK):
-            v_w[lo] = shared.tile([P, BANK], U32, name="v_w%d" % lo, align_bytes=ALIGN, offset=AT_V_WORDS + 4 * lo)
+
+        def gather_words(lo, at):
+            v_w[lo] = shared.tile([P, BANK], U32, name="v_w%d" % lo, align_bytes=ALIGN, offset=at)
             entries = offs_sb[:, lo // LIST_ROWS : (lo + BANK) // LIST_ROWS]
             nc.vector.tensor_copy(v_w[lo][:], tab_w[:].indirect(entries))
-        deal_columns(w2_w[:].bitcast(U16), w2_in[:].bitcast(U16))
-        deal_columns(w2_s, s2_in)
+
+        gather_words(0, AT_V_LOW)
+        w2_w = shared.tile([P, 2 * H], U8, name="w2_w", align_bytes=ALIGN, offset=AT_W2_DEALT)
+        deal_columns(w2_w[:].bitcast(U16), w2_in[:].bitcast(U16), "g t m")
+        gather_words(BANK, AT_V_HIGH)
+        deal_columns(w3_w, w3_in, "g m t")
+        w3_s = shared.tile([P, H], U8, name="w3_s", align_bytes=ALIGN, offset=AT_S3_DEALT)
+        deal_columns(w3_s, s3_in, "g t m")
         stage_ring = [
             shared.tile([P, PACK, GROUP], F32, name="stage%d" % k, align_bytes=ALIGN, offset=at)
-            for k, at in enumerate((AT_STAGE_0, AT_STAGE_1))
+            for k, at in enumerate(AT_STAGES)
         ]
 
         def copy_on(on_vector, out, in_):
@@ -145,7 +163,7 @@ def tile_list_triple_pair_rerank_kernel(
             return codes, scales
 
         weight_blocks = [("w1", w1, 0, g) for g in range(GROUPS)]
-        weight_blocks = weight_blocks + [("w4", w4, c_group, g) for c_group in range(GROUPS) for g in range(GROUPS)]
+        weight_blocks = weight_blocks + [("w4", w4, c_group, g) for g in range(GROUPS) for c_group in range(GROUPS)]
         weight_q = {}
 
         def quantise_weight_block(number):
@@ -155,7 +173,7 @@ def tile_list_triple_pair_rerank_kernel(
             nc.sync.dma_start(out=stage[:], in_=rows.rearrange("(p j) c -> p j c", j=PACK))
             dealt = take(dealt_ring)
             copy_on(
-                number < BLOCKS_ON_VECTOR,
+                number == 0,
                 dealt[:].rearrange("p (t m j) -> p m t j", t=PACK, j=PACK),
                 stage[:].rearrange("p j (m t) -> p m t j", t=PACK),
             )
@@ -172,58 +190,61 @@ def tile_list_triple_pair_rerank_kernel(
                     )
                     nc.scalar.copy(out=rows[:, lo : lo + BANK], in_=acc[:])
 
-        r_tail, diff, gate, h = {}, {}, {}, {}
+        q_rows, r_rows, q_head, diff, gate, h = {}, {}, {}, {}, {}, {}
 
-        def pick_r(a):
-            r = take(r_ring)
-            first_stage([(r, w3_w[:, P * a : P * (a + 1)].bitcast(FP8X4), w3_s[:, P * a : P * (a + 1)])])
-            r_tail[a] = take(tail_ring)
-            nc.vector.tensor_copy(r_tail[a][:], r[:].indirect(pos2_sb[:]))
-
-        def pick_q_less_r(a):
-            q = take(q_ring)
-            first_stage([(q, w2_w[:, 2 * P * a : 2 * P * (a + 1)].bitcast(FP4X4), w2_s[:, P * a : P * (a + 1)])])
-            diff[a] = take(diff_ring)
-            nc.vector.tensor_tensor(diff[a][:], q[:].indirect(pos1_sb[:]), r_tail[a][:], SUBTRACT)
-
-        def sigmoid_of_diff(a):
-            gate[a] = keep.tile([P, PAIRS], F32, name="gate%d" % a)
-            nc.scalar.activation(out=gate[a][:], in_=diff[a][:], func=SIGMOID)
-
-        def weigh_gate(a):
-            g, t = divmod(a, PACK)
-            nc.scalar.activation(out=gate[a][:], in_=gate[a][:], func=COPY, scale=rel_sb[:, g, t : t + 1])
-
-        def make_h_pair(first):
+        def make_q(tiles):
             jobs = []
-            for a in (first, first + 1):
-                g, t = divmod(a, PACK)
-                codes, scales = weight_q["w1", 0, g]
-                h[a] = keep.tile([P, S], F32, name="h%d" % a)
-                jobs.append((h[a], codes[:, P * t : P * (t + 1)].bitcast(FP8X4), scales[:, P * t : P * (t + 1)]))
+            for a in tiles:
+                q_rows[a] = take(q_ring)
+                jobs.append((q_rows[a], w2_w[:, 2 * P * a : 2 * P * (a + 1)].bitcast(FP4X4), w2_s[:, P * a : P * (a + 1)]))
             first_stage(jobs)
 
-        def products(g, lo, hi):
-            z = take(z_ring)[:, : PACK * (hi - lo)].rearrange("p (t i) -> p t i", t=PACK)
+        def make_r(a):
+            r_rows[a] = take(r_ring)
+            first_stage([(r_rows[a], w3_w[:, P * a : P * (a + 1)].bitcast(FP8X4), w3_s[:, P * a : P * (a + 1)])])
+
+        def make_h(a):
+            g, t = divmod(a, PACK)
+            codes, scales = weight_q["w1", 0, g]
+            h[a] = keep.tile([P, S], F32, name="h%d" % a)
+            first_stage([(h[a], codes[:, P * t : P * (t + 1)].bitcast(FP8X4), scales[:, P * t : P * (t + 1)])])
+
+        def pick_q(a):
+            q_head[a] = take(head_ring)
+            nc.vector.tensor_copy(q_head[a][:], q_rows[a][:].indirect(pos1_sb[:]))
+
+        def pick_r_less_q(a):
+            if a % 2 == 0:
+                diff[a // 2] = take(diff_ring)
+            into = diff[a // 2][:, PAIRS * (a % 2) : PAIRS * (a % 2 + 1)]
+            nc.vector.tensor_tensor(into, r_rows[a][:].indirect(pos2_sb[:]), q_head[a][:], SUBTRACT)
+
+        def gates_of_pair(pair):
+            both = keep.tile([P, 2 * PAIRS], F32, name="gate%d" % pair)
+            nc.scalar.activation(out=both[:], in_=diff[pair][:], func=SIGMOID, scale=-1.0)
+            gate[2 * pair], gate[2 * pair + 1] = both[:, :PAIRS], both[:, PAIRS:]
+
+        def products(g, z_tile, lo, hi, pair):
+            z = z_tile[:].rearrange("p (t i) -> p t i", t=PACK)
             entries = slice(lo // LIST_ROWS, hi // LIST_ROWS)
-            for pair in ((0, 1), (2, 3)):
-                gated = {}
-                for t in pair:
-                    a = PACK * g + t
-                    gated[t] = take(gated_ring)[:, : hi - lo]
-                    nc.vector.tensor_tensor(gated[t], h[a][:].indirect(pos1_sb[:, entries]), gate[a][:, lo:hi], MULT)
-                for t in pair:
-                    nc.vector.tensor_tensor(z[:, t, :], h[PACK * g + t][:].indirect(pos2_sb[:, entries]), gated[t], MULT)
-            return z
+            gated = {}
+            for t in pair:
+                a = PACK * g + t
+                gated[t] = take(gated_ring)[:, : hi - lo]
+                nc.vector.tensor_tensor(gated[t], h[a][:].indirect(pos1_sb[:, entries]), gate[a][:, lo:hi], MULT)
+            for t in pair:
+                nc.vector.tensor_tensor(z[:, t, :], h[PACK * g + t][:].indirect(pos2_sb[:, entries]), gated[t], MULT)
 
         z_q = {}
 
-        def quantise_z(g, z, lo, hi, on_vector):
+        def quantise_z(g, z_tile, lo, hi):
             woven = take(z_woven_ring)[:, : PACK * (hi - lo)]
-            copy_on(
-                on_vector,
+            runs = (hi - lo) // LINE
+            nc.vector.tensor_tensor(
                 woven.rearrange("p (run i t) -> p run t i", i=LINE, t=PACK),
-                z.rearrange("p t (run i) -> p run t i", i=LINE),
+                z_tile[:].rearrange("p (t run i) -> p run t i", t=PACK, i=LINE),
+                rel_sb[:, g, :].unsqueeze(1).unsqueeze(3).broadcast_to([P, runs, PACK, LINE]),
+                MULT,
             )
             codes, scales = quantised(hi - lo, "z%d_%d" % (g, lo), woven)
             for col in range(lo, hi, P):
@@ -254,66 +275,89 @@ def tile_list_triple_pair_rerank_kernel(
             last = hi == PAIRS
             for g in range(GROUPS):
                 y = results.tile([P, PACK, width], F32, name="y")
-                woven = results.tile([P, PACK * width], BF16, name="y_woven", align_bytes=ALIGN)
+                if lo == 0:
+                    woven = shared.tile(
+                        [P, PACK * width], BF16, name="y_first%d" % g, align_bytes=ALIGN,
+                        offset=AT_Y_WOVEN + g * Y_WOVEN_BYTES,
+                    )
+                else:
+                    woven = results.tile([P, PACK * width], BF16, name="y_woven", align_bytes=ALIGN)
                 for col in range(lo, hi, P):
                     acc = second_passes(1, g, col)
                     at = col - lo
-                    copy_on(
-                        last,
-                        woven[:, PACK * at : PACK * (at + P)].rearrange("p (i t) -> p i t", t=PACK),
-                        acc.rearrange("p t i -> p i t"),
-                    )
                     nc.scalar.copy(out=y[:, :, at : at + P], in_=acc)
+                    if not last:
+                        nc.scalar.copy(
+                            out=woven[:, PACK * at : PACK * (at + P)].rearrange("p (i t) -> p i t", t=PACK),
+                            in_=acc.rearrange("p t i -> p i t"),
+                        )
+                if last:
+                    nc.vector.tensor_copy(
+                        out=woven[:].rearrange("p (run i t) -> p run t i", i=LINE, t=PACK),
+                        in_=y[:].rearrange("p t (run i) -> p run t i", i=LINE),
+                    )
                 rows = out_0[GROUP * g : GROUP * (g + 1), lo:hi].rearrange("(p t) i -> p t i", t=PACK)
-                (nc.sync if lo == 0 else nc.scalar).dma_start(out=rows, in_=y[:])
+                (nc.scalar if last else nc.sync).dma_start(out=rows, in_=y[:])
                 nc.vector.quantize_mx(
                     out=y_codes[:, PAIRS * g + lo : PAIRS * g + hi].bitcast(FP8X4),
                     scales=y_scales[:, PAIRS * g + lo : PAIRS * g + hi],
                     in_=woven[:],
                 )
 
-        def store_codes(queue, lo, hi):
-            words = out_1.rearrange("g p i t -> p g (i t)").bitcast(I32)
-            codes = y_codes[:].bitcast(I32).rearrange("p (g i) -> p g i", g=GROUPS)
-            queue.dma_start(out=words[:, :, lo:hi], in_=codes[:, :, lo:hi])
+        def store_codes(g, lo, hi):
+            words = out_1[g].rearrange("p i t -> p (i t)").bitcast(I32)
+            nc.sync.dma_start(out=words[:, lo:hi], in_=y_codes[:, PAIRS * g + lo : PAIRS * g + hi].bitcast(I32))
 
-        pick_r(0)
-        for step in range(TILES + GATE_LAG):
-            behind = step - GATE_LAG
+        z_first = keep.tile([P, PACK * PAIRS], F32, name="z_first")
+        make_q((0, 1))
+        pick_q(0)
+        for step in range(TILES):
+            make_r(step)
+            if step + 2 < TILES:
+                make_q((step + 2,))
+            if step in BLOCK_STEPS:
+                quantise_weight_block(BLOCK_STEPS.index(step))
             if step + 1 < TILES:
-                pick_r(step + 1)
-            if behind >= 0 and behind % 2 == 0:
-                make_h_pair(behind)
-            if behind >= 0:
-                sigmoid_of_diff(behind)
-            if step < TILES:
-                pick_q_less_r(step)
-            if behind >= 0 and behind % 2 == 1:
-                weigh_gate(behind)
-                weigh_gate(behind - 1)
-            if behind == PACK - 1:
-                z_first = products(0, 0, PAIRS)
-            if behind == TILES - 1:
-                quantise_z(0, z_first, 0, PAIRS, False)
-            if step == 0 or step % 2 == 1:
-                quantise_weight_block((step + 1) // 2)
+                pick_q(step + 1)
+            pick_r_less_q(step)
+            if step == FIRST_PRODUCTS:
+                make_h(0)
+                make_h(1)
+                gates_of_pair(0)
+                products(0, z_first, 0, PAIRS, (0, 1))
+        for pair in range(1, TILES // 2):
+            make_h(2 * pair)
+            make_h(2 * pair + 1)
+            gates_of_pair(pair)
+            if pair == 1:
+                quantise_weight_block(GROUPS)
+        products(0, z_first, 0, PAIRS, (2, 3))
+        quantise_z(0, z_first, 0, PAIRS)
+        for number in range(GROUPS + 1, len(weight_blocks)):
+            quantise_weight_block(number)
 
         edges = [sum(PIECES[:k]) for k in range(len(PIECES) + 1)]
         spans = list(zip(edges[:-1], edges[1:]))
         for number, (lo, hi) in enumerate(spans):
-            quantise_z(1, products(1, lo, hi), lo, hi, True)
+            z_piece = shared.tile(
+                [P, PACK * (hi - lo)], F32, name="z_piece%d" % number, align_bytes=ALIGN, offset=AT_Z_PIECE[number]
+            )
+            for pair in ((0, 1), (2, 3)):
+                products(1, z_piece, lo, hi, pair)
+            quantise_z(1, z_piece, lo, hi)
             if number == 1:
                 open_sums(*spans[0])
                 finish(*spans[0])
-                store_codes(nc.gpsimd, *spans[0])
+                store_codes(0, *spans[0])
                 open_sums(spans[1][0], PAIRS)
         for lo, hi in spans[1:]:
             finish(lo, hi)
-        store_codes(nc.sync, spans[1][0], PAIRS)
+        store_codes(0, spans[1][0], PAIRS)
+        store_codes(1, 0, PAIRS)
 
         plane_rows = y_scales[:].bitcast(I32).rearrange("p (g i) -> p g i", g=GROUPS)
-        for quad in range(4):
-            nc.sync.dma_start(
+        for quad, queue in enumerate([nc.sync, nc.scalar] * 2):
+            queue.dma_start(
                 out=out_2[:, 4 * quad : 4 * quad + 4, :].rearrange("g row i -> row g i").bitcast(I32),
                 in_=plane_rows[32 * quad : 32 * quad + 4, :, :],
             )

@@ -39,18 +39,18 @@ DEALT_DEPTH = 4
 RESULT_DEPTH = 4
 
 STAGE_BYTES = 4 * PACK * GROUP
-AT_STAGE_FIRST = 0
-AT_S2_IN = STAGE_BYTES - ALIGN
-AT_S3_DEALT = AT_S2_IN + H
+AT_S3_DEALT = 0
 AT_TAB_WORDS = AT_S3_DEALT + H - ALIGN
-AT_STAGES = (AT_STAGE_FIRST, AT_TAB_WORDS + ALIGN, AT_TAB_WORDS + ALIGN + STAGE_BYTES)
-AT_W3_IN = AT_STAGES[2] + STAGE_BYTES
+AT_W3_IN = AT_TAB_WORDS + ALIGN + 2 * STAGE_BYTES
 AT_TAB_SCALES = AT_W3_IN + 4 * H - ALIGN
 AT_V_LOW = AT_W3_IN + 4 * H
-AT_W2_DEALT = AT_TAB_SCALES + T - ALIGN
+AT_REL = AT_V_LOW + 4 * BANK
+AT_W2_DEALT = AT_TAB_SCALES + T
 AT_W2_IN = AT_W2_DEALT + 2 * H
 AT_V_HIGH = AT_W2_IN + 2 * H - ALIGN
-AT_DEALT = AT_V_HIGH + 4 * BANK
+AT_S2_IN = AT_V_HIGH + 4 * BANK - ALIGN
+AT_STAGES = (AT_S2_IN + H - ALIGN, AT_TAB_WORDS + ALIGN, AT_TAB_WORDS + ALIGN + STAGE_BYTES)
+AT_DEALT = AT_STAGES[0] + STAGE_BYTES
 DEALT_BYTES = 2 * PACK * GROUP
 AT_Y_WOVEN = AT_DEALT + DEALT_DEPTH * DEALT_BYTES
 Y_WOVEN_BYTES = 2 * PACK * PIECES[0]
@@ -98,7 +98,6 @@ def tile_list_triple_pair_rerank_kernel(
         s2_in = shared.tile([P, H], U8, name="s2_in", align_bytes=ALIGN, offset=AT_S2_IN)
         w2_s = keep.tile([P, H], U8, name="w2_s", align_bytes=ALIGN)
         w3_w = keep.tile([P, H], I32, name="w3_w", align_bytes=ALIGN)
-        rel_sb = keep.tile([P, GROUPS, PACK], F32, name="rel_sb")
 
         def load_scales(queues, plane, rows):
             for quad, queue in enumerate(queues):
@@ -107,18 +106,19 @@ def tile_list_triple_pair_rerank_kernel(
                     in_=rows[0, 4 * quad : 4 * quad + 4, :].bitcast(I32),
                 )
 
-        nc.vector.memset(tab_s[:].bitcast(I32), 0)
-        nc.vector.memset(s3_in[:].bitcast(I32), 0)
+        words = tab_words[0].rearrange("p e t -> p (e t)").bitcast(I32)
+        nc.gpsimd.memset(tab_s[:].bitcast(I32), 0)
         nc.gpsimd.memset(s2_in[:].bitcast(I32), 0)
+        nc.gpsimd.dma_start(out=tab_w[:, T // 2 :].bitcast(I32), in_=words[:, T // 2 :])
+        nc.gpsimd.memset(s3_in[:].bitcast(I32), 0)
         nc.sync.dma_start(offs_sb[:], offs)
+        nc.sync.dma_start(out=w2_in[:].bitcast(I32), in_=w2_words[0].bitcast(I32))
+        nc.sync.dma_start(out=tab_w[:, : T // 2].bitcast(I32), in_=words[:, : T // 2])
         nc.sync.dma_start(pos1_sb[:], pos1)
         nc.sync.dma_start(pos2_sb[:], pos2)
-        nc.sync.dma_start(out=tab_w[:].bitcast(I32), in_=tab_words[0].rearrange("p e t -> p (e t)").bitcast(I32))
-        nc.sync.dma_start(out=w2_in[:].bitcast(I32), in_=w2_words[0].bitcast(I32))
         load_scales([nc.scalar] * 4, tab_s, tab_scales)
-        load_scales([nc.scalar] * 4, s3_in, w3_scales)
-        load_scales([nc.gpsimd] * 4, s2_in, w2_scales)
-        nc.gpsimd.dma_start(out=rel_sb[:], in_=rel.rearrange("(g p t) -> p g t", g=GROUPS, t=PACK))
+        load_scales([nc.scalar] * 4, s2_in, w2_scales)
+        load_scales([nc.gpsimd] * 4, s3_in, w3_scales)
 
         def deal_columns(dst, src, walk):
             nc.vector.tensor_copy(
@@ -131,6 +131,8 @@ def tile_list_triple_pair_rerank_kernel(
         deal_columns(w2_s, s2_in, "g t m")
         w3_in = shared.tile([P, H], I32, name="w3_in", align_bytes=ALIGN, offset=AT_W3_IN)
         nc.sync.dma_start(out=w3_in[:], in_=w3_words[0].rearrange("p c t -> p (c t)").bitcast(I32))
+        rel_sb = shared.tile([P, GROUPS, PACK], F32, name="rel_sb", align_bytes=ALIGN, offset=AT_REL)
+        nc.sync.dma_start(out=rel_sb[:], in_=rel.rearrange("(g p t) -> p g t", g=GROUPS, t=PACK))
         v_w = {}
 
         def gather_words(lo, at):
@@ -270,9 +272,17 @@ def tile_list_triple_pair_rerank_kernel(
         y_scales = keep.tile([P, GROUPS * PAIRS], U8, name="y_scales", align_bytes=ALIGN)
         y_codes = keep.tile([P, GROUPS * PAIRS], U32, name="y_codes", align_bytes=ALIGN)
 
+        def store_and_quantise(queue, g, lo, hi, y, woven):
+            rows = out_0[GROUP * g : GROUP * (g + 1), lo:hi].rearrange("(p t) i -> p t i", t=PACK)
+            queue.dma_start(out=rows, in_=y[:])
+            nc.vector.quantize_mx(
+                out=y_codes[:, PAIRS * g + lo : PAIRS * g + hi].bitcast(FP8X4),
+                scales=y_scales[:, PAIRS * g + lo : PAIRS * g + hi],
+                in_=woven[:],
+            )
+
         def finish(lo, hi):
             width = hi - lo
-            last = hi == PAIRS
             for g in range(GROUPS):
                 y = results.tile([P, PACK, width], F32, name="y")
                 if lo == 0:
@@ -286,23 +296,27 @@ def tile_list_triple_pair_rerank_kernel(
                     acc = second_passes(1, g, col)
                     at = col - lo
                     nc.scalar.copy(out=y[:, :, at : at + P], in_=acc)
-                    if not last:
-                        nc.scalar.copy(
-                            out=woven[:, PACK * at : PACK * (at + P)].rearrange("p (i t) -> p i t", t=PACK),
-                            in_=acc.rearrange("p t i -> p i t"),
-                        )
-                if last:
-                    nc.vector.tensor_copy(
-                        out=woven[:].rearrange("p (run i t) -> p run t i", i=LINE, t=PACK),
-                        in_=y[:].rearrange("p t (run i) -> p run t i", i=LINE),
+                    nc.scalar.copy(
+                        out=woven[:, PACK * at : PACK * (at + P)].rearrange("p (i t) -> p i t", t=PACK),
+                        in_=acc.rearrange("p t i -> p i t"),
                     )
-                rows = out_0[GROUP * g : GROUP * (g + 1), lo:hi].rearrange("(p t) i -> p t i", t=PACK)
-                (nc.scalar if last else nc.sync).dma_start(out=rows, in_=y[:])
-                nc.vector.quantize_mx(
-                    out=y_codes[:, PAIRS * g + lo : PAIRS * g + hi].bitcast(FP8X4),
-                    scales=y_scales[:, PAIRS * g + lo : PAIRS * g + hi],
-                    in_=woven[:],
-                )
+                store_and_quantise(nc.sync, g, lo, hi, y, woven)
+
+        def finish_last(lo):
+            acc = [second_passes(1, g, lo) for g in range(GROUPS)]
+            y = [results.tile([P, PACK, P], F32, name="y") for g in range(GROUPS)]
+            woven = [results.tile([P, PACK * P], BF16, name="y_woven", align_bytes=ALIGN) for g in range(GROUPS)]
+            nc.scalar.copy(out=y[0][:], in_=acc[0])
+            nc.vector.tensor_copy(
+                out=woven[1][:].rearrange("p (i t) -> p i t", t=PACK), in_=acc[1].rearrange("p t i -> p i t")
+            )
+            nc.scalar.copy(out=y[1][:], in_=acc[1])
+            nc.vector.tensor_copy(
+                out=woven[0][:].rearrange("p (run i t) -> p run t i", i=LINE, t=PACK),
+                in_=y[0][:].rearrange("p t (run i) -> p run t i", i=LINE),
+            )
+            store_and_quantise(nc.scalar, 1, lo, PAIRS, y[1], woven[1])
+            store_and_quantise(nc.sync, 0, lo, PAIRS, y[0], woven[0])
 
         def store_codes(g, lo, hi):
             words = out_1[g].rearrange("p i t -> p (i t)").bitcast(I32)
@@ -350,10 +364,11 @@ def tile_list_triple_pair_rerank_kernel(
                 finish(*spans[0])
                 store_codes(0, *spans[0])
                 open_sums(spans[1][0], PAIRS)
-        for lo, hi in spans[1:]:
-            finish(lo, hi)
+        finish(*spans[1])
+        store_codes(1, 0, spans[1][1])
+        finish_last(spans[2][0])
+        store_codes(1, *spans[2])
         store_codes(0, spans[1][0], PAIRS)
-        store_codes(1, 0, PAIRS)
 
         plane_rows = y_scales[:].bitcast(I32).rearrange("p (g i) -> p g i", g=GROUPS)
         for quad, queue in enumerate([nc.sync, nc.scalar] * 2):

@@ -13,6 +13,7 @@ U16 = mybir.dt.uint16
 U8 = mybir.dt.uint8
 FP8X4 = mybir.dt.float8_e4m3fn_x4
 FP4X4 = mybir.dt.float4_e2m1fn_x4
+COPY = mybir.ActivationFunctionType.Copy
 MULT = mybir.AluOpType.mult
 SUBTRACT = mybir.AluOpType.subtract
 SIGMOID = mybir.ActivationFunctionType.Sigmoid
@@ -30,31 +31,38 @@ ALIGN = 64
 
 PIECES = (256, 128, 128)
 FIRST_PRODUCTS = 3
-BLOCK_STEPS = (0, 4)
+RUN = 8
+BLOCKS = 16
+BLOCK_STEPS = (0, 1)
 ROW_DEPTH = 4
 HEAD_DEPTH = 3
 DIFF_DEPTH = 3
 PAIR_DEPTH = 2
-DEALT_DEPTH = 4
+DEALT_DEPTH = 3
 RESULT_DEPTH = 4
 
 STAGE_BYTES = 4 * PACK * GROUP
 AT_S3_DEALT = 0
 AT_TAB_WORDS = AT_S3_DEALT + H - ALIGN
-AT_W3_IN = AT_TAB_WORDS + ALIGN + 2 * STAGE_BYTES
-AT_TAB_SCALES = AT_W3_IN + 4 * H - ALIGN
-AT_V_LOW = AT_W3_IN + 4 * H
-AT_REL = AT_V_LOW + 4 * BANK
+AT_TAB_SCALES = AT_TAB_WORDS + ALIGN + 2 * STAGE_BYTES
+AT_V_LOW = AT_TAB_SCALES
 AT_W2_DEALT = AT_TAB_SCALES + T
 AT_W2_IN = AT_W2_DEALT + 2 * H
 AT_V_HIGH = AT_W2_IN + 2 * H - ALIGN
 AT_S2_IN = AT_V_HIGH + 4 * BANK - ALIGN
-AT_STAGES = (AT_S2_IN + H - ALIGN, AT_TAB_WORDS + ALIGN, AT_TAB_WORDS + ALIGN + STAGE_BYTES)
+AT_REL = AT_S2_IN + ALIGN
+AT_W3_DEALT = AT_S2_IN + H - ALIGN
+AT_STAGES = (AT_W3_DEALT + 4 * H, AT_TAB_WORDS + ALIGN, AT_TAB_WORDS + ALIGN + STAGE_BYTES)
 AT_DEALT = AT_STAGES[0] + STAGE_BYTES
 DEALT_BYTES = 2 * PACK * GROUP
-AT_Y_WOVEN = AT_DEALT + DEALT_DEPTH * DEALT_BYTES
-Y_WOVEN_BYTES = 2 * PACK * PIECES[0]
-AT_Z_PIECE = (AT_Y_WOVEN + GROUPS * Y_WOVEN_BYTES, AT_DEALT + DEALT_BYTES, AT_Y_WOVEN)
+AT_Z_WOVEN = AT_DEALT + DEALT_DEPTH * DEALT_BYTES
+AT_Z_ONE = AT_Z_WOVEN + 2 * PACK * PAIRS
+AT_Z_FIRST = AT_Z_ONE + 4 * PACK * PIECES[0]
+AT_Z_PIECE = (AT_Z_ONE, AT_Z_ONE, AT_Z_FIRST + DEALT_BYTES)
+AT_Y_WOVEN = AT_Z_FIRST + 4 * PACK * PAIRS
+WOVEN_BYTES = 2 * PACK * P
+Y_WOVEN_PLACE = {(0, 0): 0, (0, 1): 4, (256, 0): 8, (256, 1): 10, (384, 0): 0, (384, 1): 9}
+AT_ROUNDED = [AT_DEALT + DEALT_BYTES * k for k in (0, 1, 2, 0)] + [AT_Z_FIRST, AT_Z_FIRST + DEALT_BYTES]
 
 
 def tile_list_triple_pair_rerank_kernel(
@@ -82,11 +90,6 @@ def tile_list_triple_pair_rerank_kernel(
         diff_ring = ring_of(DIFF_DEPTH, 2 * PAIRS, F32, "diff")
         gated_ring = ring_of(PAIR_DEPTH, PAIRS, F32, "gated")
         head_ring = ring_of(HEAD_DEPTH, PAIRS, F32, "q_head")
-        z_woven_ring = ring_of(PAIR_DEPTH, PACK * PAIRS, BF16, "z_woven")
-        dealt_ring = [
-            shared.tile([P, PACK * GROUP], BF16, name="dealt%d" % k, align_bytes=ALIGN, offset=AT_DEALT + k * DEALT_BYTES)
-            for k in range(DEALT_DEPTH)
-        ]
 
         offs_sb = keep.tile([P, S // LIST_ROWS], U16, name="offs_sb")
         pos1_sb = keep.tile([P, PAIRS // LIST_ROWS], U16, name="pos1_sb")
@@ -94,10 +97,10 @@ def tile_list_triple_pair_rerank_kernel(
         tab_w = shared.tile([P, T], U32, name="tab_w", align_bytes=ALIGN, offset=AT_TAB_WORDS)
         tab_s = shared.tile([P, T], U8, name="tab_s", align_bytes=ALIGN, offset=AT_TAB_SCALES)
         w2_in = shared.tile([P, 2 * H], U8, name="w2_in", align_bytes=ALIGN, offset=AT_W2_IN)
+        w3_in = shared.tile([P, 4 * H], U8, name="w3_in", align_bytes=ALIGN, offset=AT_DEALT)
         s3_in = keep.tile([P, H], U8, name="s3_in", align_bytes=ALIGN)
         s2_in = shared.tile([P, H], U8, name="s2_in", align_bytes=ALIGN, offset=AT_S2_IN)
         w2_s = keep.tile([P, H], U8, name="w2_s", align_bytes=ALIGN)
-        w3_w = keep.tile([P, H], I32, name="w3_w", align_bytes=ALIGN)
 
         def load_scales(queues, plane, rows):
             for quad, queue in enumerate(queues):
@@ -118,21 +121,18 @@ def tile_list_triple_pair_rerank_kernel(
         nc.sync.dma_start(pos2_sb[:], pos2)
         load_scales([nc.scalar] * 4, tab_s, tab_scales)
         load_scales([nc.scalar] * 4, s2_in, w2_scales)
-        load_scales([nc.gpsimd] * 4, s3_in, w3_scales)
+        load_scales([nc.gpsimd] + [nc.scalar] * 3, s3_in, w3_scales)
+        nc.gpsimd.dma_start(out=w3_in[:].bitcast(I32), in_=w3_words[0].rearrange("p c t -> p (c t)").bitcast(I32))
 
-        def deal_columns(dst, src, walk):
+        def deal_columns(dst, src):
             nc.vector.tensor_copy(
-                out=dst[:].rearrange("p (g t m) -> p " + walk, g=GROUPS, t=PACK),
-                in_=src[:].rearrange("p (g m t) -> p " + walk, g=GROUPS, t=PACK),
+                out=dst[:].bitcast(I32).rearrange("p (g t b w) -> p g t b w", g=GROUPS, t=PACK, b=BLOCKS),
+                in_=src[:].bitcast(I32).rearrange("p (g b t w) -> p g t b w", g=GROUPS, t=PACK, b=BLOCKS),
             )
 
         v_s = keep.tile([P, S], U8, name="v_s", align_bytes=ALIGN)
         nc.vector.tensor_copy(v_s[:], tab_s[:].indirect(offs_sb[:]))
-        deal_columns(w2_s, s2_in, "g t m")
-        w3_in = shared.tile([P, H], I32, name="w3_in", align_bytes=ALIGN, offset=AT_W3_IN)
-        nc.sync.dma_start(out=w3_in[:], in_=w3_words[0].rearrange("p c t -> p (c t)").bitcast(I32))
-        rel_sb = shared.tile([P, GROUPS, PACK], F32, name="rel_sb", align_bytes=ALIGN, offset=AT_REL)
-        nc.sync.dma_start(out=rel_sb[:], in_=rel.rearrange("(g p t) -> p g t", g=GROUPS, t=PACK))
+        deal_columns(w2_s, s2_in)
         v_w = {}
 
         def gather_words(lo, at):
@@ -142,21 +142,16 @@ def tile_list_triple_pair_rerank_kernel(
 
         gather_words(0, AT_V_LOW)
         w2_w = shared.tile([P, 2 * H], U8, name="w2_w", align_bytes=ALIGN, offset=AT_W2_DEALT)
-        deal_columns(w2_w[:].bitcast(U16), w2_in[:].bitcast(U16), "g t m")
+        deal_columns(w2_w, w2_in)
         gather_words(BANK, AT_V_HIGH)
-        deal_columns(w3_w, w3_in, "g m t")
+        w3_w = shared.tile([P, 4 * H], U8, name="w3_w", align_bytes=ALIGN, offset=AT_W3_DEALT)
+        deal_columns(w3_w, w3_in)
         w3_s = shared.tile([P, H], U8, name="w3_s", align_bytes=ALIGN, offset=AT_S3_DEALT)
-        deal_columns(w3_s, s3_in, "g t m")
+        deal_columns(w3_s, s3_in)
         stage_ring = [
             shared.tile([P, PACK, GROUP], F32, name="stage%d" % k, align_bytes=ALIGN, offset=at)
             for k, at in enumerate(AT_STAGES)
         ]
-
-        def copy_on(on_vector, out, in_):
-            if on_vector:
-                nc.vector.tensor_copy(out=out, in_=in_)
-            else:
-                nc.scalar.copy(out=out, in_=in_)
 
         def quantised(width, name, woven):
             codes = keep.tile([P, width], U32, name=name + "_codes", align_bytes=ALIGN)
@@ -172,13 +167,21 @@ def tile_list_triple_pair_rerank_kernel(
             name, w, row_group, col_group = weight_blocks[number]
             stage = take(stage_ring)
             rows = w[GROUP * row_group : GROUP * (row_group + 1), GROUP * col_group : GROUP * (col_group + 1)]
-            nc.sync.dma_start(out=stage[:], in_=rows.rearrange("(p j) c -> p j c", j=PACK))
-            dealt = take(dealt_ring)
-            copy_on(
-                number == 0,
-                dealt[:].rearrange("p (t m j) -> p m t j", t=PACK, j=PACK),
-                stage[:].rearrange("p j (m t) -> p m t j", t=PACK),
-            )
+            dealt = shared.tile([P, PACK * GROUP], BF16, name="dealt%d" % number, align_bytes=ALIGN, offset=AT_ROUNDED[number])
+            if name == "w1":
+                (nc.gpsimd if number == 0 else nc.sync).dma_start(out=stage[:], in_=rows.rearrange("(p j) c -> p j c", j=PACK))
+                into = dealt[:].rearrange("p (t b e j) -> p b t e j", t=PACK, e=RUN, j=PACK)
+                source = stage[:].rearrange("p j (b t e) -> p b t e j", t=PACK, e=RUN)
+            else:
+                by_slot = rows.rearrange("(b j e) n -> j b e n", j=PACK, e=RUN)
+                for j in range(PACK):
+                    nc.sync.dma_start(out=stage[:, j, :], in_=by_slot[j])
+                into = dealt[:].rearrange("p (t m j) -> p m t j", t=PACK, j=PACK)
+                source = stage[:].rearrange("p j (m t) -> p m t j", t=PACK)
+            if name == "w1":
+                nc.vector.tensor_copy(out=into, in_=source)
+            else:
+                nc.scalar.copy(out=into, in_=source)
             weight_q[name, row_group, col_group] = quantised(GROUP, "%s_%d%d" % (name, row_group, col_group), dealt[:])
 
         def first_stage(jobs):
@@ -203,7 +206,7 @@ def tile_list_triple_pair_rerank_kernel(
 
         def make_r(a):
             r_rows[a] = take(r_ring)
-            first_stage([(r_rows[a], w3_w[:, P * a : P * (a + 1)].bitcast(FP8X4), w3_s[:, P * a : P * (a + 1)])])
+            first_stage([(r_rows[a], w3_w[:, 4 * P * a : 4 * P * (a + 1)].bitcast(FP8X4), w3_s[:, P * a : P * (a + 1)])])
 
         def make_h(a):
             g, t = divmod(a, PACK)
@@ -239,15 +242,27 @@ def tile_list_triple_pair_rerank_kernel(
 
         z_q = {}
 
-        def quantise_z(g, z_tile, lo, hi):
-            woven = take(z_woven_ring)[:, : PACK * (hi - lo)]
+        def quantise_z(g, z_tile, lo, hi, on_vector):
+            if lo == 0:
+                woven = shared.tile(
+                    [P, PACK * (hi - lo)], BF16, name="z_woven_first%d" % g, align_bytes=ALIGN, offset=AT_Z_WOVEN
+                )[:]
+            elif hi == PAIRS:
+                at = AT_Y_WOVEN + Y_WOVEN_PLACE[0, 1] * WOVEN_BYTES // 2
+                woven = shared.tile([P, PACK * (hi - lo)], BF16, name="z_woven_last", align_bytes=ALIGN, offset=at)[:]
+            else:
+                woven = keep.tile([P, PACK * (hi - lo)], BF16, name="z_woven_middle", align_bytes=ALIGN)[:]
             runs = (hi - lo) // LINE
-            nc.vector.tensor_tensor(
-                woven.rearrange("p (run i t) -> p run t i", i=LINE, t=PACK),
-                z_tile[:].rearrange("p (t run i) -> p run t i", t=PACK, i=LINE),
-                rel_sb[:, g, :].unsqueeze(1).unsqueeze(3).broadcast_to([P, runs, PACK, LINE]),
-                MULT,
-            )
+            into = woven.rearrange("p (run i t) -> p run t i", i=LINE, t=PACK)
+            z = z_tile[:].rearrange("p (t run i) -> p run t i", t=PACK, i=LINE)
+            if on_vector:
+                spread = rel_sb[:, g, :, 0:1].unsqueeze(1).broadcast_to([P, runs, PACK, LINE])
+                nc.vector.tensor_tensor(into, z, spread, MULT)
+            else:
+                for t in range(PACK):
+                    row = z_tile[:, (hi - lo) * t : (hi - lo) * (t + 1)]
+                    nc.scalar.activation(out=row, in_=row, func=COPY, scale=rel_sb[:, g, t, 0:1])
+                nc.scalar.copy(out=into, in_=z)
             codes, scales = quantised(hi - lo, "z%d_%d" % (g, lo), woven)
             for col in range(lo, hi, P):
                 z_q[g, col] = (codes[:, col - lo : col - lo + P].bitcast(FP8X4), scales[:, col - lo : col - lo + P])
@@ -272,6 +287,10 @@ def tile_list_triple_pair_rerank_kernel(
         y_scales = keep.tile([P, GROUPS * PAIRS], U8, name="y_scales", align_bytes=ALIGN)
         y_codes = keep.tile([P, GROUPS * PAIRS], U32, name="y_codes", align_bytes=ALIGN)
 
+        def woven_y(g, lo, hi):
+            at = AT_Y_WOVEN + Y_WOVEN_PLACE[lo, g] * WOVEN_BYTES // 2
+            return shared.tile([P, PACK * (hi - lo)], BF16, name="y_woven%d_%d" % (lo, g), align_bytes=ALIGN, offset=at)
+
         def store_and_quantise(queue, g, lo, hi, y, woven):
             rows = out_0[GROUP * g : GROUP * (g + 1), lo:hi].rearrange("(p t) i -> p t i", t=PACK)
             queue.dma_start(out=rows, in_=y[:])
@@ -285,13 +304,7 @@ def tile_list_triple_pair_rerank_kernel(
             width = hi - lo
             for g in range(GROUPS):
                 y = results.tile([P, PACK, width], F32, name="y")
-                if lo == 0:
-                    woven = shared.tile(
-                        [P, PACK * width], BF16, name="y_first%d" % g, align_bytes=ALIGN,
-                        offset=AT_Y_WOVEN + g * Y_WOVEN_BYTES,
-                    )
-                else:
-                    woven = results.tile([P, PACK * width], BF16, name="y_woven", align_bytes=ALIGN)
+                woven = woven_y(g, lo, hi)
                 for col in range(lo, hi, P):
                     acc = second_passes(1, g, col)
                     at = col - lo
@@ -305,7 +318,7 @@ def tile_list_triple_pair_rerank_kernel(
         def finish_last(lo):
             acc = [second_passes(1, g, lo) for g in range(GROUPS)]
             y = [results.tile([P, PACK, P], F32, name="y") for g in range(GROUPS)]
-            woven = [results.tile([P, PACK * P], BF16, name="y_woven", align_bytes=ALIGN) for g in range(GROUPS)]
+            woven = [woven_y(g, lo, PAIRS) for g in range(GROUPS)]
             nc.scalar.copy(out=y[0][:], in_=acc[0])
             nc.vector.tensor_copy(
                 out=woven[1][:].rearrange("p (i t) -> p i t", t=PACK), in_=acc[1].rearrange("p t i -> p i t")
@@ -322,18 +335,24 @@ def tile_list_triple_pair_rerank_kernel(
             words = out_1[g].rearrange("p i t -> p (i t)").bitcast(I32)
             nc.sync.dma_start(out=words[:, lo:hi], in_=y_codes[:, PAIRS * g + lo : PAIRS * g + hi].bitcast(I32))
 
-        z_first = keep.tile([P, PACK * PAIRS], F32, name="z_first")
-        make_q((0, 1))
+        rel_sb = shared.tile([P, GROUPS, PACK, RUN], F32, name="rel_sb", align_bytes=ALIGN, offset=AT_REL)
+        z_first = shared.tile([P, PACK * PAIRS], F32, name="z_first", align_bytes=ALIGN, offset=AT_Z_FIRST)
+        make_q((0, 1, 2))
         pick_q(0)
         for step in range(TILES):
             make_r(step)
-            if step + 2 < TILES:
+            if 0 < step < TILES - 2:
                 make_q((step + 2,))
             if step in BLOCK_STEPS:
                 quantise_weight_block(BLOCK_STEPS.index(step))
             if step + 1 < TILES:
                 pick_q(step + 1)
             pick_r_less_q(step)
+            if step == 0:
+                by_tile = rel.rearrange("(g b t e) -> g t b e", g=GROUPS, t=PACK, e=RUN)
+                for a in range(TILES):
+                    g, t = divmod(a, PACK)
+                    nc.sync.dma_start(out=rel_sb[:, g, t, 0:1], in_=by_tile[g, t])
             if step == FIRST_PRODUCTS:
                 make_h(0)
                 make_h(1)
@@ -346,9 +365,10 @@ def tile_list_triple_pair_rerank_kernel(
             if pair == 1:
                 quantise_weight_block(GROUPS)
         products(0, z_first, 0, PAIRS, (2, 3))
-        quantise_z(0, z_first, 0, PAIRS)
-        for number in range(GROUPS + 1, len(weight_blocks)):
-            quantise_weight_block(number)
+        quantise_weight_block(3)
+        quantise_z(0, z_first, 0, PAIRS, False)
+        quantise_weight_block(4)
+        quantise_weight_block(5)
 
         edges = [sum(PIECES[:k]) for k in range(len(PIECES) + 1)]
         spans = list(zip(edges[:-1], edges[1:]))
@@ -358,7 +378,7 @@ def tile_list_triple_pair_rerank_kernel(
             )
             for pair in ((0, 1), (2, 3)):
                 products(1, z_piece, lo, hi, pair)
-            quantise_z(1, z_piece, lo, hi)
+            quantise_z(1, z_piece, lo, hi, True)
             if number == 1:
                 open_sums(*spans[0])
                 finish(*spans[0])
@@ -371,8 +391,8 @@ def tile_list_triple_pair_rerank_kernel(
         store_codes(0, spans[1][0], PAIRS)
 
         plane_rows = y_scales[:].bitcast(I32).rearrange("p (g i) -> p g i", g=GROUPS)
-        for quad, queue in enumerate([nc.sync, nc.scalar] * 2):
-            queue.dma_start(
+        for quad in range(4):
+            nc.sync.dma_start(
                 out=out_2[:, 4 * quad : 4 * quad + 4, :].rearrange("g row i -> row g i").bitcast(I32),
                 in_=plane_rows[32 * quad : 32 * quad + 4, :, :],
             )

@@ -38,7 +38,7 @@ ROW_DEPTH = 4
 HEAD_DEPTH = 3
 DIFF_DEPTH = 3
 PAIR_DEPTH = 2
-DEALT_DEPTH = 3
+DEALT_DEPTH = 4
 RESULT_DEPTH = 4
 
 STAGE_BYTES = 4 * PACK * GROUP
@@ -57,12 +57,12 @@ AT_DEALT = AT_STAGES[0] + STAGE_BYTES
 DEALT_BYTES = 2 * PACK * GROUP
 AT_Z_WOVEN = AT_DEALT + DEALT_DEPTH * DEALT_BYTES
 AT_Z_ONE = AT_Z_WOVEN + 2 * PACK * PAIRS
+AT_Z_PIECE = (AT_Z_ONE, AT_DEALT + DEALT_BYTES, AT_Z_WOVEN + PACK * PAIRS)
 AT_Z_FIRST = AT_Z_ONE + 4 * PACK * PIECES[0]
-AT_Z_PIECE = (AT_Z_ONE, AT_Z_ONE, AT_Z_FIRST + DEALT_BYTES)
 AT_Y_WOVEN = AT_Z_FIRST + 4 * PACK * PAIRS
 WOVEN_BYTES = 2 * PACK * P
 Y_WOVEN_PLACE = {(0, 0): 0, (0, 1): 4, (256, 0): 8, (256, 1): 10, (384, 0): 0, (384, 1): 9}
-AT_ROUNDED = [AT_DEALT + DEALT_BYTES * k for k in (0, 1, 2, 0)] + [AT_Z_FIRST, AT_Z_FIRST + DEALT_BYTES]
+AT_ROUNDED = [AT_DEALT + DEALT_BYTES * k for k in (0, 1, 2, 3, 0, 1)]
 
 
 def tile_list_triple_pair_rerank_kernel(
@@ -242,27 +242,25 @@ def tile_list_triple_pair_rerank_kernel(
 
         z_q = {}
 
-        def quantise_z(g, z_tile, lo, hi, on_vector):
-            if lo == 0:
-                woven = shared.tile(
-                    [P, PACK * (hi - lo)], BF16, name="z_woven_first%d" % g, align_bytes=ALIGN, offset=AT_Z_WOVEN
-                )[:]
+        def quantise_z(g, z, lo, hi, on_vector):
+            if g == 0:
+                at = AT_Z_WOVEN + 2 * PACK * lo
+                woven = shared.tile([P, PACK * (hi - lo)], BF16, name="z_woven0_%d" % lo, align_bytes=ALIGN, offset=at)[:]
             elif hi == PAIRS:
                 at = AT_Y_WOVEN + Y_WOVEN_PLACE[0, 1] * WOVEN_BYTES // 2
                 woven = shared.tile([P, PACK * (hi - lo)], BF16, name="z_woven_last", align_bytes=ALIGN, offset=at)[:]
             else:
-                woven = keep.tile([P, PACK * (hi - lo)], BF16, name="z_woven_middle", align_bytes=ALIGN)[:]
+                woven = keep.tile([P, PACK * (hi - lo)], BF16, name="z_woven1_%d" % lo, align_bytes=ALIGN)[:]
             runs = (hi - lo) // LINE
             into = woven.rearrange("p (run i t) -> p run t i", i=LINE, t=PACK)
-            z = z_tile[:].rearrange("p (t run i) -> p run t i", t=PACK, i=LINE)
+            by_runs = z.rearrange("p t (run i) -> p run t i", i=LINE)
             if on_vector:
                 spread = rel_sb[:, g, :, 0:1].unsqueeze(1).broadcast_to([P, runs, PACK, LINE])
-                nc.vector.tensor_tensor(into, z, spread, MULT)
+                nc.vector.tensor_tensor(into, by_runs, spread, MULT)
             else:
                 for t in range(PACK):
-                    row = z_tile[:, (hi - lo) * t : (hi - lo) * (t + 1)]
-                    nc.scalar.activation(out=row, in_=row, func=COPY, scale=rel_sb[:, g, t, 0:1])
-                nc.scalar.copy(out=into, in_=z)
+                    nc.scalar.activation(out=z[:, t, :], in_=z[:, t, :], func=COPY, scale=rel_sb[:, g, t, 0:1])
+                nc.scalar.copy(out=into, in_=by_runs)
             codes, scales = quantised(hi - lo, "z%d_%d" % (g, lo), woven)
             for col in range(lo, hi, P):
                 z_q[g, col] = (codes[:, col - lo : col - lo + P].bitcast(FP8X4), scales[:, col - lo : col - lo + P])
@@ -365,10 +363,11 @@ def tile_list_triple_pair_rerank_kernel(
             if pair == 1:
                 quantise_weight_block(GROUPS)
         products(0, z_first, 0, PAIRS, (2, 3))
-        quantise_weight_block(3)
-        quantise_z(0, z_first, 0, PAIRS, False)
-        quantise_weight_block(4)
-        quantise_weight_block(5)
+        z_rows = z_first[:].rearrange("p (t i) -> p t i", t=PACK)
+        quantise_z(0, z_rows[:, :, : PIECES[0]], 0, PIECES[0], True)
+        for number in range(GROUPS + 1, len(weight_blocks)):
+            quantise_weight_block(number)
+        quantise_z(0, z_rows[:, :, PIECES[0] :], PIECES[0], PAIRS, False)
 
         edges = [sum(PIECES[:k]) for k in range(len(PIECES) + 1)]
         spans = list(zip(edges[:-1], edges[1:]))
@@ -378,7 +377,7 @@ def tile_list_triple_pair_rerank_kernel(
             )
             for pair in ((0, 1), (2, 3)):
                 products(1, z_piece, lo, hi, pair)
-            quantise_z(1, z_piece, lo, hi, True)
+            quantise_z(1, z_piece[:].rearrange("p (t i) -> p t i", t=PACK), lo, hi, True)
             if number == 1:
                 open_sums(*spans[0])
                 finish(*spans[0])

@@ -176,8 +176,8 @@ def tile_list_triple_pair_rerank_kernel(
                 by_slot = rows.rearrange("(b j e) n -> j b e n", j=PACK, e=RUN)
                 for j in range(PACK):
                     nc.sync.dma_start(out=stage[:, j, :], in_=by_slot[j])
-                into = dealt[:].rearrange("p (t m j) -> p m t j", t=PACK, j=PACK)
-                source = stage[:].rearrange("p j (m t) -> p m t j", t=PACK)
+                into = dealt[:].rearrange("p (t m j) -> p m j t", t=PACK, j=PACK)
+                source = stage[:].rearrange("p j (m t) -> p m j t", t=PACK)
             if name == "w1":
                 nc.vector.tensor_copy(out=into, in_=source)
             else:
@@ -315,23 +315,24 @@ def tile_list_triple_pair_rerank_kernel(
 
         def finish_last(lo):
             acc = [second_passes(1, g, lo) for g in range(GROUPS)]
-            y = [results.tile([P, PACK, P], F32, name="y") for g in range(GROUPS)]
+            y = [keep.tile([P, PACK, P], F32, name="y_last%d" % g) for g in range(GROUPS)]
             woven = [woven_y(g, lo, PAIRS) for g in range(GROUPS)]
             nc.scalar.copy(out=y[0][:], in_=acc[0])
-            nc.vector.tensor_copy(
-                out=woven[1][:].rearrange("p (i t) -> p i t", t=PACK), in_=acc[1].rearrange("p t i -> p i t")
+            nc.vector.tensor_copy(out=y[1][:], in_=acc[1])
+            nc.scalar.copy(
+                out=woven[0][:].rearrange("p (i t) -> p i t", t=PACK), in_=acc[0].rearrange("p t i -> p i t")
             )
-            nc.scalar.copy(out=y[1][:], in_=acc[1])
             nc.vector.tensor_copy(
-                out=woven[0][:].rearrange("p (run i t) -> p run t i", i=LINE, t=PACK),
-                in_=y[0][:].rearrange("p t (run i) -> p run t i", i=LINE),
+                out=woven[1][:].rearrange("p (run i t) -> p run t i", i=LINE, t=PACK),
+                in_=y[1][:].rearrange("p t (run i) -> p run t i", i=LINE),
             )
-            store_and_quantise(nc.scalar, 1, lo, PAIRS, y[1], woven[1])
-            store_and_quantise(nc.sync, 0, lo, PAIRS, y[0], woven[0])
+            for g in range(GROUPS):
+                store_and_quantise(nc.sync, g, lo, PAIRS, y[g], woven[g])
 
-        def store_codes(g, lo, hi):
-            words = out_1[g].rearrange("p i t -> p (i t)").bitcast(I32)
-            nc.sync.dma_start(out=words[:, lo:hi], in_=y_codes[:, PAIRS * g + lo : PAIRS * g + hi].bitcast(I32))
+        def store_codes(lo, hi):
+            words = out_1.rearrange("g p i t -> p g (i t)").bitcast(I32)
+            codes = y_codes[:].bitcast(I32).rearrange("p (g i) -> p g i", g=GROUPS)
+            nc.sync.dma_start(out=words[:, :, lo:hi], in_=codes[:, :, lo:hi])
 
         rel_sb = shared.tile([P, GROUPS, PACK, RUN], F32, name="rel_sb", align_bytes=ALIGN, offset=AT_REL)
         z_first = shared.tile([P, PACK * PAIRS], F32, name="z_first", align_bytes=ALIGN, offset=AT_Z_FIRST)
@@ -381,17 +382,15 @@ def tile_list_triple_pair_rerank_kernel(
             if number == 1:
                 open_sums(*spans[0])
                 finish(*spans[0])
-                store_codes(0, *spans[0])
                 open_sums(spans[1][0], PAIRS)
         finish(*spans[1])
-        store_codes(1, 0, spans[1][1])
+        store_codes(0, spans[1][1])
         finish_last(spans[2][0])
-        store_codes(1, *spans[2])
-        store_codes(0, spans[1][0], PAIRS)
+        store_codes(*spans[2])
 
         plane_rows = y_scales[:].bitcast(I32).rearrange("p (g i) -> p g i", g=GROUPS)
         for quad in range(4):
-            nc.sync.dma_start(
+            nc.scalar.dma_start(
                 out=out_2[:, 4 * quad : 4 * quad + 4, :].rearrange("g row i -> row g i").bitcast(I32),
                 in_=plane_rows[32 * quad : 32 * quad + 4, :, :],
             )

@@ -26,22 +26,25 @@ TILES = H // P
 BANK = 512
 BANKS = 8
 LIST_ROWS = 16
+RUN = 8
+BLOCKS = P // RUN
+QUADS = 4
 LINE = 4
 ALIGN = 64
 
 PIECES = (256, 128, 128)
+FIRST_Q_TILES = 3
 FIRST_PRODUCTS = 3
-RUN = 8
-BLOCKS = 16
-BLOCK_STEPS = (0, 1)
 ROW_DEPTH = 4
 HEAD_DEPTH = 3
 DIFF_DEPTH = 3
-PAIR_DEPTH = 2
-DEALT_DEPTH = 4
+GATED_DEPTH = 2
+ROUNDED_DEPTH = 4
 RESULT_DEPTH = 4
 
 STAGE_BYTES = 4 * PACK * GROUP
+ROUNDED_BYTES = 2 * PACK * GROUP
+WOVEN_BYTES = 2 * PACK * P
 AT_S3_DEALT = 0
 AT_TAB_WORDS = AT_S3_DEALT + H - ALIGN
 AT_TAB_SCALES = AT_TAB_WORDS + ALIGN + 2 * STAGE_BYTES
@@ -53,16 +56,20 @@ AT_S2_IN = AT_V_HIGH + 4 * BANK - ALIGN
 AT_REL = AT_S2_IN + ALIGN
 AT_W3_DEALT = AT_S2_IN + H - ALIGN
 AT_STAGES = (AT_W3_DEALT + 4 * H, AT_TAB_WORDS + ALIGN, AT_TAB_WORDS + ALIGN + STAGE_BYTES)
-AT_DEALT = AT_STAGES[0] + STAGE_BYTES
-DEALT_BYTES = 2 * PACK * GROUP
-AT_Z_WOVEN = AT_DEALT + DEALT_DEPTH * DEALT_BYTES
-AT_Z_ONE = AT_Z_WOVEN + 2 * PACK * PAIRS
-AT_Z_PIECE = (AT_Z_ONE, AT_DEALT + DEALT_BYTES, AT_Z_WOVEN + PACK * PAIRS)
-AT_Z_FIRST = AT_Z_ONE + 4 * PACK * PIECES[0]
-AT_Y_WOVEN = AT_Z_FIRST + 4 * PACK * PAIRS
-WOVEN_BYTES = 2 * PACK * P
-Y_WOVEN_PLACE = {(0, 0): 0, (0, 1): 4, (256, 0): 8, (256, 1): 10, (384, 0): 0, (384, 1): 9}
-AT_ROUNDED = [AT_DEALT + DEALT_BYTES * k for k in (0, 1, 2, 3, 0, 1)]
+AT_ROUNDED = AT_STAGES[0] + STAGE_BYTES
+AT_W3_IN = AT_ROUNDED
+AT_Z_WOVEN = AT_ROUNDED + ROUNDED_DEPTH * ROUNDED_BYTES
+AT_Z_OWN = AT_Z_WOVEN + 2 * PACK * PAIRS
+AT_Z_PIECE = (AT_Z_OWN, AT_ROUNDED + ROUNDED_BYTES, AT_Z_WOVEN + 2 * PACK * PIECES[0])
+AT_Z_FIRST = AT_Z_OWN + 4 * PACK * PIECES[0]
+AT_Y_FIRST = AT_Z_FIRST + 4 * PACK * PAIRS
+AT_Y_MIDDLE = AT_Y_FIRST + GROUPS * 2 * PACK * PIECES[0]
+AT_Y_WOVEN = (
+    (AT_Y_FIRST, AT_Y_FIRST + 2 * PACK * PIECES[0]),
+    (AT_Y_MIDDLE, AT_Y_MIDDLE + WOVEN_BYTES),
+    (AT_Y_FIRST, AT_Y_MIDDLE + WOVEN_BYTES // 2),
+)
+AT_Z_WOVEN_LAST = AT_Y_WOVEN[0][1]
 
 
 def tile_list_triple_pair_rerank_kernel(
@@ -88,7 +95,7 @@ def tile_list_triple_pair_rerank_kernel(
         r_ring = ring_of(ROW_DEPTH, S, F32, "r")
         q_ring = ring_of(ROW_DEPTH, S, F32, "q")
         diff_ring = ring_of(DIFF_DEPTH, 2 * PAIRS, F32, "diff")
-        gated_ring = ring_of(PAIR_DEPTH, PAIRS, F32, "gated")
+        gated_ring = ring_of(GATED_DEPTH, PAIRS, F32, "gated")
         head_ring = ring_of(HEAD_DEPTH, PAIRS, F32, "q_head")
 
         offs_sb = keep.tile([P, S // LIST_ROWS], U16, name="offs_sb")
@@ -97,7 +104,7 @@ def tile_list_triple_pair_rerank_kernel(
         tab_w = shared.tile([P, T], U32, name="tab_w", align_bytes=ALIGN, offset=AT_TAB_WORDS)
         tab_s = shared.tile([P, T], U8, name="tab_s", align_bytes=ALIGN, offset=AT_TAB_SCALES)
         w2_in = shared.tile([P, 2 * H], U8, name="w2_in", align_bytes=ALIGN, offset=AT_W2_IN)
-        w3_in = shared.tile([P, 4 * H], U8, name="w3_in", align_bytes=ALIGN, offset=AT_DEALT)
+        w3_in = shared.tile([P, 4 * H], U8, name="w3_in", align_bytes=ALIGN, offset=AT_W3_IN)
         s3_in = keep.tile([P, H], U8, name="s3_in", align_bytes=ALIGN)
         s2_in = shared.tile([P, H], U8, name="s2_in", align_bytes=ALIGN, offset=AT_S2_IN)
         w2_s = keep.tile([P, H], U8, name="w2_s", align_bytes=ALIGN)
@@ -109,19 +116,19 @@ def tile_list_triple_pair_rerank_kernel(
                     in_=rows[0, 4 * quad : 4 * quad + 4, :].bitcast(I32),
                 )
 
-        words = tab_words[0].rearrange("p e t -> p (e t)").bitcast(I32)
+        table = tab_words[0].rearrange("p e t -> p (e t)").bitcast(I32)
         nc.gpsimd.memset(tab_s[:].bitcast(I32), 0)
         nc.gpsimd.memset(s2_in[:].bitcast(I32), 0)
-        nc.gpsimd.dma_start(out=tab_w[:, T // 2 :].bitcast(I32), in_=words[:, T // 2 :])
+        nc.gpsimd.dma_start(out=tab_w[:, T // 2 :].bitcast(I32), in_=table[:, T // 2 :])
         nc.gpsimd.memset(s3_in[:].bitcast(I32), 0)
         nc.sync.dma_start(offs_sb[:], offs)
         nc.sync.dma_start(out=w2_in[:].bitcast(I32), in_=w2_words[0].bitcast(I32))
-        nc.sync.dma_start(out=tab_w[:, : T // 2].bitcast(I32), in_=words[:, : T // 2])
+        nc.sync.dma_start(out=tab_w[:, : T // 2].bitcast(I32), in_=table[:, : T // 2])
         nc.sync.dma_start(pos1_sb[:], pos1)
         nc.sync.dma_start(pos2_sb[:], pos2)
-        load_scales([nc.scalar] * 4, tab_s, tab_scales)
-        load_scales([nc.scalar] * 4, s2_in, w2_scales)
-        load_scales([nc.gpsimd] + [nc.scalar] * 3, s3_in, w3_scales)
+        load_scales([nc.scalar] * QUADS, tab_s, tab_scales)
+        load_scales([nc.scalar] * QUADS, s2_in, w2_scales)
+        load_scales([nc.gpsimd] + [nc.scalar] * (QUADS - 1), s3_in, w3_scales)
         nc.gpsimd.dma_start(out=w3_in[:].bitcast(I32), in_=w3_words[0].rearrange("p c t -> p (c t)").bitcast(I32))
 
         def deal_columns(dst, src):
@@ -167,22 +174,24 @@ def tile_list_triple_pair_rerank_kernel(
             name, w, row_group, col_group = weight_blocks[number]
             stage = take(stage_ring)
             rows = w[GROUP * row_group : GROUP * (row_group + 1), GROUP * col_group : GROUP * (col_group + 1)]
-            dealt = shared.tile([P, PACK * GROUP], BF16, name="dealt%d" % number, align_bytes=ALIGN, offset=AT_ROUNDED[number])
+            at = AT_ROUNDED + ROUNDED_BYTES * (number % ROUNDED_DEPTH)
+            rounded = shared.tile([P, PACK * GROUP], BF16, name="rounded%d" % number, align_bytes=ALIGN, offset=at)
             if name == "w1":
-                (nc.gpsimd if number == 0 else nc.sync).dma_start(out=stage[:], in_=rows.rearrange("(p j) c -> p j c", j=PACK))
-                into = dealt[:].rearrange("p (t b e j) -> p b t e j", t=PACK, e=RUN, j=PACK)
-                source = stage[:].rearrange("p j (b t e) -> p b t e j", t=PACK, e=RUN)
+                queue = nc.gpsimd if number == 0 else nc.sync
+                queue.dma_start(out=stage[:], in_=rows.rearrange("(p j) c -> p j c", j=PACK))
+                nc.vector.tensor_copy(
+                    out=rounded[:].rearrange("p (t b e j) -> p b t j e", t=PACK, e=RUN, j=PACK),
+                    in_=stage[:].rearrange("p j (b t e) -> p b t j e", t=PACK, e=RUN),
+                )
             else:
-                by_slot = rows.rearrange("(b j e) n -> j b e n", j=PACK, e=RUN)
+                by_place = rows.rearrange("(b j e) n -> j b e n", j=PACK, e=RUN)
                 for j in range(PACK):
-                    nc.sync.dma_start(out=stage[:, j, :], in_=by_slot[j])
-                into = dealt[:].rearrange("p (t m j) -> p m j t", t=PACK, j=PACK)
-                source = stage[:].rearrange("p j (m t) -> p m j t", t=PACK)
-            if name == "w1":
-                nc.vector.tensor_copy(out=into, in_=source)
-            else:
-                nc.scalar.copy(out=into, in_=source)
-            weight_q[name, row_group, col_group] = quantised(GROUP, "%s_%d%d" % (name, row_group, col_group), dealt[:])
+                    nc.sync.dma_start(out=stage[:, j, :], in_=by_place[j])
+                nc.scalar.copy(
+                    out=rounded[:].rearrange("p (t m j) -> p m j t", t=PACK, j=PACK),
+                    in_=stage[:].rearrange("p j (m t) -> p m j t", t=PACK),
+                )
+            weight_q[name, row_group, col_group] = quantised(GROUP, "%s_%d%d" % (name, row_group, col_group), rounded[:])
 
         def first_stage(jobs):
             for lo in range(0, S, BANK):
@@ -201,12 +210,14 @@ def tile_list_triple_pair_rerank_kernel(
             jobs = []
             for a in tiles:
                 q_rows[a] = take(q_ring)
-                jobs.append((q_rows[a], w2_w[:, 2 * P * a : 2 * P * (a + 1)].bitcast(FP4X4), w2_s[:, P * a : P * (a + 1)]))
+                codes = w2_w[:, 2 * P * a : 2 * P * (a + 1)].bitcast(FP4X4)
+                jobs.append((q_rows[a], codes, w2_s[:, P * a : P * (a + 1)]))
             first_stage(jobs)
 
         def make_r(a):
             r_rows[a] = take(r_ring)
-            first_stage([(r_rows[a], w3_w[:, 4 * P * a : 4 * P * (a + 1)].bitcast(FP8X4), w3_s[:, P * a : P * (a + 1)])])
+            codes = w3_w[:, 4 * P * a : 4 * P * (a + 1)].bitcast(FP8X4)
+            first_stage([(r_rows[a], codes, w3_s[:, P * a : P * (a + 1)])])
 
         def make_h(a):
             g, t = divmod(a, PACK)
@@ -229,41 +240,39 @@ def tile_list_triple_pair_rerank_kernel(
             nc.scalar.activation(out=both[:], in_=diff[pair][:], func=SIGMOID, scale=-1.0)
             gate[2 * pair], gate[2 * pair + 1] = both[:, :PAIRS], both[:, PAIRS:]
 
-        def products(g, z_tile, lo, hi, pair):
-            z = z_tile[:].rearrange("p (t i) -> p t i", t=PACK)
+        def products(g, z, lo, hi, places):
             entries = slice(lo // LIST_ROWS, hi // LIST_ROWS)
             gated = {}
-            for t in pair:
+            for t in places:
                 a = PACK * g + t
                 gated[t] = take(gated_ring)[:, : hi - lo]
                 nc.vector.tensor_tensor(gated[t], h[a][:].indirect(pos1_sb[:, entries]), gate[a][:, lo:hi], MULT)
-            for t in pair:
+            for t in places:
                 nc.vector.tensor_tensor(z[:, t, :], h[PACK * g + t][:].indirect(pos2_sb[:, entries]), gated[t], MULT)
+
+        def weaving(woven, rows):
+            return (
+                woven.rearrange("p (run i t) -> p run t i", i=LINE, t=PACK),
+                rows.rearrange("p t (run i) -> p run t i", i=LINE),
+            )
 
         z_q = {}
 
-        def quantise_z(g, z, lo, hi, on_vector):
-            if g == 0:
-                at = AT_Z_WOVEN + 2 * PACK * lo
-                woven = shared.tile([P, PACK * (hi - lo)], BF16, name="z_woven0_%d" % lo, align_bytes=ALIGN, offset=at)[:]
-            elif hi == PAIRS:
-                at = AT_Y_WOVEN + Y_WOVEN_PLACE[0, 1] * WOVEN_BYTES // 2
-                woven = shared.tile([P, PACK * (hi - lo)], BF16, name="z_woven_last", align_bytes=ALIGN, offset=at)[:]
-            else:
-                woven = keep.tile([P, PACK * (hi - lo)], BF16, name="z_woven1_%d" % lo, align_bytes=ALIGN)[:]
-            runs = (hi - lo) // LINE
-            into = woven.rearrange("p (run i t) -> p run t i", i=LINE, t=PACK)
-            by_runs = z.rearrange("p t (run i) -> p run t i", i=LINE)
+        def quantise_z(g, z, lo, hi, woven, on_vector):
+            into, by_runs = weaving(woven[:], z)
             if on_vector:
-                spread = rel_sb[:, g, :, 0:1].unsqueeze(1).broadcast_to([P, runs, PACK, LINE])
+                spread = rel_sb[:, g, :, 0:1].unsqueeze(1).broadcast_to([P, (hi - lo) // LINE, PACK, LINE])
                 nc.vector.tensor_tensor(into, by_runs, spread, MULT)
             else:
                 for t in range(PACK):
                     nc.scalar.activation(out=z[:, t, :], in_=z[:, t, :], func=COPY, scale=rel_sb[:, g, t, 0:1])
                 nc.scalar.copy(out=into, in_=by_runs)
-            codes, scales = quantised(hi - lo, "z%d_%d" % (g, lo), woven)
+            codes, scales = quantised(hi - lo, "z%d_%d" % (g, lo), woven[:])
             for col in range(lo, hi, P):
                 z_q[g, col] = (codes[:, col - lo : col - lo + P].bitcast(FP8X4), scales[:, col - lo : col - lo + P])
+
+        def woven_at(at, width, name):
+            return shared.tile([P, PACK * width], BF16, name=name, align_bytes=ALIGN, offset=at)
 
         def second_passes(c_group, g, col):
             acc = banks[GROUPS * (col // P) + g][:].rearrange("p (t i) -> p t i", t=PACK)
@@ -285,49 +294,38 @@ def tile_list_triple_pair_rerank_kernel(
         y_scales = keep.tile([P, GROUPS * PAIRS], U8, name="y_scales", align_bytes=ALIGN)
         y_codes = keep.tile([P, GROUPS * PAIRS], U32, name="y_codes", align_bytes=ALIGN)
 
-        def woven_y(g, lo, hi):
-            at = AT_Y_WOVEN + Y_WOVEN_PLACE[lo, g] * WOVEN_BYTES // 2
-            return shared.tile([P, PACK * (hi - lo)], BF16, name="y_woven%d_%d" % (lo, g), align_bytes=ALIGN, offset=at)
-
-        def store_and_quantise(queue, g, lo, hi, y, woven):
+        def store_and_quantise(g, lo, hi, y, woven):
             rows = out_0[GROUP * g : GROUP * (g + 1), lo:hi].rearrange("(p t) i -> p t i", t=PACK)
-            queue.dma_start(out=rows, in_=y[:])
+            nc.sync.dma_start(out=rows, in_=y[:])
             nc.vector.quantize_mx(
                 out=y_codes[:, PAIRS * g + lo : PAIRS * g + hi].bitcast(FP8X4),
                 scales=y_scales[:, PAIRS * g + lo : PAIRS * g + hi],
                 in_=woven[:],
             )
 
-        def finish(lo, hi):
-            width = hi - lo
+        def finish(piece):
+            lo, hi = spans[piece]
             for g in range(GROUPS):
-                y = results.tile([P, PACK, width], F32, name="y")
-                woven = woven_y(g, lo, hi)
+                y = results.tile([P, PACK, hi - lo], F32, name="y")
+                woven = woven_at(AT_Y_WOVEN[piece][g], hi - lo, "y_woven%d_%d" % (piece, g))
                 for col in range(lo, hi, P):
                     acc = second_passes(1, g, col)
                     at = col - lo
                     nc.scalar.copy(out=y[:, :, at : at + P], in_=acc)
-                    nc.scalar.copy(
-                        out=woven[:, PACK * at : PACK * (at + P)].rearrange("p (i t) -> p i t", t=PACK),
-                        in_=acc.rearrange("p t i -> p i t"),
-                    )
-                store_and_quantise(nc.sync, g, lo, hi, y, woven)
+                    nc.scalar.copy(*weaving(woven[:, PACK * at : PACK * (at + P)], acc))
+                store_and_quantise(g, lo, hi, y, woven)
 
-        def finish_last(lo):
+        def finish_last(piece):
+            lo, hi = spans[piece]
             acc = [second_passes(1, g, lo) for g in range(GROUPS)]
-            y = [keep.tile([P, PACK, P], F32, name="y_last%d" % g) for g in range(GROUPS)]
-            woven = [woven_y(g, lo, PAIRS) for g in range(GROUPS)]
+            y = [keep.tile([P, PACK, hi - lo], F32, name="y_last%d" % g) for g in range(GROUPS)]
+            woven = [woven_at(AT_Y_WOVEN[piece][g], hi - lo, "y_woven%d_%d" % (piece, g)) for g in range(GROUPS)]
             nc.scalar.copy(out=y[0][:], in_=acc[0])
             nc.vector.tensor_copy(out=y[1][:], in_=acc[1])
-            nc.scalar.copy(
-                out=woven[0][:].rearrange("p (i t) -> p i t", t=PACK), in_=acc[0].rearrange("p t i -> p i t")
-            )
-            nc.vector.tensor_copy(
-                out=woven[1][:].rearrange("p (run i t) -> p run t i", i=LINE, t=PACK),
-                in_=y[1][:].rearrange("p t (run i) -> p run t i", i=LINE),
-            )
+            nc.scalar.copy(*weaving(woven[0][:], acc[0]))
+            nc.vector.tensor_copy(*weaving(woven[1][:], y[1][:]))
             for g in range(GROUPS):
-                store_and_quantise(nc.sync, g, lo, PAIRS, y[g], woven[g])
+                store_and_quantise(g, lo, hi, y[g], woven[g])
 
         def store_codes(lo, hi):
             words = out_1.rearrange("g p i t -> p g (i t)").bitcast(I32)
@@ -335,15 +333,16 @@ def tile_list_triple_pair_rerank_kernel(
             nc.sync.dma_start(out=words[:, :, lo:hi], in_=codes[:, :, lo:hi])
 
         rel_sb = shared.tile([P, GROUPS, PACK, RUN], F32, name="rel_sb", align_bytes=ALIGN, offset=AT_REL)
-        z_first = shared.tile([P, PACK * PAIRS], F32, name="z_first", align_bytes=ALIGN, offset=AT_Z_FIRST)
-        make_q((0, 1, 2))
+        z_tile = shared.tile([P, PACK * PAIRS], F32, name="z_first", align_bytes=ALIGN, offset=AT_Z_FIRST)
+        z_first = z_tile[:].rearrange("p (t i) -> p t i", t=PACK)
+        make_q(range(FIRST_Q_TILES))
         pick_q(0)
         for step in range(TILES):
             make_r(step)
-            if 0 < step < TILES - 2:
+            if FIRST_Q_TILES <= step + 2 < TILES:
                 make_q((step + 2,))
-            if step in BLOCK_STEPS:
-                quantise_weight_block(BLOCK_STEPS.index(step))
+            if step < GROUPS:
+                quantise_weight_block(step)
             if step + 1 < TILES:
                 pick_q(step + 1)
             pick_r_less_q(step)
@@ -357,6 +356,7 @@ def tile_list_triple_pair_rerank_kernel(
                 make_h(1)
                 gates_of_pair(0)
                 products(0, z_first, 0, PAIRS, (0, 1))
+
         for pair in range(1, TILES // 2):
             make_h(2 * pair)
             make_h(2 * pair + 1)
@@ -364,32 +364,39 @@ def tile_list_triple_pair_rerank_kernel(
             if pair == 1:
                 quantise_weight_block(GROUPS)
         products(0, z_first, 0, PAIRS, (2, 3))
-        z_rows = z_first[:].rearrange("p (t i) -> p t i", t=PACK)
-        quantise_z(0, z_rows[:, :, : PIECES[0]], 0, PIECES[0], True)
+
+        half = PIECES[0]
+        quantise_z(0, z_first[:, :, :half], 0, half, woven_at(AT_Z_WOVEN, half, "z_woven_early"), True)
         for number in range(GROUPS + 1, len(weight_blocks)):
             quantise_weight_block(number)
-        quantise_z(0, z_rows[:, :, PIECES[0] :], PIECES[0], PAIRS, False)
+        late = woven_at(AT_Z_WOVEN + 2 * PACK * half, PAIRS - half, "z_woven_late")
+        quantise_z(0, z_first[:, :, half:], half, PAIRS, late, False)
 
         edges = [sum(PIECES[:k]) for k in range(len(PIECES) + 1)]
         spans = list(zip(edges[:-1], edges[1:]))
-        for number, (lo, hi) in enumerate(spans):
-            z_piece = shared.tile(
-                [P, PACK * (hi - lo)], F32, name="z_piece%d" % number, align_bytes=ALIGN, offset=AT_Z_PIECE[number]
+        for piece, (lo, hi) in enumerate(spans):
+            z_tile = shared.tile(
+                [P, PACK * (hi - lo)], F32, name="z_piece%d" % piece, align_bytes=ALIGN, offset=AT_Z_PIECE[piece]
             )
-            for pair in ((0, 1), (2, 3)):
-                products(1, z_piece, lo, hi, pair)
-            quantise_z(1, z_piece[:].rearrange("p (t i) -> p t i", t=PACK), lo, hi, True)
-            if number == 1:
+            z_piece = z_tile[:].rearrange("p (t i) -> p t i", t=PACK)
+            for places in ((0, 1), (2, 3)):
+                products(1, z_piece, lo, hi, places)
+            if hi == PAIRS:
+                woven = woven_at(AT_Z_WOVEN_LAST, hi - lo, "z_woven_last")
+            else:
+                woven = keep.tile([P, PACK * (hi - lo)], BF16, name="z_woven%d" % piece, align_bytes=ALIGN)
+            quantise_z(1, z_piece, lo, hi, woven, True)
+            if piece == 1:
                 open_sums(*spans[0])
-                finish(*spans[0])
-                open_sums(spans[1][0], PAIRS)
-        finish(*spans[1])
-        store_codes(0, spans[1][1])
-        finish_last(spans[2][0])
-        store_codes(*spans[2])
+                finish(0)
+                open_sums(lo, PAIRS)
+        finish(1)
+        store_codes(0, edges[2])
+        finish_last(2)
+        store_codes(edges[2], PAIRS)
 
         plane_rows = y_scales[:].bitcast(I32).rearrange("p (g i) -> p g i", g=GROUPS)
-        for quad in range(4):
+        for quad in range(QUADS):
             nc.scalar.dma_start(
                 out=out_2[:, 4 * quad : 4 * quad + 4, :].rearrange("g row i -> row g i").bitcast(I32),
                 in_=plane_rows[32 * quad : 32 * quad + 4, :, :],

@@ -30,46 +30,41 @@ RUN = 8
 BLOCKS = P // RUN
 QUADS = 4
 LINE = 4
+W3_PLANE = 4
 ALIGN = 64
 
 PIECES = (256, 128, 128)
-FIRST_Q_TILES = 3
-FIRST_PRODUCTS = 3
+FIRST_Q_TILES = 2
+BLOCKS_ON_VECTOR = 1
+A0, A1 = 3, 5
 ROW_DEPTH = 4
 HEAD_DEPTH = 3
-DIFF_DEPTH = 3
 GATED_DEPTH = 2
-ROUNDED_DEPTH = 4
 RESULT_DEPTH = 4
 
 STAGE_BYTES = 4 * PACK * GROUP
 ROUNDED_BYTES = 2 * PACK * GROUP
 WOVEN_BYTES = 2 * PACK * P
-AT_S3_DEALT = 0
-AT_TAB_WORDS = AT_S3_DEALT + H - ALIGN
+AT_W3_DEALT = 0
+AT_TAB_WORDS = AT_W3_DEALT + 4 * H - ALIGN
 AT_TAB_SCALES = AT_TAB_WORDS + ALIGN + 2 * STAGE_BYTES
-AT_V_LOW = AT_TAB_SCALES
-AT_W2_DEALT = AT_TAB_SCALES + T
-AT_W2_IN = AT_W2_DEALT + 2 * H
-AT_V_HIGH = AT_W2_IN + 2 * H - ALIGN
-AT_S2_IN = AT_V_HIGH + 4 * BANK - ALIGN
-AT_REL = AT_S2_IN + ALIGN
-AT_W3_DEALT = AT_S2_IN + H - ALIGN
-AT_STAGES = (AT_W3_DEALT + 4 * H, AT_TAB_WORDS + ALIGN, AT_TAB_WORDS + ALIGN + STAGE_BYTES)
-AT_ROUNDED = AT_STAGES[0] + STAGE_BYTES
-AT_W3_IN = AT_ROUNDED
-AT_Z_WOVEN = AT_ROUNDED + ROUNDED_DEPTH * ROUNDED_BYTES
-AT_Z_OWN = AT_Z_WOVEN + 2 * PACK * PAIRS
-AT_Z_PIECE = (AT_Z_OWN, AT_ROUNDED + ROUNDED_BYTES, AT_Z_WOVEN + 2 * PACK * PIECES[0])
-AT_Z_FIRST = AT_Z_OWN + 4 * PACK * PIECES[0]
-AT_Y_FIRST = AT_Z_FIRST + 4 * PACK * PAIRS
+AT_V_WORDS = AT_TAB_SCALES + T + H - 4 * S
+AT_SCALES_IN = AT_TAB_SCALES + T
+AT_STAGES = (AT_V_WORDS + 4 * S, AT_TAB_WORDS + ALIGN, AT_TAB_WORDS + ALIGN + STAGE_BYTES)
+AT_W2_IN = AT_STAGES[0] + STAGE_BYTES
+AT_W3_IN = AT_W2_IN + 2 * H
+AT_REL = AT_W3_IN + ALIGN
+AT_ROUNDED_FIRST = AT_W3_IN + 4 * H - ALIGN
+AT_DIFF_FIRST = AT_ROUNDED_FIRST + ROUNDED_BYTES
+AT_DIFF = tuple(AT_DIFF_FIRST + ROUNDED_BYTES * halves // 2 for halves in (0, 2, 5, 8))
+AT_ROUNDED = (AT_ROUNDED_FIRST,) + AT_DIFF[:2] + (AT_DIFF[2] - ROUNDED_BYTES // 2, AT_DIFF[2] + ROUNDED_BYTES // 2, AT_DIFF[3])
+AT_Z_WOVEN = AT_ROUNDED[5] + ROUNDED_BYTES
+AT_Z_FIRST = AT_Z_WOVEN + 2 * PACK * PAIRS
+AT_Z_PIECE = (AT_Z_FIRST + 4 * PACK * PAIRS, AT_ROUNDED[5], AT_Z_FIRST)
+AT_Y_FIRST = AT_Z_PIECE[0] + 4 * PACK * PIECES[0]
 AT_Y_MIDDLE = AT_Y_FIRST + GROUPS * 2 * PACK * PIECES[0]
-AT_Y_WOVEN = (
-    (AT_Y_FIRST, AT_Y_FIRST + 2 * PACK * PIECES[0]),
-    (AT_Y_MIDDLE, AT_Y_MIDDLE + WOVEN_BYTES),
-    (AT_Y_FIRST, AT_Y_MIDDLE + WOVEN_BYTES // 2),
-)
-AT_Z_WOVEN_LAST = AT_Y_WOVEN[0][1]
+AT_Y_WOVEN = (AT_Y_FIRST, AT_Y_MIDDLE, AT_Y_FIRST)
+AT_Y_LAST = (AT_Z_PIECE[0], AT_Y_MIDDLE)
 
 
 def tile_list_triple_pair_rerank_kernel(
@@ -94,7 +89,6 @@ def tile_list_triple_pair_rerank_kernel(
         bank_ring = list(banks)
         r_ring = ring_of(ROW_DEPTH, S, F32, "r")
         q_ring = ring_of(ROW_DEPTH, S, F32, "q")
-        diff_ring = ring_of(DIFF_DEPTH, 2 * PAIRS, F32, "diff")
         gated_ring = ring_of(GATED_DEPTH, PAIRS, F32, "gated")
         head_ring = ring_of(HEAD_DEPTH, PAIRS, F32, "q_head")
 
@@ -105,31 +99,24 @@ def tile_list_triple_pair_rerank_kernel(
         tab_s = shared.tile([P, T], U8, name="tab_s", align_bytes=ALIGN, offset=AT_TAB_SCALES)
         w2_in = shared.tile([P, 2 * H], U8, name="w2_in", align_bytes=ALIGN, offset=AT_W2_IN)
         w3_in = shared.tile([P, 4 * H], U8, name="w3_in", align_bytes=ALIGN, offset=AT_W3_IN)
-        s3_in = keep.tile([P, H], U8, name="s3_in", align_bytes=ALIGN)
-        s2_in = shared.tile([P, H], U8, name="s2_in", align_bytes=ALIGN, offset=AT_S2_IN)
-        w2_s = keep.tile([P, H], U8, name="w2_s", align_bytes=ALIGN)
+        scales_in = shared.tile([P, H], U8, name="scales_in", align_bytes=ALIGN, offset=AT_SCALES_IN)
+        v_s = keep.tile([P, S], U8, name="v_s", align_bytes=ALIGN)
 
-        def load_scales(queues, plane, rows):
-            for quad, queue in enumerate(queues):
-                queue.dma_start(
-                    out=plane[32 * quad : 32 * quad + 4, :].bitcast(I32),
-                    in_=rows[0, 4 * quad : 4 * quad + 4, :].bitcast(I32),
-                )
+        def fill_plane(queue, plane, first, rows):
+            for r in range(QUADS):
+                queue.dma_start(out=plane[first + r : P : 32, :].bitcast(I32), in_=rows(r).bitcast(I32))
 
-        table = tab_words[0].rearrange("p e t -> p (e t)").bitcast(I32)
-        nc.gpsimd.memset(tab_s[:].bitcast(I32), 0)
-        nc.gpsimd.memset(s2_in[:].bitcast(I32), 0)
-        nc.gpsimd.dma_start(out=tab_w[:, T // 2 :].bitcast(I32), in_=table[:, T // 2 :])
-        nc.gpsimd.memset(s3_in[:].bitcast(I32), 0)
+        for plane in (tab_s, scales_in, v_s):
+            nc.vector.memset(plane[:].bitcast(I32), 0)
+        nc.gpsimd.dma_start(out=tab_w[:].bitcast(I32), in_=tab_words[0].rearrange("p e t -> p (e t)").bitcast(I32))
+        nc.gpsimd.dma_start(out=w3_in[:].bitcast(I32), in_=w3_words[0].rearrange("p c t -> p (c t)").bitcast(I32))
         nc.sync.dma_start(offs_sb[:], offs)
         nc.sync.dma_start(out=w2_in[:].bitcast(I32), in_=w2_words[0].bitcast(I32))
-        nc.sync.dma_start(out=tab_w[:, : T // 2].bitcast(I32), in_=table[:, : T // 2])
         nc.sync.dma_start(pos1_sb[:], pos1)
         nc.sync.dma_start(pos2_sb[:], pos2)
-        load_scales([nc.scalar] * QUADS, tab_s, tab_scales)
-        load_scales([nc.scalar] * QUADS, s2_in, w2_scales)
-        load_scales([nc.gpsimd] + [nc.scalar] * (QUADS - 1), s3_in, w3_scales)
-        nc.gpsimd.dma_start(out=w3_in[:].bitcast(I32), in_=w3_words[0].rearrange("p c t -> p (c t)").bitcast(I32))
+        nc.scalar.dma_start(out=tab_s[0:P:RUN, :].bitcast(I32), in_=tab_scales[0].bitcast(I32))
+        fill_plane(nc.sync, scales_in, 0, lambda r: w2_scales[0, r:BLOCKS:QUADS, :])
+        fill_plane(nc.scalar, scales_in, W3_PLANE, lambda r: w3_scales[0, r:BLOCKS:QUADS, :])
 
         def deal_columns(dst, src):
             nc.vector.tensor_copy(
@@ -137,24 +124,20 @@ def tile_list_triple_pair_rerank_kernel(
                 in_=src[:].bitcast(I32).rearrange("p (g b t w) -> p g t b w", g=GROUPS, t=PACK, b=BLOCKS),
             )
 
-        v_s = keep.tile([P, S], U8, name="v_s", align_bytes=ALIGN)
-        nc.vector.tensor_copy(v_s[:], tab_s[:].indirect(offs_sb[:]))
-        deal_columns(w2_s, s2_in)
-        v_w = {}
-
-        def gather_words(lo, at):
-            v_w[lo] = shared.tile([P, BANK], U32, name="v_w%d" % lo, align_bytes=ALIGN, offset=at)
-            entries = offs_sb[:, lo // LIST_ROWS : (lo + BANK) // LIST_ROWS]
-            nc.vector.tensor_copy(v_w[lo][:], tab_w[:].indirect(entries))
-
-        gather_words(0, AT_V_LOW)
-        w2_w = shared.tile([P, 2 * H], U8, name="w2_w", align_bytes=ALIGN, offset=AT_W2_DEALT)
+        w2_w = keep.tile([P, 2 * H], U8, name="w2_w", align_bytes=ALIGN)
         deal_columns(w2_w, w2_in)
-        gather_words(BANK, AT_V_HIGH)
+
+        picked_s = keep.tile([P, S], U8, name="picked_s", align_bytes=ALIGN)
+        nc.vector.tensor_copy(picked_s[:], tab_s[:].indirect(offs_sb[:]))
+        fill_plane(nc.sync, v_s, 0, lambda r: picked_s[RUN * r : P : 32, :])
+        w_s = keep.tile([P, H], U8, name="w_s", align_bytes=ALIGN)
+        deal_columns(w_s, scales_in)
+        v_w = shared.tile([P, S], U32, name="v_w", align_bytes=ALIGN, offset=AT_V_WORDS)
+        for lo in range(0, S, BANK):
+            entries = offs_sb[:, lo // LIST_ROWS : (lo + BANK) // LIST_ROWS]
+            nc.vector.tensor_copy(v_w[:, lo : lo + BANK], tab_w[:].indirect(entries))
         w3_w = shared.tile([P, 4 * H], U8, name="w3_w", align_bytes=ALIGN, offset=AT_W3_DEALT)
         deal_columns(w3_w, w3_in)
-        w3_s = shared.tile([P, H], U8, name="w3_s", align_bytes=ALIGN, offset=AT_S3_DEALT)
-        deal_columns(w3_s, s3_in)
         stage_ring = [
             shared.tile([P, PACK, GROUP], F32, name="stage%d" % k, align_bytes=ALIGN, offset=at)
             for k, at in enumerate(AT_STAGES)
@@ -174,12 +157,13 @@ def tile_list_triple_pair_rerank_kernel(
             name, w, row_group, col_group = weight_blocks[number]
             stage = take(stage_ring)
             rows = w[GROUP * row_group : GROUP * (row_group + 1), GROUP * col_group : GROUP * (col_group + 1)]
-            at = AT_ROUNDED + ROUNDED_BYTES * (number % ROUNDED_DEPTH)
+            at = AT_ROUNDED[number]
             rounded = shared.tile([P, PACK * GROUP], BF16, name="rounded%d" % number, align_bytes=ALIGN, offset=at)
+            copy = nc.vector.tensor_copy if number < BLOCKS_ON_VECTOR else nc.scalar.copy
             if name == "w1":
                 queue = nc.gpsimd if number == 0 else nc.sync
                 queue.dma_start(out=stage[:], in_=rows.rearrange("(p j) c -> p j c", j=PACK))
-                nc.vector.tensor_copy(
+                copy(
                     out=rounded[:].rearrange("p (t b e j) -> p b t j e", t=PACK, e=RUN, j=PACK),
                     in_=stage[:].rearrange("p j (b t e) -> p b t j e", t=PACK, e=RUN),
                 )
@@ -187,7 +171,7 @@ def tile_list_triple_pair_rerank_kernel(
                 by_place = rows.rearrange("(b j e) n -> j b e n", j=PACK, e=RUN)
                 for j in range(PACK):
                     nc.sync.dma_start(out=stage[:, j, :], in_=by_place[j])
-                nc.scalar.copy(
+                copy(
                     out=rounded[:].rearrange("p (t m j) -> p m j t", t=PACK, j=PACK),
                     in_=stage[:].rearrange("p j (m t) -> p m j t", t=PACK),
                 )
@@ -199,7 +183,7 @@ def tile_list_triple_pair_rerank_kernel(
                     acc = take(bank_ring)
                     nc.tensor.matmul_mx(
                         out=acc[:], lhsT=codes, lhsT_scale=scales,
-                        rhs=v_w[lo][:].bitcast(FP8X4), rhs_scale=v_s[:, lo : lo + BANK],
+                        rhs=v_w[:, lo : lo + BANK].bitcast(FP8X4), rhs_scale=v_s[:, lo : lo + BANK],
                         start=True, stop=True,
                     )
                     nc.scalar.copy(out=rows[:, lo : lo + BANK], in_=acc[:])
@@ -211,13 +195,13 @@ def tile_list_triple_pair_rerank_kernel(
             for a in tiles:
                 q_rows[a] = take(q_ring)
                 codes = w2_w[:, 2 * P * a : 2 * P * (a + 1)].bitcast(FP4X4)
-                jobs.append((q_rows[a], codes, w2_s[:, P * a : P * (a + 1)]))
+                jobs.append((q_rows[a], codes, w_s[:, P * a : P * (a + 1)]))
             first_stage(jobs)
 
         def make_r(a):
             r_rows[a] = take(r_ring)
             codes = w3_w[:, 4 * P * a : 4 * P * (a + 1)].bitcast(FP8X4)
-            first_stage([(r_rows[a], codes, w3_s[:, P * a : P * (a + 1)])])
+            first_stage([(r_rows[a], codes, w_s[W3_PLANE:, P * a : P * (a + 1)])])
 
         def make_h(a):
             g, t = divmod(a, PACK)
@@ -231,7 +215,9 @@ def tile_list_triple_pair_rerank_kernel(
 
         def pick_r_less_q(a):
             if a % 2 == 0:
-                diff[a // 2] = take(diff_ring)
+                diff[a // 2] = shared.tile(
+                    [P, 2 * PAIRS], F32, name="diff%d" % (a // 2), align_bytes=ALIGN, offset=AT_DIFF[a // 2]
+                )
             into = diff[a // 2][:, PAIRS * (a % 2) : PAIRS * (a % 2 + 1)]
             nc.vector.tensor_tensor(into, r_rows[a][:].indirect(pos2_sb[:]), q_head[a][:], SUBTRACT)
 
@@ -258,15 +244,10 @@ def tile_list_triple_pair_rerank_kernel(
 
         z_q = {}
 
-        def quantise_z(g, z, lo, hi, woven, on_vector):
+        def quantise_z(g, z, lo, hi, woven):
             into, by_runs = weaving(woven[:], z)
-            if on_vector:
-                spread = rel_sb[:, g, :, 0:1].unsqueeze(1).broadcast_to([P, (hi - lo) // LINE, PACK, LINE])
-                nc.vector.tensor_tensor(into, by_runs, spread, MULT)
-            else:
-                for t in range(PACK):
-                    nc.scalar.activation(out=z[:, t, :], in_=z[:, t, :], func=COPY, scale=rel_sb[:, g, t, 0:1])
-                nc.scalar.copy(out=into, in_=by_runs)
+            spread = rel_sb[:, g, :, 0:1].unsqueeze(1).broadcast_to([P, (hi - lo) // LINE, PACK, LINE])
+            nc.vector.tensor_tensor(into, by_runs, spread, MULT)
             codes, scales = quantised(hi - lo, "z%d_%d" % (g, lo), woven[:])
             for col in range(lo, hi, P):
                 z_q[g, col] = (codes[:, col - lo : col - lo + P].bitcast(FP8X4), scales[:, col - lo : col - lo + P])
@@ -303,11 +284,16 @@ def tile_list_triple_pair_rerank_kernel(
                 in_=woven[:],
             )
 
+        def woven_results(piece, g):
+            lo, hi = spans[piece]
+            at = AT_Y_WOVEN[piece] + 2 * PACK * (hi - lo) * g
+            return woven_at(at, hi - lo, "y_woven%d_%d" % (piece, g))
+
         def finish(piece):
             lo, hi = spans[piece]
             for g in range(GROUPS):
                 y = results.tile([P, PACK, hi - lo], F32, name="y")
-                woven = woven_at(AT_Y_WOVEN[piece][g], hi - lo, "y_woven%d_%d" % (piece, g))
+                woven = woven_results(piece, g)
                 for col in range(lo, hi, P):
                     acc = second_passes(1, g, col)
                     at = col - lo
@@ -318,8 +304,11 @@ def tile_list_triple_pair_rerank_kernel(
         def finish_last(piece):
             lo, hi = spans[piece]
             acc = [second_passes(1, g, lo) for g in range(GROUPS)]
-            y = [keep.tile([P, PACK, hi - lo], F32, name="y_last%d" % g) for g in range(GROUPS)]
-            woven = [woven_at(AT_Y_WOVEN[piece][g], hi - lo, "y_woven%d_%d" % (piece, g)) for g in range(GROUPS)]
+            y = [
+                shared.tile([P, PACK, hi - lo], F32, name="y_last%d" % g, align_bytes=ALIGN, offset=AT_Y_LAST[g])
+                for g in range(GROUPS)
+            ]
+            woven = [woven_results(piece, g) for g in range(GROUPS)]
             nc.scalar.copy(out=y[0][:], in_=acc[0])
             nc.vector.tensor_copy(out=y[1][:], in_=acc[1])
             nc.scalar.copy(*weaving(woven[0][:], acc[0]))
@@ -335,42 +324,48 @@ def tile_list_triple_pair_rerank_kernel(
         rel_sb = shared.tile([P, GROUPS, PACK, RUN], F32, name="rel_sb", align_bytes=ALIGN, offset=AT_REL)
         z_tile = shared.tile([P, PACK * PAIRS], F32, name="z_first", align_bytes=ALIGN, offset=AT_Z_FIRST)
         z_first = z_tile[:].rearrange("p (t i) -> p t i", t=PACK)
-        make_q(range(FIRST_Q_TILES))
-        pick_q(0)
-        for step in range(TILES):
-            make_r(step)
-            if FIRST_Q_TILES <= step + 2 < TILES:
-                make_q((step + 2,))
-            if step < GROUPS:
-                quantise_weight_block(step)
-            if step + 1 < TILES:
-                pick_q(step + 1)
-            pick_r_less_q(step)
-            if step == 0:
-                by_tile = rel.rearrange("(g b t e) -> g t b e", g=GROUPS, t=PACK, e=RUN)
-                for a in range(TILES):
-                    g, t = divmod(a, PACK)
-                    nc.sync.dma_start(out=rel_sb[:, g, t, 0:1], in_=by_tile[g, t])
-            if step == FIRST_PRODUCTS:
-                make_h(0)
-                make_h(1)
-                gates_of_pair(0)
-                products(0, z_first, 0, PAIRS, (0, 1))
 
-        for pair in range(1, TILES // 2):
+        def difference(a):
+            make_r(a)
+            if a + FIRST_Q_TILES < TILES:
+                make_q((a + FIRST_Q_TILES,))
+            if a + 1 < TILES:
+                pick_q(a + 1)
+            pick_r_less_q(a)
+
+        def pair_of_tiles(pair):
             make_h(2 * pair)
             make_h(2 * pair + 1)
             gates_of_pair(pair)
-            if pair == 1:
-                quantise_weight_block(GROUPS)
-        products(0, z_first, 0, PAIRS, (2, 3))
 
-        half = PIECES[0]
-        quantise_z(0, z_first[:, :, :half], 0, half, woven_at(AT_Z_WOVEN, half, "z_woven_early"), True)
-        for number in range(GROUPS + 1, len(weight_blocks)):
+        make_q(range(FIRST_Q_TILES))
+        pick_q(0)
+        for a in range(TILES):
+            difference(a)
+            if a == 0:
+                quantise_weight_block(0)
+                by_tile = rel.rearrange("(g b t e) -> g t b e", g=GROUPS, t=PACK, e=RUN)
+                for c_tile in range(TILES):
+                    g, t = divmod(c_tile, PACK)
+                    nc.sync.dma_start(out=rel_sb[:, g, t, 0:1], in_=by_tile[g, t])
+            if a == A0:
+                pair_of_tiles(0)
+                products(0, z_first, 0, PAIRS, (0, 1))
+            if a == A0 + 1:
+                quantise_weight_block(1)
+            if a == A1:
+                pair_of_tiles(1)
+                products(0, z_first, 0, PAIRS, (2, 3))
+                quantise_z(0, z_first, 0, PAIRS, woven_at(AT_Z_WOVEN, PAIRS, "z_woven_first"))
+            if a == A1 + 1:
+                quantise_weight_block(2)
+        pair_of_tiles(2)
+        make_h(6)
+        make_h(7)
+        quantise_weight_block(3)
+        gates_of_pair(3)
+        for number in range(4, len(weight_blocks)):
             quantise_weight_block(number)
-        late = woven_at(AT_Z_WOVEN + 2 * PACK * half, PAIRS - half, "z_woven_late")
-        quantise_z(0, z_first[:, :, half:], half, PAIRS, late, False)
 
         edges = [sum(PIECES[:k]) for k in range(len(PIECES) + 1)]
         spans = list(zip(edges[:-1], edges[1:]))
@@ -381,11 +376,8 @@ def tile_list_triple_pair_rerank_kernel(
             z_piece = z_tile[:].rearrange("p (t i) -> p t i", t=PACK)
             for places in ((0, 1), (2, 3)):
                 products(1, z_piece, lo, hi, places)
-            if hi == PAIRS:
-                woven = woven_at(AT_Z_WOVEN_LAST, hi - lo, "z_woven_last")
-            else:
-                woven = keep.tile([P, PACK * (hi - lo)], BF16, name="z_woven%d" % piece, align_bytes=ALIGN)
-            quantise_z(1, z_piece, lo, hi, woven, True)
+            woven = keep.tile([P, PACK * (hi - lo)], BF16, name="z_woven%d" % piece, align_bytes=ALIGN)
+            quantise_z(1, z_piece, lo, hi, woven)
             if piece == 1:
                 open_sums(*spans[0])
                 finish(0)

@@ -15,6 +15,7 @@ FP8X4 = mybir.dt.float8_e4m3fn_x4
 FP4X4 = mybir.dt.float4_e2m1fn_x4
 COPY = mybir.ActivationFunctionType.Copy
 MULT = mybir.AluOpType.mult
+ADD = mybir.AluOpType.add
 SUBTRACT = mybir.AluOpType.subtract
 SIGMOID = mybir.ActivationFunctionType.Sigmoid
 
@@ -35,12 +36,10 @@ ALIGN = 64
 
 PIECES = (256, 128, 128)
 FIRST_Q_TILES = 2
-BLOCKS_ON_VECTOR = 1
 A0, A1 = 3, 5
 ROW_DEPTH = 4
-HEAD_DEPTH = 3
+HEAD_DEPTH = 8
 GATED_DEPTH = 2
-RESULT_DEPTH = 4
 
 STAGE_BYTES = 4 * PACK * GROUP
 ROUNDED_BYTES = 2 * PACK * GROUP
@@ -54,10 +53,10 @@ AT_STAGES = (AT_V_WORDS + 4 * S, AT_TAB_WORDS + ALIGN, AT_TAB_WORDS + ALIGN + ST
 AT_W2_IN = AT_STAGES[0] + STAGE_BYTES
 AT_W3_IN = AT_W2_IN + 2 * H
 AT_REL = AT_W3_IN + ALIGN
-AT_ROUNDED_FIRST = AT_W3_IN + 4 * H - ALIGN
-AT_DIFF_FIRST = AT_ROUNDED_FIRST + ROUNDED_BYTES
-AT_DIFF = tuple(AT_DIFF_FIRST + ROUNDED_BYTES * halves // 2 for halves in (0, 2, 5, 8))
-AT_ROUNDED = (AT_ROUNDED_FIRST,) + AT_DIFF[:2] + (AT_DIFF[2] - ROUNDED_BYTES // 2, AT_DIFF[2] + ROUNDED_BYTES // 2, AT_DIFF[3])
+AT_W1_ROUNDED = AT_W3_IN + 4 * H
+AT_Q_LAST = AT_W1_ROUNDED + GROUPS * ROUNDED_BYTES
+AT_DIFF = tuple(AT_Q_LAST + 4 * S + ROUNDED_BYTES * k for k in range(4))
+AT_ROUNDED = (AT_W1_ROUNDED, AT_W1_ROUNDED + ROUNDED_BYTES) + AT_DIFF
 AT_Z_WOVEN = AT_ROUNDED[5] + ROUNDED_BYTES
 AT_Z_FIRST = AT_Z_WOVEN + 2 * PACK * PAIRS
 AT_Z_PIECE = (AT_Z_FIRST + 4 * PACK * PAIRS, AT_ROUNDED[5], AT_Z_FIRST)
@@ -74,7 +73,6 @@ def tile_list_triple_pair_rerank_kernel(
     nc = tc.nc
     with ExitStack() as ctx:
         keep = ctx.enter_context(tc.tile_pool(name="keep", bufs=1))
-        results = ctx.enter_context(tc.tile_pool(name="results", bufs=RESULT_DEPTH))
         shared = ctx.enter_context(tc.tile_pool(name="shared", bufs=1))
         psum = ctx.enter_context(tc.psum_pool(name="psum", bufs=1))
 
@@ -143,8 +141,11 @@ def tile_list_triple_pair_rerank_kernel(
             for k, at in enumerate(AT_STAGES)
         ]
 
-        def quantised(width, name, woven):
-            codes = keep.tile([P, width], U32, name=name + "_codes", align_bytes=ALIGN)
+        def quantised(width, name, woven, at=None):
+            if at is None:
+                codes = keep.tile([P, width], U32, name=name + "_codes", align_bytes=ALIGN)
+            else:
+                codes = shared.tile([P, width], U32, name=name + "_codes", align_bytes=ALIGN, offset=at)
             scales = keep.tile([P, width], U8, name=name + "_scales", align_bytes=ALIGN)
             nc.vector.quantize_mx(out=codes[:].bitcast(FP8X4), scales=scales[:], in_=woven)
             return codes, scales
@@ -159,23 +160,25 @@ def tile_list_triple_pair_rerank_kernel(
             rows = w[GROUP * row_group : GROUP * (row_group + 1), GROUP * col_group : GROUP * (col_group + 1)]
             at = AT_ROUNDED[number]
             rounded = shared.tile([P, PACK * GROUP], BF16, name="rounded%d" % number, align_bytes=ALIGN, offset=at)
-            copy = nc.vector.tensor_copy if number < BLOCKS_ON_VECTOR else nc.scalar.copy
             if name == "w1":
                 queue = nc.gpsimd if number == 0 else nc.sync
                 queue.dma_start(out=stage[:], in_=rows.rearrange("(p j) c -> p j c", j=PACK))
-                copy(
-                    out=rounded[:].rearrange("p (t b e j) -> p b t j e", t=PACK, e=RUN, j=PACK),
-                    in_=stage[:].rearrange("p j (b t e) -> p b t j e", t=PACK, e=RUN),
-                )
+                into = rounded[:].rearrange("p (t b e j) -> p t b e j", t=PACK, e=RUN, j=PACK)
+                by_place = stage[:].rearrange("p j (b t e) -> p t b e j", t=PACK, e=RUN)
+                for t in range(PACK):
+                    nc.gpsimd.tensor_scalar(into[:, t], by_place[:, t], 1.0, 0.0, MULT, ADD)
             else:
                 by_place = rows.rearrange("(b j e) n -> j b e n", j=PACK, e=RUN)
                 for j in range(PACK):
                     nc.sync.dma_start(out=stage[:, j, :], in_=by_place[j])
-                copy(
+                nc.scalar.copy(
                     out=rounded[:].rearrange("p (t m j) -> p m j t", t=PACK, j=PACK),
                     in_=stage[:].rearrange("p j (m t) -> p m j t", t=PACK),
                 )
-            weight_q[name, row_group, col_group] = quantised(GROUP, "%s_%d%d" % (name, row_group, col_group), rounded[:])
+            weight_q[name, row_group, col_group] = quantised(
+                GROUP, "%s_%d%d" % (name, row_group, col_group), rounded[:],
+                AT_Q_LAST + 4 * GROUP * number if name == "w1" else None,
+            )
 
         def first_stage(jobs):
             for lo in range(0, S, BANK):
@@ -193,7 +196,10 @@ def tile_list_triple_pair_rerank_kernel(
         def make_q(tiles):
             jobs = []
             for a in tiles:
-                q_rows[a] = take(q_ring)
+                if a == TILES - 1:
+                    q_rows[a] = shared.tile([P, S], F32, name="q_last", align_bytes=ALIGN, offset=AT_Q_LAST)
+                else:
+                    q_rows[a] = take(q_ring)
                 codes = w2_w[:, 2 * P * a : 2 * P * (a + 1)].bitcast(FP4X4)
                 jobs.append((q_rows[a], codes, w_s[:, P * a : P * (a + 1)]))
             first_stage(jobs)
@@ -277,7 +283,7 @@ def tile_list_triple_pair_rerank_kernel(
 
         def store_and_quantise(g, lo, hi, y, woven):
             rows = out_0[GROUP * g : GROUP * (g + 1), lo:hi].rearrange("(p t) i -> p t i", t=PACK)
-            nc.sync.dma_start(out=rows, in_=y[:])
+            nc.sync.dma_start(out=rows, in_=y)
             nc.vector.quantize_mx(
                 out=y_codes[:, PAIRS * g + lo : PAIRS * g + hi].bitcast(FP8X4),
                 scales=y_scales[:, PAIRS * g + lo : PAIRS * g + hi],
@@ -292,7 +298,7 @@ def tile_list_triple_pair_rerank_kernel(
         def finish(piece):
             lo, hi = spans[piece]
             for g in range(GROUPS):
-                y = results.tile([P, PACK, hi - lo], F32, name="y")
+                y = take(r_ring)[:, : PACK * (hi - lo)].rearrange("p (t i) -> p t i", t=PACK)
                 woven = woven_results(piece, g)
                 for col in range(lo, hi, P):
                     acc = second_passes(1, g, col)
@@ -314,7 +320,7 @@ def tile_list_triple_pair_rerank_kernel(
             nc.scalar.copy(*weaving(woven[0][:], acc[0]))
             nc.vector.tensor_copy(*weaving(woven[1][:], y[1][:]))
             for g in range(GROUPS):
-                store_and_quantise(g, lo, hi, y[g], woven[g])
+                store_and_quantise(g, lo, hi, y[g][:], woven[g])
 
         def store_codes(lo, hi):
             words = out_1.rearrange("g p i t -> p g (i t)").bitcast(I32)
@@ -325,47 +331,42 @@ def tile_list_triple_pair_rerank_kernel(
         z_tile = shared.tile([P, PACK * PAIRS], F32, name="z_first", align_bytes=ALIGN, offset=AT_Z_FIRST)
         z_first = z_tile[:].rearrange("p (t i) -> p t i", t=PACK)
 
-        def difference(a):
-            make_r(a)
-            if a + FIRST_Q_TILES < TILES:
-                make_q((a + FIRST_Q_TILES,))
-            if a + 1 < TILES:
-                pick_q(a + 1)
-            pick_r_less_q(a)
-
         def pair_of_tiles(pair):
             make_h(2 * pair)
             make_h(2 * pair + 1)
             gates_of_pair(pair)
 
         make_q(range(FIRST_Q_TILES))
-        pick_q(0)
         for a in range(TILES):
-            difference(a)
-            if a == 0:
-                quantise_weight_block(0)
-                by_tile = rel.rearrange("(g b t e) -> g t b e", g=GROUPS, t=PACK, e=RUN)
-                for c_tile in range(TILES):
-                    g, t = divmod(c_tile, PACK)
-                    nc.sync.dma_start(out=rel_sb[:, g, t, 0:1], in_=by_tile[g, t])
+            if a >= FIRST_Q_TILES:
+                make_q((a,))
+            pick_q(a)
+        for number in range(GROUPS):
+            quantise_weight_block(number)
+        by_tile = rel.rearrange("(g b t e) -> g t b e", g=GROUPS, t=PACK, e=RUN)
+        for c_tile in range(TILES):
+            g, t = divmod(c_tile, PACK)
+            nc.sync.dma_start(out=rel_sb[:, g, t, 0:1], in_=by_tile[g, t])
+        for a in range(TILES):
+            make_r(a)
+            pick_r_less_q(a)
             if a == A0:
                 pair_of_tiles(0)
                 products(0, z_first, 0, PAIRS, (0, 1))
             if a == A0 + 1:
-                quantise_weight_block(1)
+                quantise_weight_block(2)
             if a == A1:
                 pair_of_tiles(1)
                 products(0, z_first, 0, PAIRS, (2, 3))
                 quantise_z(0, z_first, 0, PAIRS, woven_at(AT_Z_WOVEN, PAIRS, "z_woven_first"))
             if a == A1 + 1:
-                quantise_weight_block(2)
+                quantise_weight_block(3)
         pair_of_tiles(2)
         make_h(6)
         make_h(7)
-        quantise_weight_block(3)
+        quantise_weight_block(4)
         gates_of_pair(3)
-        for number in range(4, len(weight_blocks)):
-            quantise_weight_block(number)
+        quantise_weight_block(5)
 
         edges = [sum(PIECES[:k]) for k in range(len(PIECES) + 1)]
         spans = list(zip(edges[:-1], edges[1:]))

@@ -36,7 +36,9 @@ ALIGN = 64
 
 PIECES = (256, 128, 128)
 FIRST_Q_TILES = 2
-A0, A1 = 3, 5
+FIRST_RUN = 5
+Z_ON_GPSIMD = 128
+REST_ON_SCALAR = False
 ROW_DEPTH = 4
 HEAD_DEPTH = 8
 GATED_DEPTH = 2
@@ -49,12 +51,16 @@ AT_TAB_WORDS = AT_W3_DEALT + 4 * H - ALIGN
 AT_TAB_SCALES = AT_TAB_WORDS + ALIGN + 2 * STAGE_BYTES
 AT_V_WORDS = AT_TAB_SCALES + T + H - 4 * S
 AT_SCALES_IN = AT_TAB_SCALES + T
-AT_STAGES = (AT_V_WORDS + 4 * S, AT_TAB_WORDS + ALIGN, AT_TAB_WORDS + ALIGN + STAGE_BYTES)
-AT_W2_IN = AT_STAGES[0] + STAGE_BYTES
+AT_W1_STAGE = AT_V_WORDS + 4 * S
+AT_W2_IN = AT_W1_STAGE + GROUPS * STAGE_BYTES
 AT_W3_IN = AT_W2_IN + 2 * H
 AT_REL = AT_W3_IN + ALIGN
 AT_W1_ROUNDED = AT_W3_IN + 4 * H
-AT_Q_LAST = AT_W1_ROUNDED + GROUPS * ROUNDED_BYTES
+AT_W4_STAGE = AT_W1_ROUNDED + GROUPS * ROUNDED_BYTES - ALIGN
+AT_STAGES = (AT_W1_STAGE, AT_W1_STAGE + STAGE_BYTES) * 2 + (AT_W4_STAGE, AT_W1_STAGE)
+AT_H_FIRST = AT_TAB_WORDS + ALIGN
+AT_Z_WEIGHED = AT_H_FIRST + 2 * 4 * S
+AT_Q_LAST = AT_W4_STAGE + STAGE_BYTES
 AT_DIFF = tuple(AT_Q_LAST + 4 * S + ROUNDED_BYTES * k for k in range(4))
 AT_ROUNDED = (AT_W1_ROUNDED, AT_W1_ROUNDED + ROUNDED_BYTES) + AT_DIFF
 AT_Z_WOVEN = AT_ROUNDED[5] + ROUNDED_BYTES
@@ -136,10 +142,6 @@ def tile_list_triple_pair_rerank_kernel(
             nc.vector.tensor_copy(v_w[:, lo : lo + BANK], tab_w[:].indirect(entries))
         w3_w = shared.tile([P, 4 * H], U8, name="w3_w", align_bytes=ALIGN, offset=AT_W3_DEALT)
         deal_columns(w3_w, w3_in)
-        stage_ring = [
-            shared.tile([P, PACK, GROUP], F32, name="stage%d" % k, align_bytes=ALIGN, offset=at)
-            for k, at in enumerate(AT_STAGES)
-        ]
 
         def quantised(width, name, woven, at=None):
             if at is None:
@@ -156,13 +158,12 @@ def tile_list_triple_pair_rerank_kernel(
 
         def quantise_weight_block(number):
             name, w, row_group, col_group = weight_blocks[number]
-            stage = take(stage_ring)
+            stage = shared.tile([P, PACK, GROUP], F32, name="stage%d" % number, align_bytes=ALIGN, offset=AT_STAGES[number])
             rows = w[GROUP * row_group : GROUP * (row_group + 1), GROUP * col_group : GROUP * (col_group + 1)]
             at = AT_ROUNDED[number]
             rounded = shared.tile([P, PACK * GROUP], BF16, name="rounded%d" % number, align_bytes=ALIGN, offset=at)
             if name == "w1":
-                queue = nc.gpsimd if number == 0 else nc.sync
-                queue.dma_start(out=stage[:], in_=rows.rearrange("(p j) c -> p j c", j=PACK))
+                nc.gpsimd.dma_start(out=stage[:], in_=rows.rearrange("(p j) c -> p j c", j=PACK))
                 into = rounded[:].rearrange("p (t b e j) -> p t b e j", t=PACK, e=RUN, j=PACK)
                 by_place = stage[:].rearrange("p j (b t e) -> p t b e j", t=PACK, e=RUN)
                 for t in range(PACK):
@@ -196,7 +197,7 @@ def tile_list_triple_pair_rerank_kernel(
         def make_q(tiles):
             jobs = []
             for a in tiles:
-                if a == TILES - 1:
+                if a == FIRST_RUN - 1:
                     q_rows[a] = shared.tile([P, S], F32, name="q_last", align_bytes=ALIGN, offset=AT_Q_LAST)
                 else:
                     q_rows[a] = take(q_ring)
@@ -212,7 +213,10 @@ def tile_list_triple_pair_rerank_kernel(
         def make_h(a):
             g, t = divmod(a, PACK)
             codes, scales = weight_q["w1", 0, g]
-            h[a] = keep.tile([P, S], F32, name="h%d" % a)
+            if g == 0:
+                h[a] = shared.tile([P, S], F32, name="h%d" % a, align_bytes=ALIGN, offset=AT_H_FIRST + 4 * S * t)
+            else:
+                h[a] = keep.tile([P, S], F32, name="h%d" % a)
             first_stage([(h[a], codes[:, P * t : P * (t + 1)].bitcast(FP8X4), scales[:, P * t : P * (t + 1)])])
 
         def pick_q(a):
@@ -254,6 +258,27 @@ def tile_list_triple_pair_rerank_kernel(
             into, by_runs = weaving(woven[:], z)
             spread = rel_sb[:, g, :, 0:1].unsqueeze(1).broadcast_to([P, (hi - lo) // LINE, PACK, LINE])
             nc.vector.tensor_tensor(into, by_runs, spread, MULT)
+            codes, scales = quantised(hi - lo, "z%d_%d" % (g, lo), woven[:])
+            for col in range(lo, hi, P):
+                z_q[g, col] = (codes[:, col - lo : col - lo + P].bitcast(FP8X4), scales[:, col - lo : col - lo + P])
+
+        def weigh_first_z(z):
+            weighed = shared.tile([P, PACK, PAIRS], F32, name="z_weighed", align_bytes=ALIGN, offset=AT_Z_WEIGHED)
+            for t in range(PACK):
+                nc.gpsimd.tensor_scalar(weighed[:, t, :], z[:, t, :], rel_sb[:, 0, t, 0:1], 0.0, MULT, ADD)
+            woven = woven_at(AT_Z_WOVEN, PAIRS, "z_woven_first")
+            for lo in range(0, Z_ON_GPSIMD, P):
+                into = woven[:, PACK * lo : PACK * (lo + P)].rearrange("p (i t) -> p i t", t=PACK)
+                nc.gpsimd.tensor_scalar(into, weighed[:, :, lo : lo + P].rearrange("p t i -> p i t"), 1.0, 0.0, MULT, ADD)
+            return weighed, woven
+
+        def weave_rest(weighed, woven):
+            if Z_ON_GPSIMD < PAIRS:
+                copy = nc.scalar.copy if REST_ON_SCALAR else nc.vector.tensor_copy
+                copy(*weaving(woven[:, PACK * Z_ON_GPSIMD :], weighed[:, :, Z_ON_GPSIMD:]))
+            keep_z(0, 0, PAIRS, woven)
+
+        def keep_z(g, lo, hi, woven):
             codes, scales = quantised(hi - lo, "z%d_%d" % (g, lo), woven[:])
             for col in range(lo, hi, P):
                 z_q[g, col] = (codes[:, col - lo : col - lo + P].bitcast(FP8X4), scales[:, col - lo : col - lo + P])
@@ -336,37 +361,40 @@ def tile_list_triple_pair_rerank_kernel(
             make_h(2 * pair + 1)
             gates_of_pair(pair)
 
+        def run_of_q(tiles):
+            for a in tiles:
+                if a >= FIRST_Q_TILES:
+                    make_q((a,))
+                pick_q(a)
+
+        def differences(tiles):
+            for a in tiles:
+                make_r(a)
+                pick_r_less_q(a)
+
         make_q(range(FIRST_Q_TILES))
-        for a in range(TILES):
-            if a >= FIRST_Q_TILES:
-                make_q((a,))
-            pick_q(a)
+        run_of_q(range(FIRST_RUN))
         for number in range(GROUPS):
             quantise_weight_block(number)
         by_tile = rel.rearrange("(g b t e) -> g t b e", g=GROUPS, t=PACK, e=RUN)
         for c_tile in range(TILES):
             g, t = divmod(c_tile, PACK)
             nc.sync.dma_start(out=rel_sb[:, g, t, 0:1], in_=by_tile[g, t])
-        for a in range(TILES):
-            make_r(a)
-            pick_r_less_q(a)
-            if a == A0:
-                pair_of_tiles(0)
-                products(0, z_first, 0, PAIRS, (0, 1))
-            if a == A0 + 1:
-                quantise_weight_block(2)
-            if a == A1:
-                pair_of_tiles(1)
-                products(0, z_first, 0, PAIRS, (2, 3))
-                quantise_z(0, z_first, 0, PAIRS, woven_at(AT_Z_WOVEN, PAIRS, "z_woven_first"))
-            if a == A1 + 1:
-                quantise_weight_block(3)
-        pair_of_tiles(2)
-        make_h(6)
-        make_h(7)
-        quantise_weight_block(4)
+        differences(range(PACK))
+        for pair in range(2):
+            pair_of_tiles(pair)
+            products(0, z_first, 0, PAIRS, (2 * pair, 2 * pair + 1))
+        run_of_q(range(FIRST_RUN, TILES))
+        first_z = weigh_first_z(z_first)
+        differences(range(PACK, TILES))
+        for a in range(PACK, TILES):
+            make_h(a)
+        quantise_weight_block(2)
+        gates_of_pair(2)
         gates_of_pair(3)
-        quantise_weight_block(5)
+        weave_rest(*first_z)
+        for number in range(3, len(weight_blocks)):
+            quantise_weight_block(number)
 
         edges = [sum(PIECES[:k]) for k in range(len(PIECES) + 1)]
         spans = list(zip(edges[:-1], edges[1:]))

@@ -38,7 +38,8 @@ PIECES = (256, 128, 128)
 FIRST_Q_TILES = 2
 FIRST_RUN = 5
 Z_ON_GPSIMD = 128
-REST_ON_SCALAR = False
+REST_ON_SCALAR = True
+ON_VECTOR = (2,)
 ROW_DEPTH = 4
 HEAD_DEPTH = 8
 GATED_DEPTH = 2
@@ -48,26 +49,28 @@ ROUNDED_BYTES = 2 * PACK * GROUP
 WOVEN_BYTES = 2 * PACK * P
 AT_W3_DEALT = 0
 AT_TAB_WORDS = AT_W3_DEALT + 4 * H - ALIGN
-AT_TAB_SCALES = AT_TAB_WORDS + ALIGN + 2 * STAGE_BYTES
+AT_W1_STAGE = AT_TAB_WORDS + ALIGN + 2 * STAGE_BYTES
+AT_TAB_SCALES = AT_W1_STAGE + GROUPS * STAGE_BYTES
 AT_V_WORDS = AT_TAB_SCALES + T + H - 4 * S
 AT_SCALES_IN = AT_TAB_SCALES + T
-AT_W1_STAGE = AT_V_WORDS + 4 * S
-AT_W2_IN = AT_W1_STAGE + GROUPS * STAGE_BYTES
+AT_W2_IN = AT_V_WORDS + 4 * S
 AT_W3_IN = AT_W2_IN + 2 * H
 AT_REL = AT_W3_IN + ALIGN
-AT_W1_ROUNDED = AT_W3_IN + 4 * H
+AT_W1_ROUNDED = AT_W3_IN + 4 * H + ALIGN
 AT_W4_STAGE = AT_W1_ROUNDED + GROUPS * ROUNDED_BYTES - ALIGN
-AT_STAGES = (AT_W1_STAGE, AT_W1_STAGE + STAGE_BYTES) * 2 + (AT_W4_STAGE, AT_W1_STAGE)
+AT_STAGES = (AT_W1_STAGE, AT_W1_STAGE + STAGE_BYTES, AT_W4_STAGE, AT_W1_STAGE)
 AT_H_FIRST = AT_TAB_WORDS + ALIGN
 AT_Z_WEIGHED = AT_H_FIRST + 2 * 4 * S
 AT_Q_LAST = AT_W4_STAGE + STAGE_BYTES
-AT_DIFF = tuple(AT_Q_LAST + 4 * S + ROUNDED_BYTES * k for k in range(4))
-AT_ROUNDED = (AT_W1_ROUNDED, AT_W1_ROUNDED + ROUNDED_BYTES) + AT_DIFF
-AT_Z_WOVEN = AT_ROUNDED[5] + ROUNDED_BYTES
+AT_DIFF_THIRD = AT_Q_LAST + 4 * S
+AT_DIFF = (AT_W1_ROUNDED - ALIGN, AT_W1_ROUNDED + ROUNDED_BYTES - ALIGN, AT_DIFF_THIRD, AT_DIFF_THIRD + 3 * ROUNDED_BYTES // 2)
+AT_Z_WOVEN = AT_DIFF_THIRD + 3 * ROUNDED_BYTES
 AT_Z_FIRST = AT_Z_WOVEN + 2 * PACK * PAIRS
+AT_ROUNDED = (0, 0, AT_Z_WOVEN, AT_DIFF[2], AT_DIFF[3] - ROUNDED_BYTES // 2, AT_DIFF[3] + ROUNDED_BYTES // 2)
 AT_Z_PIECE = (AT_Z_FIRST + 4 * PACK * PAIRS, AT_ROUNDED[5], AT_Z_FIRST)
 AT_Y_FIRST = AT_Z_PIECE[0] + 4 * PACK * PIECES[0]
 AT_Y_MIDDLE = AT_Y_FIRST + GROUPS * 2 * PACK * PIECES[0]
+AT_GATED_LAST = AT_Z_PIECE[1]
 AT_Y_WOVEN = (AT_Y_FIRST, AT_Y_MIDDLE, AT_Y_FIRST)
 AT_Y_LAST = (AT_Z_PIECE[0], AT_Y_MIDDLE)
 
@@ -137,9 +140,9 @@ def tile_list_triple_pair_rerank_kernel(
         w_s = keep.tile([P, H], U8, name="w_s", align_bytes=ALIGN)
         deal_columns(w_s, scales_in)
         v_w = shared.tile([P, S], U32, name="v_w", align_bytes=ALIGN, offset=AT_V_WORDS)
-        for lo in range(0, S, BANK):
-            entries = offs_sb[:, lo // LIST_ROWS : (lo + BANK) // LIST_ROWS]
-            nc.vector.tensor_copy(v_w[:, lo : lo + BANK], tab_w[:].indirect(entries))
+        for lo, hi in ((0, BANK), (BANK, S)):
+            entries = offs_sb[:, lo // LIST_ROWS : hi // LIST_ROWS]
+            nc.vector.tensor_copy(v_w[:, lo:hi], tab_w[:].indirect(entries))
         w3_w = shared.tile([P, 4 * H], U8, name="w3_w", align_bytes=ALIGN, offset=AT_W3_DEALT)
         deal_columns(w3_w, w3_in)
 
@@ -155,31 +158,36 @@ def tile_list_triple_pair_rerank_kernel(
         weight_blocks = [("w1", w1, 0, g) for g in range(GROUPS)]
         weight_blocks = weight_blocks + [("w4", w4, c_group, g) for g in range(GROUPS) for c_group in range(GROUPS)]
         weight_q = {}
+        w1_stage = shared.tile([P, GROUPS, PACK, GROUP], F32, name="w1_stage", align_bytes=ALIGN, offset=AT_W1_STAGE)
+
+        def quantise_w1():
+            rounded = shared.tile([P, PACK * H], BF16, name="w1_rounded", align_bytes=ALIGN, offset=AT_W1_ROUNDED)
+            into = rounded[:].rearrange("p (g t b e j) -> p g t b e j", g=GROUPS, t=PACK, e=RUN, j=PACK)
+            for g in range(GROUPS):
+                rows = w1[:, GROUP * g : GROUP * (g + 1)]
+                nc.gpsimd.dma_start(out=w1_stage[:, g], in_=rows.rearrange("(p j) c -> p j c", j=PACK))
+            for g in range(GROUPS):
+                by_place = w1_stage[:, g].rearrange("p j (b t e) -> p t b e j", t=PACK, e=RUN)
+                for t in range(PACK):
+                    nc.gpsimd.tensor_scalar(into[:, g, t], by_place[:, t], 1.0, 0.0, MULT, ADD)
+            weight_q["w1"] = quantised(H, "w1", rounded[:], AT_Q_LAST)
 
         def quantise_weight_block(number):
             name, w, row_group, col_group = weight_blocks[number]
-            stage = shared.tile([P, PACK, GROUP], F32, name="stage%d" % number, align_bytes=ALIGN, offset=AT_STAGES[number])
+            at = AT_STAGES[number - GROUPS]
+            stage = shared.tile([P, PACK, GROUP], F32, name="stage%d" % number, align_bytes=ALIGN, offset=at)
             rows = w[GROUP * row_group : GROUP * (row_group + 1), GROUP * col_group : GROUP * (col_group + 1)]
             at = AT_ROUNDED[number]
             rounded = shared.tile([P, PACK * GROUP], BF16, name="rounded%d" % number, align_bytes=ALIGN, offset=at)
-            if name == "w1":
-                nc.gpsimd.dma_start(out=stage[:], in_=rows.rearrange("(p j) c -> p j c", j=PACK))
-                into = rounded[:].rearrange("p (t b e j) -> p t b e j", t=PACK, e=RUN, j=PACK)
-                by_place = stage[:].rearrange("p j (b t e) -> p t b e j", t=PACK, e=RUN)
-                for t in range(PACK):
-                    nc.gpsimd.tensor_scalar(into[:, t], by_place[:, t], 1.0, 0.0, MULT, ADD)
-            else:
-                by_place = rows.rearrange("(b j e) n -> j b e n", j=PACK, e=RUN)
-                for j in range(PACK):
-                    nc.sync.dma_start(out=stage[:, j, :], in_=by_place[j])
-                nc.scalar.copy(
-                    out=rounded[:].rearrange("p (t m j) -> p m j t", t=PACK, j=PACK),
-                    in_=stage[:].rearrange("p j (m t) -> p m j t", t=PACK),
-                )
-            weight_q[name, row_group, col_group] = quantised(
-                GROUP, "%s_%d%d" % (name, row_group, col_group), rounded[:],
-                AT_Q_LAST + 4 * GROUP * number if name == "w1" else None,
+            by_place = rows.rearrange("(b j e) n -> j b e n", j=PACK, e=RUN)
+            for j in range(PACK):
+                nc.sync.dma_start(out=stage[:, j, :], in_=by_place[j])
+            copy = nc.vector.tensor_copy if number in ON_VECTOR else nc.scalar.copy
+            copy(
+                out=rounded[:].rearrange("p (t m j) -> p m j t", t=PACK, j=PACK),
+                in_=stage[:].rearrange("p j (m t) -> p m j t", t=PACK),
             )
+            weight_q[name, row_group, col_group] = quantised(GROUP, "%s_%d%d" % (name, row_group, col_group), rounded[:])
 
         def first_stage(jobs):
             for lo in range(0, S, BANK):
@@ -197,7 +205,7 @@ def tile_list_triple_pair_rerank_kernel(
         def make_q(tiles):
             jobs = []
             for a in tiles:
-                if a == FIRST_RUN - 1:
+                if a == FIRST_RUN - 2:
                     q_rows[a] = shared.tile([P, S], F32, name="q_last", align_bytes=ALIGN, offset=AT_Q_LAST)
                 else:
                     q_rows[a] = take(q_ring)
@@ -212,12 +220,12 @@ def tile_list_triple_pair_rerank_kernel(
 
         def make_h(a):
             g, t = divmod(a, PACK)
-            codes, scales = weight_q["w1", 0, g]
+            codes, scales = weight_q["w1"]
             if g == 0:
                 h[a] = shared.tile([P, S], F32, name="h%d" % a, align_bytes=ALIGN, offset=AT_H_FIRST + 4 * S * t)
             else:
                 h[a] = keep.tile([P, S], F32, name="h%d" % a)
-            first_stage([(h[a], codes[:, P * t : P * (t + 1)].bitcast(FP8X4), scales[:, P * t : P * (t + 1)])])
+            first_stage([(h[a], codes[:, P * a : P * (a + 1)].bitcast(FP8X4), scales[:, P * a : P * (a + 1)])])
 
         def pick_q(a):
             q_head[a] = take(head_ring)
@@ -241,7 +249,10 @@ def tile_list_triple_pair_rerank_kernel(
             gated = {}
             for t in places:
                 a = PACK * g + t
-                gated[t] = take(gated_ring)[:, : hi - lo]
+                if lo == 3 * P and t == 2:
+                    gated[t] = shared.tile([P, P], F32, name="gated_last", align_bytes=ALIGN, offset=AT_GATED_LAST)[:]
+                else:
+                    gated[t] = take(gated_ring)[:, : hi - lo]
                 nc.vector.tensor_tensor(gated[t], h[a][:].indirect(pos1_sb[:, entries]), gate[a][:, lo:hi], MULT)
             for t in places:
                 nc.vector.tensor_tensor(z[:, t, :], h[PACK * g + t][:].indirect(pos2_sb[:, entries]), gated[t], MULT)
@@ -276,10 +287,11 @@ def tile_list_triple_pair_rerank_kernel(
             if Z_ON_GPSIMD < PAIRS:
                 copy = nc.scalar.copy if REST_ON_SCALAR else nc.vector.tensor_copy
                 copy(*weaving(woven[:, PACK * Z_ON_GPSIMD :], weighed[:, :, Z_ON_GPSIMD:]))
-            keep_z(0, 0, PAIRS, woven)
+            keep_z(0, 0, 2 * P, woven[:, : PACK * 2 * P])
+            keep_z(0, 2 * P, 3 * P, woven[:, PACK * 2 * P : PACK * 3 * P])
 
-        def keep_z(g, lo, hi, woven):
-            codes, scales = quantised(hi - lo, "z%d_%d" % (g, lo), woven[:])
+        def keep_z(g, lo, hi, woven, at=None):
+            codes, scales = quantised(hi - lo, "z%d_%d" % (g, lo), woven, at)
             for col in range(lo, hi, P):
                 z_q[g, col] = (codes[:, col - lo : col - lo + P].bitcast(FP8X4), scales[:, col - lo : col - lo + P])
 
@@ -374,13 +386,13 @@ def tile_list_triple_pair_rerank_kernel(
 
         make_q(range(FIRST_Q_TILES))
         run_of_q(range(FIRST_RUN))
-        for number in range(GROUPS):
-            quantise_weight_block(number)
+        quantise_w1()
         by_tile = rel.rearrange("(g b t e) -> g t b e", g=GROUPS, t=PACK, e=RUN)
         for c_tile in range(TILES):
             g, t = divmod(c_tile, PACK)
             nc.sync.dma_start(out=rel_sb[:, g, t, 0:1], in_=by_tile[g, t])
         differences(range(PACK))
+        quantise_weight_block(2)
         for pair in range(2):
             pair_of_tiles(pair)
             products(0, z_first, 0, PAIRS, (2 * pair, 2 * pair + 1))
@@ -389,10 +401,9 @@ def tile_list_triple_pair_rerank_kernel(
         differences(range(PACK, TILES))
         for a in range(PACK, TILES):
             make_h(a)
-        quantise_weight_block(2)
+        weave_rest(*first_z)
         gates_of_pair(2)
         gates_of_pair(3)
-        weave_rest(*first_z)
         for number in range(3, len(weight_blocks)):
             quantise_weight_block(number)
 
@@ -405,20 +416,20 @@ def tile_list_triple_pair_rerank_kernel(
             z_piece = z_tile[:].rearrange("p (t i) -> p t i", t=PACK)
             for places in ((0, 1), (2, 3)):
                 products(1, z_piece, lo, hi, places)
+            if piece == 2:
+                keep_z(0, lo, hi, first_z[1][:, PACK * lo :], AT_GATED_LAST)
+                open_sums(lo, hi)
             woven = keep.tile([P, PACK * (hi - lo)], BF16, name="z_woven%d" % piece, align_bytes=ALIGN)
             quantise_z(1, z_piece, lo, hi, woven)
             if piece == 1:
                 open_sums(*spans[0])
                 finish(0)
-                open_sums(lo, PAIRS)
+                open_sums(lo, hi)
         finish(1)
         store_codes(0, edges[2])
         finish_last(2)
         store_codes(edges[2], PAIRS)
-
-        plane_rows = y_scales[:].bitcast(I32).rearrange("p (g i) -> p g i", g=GROUPS)
-        for quad in range(QUADS):
-            nc.scalar.dma_start(
-                out=out_2[:, 4 * quad : 4 * quad + 4, :].rearrange("g row i -> row g i").bitcast(I32),
-                in_=plane_rows[32 * quad : 32 * quad + 4, :, :],
-            )
+        plane = y_scales[:].rearrange("p (g i) -> p g i", g=GROUPS)
+        for r in range(QUADS):
+            rows = out_2[:, r:BLOCKS:QUADS, :].rearrange("g row i -> row g i")
+            nc.scalar.dma_start(out=rows.bitcast(I32), in_=plane[r:P:32].bitcast(I32))

@@ -39,7 +39,7 @@ FIRST_Q_TILES = 2
 FIRST_RUN = 5
 Z_ON_GPSIMD = 128
 REST_ON_SCALAR = True
-ON_VECTOR = (2,)
+ON_GPSIMD = (2,)
 ROW_DEPTH = 4
 HEAD_DEPTH = 8
 GATED_DEPTH = 2
@@ -56,17 +56,21 @@ AT_SCALES_IN = AT_TAB_SCALES + T
 AT_W2_IN = AT_V_WORDS + 4 * S
 AT_W3_IN = AT_W2_IN + 2 * H
 AT_REL = AT_W3_IN + ALIGN
-AT_W1_ROUNDED = AT_W3_IN + 4 * H + ALIGN
-AT_W4_STAGE = AT_W1_ROUNDED + GROUPS * ROUNDED_BYTES - ALIGN
-AT_STAGES = (AT_W1_STAGE, AT_W1_STAGE + STAGE_BYTES, AT_W4_STAGE, AT_W1_STAGE)
+AT_W4_STAGE = AT_W3_IN + 4 * H - ALIGN
+AT_DIFF_FIRST = AT_W4_STAGE + STAGE_BYTES
+AT_W1_ROUNDED = (AT_DIFF_FIRST + ROUNDED_BYTES // 2, AT_DIFF_FIRST + 2 * ROUNDED_BYTES)
+AT_W4_ROUNDED = AT_W1_ROUNDED[1] + ROUNDED_BYTES
+AT_STAGES = (AT_W4_STAGE, AT_W1_STAGE, AT_W1_STAGE + STAGE_BYTES, AT_W4_STAGE)
 AT_H_FIRST = AT_TAB_WORDS + ALIGN
 AT_Z_WEIGHED = AT_H_FIRST + 2 * 4 * S
-AT_Q_LAST = AT_W4_STAGE + STAGE_BYTES
-AT_DIFF_THIRD = AT_Q_LAST + 4 * S
-AT_DIFF = (AT_W1_ROUNDED - ALIGN, AT_W1_ROUNDED + ROUNDED_BYTES - ALIGN, AT_DIFF_THIRD, AT_DIFF_THIRD + 3 * ROUNDED_BYTES // 2)
+AT_Q_LAST = AT_W4_ROUNDED + ROUNDED_BYTES
+AT_GATE_SECOND = AT_Q_LAST + 4 * S
+AT_W1_CODES = (AT_Q_LAST, AT_GATE_SECOND)
+AT_DIFF_THIRD = AT_GATE_SECOND + 4 * S
+AT_DIFF = (AT_DIFF_FIRST, AT_DIFF_FIRST + ROUNDED_BYTES, AT_DIFF_THIRD, AT_DIFF_THIRD + 3 * ROUNDED_BYTES // 2)
 AT_Z_WOVEN = AT_DIFF_THIRD + 3 * ROUNDED_BYTES
 AT_Z_FIRST = AT_Z_WOVEN + 2 * PACK * PAIRS
-AT_ROUNDED = (0, 0, AT_Z_WOVEN, AT_DIFF[2], AT_DIFF[3] - ROUNDED_BYTES // 2, AT_DIFF[3] + ROUNDED_BYTES // 2)
+AT_ROUNDED = (0, 0, AT_W4_ROUNDED, AT_DIFF[2], AT_DIFF[3] - ROUNDED_BYTES // 2, AT_DIFF[3] + ROUNDED_BYTES // 2)
 AT_Z_PIECE = (AT_Z_FIRST + 4 * PACK * PAIRS, AT_ROUNDED[5], AT_Z_FIRST)
 AT_Y_FIRST = AT_Z_PIECE[0] + 4 * PACK * PIECES[0]
 AT_Y_MIDDLE = AT_Y_FIRST + GROUPS * 2 * PACK * PIECES[0]
@@ -157,22 +161,25 @@ def tile_list_triple_pair_rerank_kernel(
 
         weight_blocks = [("w1", w1, 0, g) for g in range(GROUPS)]
         weight_blocks = weight_blocks + [("w4", w4, c_group, g) for g in range(GROUPS) for c_group in range(GROUPS)]
-        weight_q = {}
+        weight_q, w1_rounded, w4_rounded = {}, {}, {}
         w1_stage = shared.tile([P, GROUPS, PACK, GROUP], F32, name="w1_stage", align_bytes=ALIGN, offset=AT_W1_STAGE)
 
         def quantise_w1():
-            rounded = shared.tile([P, PACK * H], BF16, name="w1_rounded", align_bytes=ALIGN, offset=AT_W1_ROUNDED)
-            into = rounded[:].rearrange("p (g t b e j) -> p g t b e j", g=GROUPS, t=PACK, e=RUN, j=PACK)
             for g in range(GROUPS):
                 rows = w1[:, GROUP * g : GROUP * (g + 1)]
                 nc.gpsimd.dma_start(out=w1_stage[:, g], in_=rows.rearrange("(p j) c -> p j c", j=PACK))
             for g in range(GROUPS):
+                at = AT_W1_ROUNDED[g]
+                w1_rounded[g] = shared.tile([P, PACK * GROUP], BF16, name="w1_rounded%d" % g, align_bytes=ALIGN, offset=at)
+                into = w1_rounded[g][:].rearrange("p (t b e j) -> p t b e j", t=PACK, e=RUN, j=PACK)
                 by_place = w1_stage[:, g].rearrange("p j (b t e) -> p t b e j", t=PACK, e=RUN)
                 for t in range(PACK):
-                    nc.gpsimd.tensor_scalar(into[:, g, t], by_place[:, t], 1.0, 0.0, MULT, ADD)
-            weight_q["w1"] = quantised(H, "w1", rounded[:], AT_Q_LAST)
+                    nc.gpsimd.tensor_scalar(into[:, t], by_place[:, t], 1.0, 0.0, MULT, ADD)
 
-        def quantise_weight_block(number):
+        def quantise_w1_block(g):
+            weight_q["w1", g] = quantised(GROUP, "w1_%d" % g, w1_rounded[g][:], AT_W1_CODES[g])
+
+        def round_weight_block(number):
             name, w, row_group, col_group = weight_blocks[number]
             at = AT_STAGES[number - GROUPS]
             stage = shared.tile([P, PACK, GROUP], F32, name="stage%d" % number, align_bytes=ALIGN, offset=at)
@@ -182,12 +189,23 @@ def tile_list_triple_pair_rerank_kernel(
             by_place = rows.rearrange("(b j e) n -> j b e n", j=PACK, e=RUN)
             for j in range(PACK):
                 nc.sync.dma_start(out=stage[:, j, :], in_=by_place[j])
-            copy = nc.vector.tensor_copy if number in ON_VECTOR else nc.scalar.copy
-            copy(
-                out=rounded[:].rearrange("p (t m j) -> p m j t", t=PACK, j=PACK),
-                in_=stage[:].rearrange("p j (m t) -> p m j t", t=PACK),
+            if number in ON_GPSIMD:
+                into = rounded[:].rearrange("p (t m j) -> p t m j", t=PACK, j=PACK)
+                by_column = stage[:].rearrange("p j (m t) -> p t m j", t=PACK)
+                for t in range(PACK):
+                    nc.gpsimd.tensor_scalar(into[:, t], by_column[:, t], 1.0, 0.0, MULT, ADD)
+            else:
+                nc.scalar.copy(
+                    out=rounded[:].rearrange("p (t m j) -> p m j t", t=PACK, j=PACK),
+                    in_=stage[:].rearrange("p j (m t) -> p m j t", t=PACK),
+                )
+            w4_rounded[number] = rounded
+
+        def quantise_weight_block(number, at=None):
+            name, w, row_group, col_group = weight_blocks[number]
+            weight_q[name, row_group, col_group] = quantised(
+                GROUP, "%s_%d%d" % (name, row_group, col_group), w4_rounded[number][:], at
             )
-            weight_q[name, row_group, col_group] = quantised(GROUP, "%s_%d%d" % (name, row_group, col_group), rounded[:])
 
         def first_stage(jobs):
             for lo in range(0, S, BANK):
@@ -220,12 +238,12 @@ def tile_list_triple_pair_rerank_kernel(
 
         def make_h(a):
             g, t = divmod(a, PACK)
-            codes, scales = weight_q["w1"]
+            codes, scales = weight_q["w1", g]
             if g == 0:
                 h[a] = shared.tile([P, S], F32, name="h%d" % a, align_bytes=ALIGN, offset=AT_H_FIRST + 4 * S * t)
             else:
                 h[a] = keep.tile([P, S], F32, name="h%d" % a)
-            first_stage([(h[a], codes[:, P * a : P * (a + 1)].bitcast(FP8X4), scales[:, P * a : P * (a + 1)])])
+            first_stage([(h[a], codes[:, P * t : P * (t + 1)].bitcast(FP8X4), scales[:, P * t : P * (t + 1)])])
 
         def pick_q(a):
             q_head[a] = take(head_ring)
@@ -240,7 +258,10 @@ def tile_list_triple_pair_rerank_kernel(
             nc.vector.tensor_tensor(into, r_rows[a][:].indirect(pos2_sb[:]), q_head[a][:], SUBTRACT)
 
         def gates_of_pair(pair):
-            both = keep.tile([P, 2 * PAIRS], F32, name="gate%d" % pair)
+            if pair == 1:
+                both = shared.tile([P, 2 * PAIRS], F32, name="gate1", align_bytes=ALIGN, offset=AT_GATE_SECOND)
+            else:
+                both = keep.tile([P, 2 * PAIRS], F32, name="gate%d" % pair)
             nc.scalar.activation(out=both[:], in_=diff[pair][:], func=SIGMOID, scale=-1.0)
             gate[2 * pair], gate[2 * pair + 1] = both[:, :PAIRS], both[:, PAIRS:]
 
@@ -387,24 +408,28 @@ def tile_list_triple_pair_rerank_kernel(
         make_q(range(FIRST_Q_TILES))
         run_of_q(range(FIRST_RUN))
         quantise_w1()
+        round_weight_block(2)
+        quantise_w1_block(0)
         by_tile = rel.rearrange("(g b t e) -> g t b e", g=GROUPS, t=PACK, e=RUN)
         for c_tile in range(TILES):
             g, t = divmod(c_tile, PACK)
             nc.sync.dma_start(out=rel_sb[:, g, t, 0:1], in_=by_tile[g, t])
         differences(range(PACK))
-        quantise_weight_block(2)
         for pair in range(2):
             pair_of_tiles(pair)
             products(0, z_first, 0, PAIRS, (2 * pair, 2 * pair + 1))
+        quantise_w1_block(1)
         run_of_q(range(FIRST_RUN, TILES))
         first_z = weigh_first_z(z_first)
         differences(range(PACK, TILES))
         for a in range(PACK, TILES):
             make_h(a)
         weave_rest(*first_z)
+        quantise_weight_block(2, AT_Z_FIRST + 4096)
         gates_of_pair(2)
         gates_of_pair(3)
         for number in range(3, len(weight_blocks)):
+            round_weight_block(number)
             quantise_weight_block(number)
 
         edges = [sum(PIECES[:k]) for k in range(len(PIECES) + 1)]

@@ -36,12 +36,13 @@ ALIGN = 64
 
 PIECES = (256, 128, 128)
 FIRST_Q_TILES = 2
-FIRST_RUN = 5
-Z_ON_GPSIMD = 128
-REST_ON_SCALAR = True
-ON_GPSIMD = (2,)
+FIRST_RUN = 4
+Z_ON_GPSIMD = 0
+Z_ON_VECTOR = 256
+LATE_AT = 5
+ON_GPSIMD = ()
 ROW_DEPTH = 4
-HEAD_DEPTH = 8
+HEAD_DEPTH = 4
 GATED_DEPTH = 2
 
 STAGE_BYTES = 4 * PACK * GROUP
@@ -49,28 +50,29 @@ ROUNDED_BYTES = 2 * PACK * GROUP
 WOVEN_BYTES = 2 * PACK * P
 AT_W3_DEALT = 0
 AT_TAB_WORDS = AT_W3_DEALT + 4 * H - ALIGN
-AT_W1_STAGE = AT_TAB_WORDS + ALIGN + 2 * STAGE_BYTES
-AT_TAB_SCALES = AT_W1_STAGE + GROUPS * STAGE_BYTES
+AT_W1_STAGE = (AT_TAB_WORDS + ALIGN + 2 * STAGE_BYTES, AT_TAB_WORDS + ALIGN + 3 * STAGE_BYTES)
+AT_HEADS = AT_W1_STAGE[0]
+AT_TAB_SCALES = AT_W1_STAGE[1] + STAGE_BYTES
 AT_V_WORDS = AT_TAB_SCALES + T + H - 4 * S
 AT_SCALES_IN = AT_TAB_SCALES + T
 AT_W2_IN = AT_V_WORDS + 4 * S
 AT_W3_IN = AT_W2_IN + 2 * H
 AT_REL = AT_W3_IN + ALIGN
-AT_W4_STAGE = AT_W3_IN + 4 * H - ALIGN
-AT_DIFF_FIRST = AT_W4_STAGE + STAGE_BYTES
-AT_W1_ROUNDED = (AT_DIFF_FIRST + ROUNDED_BYTES // 2, AT_DIFF_FIRST + 2 * ROUNDED_BYTES)
-AT_W4_ROUNDED = AT_W1_ROUNDED[1] + ROUNDED_BYTES
-AT_STAGES = (AT_W4_STAGE, AT_W1_STAGE, AT_W1_STAGE + STAGE_BYTES, AT_W4_STAGE)
+AT_W1_ROUNDED_FIRST = AT_W3_IN + 4 * H - ALIGN
+AT_DIFF_FIRST = AT_W1_ROUNDED_FIRST + ROUNDED_BYTES - 2 * ALIGN
+AT_W1_ROUNDED = (AT_W1_ROUNDED_FIRST, AT_DIFF_FIRST + 2 * ROUNDED_BYTES)
+AT_W4_STAGE = AT_W1_ROUNDED[1] + ROUNDED_BYTES - ALIGN
+AT_STAGES = (AT_W1_STAGE[1], AT_W1_STAGE[0], AT_W4_STAGE, AT_W1_STAGE[1])
 AT_H_FIRST = AT_TAB_WORDS + ALIGN
 AT_Z_WEIGHED = AT_H_FIRST + 2 * 4 * S
-AT_Q_LAST = AT_W4_ROUNDED + ROUNDED_BYTES
-AT_GATE_SECOND = AT_Q_LAST + 4 * S
-AT_W1_CODES = (AT_Q_LAST, AT_GATE_SECOND)
-AT_DIFF_THIRD = AT_GATE_SECOND + 4 * S
-AT_DIFF = (AT_DIFF_FIRST, AT_DIFF_FIRST + ROUNDED_BYTES, AT_DIFF_THIRD, AT_DIFF_THIRD + 3 * ROUNDED_BYTES // 2)
+AT_Q_LAST = AT_W4_STAGE + STAGE_BYTES
+AT_DIFF_THIRD = AT_Q_LAST + 4 * S
+AT_DIFF_LATE = (AT_DIFF_THIRD, AT_DIFF_THIRD + 3 * ROUNDED_BYTES // 2)
 AT_Z_WOVEN = AT_DIFF_THIRD + 3 * ROUNDED_BYTES
-AT_Z_FIRST = AT_Z_WOVEN + 2 * PACK * PAIRS
-AT_ROUNDED = (0, 0, AT_W4_ROUNDED, AT_DIFF[2], AT_DIFF[3] - ROUNDED_BYTES // 2, AT_DIFF[3] + ROUNDED_BYTES // 2)
+AT_GATE_FIRST = AT_Z_WOVEN + 2 * PACK * PAIRS
+AT_Z_FIRST = AT_GATE_FIRST + 4 * GROUP
+AT_W1_CODES = (AT_Q_LAST, AT_GATE_FIRST)
+AT_ROUNDED = (0, 0, AT_Z_FIRST, AT_DIFF_LATE[0], AT_DIFF_LATE[1] - ROUNDED_BYTES // 2, AT_DIFF_LATE[1] + ROUNDED_BYTES // 2)
 AT_Z_PIECE = (AT_Z_FIRST + 4 * PACK * PAIRS, AT_ROUNDED[5], AT_Z_FIRST)
 AT_Y_FIRST = AT_Z_PIECE[0] + 4 * PACK * PIECES[0]
 AT_Y_MIDDLE = AT_Y_FIRST + GROUPS * 2 * PACK * PIECES[0]
@@ -162,19 +164,27 @@ def tile_list_triple_pair_rerank_kernel(
         weight_blocks = [("w1", w1, 0, g) for g in range(GROUPS)]
         weight_blocks = weight_blocks + [("w4", w4, c_group, g) for g in range(GROUPS) for c_group in range(GROUPS)]
         weight_q, w1_rounded, w4_rounded = {}, {}, {}
-        w1_stage = shared.tile([P, GROUPS, PACK, GROUP], F32, name="w1_stage", align_bytes=ALIGN, offset=AT_W1_STAGE)
+        w1_stage = [
+            shared.tile([P, PACK, GROUP], F32, name="w1_stage%d" % g, align_bytes=ALIGN, offset=AT_W1_STAGE[g])
+            for g in range(GROUPS)
+        ]
+        first_heads = shared.tile([P, PACK, PAIRS], F32, name="first_heads", align_bytes=ALIGN, offset=AT_HEADS)
 
         def quantise_w1():
             for g in range(GROUPS):
                 rows = w1[:, GROUP * g : GROUP * (g + 1)]
-                nc.gpsimd.dma_start(out=w1_stage[:, g], in_=rows.rearrange("(p j) c -> p j c", j=PACK))
+                nc.gpsimd.dma_start(out=w1_stage[g][:], in_=rows.rearrange("(p j) c -> p j c", j=PACK))
             for g in range(GROUPS):
                 at = AT_W1_ROUNDED[g]
                 w1_rounded[g] = shared.tile([P, PACK * GROUP], BF16, name="w1_rounded%d" % g, align_bytes=ALIGN, offset=at)
-                into = w1_rounded[g][:].rearrange("p (t b e j) -> p t b e j", t=PACK, e=RUN, j=PACK)
-                by_place = w1_stage[:, g].rearrange("p j (b t e) -> p t b e j", t=PACK, e=RUN)
-                for t in range(PACK):
-                    nc.gpsimd.tensor_scalar(into[:, t], by_place[:, t], 1.0, 0.0, MULT, ADD)
+            nc.vector.tensor_copy(
+                out=w1_rounded[0][:].rearrange("p (t b e j) -> p b t j e", t=PACK, e=RUN, j=PACK),
+                in_=w1_stage[0][:].rearrange("p j (b t e) -> p b t j e", t=PACK, e=RUN),
+            )
+            into = w1_rounded[1][:].rearrange("p (t b e j) -> p t b e j", t=PACK, e=RUN, j=PACK)
+            by_place = w1_stage[1][:].rearrange("p j (b t e) -> p t b e j", t=PACK, e=RUN)
+            for t in range(PACK):
+                nc.gpsimd.tensor_scalar(into[:, t], by_place[:, t], 1.0, 0.0, MULT, ADD)
 
         def quantise_w1_block(g):
             weight_q["w1", g] = quantised(GROUP, "w1_%d" % g, w1_rounded[g][:], AT_W1_CODES[g])
@@ -223,7 +233,7 @@ def tile_list_triple_pair_rerank_kernel(
         def make_q(tiles):
             jobs = []
             for a in tiles:
-                if a == FIRST_RUN - 2:
+                if a == FIRST_RUN - 1:
                     q_rows[a] = shared.tile([P, S], F32, name="q_last", align_bytes=ALIGN, offset=AT_Q_LAST)
                 else:
                     q_rows[a] = take(q_ring)
@@ -246,23 +256,25 @@ def tile_list_triple_pair_rerank_kernel(
             first_stage([(h[a], codes[:, P * t : P * (t + 1)].bitcast(FP8X4), scales[:, P * t : P * (t + 1)])])
 
         def pick_q(a):
-            q_head[a] = take(head_ring)
-            nc.vector.tensor_copy(q_head[a][:], q_rows[a][:].indirect(pos1_sb[:]))
+            q_head[a] = first_heads[:, a, :] if a < PACK else take(head_ring)[:]
+            nc.vector.tensor_copy(q_head[a], q_rows[a][:].indirect(pos1_sb[:]))
 
         def pick_r_less_q(a):
-            if a % 2 == 0:
-                diff[a // 2] = shared.tile(
-                    [P, 2 * PAIRS], F32, name="diff%d" % (a // 2), align_bytes=ALIGN, offset=AT_DIFF[a // 2]
-                )
+            if a == 0:
+                first = shared.tile([P, PACK * PAIRS], F32, name="diff_first", align_bytes=ALIGN, offset=AT_DIFF_FIRST)
+                diff[0], diff[1] = first[:, : 2 * PAIRS], first[:, 2 * PAIRS :]
+            elif a in (4, 6):
+                at = AT_DIFF_LATE[a // 2 - 2]
+                diff[a // 2] = shared.tile([P, 2 * PAIRS], F32, name="diff%d" % (a // 2), align_bytes=ALIGN, offset=at)[:]
             into = diff[a // 2][:, PAIRS * (a % 2) : PAIRS * (a % 2 + 1)]
-            nc.vector.tensor_tensor(into, r_rows[a][:].indirect(pos2_sb[:]), q_head[a][:], SUBTRACT)
+            nc.vector.tensor_tensor(into, r_rows[a][:].indirect(pos2_sb[:]), q_head[a], SUBTRACT)
 
         def gates_of_pair(pair):
-            if pair == 1:
-                both = shared.tile([P, 2 * PAIRS], F32, name="gate1", align_bytes=ALIGN, offset=AT_GATE_SECOND)
+            if pair == 0:
+                both = shared.tile([P, 2 * PAIRS], F32, name="gate0", align_bytes=ALIGN, offset=AT_GATE_FIRST)
             else:
                 both = keep.tile([P, 2 * PAIRS], F32, name="gate%d" % pair)
-            nc.scalar.activation(out=both[:], in_=diff[pair][:], func=SIGMOID, scale=-1.0)
+            nc.scalar.activation(out=both[:], in_=diff[pair], func=SIGMOID, scale=-1.0)
             gate[2 * pair], gate[2 * pair + 1] = both[:, :PAIRS], both[:, PAIRS:]
 
         def products(g, z, lo, hi, places):
@@ -304,11 +316,12 @@ def tile_list_triple_pair_rerank_kernel(
                 nc.gpsimd.tensor_scalar(into, weighed[:, :, lo : lo + P].rearrange("p t i -> p i t"), 1.0, 0.0, MULT, ADD)
             return weighed, woven
 
-        def weave_rest(weighed, woven):
-            if Z_ON_GPSIMD < PAIRS:
-                copy = nc.scalar.copy if REST_ON_SCALAR else nc.vector.tensor_copy
-                copy(*weaving(woven[:, PACK * Z_ON_GPSIMD :], weighed[:, :, Z_ON_GPSIMD:]))
+        def weave_early(weighed, woven):
+            nc.vector.tensor_copy(*weaving(woven[:, : PACK * Z_ON_VECTOR], weighed[:, :, :Z_ON_VECTOR]))
             keep_z(0, 0, 2 * P, woven[:, : PACK * 2 * P])
+
+        def weave_late(weighed, woven):
+            nc.scalar.copy(*weaving(woven[:, PACK * Z_ON_VECTOR :], weighed[:, :, Z_ON_VECTOR:]))
             keep_z(0, 2 * P, 3 * P, woven[:, PACK * 2 * P : PACK * 3 * P])
 
         def keep_z(g, lo, hi, woven, at=None):
@@ -386,8 +399,6 @@ def tile_list_triple_pair_rerank_kernel(
             nc.sync.dma_start(out=words[:, :, lo:hi], in_=codes[:, :, lo:hi])
 
         rel_sb = shared.tile([P, GROUPS, PACK, RUN], F32, name="rel_sb", align_bytes=ALIGN, offset=AT_REL)
-        z_tile = shared.tile([P, PACK * PAIRS], F32, name="z_first", align_bytes=ALIGN, offset=AT_Z_FIRST)
-        z_first = z_tile[:].rearrange("p (t i) -> p t i", t=PACK)
 
         def pair_of_tiles(pair):
             make_h(2 * pair)
@@ -405,32 +416,39 @@ def tile_list_triple_pair_rerank_kernel(
                 make_r(a)
                 pick_r_less_q(a)
 
+        quantise_w1()
         make_q(range(FIRST_Q_TILES))
         run_of_q(range(FIRST_RUN))
-        quantise_w1()
-        round_weight_block(2)
         quantise_w1_block(0)
         by_tile = rel.rearrange("(g b t e) -> g t b e", g=GROUPS, t=PACK, e=RUN)
         for c_tile in range(TILES):
             g, t = divmod(c_tile, PACK)
             nc.sync.dma_start(out=rel_sb[:, g, t, 0:1], in_=by_tile[g, t])
         differences(range(PACK))
-        for pair in range(2):
-            pair_of_tiles(pair)
-            products(0, z_first, 0, PAIRS, (2 * pair, 2 * pair + 1))
+        make_h(0)
+        gates_of_pair(0)
+        make_h(1)
+        z_tile = shared.tile([P, PACK * PAIRS], F32, name="z_first", align_bytes=ALIGN, offset=AT_Z_FIRST)
+        z_first = z_tile[:].rearrange("p (t i) -> p t i", t=PACK)
+        products(0, z_first, 0, PAIRS, (0, 1))
         quantise_w1_block(1)
+        pair_of_tiles(1)
+        products(0, z_first, 0, PAIRS, (2, 3))
         run_of_q(range(FIRST_RUN, TILES))
         first_z = weigh_first_z(z_first)
         differences(range(PACK, TILES))
         for a in range(PACK, TILES):
             make_h(a)
-        weave_rest(*first_z)
-        quantise_weight_block(2, AT_Z_FIRST + 4096)
+        round_weight_block(2)
+        weave_early(*first_z)
+        quantise_weight_block(2)
         gates_of_pair(2)
         gates_of_pair(3)
         for number in range(3, len(weight_blocks)):
             round_weight_block(number)
             quantise_weight_block(number)
+            if number == LATE_AT:
+                weave_late(*first_z)
 
         edges = [sum(PIECES[:k]) for k in range(len(PIECES) + 1)]
         spans = list(zip(edges[:-1], edges[1:]))

@@ -31,54 +31,45 @@ RUN = 8
 BLOCKS = P // RUN
 QUADS = 4
 LINE = 4
-W3_PLANE = 4
+SCALE_FIRST, SCALE_STEP = 32, 4
 ALIGN = 64
 
 PIECES = (256, 128, 128)
-FIRST_Q_TILES = 2
-FIRST_RUN = 4
-Z_ON_GPSIMD = 0
-Z_ON_VECTOR = 256
-LATE_AT = 5
-ON_GPSIMD = ()
-ROW_DEPTH = 4
-HEAD_DEPTH = 4
-GATED_DEPTH = 2
+HALF = GROUP // 2
+EARLY_Q = 2
 
-STAGE_BYTES = 4 * PACK * GROUP
-ROUNDED_BYTES = 2 * PACK * GROUP
-WOVEN_BYTES = 2 * PACK * P
-AT_W3_DEALT = 0
-AT_TAB_WORDS = AT_W3_DEALT + 4 * H - ALIGN
-AT_W1_STAGE = (AT_TAB_WORDS + ALIGN + 2 * STAGE_BYTES, AT_TAB_WORDS + ALIGN + 3 * STAGE_BYTES)
-AT_HEADS = AT_W1_STAGE[0]
-AT_TAB_SCALES = AT_W1_STAGE[1] + STAGE_BYTES
-AT_V_WORDS = AT_TAB_SCALES + T + H - 4 * S
-AT_SCALES_IN = AT_TAB_SCALES + T
-AT_W2_IN = AT_V_WORDS + 4 * S
-AT_W3_IN = AT_W2_IN + 2 * H
-AT_REL = AT_W3_IN + ALIGN
-AT_W1_ROUNDED_FIRST = AT_W3_IN + 4 * H - ALIGN
-AT_DIFF_FIRST = AT_W1_ROUNDED_FIRST + ROUNDED_BYTES - 2 * ALIGN
-AT_W1_ROUNDED = (AT_W1_ROUNDED_FIRST, AT_DIFF_FIRST + 2 * ROUNDED_BYTES)
-AT_W4_STAGE = AT_W1_ROUNDED[1] + ROUNDED_BYTES - ALIGN
-AT_STAGES = (AT_W1_STAGE[1], AT_W1_STAGE[0], AT_W4_STAGE, AT_W1_STAGE[1])
-AT_H_FIRST = AT_TAB_WORDS + ALIGN
-AT_Z_WEIGHED = AT_H_FIRST + 2 * 4 * S
-AT_Q_LAST = AT_W4_STAGE + STAGE_BYTES
-AT_DIFF_THIRD = AT_Q_LAST + 4 * S
-AT_DIFF_LATE = (AT_DIFF_THIRD, AT_DIFF_THIRD + 3 * ROUNDED_BYTES // 2)
-AT_Z_WOVEN = AT_DIFF_THIRD + 3 * ROUNDED_BYTES
-AT_GATE_FIRST = AT_Z_WOVEN + 2 * PACK * PAIRS
-AT_Z_FIRST = AT_GATE_FIRST + 4 * GROUP
-AT_W1_CODES = (AT_Q_LAST, AT_GATE_FIRST)
-AT_ROUNDED = (0, 0, AT_Z_FIRST, AT_DIFF_LATE[0], AT_DIFF_LATE[1] - ROUNDED_BYTES // 2, AT_DIFF_LATE[1] + ROUNDED_BYTES // 2)
-AT_Z_PIECE = (AT_Z_FIRST + 4 * PACK * PAIRS, AT_ROUNDED[5], AT_Z_FIRST)
-AT_Y_FIRST = AT_Z_PIECE[0] + 4 * PACK * PIECES[0]
-AT_Y_MIDDLE = AT_Y_FIRST + GROUPS * 2 * PACK * PIECES[0]
-AT_GATED_LAST = AT_Z_PIECE[1]
-AT_Y_WOVEN = (AT_Y_FIRST, AT_Y_MIDDLE, AT_Y_FIRST)
-AT_Y_LAST = (AT_Z_PIECE[0], AT_Y_MIDDLE)
+ROW = 4 * S
+STAGE = 2 * ROW
+AT_TABLE = 0
+AT_W3_PLANE = AT_TABLE
+AT_W3_WORDS = AT_W3_PLANE + H
+AT_W1_LATE = AT_W3_WORDS + 4 * H
+AT_W4_SECOND = AT_W1_LATE + STAGE
+AT_W3_IN = AT_W4_SECOND + STAGE
+AT_REL = AT_W3_IN
+AT_W2_PLANE = AT_W3_IN + 4 * H
+AT_W1_EARLY = AT_W2_PLANE + H
+AT_TABLE_SCALES = AT_W2_PLANE - ALIGN
+AT_W4_STAGE = (AT_W4_SECOND, AT_W1_EARLY, AT_W4_SECOND, AT_W1_LATE)
+AT_W1_ROUNDED_LATE = AT_W1_EARLY + STAGE - ALIGN
+AT_Q = AT_W1_ROUNDED_LATE + ROW
+AT_W1_CODES = AT_Q + (PACK - 2) * ROW
+AT_R = AT_Q + PACK * ROW
+AT_DIFF = (AT_W1_EARLY, AT_R + PACK * ROW)
+AT_W1_ROUNDED = (AT_DIFF[1], AT_W1_ROUNDED_LATE)
+AT_HEADS = AT_DIFF[1] + 2 * ROW
+AT_H_LATE = AT_HEADS + 2 * ROW - ALIGN
+AT_WEIGHED = AT_H_LATE + ALIGN
+AT_H_EARLY = AT_WEIGHED + 2 * ROW
+AT_H = (AT_H_EARLY, AT_H_EARLY + ROW, AT_H_LATE, AT_H_LATE + ROW)
+AT_W4_ROUNDED = (AT_R + 2 * ROW, AT_H[1], AT_HEADS, AT_HEADS + ROW)
+AT_GATED = AT_H_EARLY + 2 * ROW
+AT_GATES = (AT_GATED + 2 * ROW, AT_GATED + ROW)
+AT_Z = (AT_GATES[0] + ROW, AT_W1_LATE)
+AT_Z_PIECE = (AT_Z[0], AT_W1_LATE, AT_W1_LATE + ROW // 2)
+AT_GATED_LATE = AT_W1_LATE + ROW
+AT_Z_WOVEN_LAST = AT_Z[0] + ROW
+AT_Y_CODES = AT_Z_WOVEN_LAST
 
 
 def tile_list_triple_pair_rerank_kernel(
@@ -91,136 +82,128 @@ def tile_list_triple_pair_rerank_kernel(
         shared = ctx.enter_context(tc.tile_pool(name="shared", bufs=1))
         psum = ctx.enter_context(tc.psum_pool(name="psum", bufs=1))
 
-        def ring_of(depth, columns, dtype, name):
-            return [keep.tile([P, columns], dtype, name="%s%d" % (name, k), align_bytes=ALIGN) for k in range(depth)]
+        def own(shape, dtype, name):
+            return keep.tile([P] + shape, dtype, name=name, align_bytes=ALIGN)
 
-        def take(ring):
-            ring.append(ring.pop(0))
-            return ring[-1]
+        def placed(shape, dtype, name, at):
+            return shared.tile([P] + shape, dtype, name=name, align_bytes=ALIGN, offset=at)
 
         banks = [psum.tile([P, BANK], F32, name="bank%d" % k) for k in range(BANKS)]
         bank_ring = list(banks)
-        r_ring = ring_of(ROW_DEPTH, S, F32, "r")
-        q_ring = ring_of(ROW_DEPTH, S, F32, "q")
-        gated_ring = ring_of(GATED_DEPTH, PAIRS, F32, "gated")
-        head_ring = ring_of(HEAD_DEPTH, PAIRS, F32, "q_head")
+
+        def next_bank():
+            bank_ring.append(bank_ring.pop(0))
+            return bank_ring[-1]
 
         offs_sb = keep.tile([P, S // LIST_ROWS], U16, name="offs_sb")
         pos1_sb = keep.tile([P, PAIRS // LIST_ROWS], U16, name="pos1_sb")
         pos2_sb = keep.tile([P, PAIRS // LIST_ROWS], U16, name="pos2_sb")
-        tab_w = shared.tile([P, T], U32, name="tab_w", align_bytes=ALIGN, offset=AT_TAB_WORDS)
-        tab_s = shared.tile([P, T], U8, name="tab_s", align_bytes=ALIGN, offset=AT_TAB_SCALES)
-        w2_in = shared.tile([P, 2 * H], U8, name="w2_in", align_bytes=ALIGN, offset=AT_W2_IN)
-        w3_in = shared.tile([P, 4 * H], U8, name="w3_in", align_bytes=ALIGN, offset=AT_W3_IN)
-        scales_in = shared.tile([P, H], U8, name="scales_in", align_bytes=ALIGN, offset=AT_SCALES_IN)
-        v_s = keep.tile([P, S], U8, name="v_s", align_bytes=ALIGN)
+        tab_w = placed([T], U32, "tab_w", AT_TABLE)
+        tab_s = placed([T], U8, "tab_s", AT_TABLE_SCALES)
+        w2_in = own([2 * H], U8, "w2_in")
+        w3_in = placed([4 * H], U8, "w3_in", AT_W3_IN)
+        w2_plane_in = own([H], U8, "w2_plane_in")
+        w3_plane_in = own([H], U8, "w3_plane_in")
+        v_s = own([S], U8, "v_s")
 
-        def fill_plane(queue, plane, first, rows):
+        def fill_plane(queue, plane, rows):
             for r in range(QUADS):
-                queue.dma_start(out=plane[first + r : P : 32, :].bitcast(I32), in_=rows(r).bitcast(I32))
+                queue.dma_start(out=plane[r:P:32, :].bitcast(I32), in_=rows(r).bitcast(I32))
 
-        for plane in (tab_s, scales_in, v_s):
+        for plane in (w2_plane_in, tab_s, w3_plane_in, v_s):
             nc.vector.memset(plane[:].bitcast(I32), 0)
-        nc.gpsimd.dma_start(out=tab_w[:].bitcast(I32), in_=tab_words[0].rearrange("p e t -> p (e t)").bitcast(I32))
-        nc.gpsimd.dma_start(out=w3_in[:].bitcast(I32), in_=w3_words[0].rearrange("p c t -> p (c t)").bitcast(I32))
         nc.sync.dma_start(offs_sb[:], offs)
-        nc.sync.dma_start(out=w2_in[:].bitcast(I32), in_=w2_words[0].bitcast(I32))
         nc.sync.dma_start(pos1_sb[:], pos1)
         nc.sync.dma_start(pos2_sb[:], pos2)
-        nc.scalar.dma_start(out=tab_s[0:P:RUN, :].bitcast(I32), in_=tab_scales[0].bitcast(I32))
-        fill_plane(nc.sync, scales_in, 0, lambda r: w2_scales[0, r:BLOCKS:QUADS, :])
-        fill_plane(nc.scalar, scales_in, W3_PLANE, lambda r: w3_scales[0, r:BLOCKS:QUADS, :])
+        nc.sync.dma_start(out=tab_w[:].bitcast(I32), in_=tab_words[0].rearrange("p e t -> p (e t)").bitcast(I32))
+        nc.sync.dma_start(out=w2_in[:].bitcast(I32), in_=w2_words[0].bitcast(I32))
+        nc.scalar.dma_start(out=tab_s[SCALE_FIRST : SCALE_FIRST + BLOCKS * SCALE_STEP : SCALE_STEP, :].bitcast(I32),
+                            in_=tab_scales[0].bitcast(I32))
+        fill_plane(nc.gpsimd, w2_plane_in, lambda r: w2_scales[0, r:BLOCKS:QUADS, :])
+        fill_plane(nc.gpsimd, w3_plane_in, lambda r: w3_scales[0, r:BLOCKS:QUADS, :])
 
-        def deal_columns(dst, src):
-            nc.vector.tensor_copy(
-                out=dst[:].bitcast(I32).rearrange("p (g t b w) -> p g t b w", g=GROUPS, t=PACK, b=BLOCKS),
-                in_=src[:].bitcast(I32).rearrange("p (g b t w) -> p g t b w", g=GROUPS, t=PACK, b=BLOCKS),
+        def deal_columns(copy, dst, src):
+            copy(
+                out=dst[:].bitcast(U32).rearrange("p (g t b w) -> p g t b w", g=GROUPS, t=PACK, b=BLOCKS),
+                in_=src[:].bitcast(U32).rearrange("p (g b t w) -> p g t b w", g=GROUPS, t=PACK, b=BLOCKS),
             )
 
-        w2_w = keep.tile([P, 2 * H], U8, name="w2_w", align_bytes=ALIGN)
-        deal_columns(w2_w, w2_in)
-
-        picked_s = keep.tile([P, S], U8, name="picked_s", align_bytes=ALIGN)
+        picked_s = own([S], U8, "picked_s")
         nc.vector.tensor_copy(picked_s[:], tab_s[:].indirect(offs_sb[:]))
-        fill_plane(nc.sync, v_s, 0, lambda r: picked_s[RUN * r : P : 32, :])
-        w_s = keep.tile([P, H], U8, name="w_s", align_bytes=ALIGN)
-        deal_columns(w_s, scales_in)
-        v_w = shared.tile([P, S], U32, name="v_w", align_bytes=ALIGN, offset=AT_V_WORDS)
-        for lo, hi in ((0, BANK), (BANK, S)):
-            entries = offs_sb[:, lo // LIST_ROWS : hi // LIST_ROWS]
-            nc.vector.tensor_copy(v_w[:, lo:hi], tab_w[:].indirect(entries))
-        w3_w = shared.tile([P, 4 * H], U8, name="w3_w", align_bytes=ALIGN, offset=AT_W3_DEALT)
-        deal_columns(w3_w, w3_in)
+        step = QUADS * SCALE_STEP
+        fill_plane(nc.sync, v_s, lambda r: picked_s[SCALE_FIRST + SCALE_STEP * r : SCALE_FIRST + BLOCKS * SCALE_STEP : step, :])
+        nc.sync.dma_start(out=w3_in[:].bitcast(I32), in_=w3_words[0].rearrange("p c t -> p (c t)").bitcast(I32))
+        w2_s = placed([H], U8, "w2_s", AT_W2_PLANE)
+        deal_columns(nc.vector.tensor_copy, w2_s, w2_plane_in)
+
+        w2_w = own([2 * H], U8, "w2_w")
+        deal_columns(nc.scalar.copy, w2_w, w2_in)
+
+        w1_rows = w1.rearrange("(p j) c -> p j c", j=PACK)
+        w1_early = placed([2, PACK, HALF], F32, "w1_early", AT_W1_EARLY)
+        for half in range(2):
+            nc.sync.dma_start(out=w1_early[:, half], in_=w1_rows[:, :, HALF * half : HALF * (half + 1)])
+
+        v_w = own([S], U32, "v_w")
+        for lo in range(0, S, BANK):
+            entries = offs_sb[:, lo // LIST_ROWS : (lo + BANK) // LIST_ROWS]
+            nc.vector.tensor_copy(v_w[:, lo : lo + BANK], tab_w[:].indirect(entries))
+        w3_w = placed([4 * H], U8, "w3_w", AT_W3_WORDS)
+        deal_columns(nc.vector.tensor_copy, w3_w, w3_in)
+        w3_s = placed([H], U8, "w3_s", AT_W3_PLANE)
+        deal_columns(nc.vector.tensor_copy, w3_s, w3_plane_in)
+
+        w1_late = placed([PACK, GROUP], F32, "w1_late", AT_W1_LATE)
+        nc.sync.dma_start(out=w1_late[:], in_=w1_rows[:, :, GROUP:])
+
+        w4_blocks = [(c_group, g) for g in range(GROUPS) for c_group in range(GROUPS)]
+        w4_stage, w4_q, w1_q = {}, {}, {}
+
+        def load_w4(number):
+            c_group, g = w4_blocks[number]
+            w4_stage[number] = placed([PACK, GROUP], F32, "w4_stage%d" % number, AT_W4_STAGE[number])
+            rows = w4[GROUP * c_group : GROUP * (c_group + 1), GROUP * g : GROUP * (g + 1)]
+            by_place = rows.rearrange("(b j e) n -> j b e n", j=PACK, e=RUN)
+            for j in range(PACK):
+                nc.sync.dma_start(out=w4_stage[number][:, j, :], in_=by_place[j])
+
+        load_w4(0)
+        rel_sb = placed([GROUPS, PACK, RUN], F32, "rel_sb", AT_REL)
+        by_tile = rel.rearrange("(g b t e) -> g t b e", g=GROUPS, t=PACK, e=RUN)
+        for a in range(TILES):
+            g, t = divmod(a, PACK)
+            nc.sync.dma_start(out=rel_sb[:, g, t, 0:1], in_=by_tile[g, t])
 
         def quantised(width, name, woven, at=None):
-            if at is None:
-                codes = keep.tile([P, width], U32, name=name + "_codes", align_bytes=ALIGN)
-            else:
-                codes = shared.tile([P, width], U32, name=name + "_codes", align_bytes=ALIGN, offset=at)
-            scales = keep.tile([P, width], U8, name=name + "_scales", align_bytes=ALIGN)
+            codes = own([width], U32, name + "_codes") if at is None else placed([width], U32, name + "_codes", at)
+            scales = own([width], U8, name + "_scales")
             nc.vector.quantize_mx(out=codes[:].bitcast(FP8X4), scales=scales[:], in_=woven)
             return codes, scales
 
-        weight_blocks = [("w1", w1, 0, g) for g in range(GROUPS)]
-        weight_blocks = weight_blocks + [("w4", w4, c_group, g) for g in range(GROUPS) for c_group in range(GROUPS)]
-        weight_q, w1_rounded, w4_rounded = {}, {}, {}
-        w1_stage = [
-            shared.tile([P, PACK, GROUP], F32, name="w1_stage%d" % g, align_bytes=ALIGN, offset=AT_W1_STAGE[g])
-            for g in range(GROUPS)
-        ]
-        first_heads = shared.tile([P, PACK, PAIRS], F32, name="first_heads", align_bytes=ALIGN, offset=AT_HEADS)
-
-        def quantise_w1():
-            for g in range(GROUPS):
-                rows = w1[:, GROUP * g : GROUP * (g + 1)]
-                nc.gpsimd.dma_start(out=w1_stage[g][:], in_=rows.rearrange("(p j) c -> p j c", j=PACK))
-            for g in range(GROUPS):
-                at = AT_W1_ROUNDED[g]
-                w1_rounded[g] = shared.tile([P, PACK * GROUP], BF16, name="w1_rounded%d" % g, align_bytes=ALIGN, offset=at)
-            nc.vector.tensor_copy(
-                out=w1_rounded[0][:].rearrange("p (t b e j) -> p b t j e", t=PACK, e=RUN, j=PACK),
-                in_=w1_stage[0][:].rearrange("p j (b t e) -> p b t j e", t=PACK, e=RUN),
-            )
-            into = w1_rounded[1][:].rearrange("p (t b e j) -> p t b e j", t=PACK, e=RUN, j=PACK)
-            by_place = w1_stage[1][:].rearrange("p j (b t e) -> p t b e j", t=PACK, e=RUN)
-            for t in range(PACK):
-                nc.gpsimd.tensor_scalar(into[:, t], by_place[:, t], 1.0, 0.0, MULT, ADD)
-
-        def quantise_w1_block(g):
-            weight_q["w1", g] = quantised(GROUP, "w1_%d" % g, w1_rounded[g][:], AT_W1_CODES[g])
-
-        def round_weight_block(number):
-            name, w, row_group, col_group = weight_blocks[number]
-            at = AT_STAGES[number - GROUPS]
-            stage = shared.tile([P, PACK, GROUP], F32, name="stage%d" % number, align_bytes=ALIGN, offset=at)
-            rows = w[GROUP * row_group : GROUP * (row_group + 1), GROUP * col_group : GROUP * (col_group + 1)]
-            at = AT_ROUNDED[number]
-            rounded = shared.tile([P, PACK * GROUP], BF16, name="rounded%d" % number, align_bytes=ALIGN, offset=at)
-            by_place = rows.rearrange("(b j e) n -> j b e n", j=PACK, e=RUN)
-            for j in range(PACK):
-                nc.sync.dma_start(out=stage[:, j, :], in_=by_place[j])
-            if number in ON_GPSIMD:
-                into = rounded[:].rearrange("p (t m j) -> p t m j", t=PACK, j=PACK)
-                by_column = stage[:].rearrange("p j (m t) -> p t m j", t=PACK)
+        def round_w1(halves):
+            rounded = placed([PACK * GROUP], BF16, "w1_rounded0", AT_W1_ROUNDED[0])
+            into = rounded[:].rearrange("p (t half b e j) -> p half t b e j", t=PACK, half=2, e=RUN, j=PACK)
+            for half in range(2):
+                by_place = halves[:, half].rearrange("p j (b t e) -> p t b e j", t=PACK, e=RUN)
                 for t in range(PACK):
-                    nc.gpsimd.tensor_scalar(into[:, t], by_column[:, t], 1.0, 0.0, MULT, ADD)
-            else:
-                nc.scalar.copy(
-                    out=rounded[:].rearrange("p (t m j) -> p m j t", t=PACK, j=PACK),
-                    in_=stage[:].rearrange("p j (m t) -> p m j t", t=PACK),
-                )
-            w4_rounded[number] = rounded
+                    nc.gpsimd.tensor_scalar(into[:, half, t], by_place[:, t], 1.0, 0.0, MULT, ADD)
+            return rounded
 
-        def quantise_weight_block(number, at=None):
-            name, w, row_group, col_group = weight_blocks[number]
-            weight_q[name, row_group, col_group] = quantised(
-                GROUP, "%s_%d%d" % (name, row_group, col_group), w4_rounded[number][:], at
+        def round_w4(number, copy):
+            rounded = placed([PACK * GROUP], BF16, "w4_rounded%d" % number, AT_W4_ROUNDED[number])
+            copy(
+                out=rounded[:].rearrange("p (t m j) -> p m j t", t=PACK, j=PACK),
+                in_=w4_stage[number][:].rearrange("p j (m t) -> p m j t", t=PACK),
             )
+            return rounded
+
+        def quantise_w4(number, rounded):
+            w4_q[w4_blocks[number]] = quantised(GROUP, "w4_%d" % number, rounded[:])
 
         def first_stage(jobs):
             for lo in range(0, S, BANK):
                 for rows, codes, scales in jobs:
-                    acc = take(bank_ring)
+                    acc = next_bank()
                     nc.tensor.matmul_mx(
                         out=acc[:], lhsT=codes, lhsT_scale=scales,
                         rhs=v_w[:, lo : lo + BANK].bitcast(FP8X4), rhs_scale=v_s[:, lo : lo + BANK],
@@ -228,67 +211,53 @@ def tile_list_triple_pair_rerank_kernel(
                     )
                     nc.scalar.copy(out=rows[:, lo : lo + BANK], in_=acc[:])
 
-        q_rows, r_rows, q_head, diff, gate, h = {}, {}, {}, {}, {}, {}
+        q, r, h, gate = {}, {}, {}, {}
 
         def make_q(tiles):
             jobs = []
             for a in tiles:
-                if a == FIRST_RUN - 1:
-                    q_rows[a] = shared.tile([P, S], F32, name="q_last", align_bytes=ALIGN, offset=AT_Q_LAST)
-                else:
-                    q_rows[a] = take(q_ring)
+                q[a] = placed([S], F32, "q%d" % a, AT_Q + ROW * (a % PACK))
                 codes = w2_w[:, 2 * P * a : 2 * P * (a + 1)].bitcast(FP4X4)
-                jobs.append((q_rows[a], codes, w_s[:, P * a : P * (a + 1)]))
+                jobs.append((q[a], codes, w2_s[:, P * a : P * (a + 1)]))
             first_stage(jobs)
 
         def make_r(a):
-            r_rows[a] = take(r_ring)
+            r[a] = placed([S], F32, "r%d" % a, AT_R + ROW * (a % PACK))
             codes = w3_w[:, 4 * P * a : 4 * P * (a + 1)].bitcast(FP8X4)
-            first_stage([(r_rows[a], codes, w_s[W3_PLANE:, P * a : P * (a + 1)])])
+            first_stage([(r[a], codes, w3_s[:, P * a : P * (a + 1)])])
 
         def make_h(a):
             g, t = divmod(a, PACK)
-            codes, scales = weight_q["w1", g]
-            if g == 0:
-                h[a] = shared.tile([P, S], F32, name="h%d" % a, align_bytes=ALIGN, offset=AT_H_FIRST + 4 * S * t)
-            else:
-                h[a] = keep.tile([P, S], F32, name="h%d" % a)
+            codes, scales = w1_q[g]
+            h[a] = placed([S], F32, "h%d" % a, AT_H[t]) if g == 0 else own([S], F32, "h%d" % a)
             first_stage([(h[a], codes[:, P * t : P * (t + 1)].bitcast(FP8X4), scales[:, P * t : P * (t + 1)])])
 
-        def pick_q(a):
-            q_head[a] = first_heads[:, a, :] if a < PACK else take(head_ring)[:]
-            nc.vector.tensor_copy(q_head[a], q_rows[a][:].indirect(pos1_sb[:]))
+        def pick_heads(g):
+            heads = placed([PACK, PAIRS], F32, "heads%d" % g, AT_HEADS)
+            for t in range(PACK):
+                nc.vector.tensor_copy(heads[:, t, :], q[PACK * g + t][:].indirect(pos1_sb[:]))
+            return heads
 
-        def pick_r_less_q(a):
-            if a == 0:
-                first = shared.tile([P, PACK * PAIRS], F32, name="diff_first", align_bytes=ALIGN, offset=AT_DIFF_FIRST)
-                diff[0], diff[1] = first[:, : 2 * PAIRS], first[:, 2 * PAIRS :]
-            elif a in (4, 6):
-                at = AT_DIFF_LATE[a // 2 - 2]
-                diff[a // 2] = shared.tile([P, 2 * PAIRS], F32, name="diff%d" % (a // 2), align_bytes=ALIGN, offset=at)[:]
-            into = diff[a // 2][:, PAIRS * (a % 2) : PAIRS * (a % 2 + 1)]
-            nc.vector.tensor_tensor(into, r_rows[a][:].indirect(pos2_sb[:]), q_head[a], SUBTRACT)
+        def differences(g, heads):
+            diff = placed([PACK, PAIRS], F32, "diff%d" % g, AT_DIFF[g])
+            for t in range(PACK):
+                nc.vector.tensor_tensor(diff[:, t, :], r[PACK * g + t][:].indirect(pos2_sb[:]), heads[:, t, :], SUBTRACT)
+            return diff
 
-        def gates_of_pair(pair):
-            if pair == 0:
-                both = shared.tile([P, 2 * PAIRS], F32, name="gate0", align_bytes=ALIGN, offset=AT_GATE_FIRST)
-            else:
-                both = keep.tile([P, 2 * PAIRS], F32, name="gate%d" % pair)
-            nc.scalar.activation(out=both[:], in_=diff[pair], func=SIGMOID, scale=-1.0)
-            gate[2 * pair], gate[2 * pair + 1] = both[:, :PAIRS], both[:, PAIRS:]
+        def gates_of_pair(g, pair, diff):
+            both = placed([2, PAIRS], F32, "gate%d_%d" % (g, pair), AT_GATES[pair])
+            nc.scalar.activation(out=both[:], in_=diff[:, 2 * pair : 2 * pair + 2, :], func=SIGMOID, scale=-1.0)
+            for k in range(2):
+                gate[PACK * g + 2 * pair + k] = both[:, k, :]
 
-        def products(g, z, lo, hi, places):
+        def products(g, pair, lo, hi, gated, z):
             entries = slice(lo // LIST_ROWS, hi // LIST_ROWS)
-            gated = {}
+            places = (2 * pair, 2 * pair + 1)
             for t in places:
                 a = PACK * g + t
-                if lo == 3 * P and t == 2:
-                    gated[t] = shared.tile([P, P], F32, name="gated_last", align_bytes=ALIGN, offset=AT_GATED_LAST)[:]
-                else:
-                    gated[t] = take(gated_ring)[:, : hi - lo]
-                nc.vector.tensor_tensor(gated[t], h[a][:].indirect(pos1_sb[:, entries]), gate[a][:, lo:hi], MULT)
+                nc.vector.tensor_tensor(gated(t), h[a][:].indirect(pos1_sb[:, entries]), gate[a][:, lo:hi], MULT)
             for t in places:
-                nc.vector.tensor_tensor(z[:, t, :], h[PACK * g + t][:].indirect(pos2_sb[:, entries]), gated[t], MULT)
+                nc.vector.tensor_tensor(z(t), h[PACK * g + t][:].indirect(pos2_sb[:, entries]), gated(t), MULT)
 
         def weaving(woven, rows):
             return (
@@ -296,45 +265,21 @@ def tile_list_triple_pair_rerank_kernel(
                 rows.rearrange("p t (run i) -> p run t i", i=LINE),
             )
 
+        def weigh_and_weave(g, z, woven):
+            into, by_runs = weaving(woven[:], z)
+            runs = z.shape[2] // LINE
+            nc.vector.tensor_tensor(into, by_runs, rel_sb[:, g, :, 0:1].unsqueeze(1).broadcast_to([P, runs, PACK, LINE]), MULT)
+
         z_q = {}
 
-        def quantise_z(g, z, lo, hi, woven):
-            into, by_runs = weaving(woven[:], z)
-            spread = rel_sb[:, g, :, 0:1].unsqueeze(1).broadcast_to([P, (hi - lo) // LINE, PACK, LINE])
-            nc.vector.tensor_tensor(into, by_runs, spread, MULT)
+        def quantise_z(g, lo, hi, woven):
             codes, scales = quantised(hi - lo, "z%d_%d" % (g, lo), woven[:])
             for col in range(lo, hi, P):
                 z_q[g, col] = (codes[:, col - lo : col - lo + P].bitcast(FP8X4), scales[:, col - lo : col - lo + P])
 
-        def weigh_first_z(z):
-            weighed = shared.tile([P, PACK, PAIRS], F32, name="z_weighed", align_bytes=ALIGN, offset=AT_Z_WEIGHED)
-            for t in range(PACK):
-                nc.gpsimd.tensor_scalar(weighed[:, t, :], z[:, t, :], rel_sb[:, 0, t, 0:1], 0.0, MULT, ADD)
-            woven = woven_at(AT_Z_WOVEN, PAIRS, "z_woven_first")
-            for lo in range(0, Z_ON_GPSIMD, P):
-                into = woven[:, PACK * lo : PACK * (lo + P)].rearrange("p (i t) -> p i t", t=PACK)
-                nc.gpsimd.tensor_scalar(into, weighed[:, :, lo : lo + P].rearrange("p t i -> p i t"), 1.0, 0.0, MULT, ADD)
-            return weighed, woven
-
-        def weave_early(weighed, woven):
-            nc.vector.tensor_copy(*weaving(woven[:, : PACK * Z_ON_VECTOR], weighed[:, :, :Z_ON_VECTOR]))
-            keep_z(0, 0, 2 * P, woven[:, : PACK * 2 * P])
-
-        def weave_late(weighed, woven):
-            nc.scalar.copy(*weaving(woven[:, PACK * Z_ON_VECTOR :], weighed[:, :, Z_ON_VECTOR:]))
-            keep_z(0, 2 * P, 3 * P, woven[:, PACK * 2 * P : PACK * 3 * P])
-
-        def keep_z(g, lo, hi, woven, at=None):
-            codes, scales = quantised(hi - lo, "z%d_%d" % (g, lo), woven, at)
-            for col in range(lo, hi, P):
-                z_q[g, col] = (codes[:, col - lo : col - lo + P].bitcast(FP8X4), scales[:, col - lo : col - lo + P])
-
-        def woven_at(at, width, name):
-            return shared.tile([P, PACK * width], BF16, name=name, align_bytes=ALIGN, offset=at)
-
         def second_passes(c_group, g, col):
             acc = banks[GROUPS * (col // P) + g][:].rearrange("p (t i) -> p t i", t=PACK)
-            codes, scales = weight_q["w4", c_group, g]
+            codes, scales = w4_q[c_group, g]
             for t in range(PACK):
                 nc.tensor.matmul_mx(
                     out=acc[:, t, :],
@@ -344,135 +289,118 @@ def tile_list_triple_pair_rerank_kernel(
                 )
             return acc
 
-        def open_sums(lo, hi):
-            for g in range(GROUPS):
-                for col in range(lo, hi, P):
-                    second_passes(0, g, col)
-
-        y_scales = keep.tile([P, GROUPS * PAIRS], U8, name="y_scales", align_bytes=ALIGN)
-        y_codes = keep.tile([P, GROUPS * PAIRS], U32, name="y_codes", align_bytes=ALIGN)
-
-        def store_and_quantise(g, lo, hi, y, woven):
-            rows = out_0[GROUP * g : GROUP * (g + 1), lo:hi].rearrange("(p t) i -> p t i", t=PACK)
-            nc.sync.dma_start(out=rows, in_=y)
-            nc.vector.quantize_mx(
-                out=y_codes[:, PAIRS * g + lo : PAIRS * g + hi].bitcast(FP8X4),
-                scales=y_scales[:, PAIRS * g + lo : PAIRS * g + hi],
-                in_=woven[:],
-            )
-
-        def woven_results(piece, g):
-            lo, hi = spans[piece]
-            at = AT_Y_WOVEN[piece] + 2 * PACK * (hi - lo) * g
-            return woven_at(at, hi - lo, "y_woven%d_%d" % (piece, g))
-
-        def finish(piece):
-            lo, hi = spans[piece]
-            for g in range(GROUPS):
-                y = take(r_ring)[:, : PACK * (hi - lo)].rearrange("p (t i) -> p t i", t=PACK)
-                woven = woven_results(piece, g)
-                for col in range(lo, hi, P):
-                    acc = second_passes(1, g, col)
-                    at = col - lo
-                    nc.scalar.copy(out=y[:, :, at : at + P], in_=acc)
-                    nc.scalar.copy(*weaving(woven[:, PACK * at : PACK * (at + P)], acc))
-                store_and_quantise(g, lo, hi, y, woven)
-
-        def finish_last(piece):
-            lo, hi = spans[piece]
-            acc = [second_passes(1, g, lo) for g in range(GROUPS)]
-            y = [
-                shared.tile([P, PACK, hi - lo], F32, name="y_last%d" % g, align_bytes=ALIGN, offset=AT_Y_LAST[g])
-                for g in range(GROUPS)
-            ]
-            woven = [woven_results(piece, g) for g in range(GROUPS)]
-            nc.scalar.copy(out=y[0][:], in_=acc[0])
-            nc.vector.tensor_copy(out=y[1][:], in_=acc[1])
-            nc.scalar.copy(*weaving(woven[0][:], acc[0]))
-            nc.vector.tensor_copy(*weaving(woven[1][:], y[1][:]))
-            for g in range(GROUPS):
-                store_and_quantise(g, lo, hi, y[g][:], woven[g])
-
-        def store_codes(lo, hi):
-            words = out_1.rearrange("g p i t -> p g (i t)").bitcast(I32)
-            codes = y_codes[:].bitcast(I32).rearrange("p (g i) -> p g i", g=GROUPS)
-            nc.sync.dma_start(out=words[:, :, lo:hi], in_=codes[:, :, lo:hi])
-
-        rel_sb = shared.tile([P, GROUPS, PACK, RUN], F32, name="rel_sb", align_bytes=ALIGN, offset=AT_REL)
-
-        def pair_of_tiles(pair):
+        rounded = round_w1(w1_early)
+        make_q(range(EARLY_Q))
+        for a in range(EARLY_Q, PACK):
+            make_q((a,))
+        heads = pick_heads(0)
+        w1_q[0] = quantised(GROUP, "w1_0", rounded[:], AT_W1_CODES)
+        for a in range(PACK):
+            make_r(a)
+        diff = differences(0, heads)
+        rounded = round_w4(0, nc.vector.tensor_copy)
+        load_w4(2)
+        gated_first = [placed([PAIRS], F32, "gated_first%d" % k, AT_GATED + 4 * PAIRS * k) for k in range(2)]
+        z_first = []
+        for pair in range(2):
             make_h(2 * pair)
             make_h(2 * pair + 1)
-            gates_of_pair(pair)
+            gates_of_pair(0, pair, diff)
+            if pair == 1:
+                rounded = placed([PACK * GROUP], BF16, "w1_rounded1", AT_W1_ROUNDED[1])
+                nc.scalar.copy(
+                    out=rounded[:].rearrange("p (t b e j) -> p b t j e", t=PACK, e=RUN, j=PACK),
+                    in_=w1_late[:].rearrange("p j (b t e) -> p b t j e", t=PACK, e=RUN),
+                )
+                w1_q[1] = quantised(GROUP, "w1_1", rounded[:])
+                load_w4(1)
+            z_first.append(placed([2, PAIRS], F32, "z_first%d" % pair, AT_Z[pair]))
+            products(0, pair, 0, PAIRS, lambda t: gated_first[t % 2][:], lambda t: z_first[pair][:, t % 2, :])
+            if pair == 0:
+                quantise_w4(0, rounded)
+        weighed = placed([PACK, PAIRS], F32, "weighed", AT_WEIGHED)
+        for t in range(PACK):
+            nc.gpsimd.tensor_scalar(weighed[:, t, :], z_first[t // 2][:, t % 2, :], rel_sb[:, 0, t, 0:1], 0.0, MULT, ADD)
+        load_w4(3)
 
-        def run_of_q(tiles):
-            for a in tiles:
-                if a >= FIRST_Q_TILES:
-                    make_q((a,))
-                pick_q(a)
-
-        def differences(tiles):
-            for a in tiles:
-                make_r(a)
-                pick_r_less_q(a)
-
-        quantise_w1()
-        make_q(range(FIRST_Q_TILES))
-        run_of_q(range(FIRST_RUN))
-        quantise_w1_block(0)
-        by_tile = rel.rearrange("(g b t e) -> g t b e", g=GROUPS, t=PACK, e=RUN)
-        for c_tile in range(TILES):
-            g, t = divmod(c_tile, PACK)
-            nc.sync.dma_start(out=rel_sb[:, g, t, 0:1], in_=by_tile[g, t])
-        differences(range(PACK))
-        make_h(0)
-        gates_of_pair(0)
-        make_h(1)
-        z_tile = shared.tile([P, PACK * PAIRS], F32, name="z_first", align_bytes=ALIGN, offset=AT_Z_FIRST)
-        z_first = z_tile[:].rearrange("p (t i) -> p t i", t=PACK)
-        products(0, z_first, 0, PAIRS, (0, 1))
-        quantise_w1_block(1)
-        pair_of_tiles(1)
-        products(0, z_first, 0, PAIRS, (2, 3))
-        run_of_q(range(FIRST_RUN, TILES))
-        first_z = weigh_first_z(z_first)
-        differences(range(PACK, TILES))
         for a in range(PACK, TILES):
-            make_h(a)
-        round_weight_block(2)
-        weave_early(*first_z)
-        quantise_weight_block(2)
-        gates_of_pair(2)
-        gates_of_pair(3)
-        for number in range(3, len(weight_blocks)):
-            round_weight_block(number)
-            quantise_weight_block(number)
-            if number == LATE_AT:
-                weave_late(*first_z)
+            make_q((a,))
+        heads = pick_heads(1)
+        for a in range(PACK, TILES):
+            make_r(a)
+        diff = differences(1, heads)
+
+        def weave_first_z(half, copy):
+            woven = own([PACK * HALF], BF16, "z_woven_half%d" % half)
+            copy(*weaving(woven[:], weighed[:, :, HALF * half : HALF * (half + 1)]))
+            return woven
+
+        woven = weave_first_z(0, nc.vector.tensor_copy)
+        for pair in range(2):
+            make_h(PACK + 2 * pair)
+            make_h(PACK + 2 * pair + 1)
+            gates_of_pair(1, pair, diff)
+        quantise_z(0, 0, HALF, woven)
+        for number in range(1, len(w4_blocks)):
+            quantise_w4(number, round_w4(number, nc.scalar.copy))
+        quantise_z(0, HALF, PAIRS, weave_first_z(1, nc.scalar.copy))
 
         edges = [sum(PIECES[:k]) for k in range(len(PIECES) + 1)]
         spans = list(zip(edges[:-1], edges[1:]))
+        last = len(PIECES) - 1
+        y_scales = own([GROUPS * PAIRS], U8, "y_scales")
+        y_woven = {}
+
+        def second_group_z(piece):
+            lo, hi = spans[piece]
+            at = AT_GATED if piece == 0 else AT_GATED_LATE + 4 * PACK * (lo - edges[1])
+            gated = placed([PACK, hi - lo], F32, "gated_piece%d" % piece, at)
+            z = placed([PACK, hi - lo], F32, "z_piece%d" % piece, AT_Z_PIECE[piece])
+            for pair in range(2):
+                products(1, pair, lo, hi, lambda t: gated[:, t, :], lambda t: z[:, t, :])
+            name = "z_woven%d" % piece
+            woven = placed([PACK * (hi - lo)], BF16, name, AT_Z_WOVEN_LAST) if piece == last else own([PACK * (hi - lo)], BF16, name)
+            weigh_and_weave(1, z[:], woven)
+            quantise_z(1, lo, hi, woven)
+
+        def results(piece):
+            lo, hi = spans[piece]
+            for g in range(GROUPS):
+                place = GROUPS * lo + g * (hi - lo)
+                y = placed([PACK, hi - lo], F32, "y%d_%d" % (piece, g), AT_R + 4 * PACK * place)
+                y_woven[piece, g] = placed([PACK * (hi - lo)], BF16, "y_woven%d_%d" % (piece, g), AT_HEADS + 2 * PACK * place)
+                for col in range(lo, hi, P):
+                    second_passes(0, g, col)
+                    acc = second_passes(1, g, col)
+                    at = col - lo
+                    into = y_woven[piece, g][:, PACK * at : PACK * (at + P)]
+                    if piece == last and g == GROUPS - 1:
+                        nc.vector.tensor_copy(out=y[:], in_=acc)
+                        nc.vector.tensor_copy(*weaving(into, y[:]))
+                    else:
+                        nc.scalar.copy(out=y[:, :, at : at + P], in_=acc)
+                        nc.scalar.copy(*weaving(into, acc))
+                rows = out_0[GROUP * g : GROUP * (g + 1), lo:hi].rearrange("(p t) i -> p t i", t=PACK)
+                nc.sync.dma_start(out=rows, in_=y[:])
+
+        for piece in range(len(PIECES)):
+            second_group_z(piece)
+            results(piece)
+
+        y_codes = placed([GROUPS * PAIRS], U32, "y_codes", AT_Y_CODES)
+        words = out_1.rearrange("g p i t -> p g (i t)").bitcast(I32)
+        codes = y_codes[:].bitcast(I32).rearrange("p (g i) -> p g i", g=GROUPS)
         for piece, (lo, hi) in enumerate(spans):
-            z_tile = shared.tile(
-                [P, PACK * (hi - lo)], F32, name="z_piece%d" % piece, align_bytes=ALIGN, offset=AT_Z_PIECE[piece]
-            )
-            z_piece = z_tile[:].rearrange("p (t i) -> p t i", t=PACK)
-            for places in ((0, 1), (2, 3)):
-                products(1, z_piece, lo, hi, places)
-            if piece == 2:
-                keep_z(0, lo, hi, first_z[1][:, PACK * lo :], AT_GATED_LAST)
-                open_sums(lo, hi)
-            woven = keep.tile([P, PACK * (hi - lo)], BF16, name="z_woven%d" % piece, align_bytes=ALIGN)
-            quantise_z(1, z_piece, lo, hi, woven)
-            if piece == 1:
-                open_sums(*spans[0])
-                finish(0)
-                open_sums(lo, hi)
-        finish(1)
-        store_codes(0, edges[2])
-        finish_last(2)
-        store_codes(edges[2], PAIRS)
+            for g in range(GROUPS):
+                nc.vector.quantize_mx(
+                    out=y_codes[:, PAIRS * g + lo : PAIRS * g + hi].bitcast(FP8X4),
+                    scales=y_scales[:, PAIRS * g + lo : PAIRS * g + hi],
+                    in_=y_woven[piece, g][:],
+                )
+            if piece in (0, last):
+                begin = 0 if piece == 0 else edges[1]
+                nc.sync.dma_start(out=words[:, :, begin:hi], in_=codes[:, :, begin:hi])
         plane = y_scales[:].rearrange("p (g i) -> p g i", g=GROUPS)
-        for r in range(QUADS):
-            rows = out_2[:, r:BLOCKS:QUADS, :].rearrange("g row i -> row g i")
-            nc.scalar.dma_start(out=rows.bitcast(I32), in_=plane[r:P:32].bitcast(I32))
+        for k in range(QUADS):
+            rows = out_2[:, k:BLOCKS:QUADS, :].rearrange("g row i -> row g i")
+            nc.scalar.dma_start(out=rows.bitcast(I32), in_=plane[k:P:32].bitcast(I32))

@@ -27,11 +27,11 @@ TILES = H // P
 BANK = 512
 BANKS = 8
 LIST_ROWS = 16
+W3_PLANE = 4
 RUN = 8
 BLOCKS = P // RUN
 QUADS = 4
 LINE = 4
-SCALE_FIRST, SCALE_STEP = 32, 4
 ALIGN = 64
 
 PIECES = (256, 128, 128)
@@ -41,34 +41,32 @@ EARLY_Q = 2
 ROW = 4 * S
 STAGE = 2 * ROW
 AT_TABLE = 0
-AT_W3_PLANE = AT_TABLE
-AT_W3_WORDS = AT_W3_PLANE + H
-AT_W1_LATE = AT_W3_WORDS + 4 * H
-AT_W4_SECOND = AT_W1_LATE + STAGE
-AT_W3_IN = AT_W4_SECOND + STAGE
+AT_W3_WORDS = AT_TABLE
+AT_TABLE_SCALES = AT_TABLE + 4 * T
+AT_PLANES = AT_TABLE_SCALES
+AT_W3_IN = AT_TABLE_SCALES + T
 AT_REL = AT_W3_IN
-AT_W2_PLANE = AT_W3_IN + 4 * H
-AT_W1_EARLY = AT_W2_PLANE + H
-AT_TABLE_SCALES = AT_W2_PLANE - ALIGN
-AT_W4_STAGE = (AT_W4_SECOND, AT_W1_EARLY, AT_W4_SECOND, AT_W1_LATE)
-AT_W1_ROUNDED_LATE = AT_W1_EARLY + STAGE - ALIGN
-AT_Q = AT_W1_ROUNDED_LATE + ROW
-AT_W1_CODES = AT_Q + (PACK - 2) * ROW
+AT_W4_FIRST = AT_W3_IN + 4 * H - ALIGN
+AT_W1_LATE = AT_W4_FIRST + STAGE
+AT_W1_EARLY = AT_W1_LATE + STAGE
+AT_W4_STAGE = (AT_W4_FIRST, AT_W1_LATE, AT_W1_EARLY, AT_W4_FIRST)
+AT_Q = AT_W1_EARLY + STAGE
 AT_R = AT_Q + PACK * ROW
 AT_DIFF = (AT_W1_EARLY, AT_R + PACK * ROW)
-AT_W1_ROUNDED = (AT_DIFF[1], AT_W1_ROUNDED_LATE)
+AT_W1_ROUNDED = (AT_DIFF[1], AT_R + 2 * ROW)
 AT_HEADS = AT_DIFF[1] + 2 * ROW
 AT_H_LATE = AT_HEADS + 2 * ROW - ALIGN
 AT_WEIGHED = AT_H_LATE + ALIGN
 AT_H_EARLY = AT_WEIGHED + 2 * ROW
 AT_H = (AT_H_EARLY, AT_H_EARLY + ROW, AT_H_LATE, AT_H_LATE + ROW)
-AT_W4_ROUNDED = (AT_R + 2 * ROW, AT_H[1], AT_HEADS, AT_HEADS + ROW)
+AT_W4_ROUNDED = (AT_H[0], AT_H[1], AT_HEADS, AT_HEADS + ROW)
 AT_GATED = AT_H_EARLY + 2 * ROW
 AT_GATES = (AT_GATED + 2 * ROW, AT_GATED + ROW)
-AT_Z = (AT_GATES[0] + ROW, AT_W1_LATE)
-AT_Z_PIECE = (AT_Z[0], AT_W1_LATE, AT_W1_LATE + ROW // 2)
-AT_GATED_LATE = AT_W1_LATE + ROW
-AT_Z_WOVEN_LAST = AT_Z[0] + ROW
+AT_Z = AT_GATES[0] + ROW
+AT_W1_CODES = (AT_Q + 2 * ROW, AT_Z + 2 * ROW)
+AT_Z_PIECE = (AT_Z, AT_W4_FIRST, AT_W4_FIRST + ROW // 2)
+AT_GATED_LATE = AT_W4_FIRST + ROW
+AT_Z_WOVEN_LAST = AT_W1_CODES[1] + ROW // 2
 AT_Y_CODES = AT_Z_WOVEN_LAST
 
 
@@ -102,25 +100,30 @@ def tile_list_triple_pair_rerank_kernel(
         tab_s = placed([T], U8, "tab_s", AT_TABLE_SCALES)
         w2_in = own([2 * H], U8, "w2_in")
         w3_in = placed([4 * H], U8, "w3_in", AT_W3_IN)
-        w2_plane_in = own([H], U8, "w2_plane_in")
-        w3_plane_in = own([H], U8, "w3_plane_in")
+        planes_in = own([H], U8, "planes_in")
         v_s = own([S], U8, "v_s")
 
-        def fill_plane(queue, plane, rows):
+        def fill_plane(queue, plane, first, rows):
             for r in range(QUADS):
-                queue.dma_start(out=plane[r:P:32, :].bitcast(I32), in_=rows(r).bitcast(I32))
+                queue.dma_start(out=plane[first + r : P : 32, :].bitcast(I32), in_=rows(r).bitcast(I32))
 
-        for plane in (w2_plane_in, tab_s, w3_plane_in, v_s):
+        for plane in (tab_s, planes_in, v_s):
             nc.vector.memset(plane[:].bitcast(I32), 0)
+        nc.gpsimd.dma_start(out=tab_w[:].bitcast(I32), in_=tab_words[0].rearrange("p e t -> p (e t)").bitcast(I32))
+        nc.gpsimd.dma_start(out=w3_in[:].bitcast(I32), in_=w3_words[0].rearrange("p c t -> p (c t)").bitcast(I32))
+        w1_rows = w1.rearrange("(p j) c -> p j c", j=PACK)
+        w1_early = placed([2, PACK, HALF], F32, "w1_early", AT_W1_EARLY)
+        for half in range(2):
+            nc.gpsimd.dma_start(out=w1_early[:, half], in_=w1_rows[:, :, HALF * half : HALF * (half + 1)])
+        w1_late = placed([PACK, GROUP], F32, "w1_late", AT_W1_LATE)
+        nc.gpsimd.dma_start(out=w1_late[:], in_=w1_rows[:, :, GROUP:])
         nc.sync.dma_start(offs_sb[:], offs)
+        nc.sync.dma_start(out=w2_in[:].bitcast(I32), in_=w2_words[0].bitcast(I32))
         nc.sync.dma_start(pos1_sb[:], pos1)
         nc.sync.dma_start(pos2_sb[:], pos2)
-        nc.sync.dma_start(out=tab_w[:].bitcast(I32), in_=tab_words[0].rearrange("p e t -> p (e t)").bitcast(I32))
-        nc.sync.dma_start(out=w2_in[:].bitcast(I32), in_=w2_words[0].bitcast(I32))
-        nc.scalar.dma_start(out=tab_s[SCALE_FIRST : SCALE_FIRST + BLOCKS * SCALE_STEP : SCALE_STEP, :].bitcast(I32),
-                            in_=tab_scales[0].bitcast(I32))
-        fill_plane(nc.gpsimd, w2_plane_in, lambda r: w2_scales[0, r:BLOCKS:QUADS, :])
-        fill_plane(nc.gpsimd, w3_plane_in, lambda r: w3_scales[0, r:BLOCKS:QUADS, :])
+        nc.scalar.dma_start(out=tab_s[0:P:RUN, :].bitcast(I32), in_=tab_scales[0].bitcast(I32))
+        fill_plane(nc.sync, planes_in, 0, lambda r: w2_scales[0, r:BLOCKS:QUADS, :])
+        fill_plane(nc.scalar, planes_in, W3_PLANE, lambda r: w3_scales[0, r:BLOCKS:QUADS, :])
 
         def deal_columns(copy, dst, src):
             copy(
@@ -128,21 +131,14 @@ def tile_list_triple_pair_rerank_kernel(
                 in_=src[:].bitcast(U32).rearrange("p (g b t w) -> p g t b w", g=GROUPS, t=PACK, b=BLOCKS),
             )
 
+        w2_w = own([2 * H], U8, "w2_w")
+        deal_columns(nc.vector.tensor_copy, w2_w, w2_in)
+
         picked_s = own([S], U8, "picked_s")
         nc.vector.tensor_copy(picked_s[:], tab_s[:].indirect(offs_sb[:]))
-        step = QUADS * SCALE_STEP
-        fill_plane(nc.sync, v_s, lambda r: picked_s[SCALE_FIRST + SCALE_STEP * r : SCALE_FIRST + BLOCKS * SCALE_STEP : step, :])
-        nc.sync.dma_start(out=w3_in[:].bitcast(I32), in_=w3_words[0].rearrange("p c t -> p (c t)").bitcast(I32))
-        w2_s = placed([H], U8, "w2_s", AT_W2_PLANE)
-        deal_columns(nc.vector.tensor_copy, w2_s, w2_plane_in)
-
-        w2_w = own([2 * H], U8, "w2_w")
-        deal_columns(nc.scalar.copy, w2_w, w2_in)
-
-        w1_rows = w1.rearrange("(p j) c -> p j c", j=PACK)
-        w1_early = placed([2, PACK, HALF], F32, "w1_early", AT_W1_EARLY)
-        for half in range(2):
-            nc.sync.dma_start(out=w1_early[:, half], in_=w1_rows[:, :, HALF * half : HALF * (half + 1)])
+        fill_plane(nc.sync, v_s, 0, lambda r: picked_s[RUN * r : P : 32, :])
+        w_s = placed([H], U8, "w_s", AT_PLANES)
+        deal_columns(nc.vector.tensor_copy, w_s, planes_in)
 
         v_w = own([S], U32, "v_w")
         for lo in range(0, S, BANK):
@@ -150,11 +146,6 @@ def tile_list_triple_pair_rerank_kernel(
             nc.vector.tensor_copy(v_w[:, lo : lo + BANK], tab_w[:].indirect(entries))
         w3_w = placed([4 * H], U8, "w3_w", AT_W3_WORDS)
         deal_columns(nc.vector.tensor_copy, w3_w, w3_in)
-        w3_s = placed([H], U8, "w3_s", AT_W3_PLANE)
-        deal_columns(nc.vector.tensor_copy, w3_s, w3_plane_in)
-
-        w1_late = placed([PACK, GROUP], F32, "w1_late", AT_W1_LATE)
-        nc.sync.dma_start(out=w1_late[:], in_=w1_rows[:, :, GROUP:])
 
         w4_blocks = [(c_group, g) for g in range(GROUPS) for c_group in range(GROUPS)]
         w4_stage, w4_q, w1_q = {}, {}, {}
@@ -218,13 +209,13 @@ def tile_list_triple_pair_rerank_kernel(
             for a in tiles:
                 q[a] = placed([S], F32, "q%d" % a, AT_Q + ROW * (a % PACK))
                 codes = w2_w[:, 2 * P * a : 2 * P * (a + 1)].bitcast(FP4X4)
-                jobs.append((q[a], codes, w2_s[:, P * a : P * (a + 1)]))
+                jobs.append((q[a], codes, w_s[:, P * a : P * (a + 1)]))
             first_stage(jobs)
 
         def make_r(a):
             r[a] = placed([S], F32, "r%d" % a, AT_R + ROW * (a % PACK))
             codes = w3_w[:, 4 * P * a : 4 * P * (a + 1)].bitcast(FP8X4)
-            first_stage([(r[a], codes, w3_s[:, P * a : P * (a + 1)])])
+            first_stage([(r[a], codes, w_s[W3_PLANE:, P * a : P * (a + 1)])])
 
         def make_h(a):
             g, t = divmod(a, PACK)
@@ -250,14 +241,16 @@ def tile_list_triple_pair_rerank_kernel(
             for k in range(2):
                 gate[PACK * g + 2 * pair + k] = both[:, k, :]
 
-        def products(g, pair, lo, hi, gated, z):
-            entries = slice(lo // LIST_ROWS, hi // LIST_ROWS)
-            places = (2 * pair, 2 * pair + 1)
-            for t in places:
+        def gated_heads(g, pair, lo, hi, gated):
+            for t in (2 * pair, 2 * pair + 1):
                 a = PACK * g + t
-                nc.vector.tensor_tensor(gated(t), h[a][:].indirect(pos1_sb[:, entries]), gate[a][:, lo:hi], MULT)
-            for t in places:
-                nc.vector.tensor_tensor(z(t), h[PACK * g + t][:].indirect(pos2_sb[:, entries]), gated(t), MULT)
+                entries = pos1_sb[:, lo // LIST_ROWS : hi // LIST_ROWS]
+                nc.vector.tensor_tensor(gated(t), h[a][:].indirect(entries), gate[a][:, lo:hi], MULT)
+
+        def times_tails(g, pair, lo, hi, gated, z):
+            for t in (2 * pair, 2 * pair + 1):
+                entries = pos2_sb[:, lo // LIST_ROWS : hi // LIST_ROWS]
+                nc.vector.tensor_tensor(z(t), h[PACK * g + t][:].indirect(entries), gated(t), MULT)
 
         def weaving(woven, rows):
             return (
@@ -294,34 +287,30 @@ def tile_list_triple_pair_rerank_kernel(
         for a in range(EARLY_Q, PACK):
             make_q((a,))
         heads = pick_heads(0)
-        w1_q[0] = quantised(GROUP, "w1_0", rounded[:], AT_W1_CODES)
+        w1_q[0] = quantised(GROUP, "w1_0", rounded[:], AT_W1_CODES[0])
         for a in range(PACK):
             make_r(a)
         diff = differences(0, heads)
-        rounded = round_w4(0, nc.vector.tensor_copy)
-        load_w4(2)
+        rounded = placed([PACK * GROUP], BF16, "w1_rounded1", AT_W1_ROUNDED[1])
+        nc.vector.tensor_copy(
+            out=rounded[:].rearrange("p (t b e j) -> p b t j e", t=PACK, e=RUN, j=PACK),
+            in_=w1_late[:].rearrange("p j (b t e) -> p b t j e", t=PACK, e=RUN),
+        )
+        load_w4(1)
         gated_first = [placed([PAIRS], F32, "gated_first%d" % k, AT_GATED + 4 * PAIRS * k) for k in range(2)]
-        z_first = []
+        z_first = placed([PACK, PAIRS], F32, "z_first", AT_Z)
         for pair in range(2):
             make_h(2 * pair)
             make_h(2 * pair + 1)
             gates_of_pair(0, pair, diff)
-            if pair == 1:
-                rounded = placed([PACK * GROUP], BF16, "w1_rounded1", AT_W1_ROUNDED[1])
-                nc.scalar.copy(
-                    out=rounded[:].rearrange("p (t b e j) -> p b t j e", t=PACK, e=RUN, j=PACK),
-                    in_=w1_late[:].rearrange("p j (b t e) -> p b t j e", t=PACK, e=RUN),
-                )
-                w1_q[1] = quantised(GROUP, "w1_1", rounded[:])
-                load_w4(1)
-            z_first.append(placed([2, PAIRS], F32, "z_first%d" % pair, AT_Z[pair]))
-            products(0, pair, 0, PAIRS, lambda t: gated_first[t % 2][:], lambda t: z_first[pair][:, t % 2, :])
+            gated_heads(0, pair, 0, PAIRS, lambda t: gated_first[t % 2][:])
+            times_tails(0, pair, 0, PAIRS, lambda t: gated_first[t % 2][:], lambda t: z_first[:, t, :])
             if pair == 0:
-                quantise_w4(0, rounded)
+                w1_q[1] = quantised(GROUP, "w1_1", rounded[:], AT_W1_CODES[1])
+        load_w4(2)
         weighed = placed([PACK, PAIRS], F32, "weighed", AT_WEIGHED)
         for t in range(PACK):
-            nc.gpsimd.tensor_scalar(weighed[:, t, :], z_first[t // 2][:, t % 2, :], rel_sb[:, 0, t, 0:1], 0.0, MULT, ADD)
-        load_w4(3)
+            nc.gpsimd.tensor_scalar(weighed[:, t, :], z_first[:, t, :], rel_sb[:, 0, t, 0:1], 0.0, MULT, ADD)
 
         for a in range(PACK, TILES):
             make_q((a,))
@@ -336,6 +325,8 @@ def tile_list_triple_pair_rerank_kernel(
             return woven
 
         woven = weave_first_z(0, nc.vector.tensor_copy)
+        quantise_w4(0, round_w4(0, nc.scalar.copy))
+        load_w4(3)
         for pair in range(2):
             make_h(PACK + 2 * pair)
             make_h(PACK + 2 * pair + 1)
@@ -349,15 +340,18 @@ def tile_list_triple_pair_rerank_kernel(
         spans = list(zip(edges[:-1], edges[1:]))
         last = len(PIECES) - 1
         y_scales = own([GROUPS * PAIRS], U8, "y_scales")
-        y_woven = {}
+        y_woven, gated = {}, {}
 
         def second_group_z(piece):
             lo, hi = spans[piece]
-            at = AT_GATED if piece == 0 else AT_GATED_LATE + 4 * PACK * (lo - edges[1])
-            gated = placed([PACK, hi - lo], F32, "gated_piece%d" % piece, at)
+            half, at = divmod(lo, HALF)
+            if at == 0:
+                gated[half] = placed([PACK, HALF], F32, "gated_half%d" % half, (AT_GATED, AT_GATED_LATE)[half])
             z = placed([PACK, hi - lo], F32, "z_piece%d" % piece, AT_Z_PIECE[piece])
             for pair in range(2):
-                products(1, pair, lo, hi, lambda t: gated[:, t, :], lambda t: z[:, t, :])
+                if at == 0:
+                    gated_heads(1, pair, lo, lo + HALF, lambda t: gated[half][:, t, :])
+                times_tails(1, pair, lo, hi, lambda t: gated[half][:, t, at : at + hi - lo], lambda t: z[:, t, :])
             name = "z_woven%d" % piece
             woven = placed([PACK * (hi - lo)], BF16, name, AT_Z_WOVEN_LAST) if piece == last else own([PACK * (hi - lo)], BF16, name)
             weigh_and_weave(1, z[:], woven)
@@ -381,7 +375,8 @@ def tile_list_triple_pair_rerank_kernel(
                         nc.scalar.copy(out=y[:, :, at : at + P], in_=acc)
                         nc.scalar.copy(*weaving(into, acc))
                 rows = out_0[GROUP * g : GROUP * (g + 1), lo:hi].rearrange("(p t) i -> p t i", t=PACK)
-                nc.sync.dma_start(out=rows, in_=y[:])
+                queue = nc.scalar if piece == last and g == GROUPS - 1 else nc.sync
+                queue.dma_start(out=rows, in_=y[:])
 
         for piece in range(len(PIECES)):
             second_group_z(piece)
@@ -399,7 +394,8 @@ def tile_list_triple_pair_rerank_kernel(
                 )
             if piece in (0, last):
                 begin = 0 if piece == 0 else edges[1]
-                nc.sync.dma_start(out=words[:, :, begin:hi], in_=codes[:, :, begin:hi])
+                queue = nc.gpsimd if piece == 0 else nc.sync
+                queue.dma_start(out=words[:, :, begin:hi], in_=codes[:, :, begin:hi])
         plane = y_scales[:].rearrange("p (g i) -> p g i", g=GROUPS)
         for k in range(QUADS):
             rows = out_2[:, k:BLOCKS:QUADS, :].rearrange("g row i -> row g i")

@@ -27,7 +27,7 @@ TILES = H // P
 BANK = 512
 BANKS = 8
 LIST_ROWS = 16
-W3_PLANE = 4
+SCALE_ROWS = 112
 RUN = 8
 BLOCKS = P // RUN
 QUADS = 4
@@ -41,33 +41,33 @@ EARLY_Q = 2
 ROW = 4 * S
 STAGE = 2 * ROW
 AT_TABLE = 0
-AT_W3_WORDS = AT_TABLE
-AT_TABLE_SCALES = AT_TABLE + 4 * T
-AT_PLANES = AT_TABLE_SCALES
-AT_W3_IN = AT_TABLE_SCALES + T
+AT_W3_PLANE = AT_TABLE
+AT_W3_WORDS = AT_W3_PLANE + H
+AT_W3_IN = AT_TABLE + 4 * T
 AT_REL = AT_W3_IN
-AT_W4_FIRST = AT_W3_IN + 4 * H - ALIGN
-AT_W1_LATE = AT_W4_FIRST + STAGE
-AT_W1_EARLY = AT_W1_LATE + STAGE
-AT_W4_STAGE = (AT_W4_FIRST, AT_W1_LATE, AT_W1_EARLY, AT_W4_FIRST)
-AT_Q = AT_W1_EARLY + STAGE
+AT_W1_EARLY = AT_W3_IN + 4 * H
+AT_TABLE_SCALES = AT_W1_EARLY - ALIGN
+AT_W1_LATE = AT_W1_EARLY + STAGE
+AT_PICKED_SCALES = AT_W1_LATE
+AT_Q = AT_W1_LATE + STAGE
 AT_R = AT_Q + PACK * ROW
-AT_DIFF = (AT_W1_EARLY, AT_R + PACK * ROW)
-AT_W1_ROUNDED = (AT_DIFF[1], AT_R + 2 * ROW)
-AT_HEADS = AT_DIFF[1] + 2 * ROW
-AT_H_LATE = AT_HEADS + 2 * ROW - ALIGN
+AT_DIFF = AT_R + PACK * ROW
+AT_HEADS = (AT_W1_EARLY, AT_DIFF + 2 * ROW)
+AT_H_LATE = AT_HEADS[1] + 2 * ROW - ALIGN
 AT_WEIGHED = AT_H_LATE + ALIGN
 AT_H_EARLY = AT_WEIGHED + 2 * ROW
 AT_H = (AT_H_EARLY, AT_H_EARLY + ROW, AT_H_LATE, AT_H_LATE + ROW)
-AT_W4_ROUNDED = (AT_H[0], AT_H[1], AT_HEADS, AT_HEADS + ROW)
+AT_W4_ROUNDED = (AT_H[0], AT_H[1], AT_HEADS[1], AT_HEADS[1] + ROW)
 AT_GATED = AT_H_EARLY + 2 * ROW
 AT_GATES = (AT_GATED + 2 * ROW, AT_GATED + ROW)
 AT_Z = AT_GATES[0] + ROW
-AT_W1_CODES = (AT_Q + 2 * ROW, AT_Z + 2 * ROW)
-AT_Z_PIECE = (AT_Z, AT_W4_FIRST, AT_W4_FIRST + ROW // 2)
-AT_GATED_LATE = AT_W4_FIRST + ROW
-AT_Z_WOVEN_LAST = AT_W1_CODES[1] + ROW // 2
-AT_Y_CODES = AT_Z_WOVEN_LAST
+AT_W1_ROUNDED = (AT_Z, AT_Z + ROW)
+AT_Z_PIECE = (AT_Z, AT_W1_LATE, AT_W1_LATE + ROW // 2)
+AT_W4_THIRD = AT_Z + 2 * ROW - ALIGN
+AT_W4_STAGE = (AT_W1_LATE, AT_W1_EARLY, AT_W4_THIRD, AT_W1_LATE)
+AT_GATED_PIECE = (AT_GATED, AT_W4_THIRD + ALIGN, AT_W1_LATE + ROW)
+AT_Q_THIRD = AT_W4_THIRD + STAGE
+AT_W1_CODES = AT_Q_THIRD
 
 
 def tile_list_triple_pair_rerank_kernel(
@@ -100,45 +100,47 @@ def tile_list_triple_pair_rerank_kernel(
         tab_s = placed([T], U8, "tab_s", AT_TABLE_SCALES)
         w2_in = own([2 * H], U8, "w2_in")
         w3_in = placed([4 * H], U8, "w3_in", AT_W3_IN)
-        planes_in = own([H], U8, "planes_in")
+        w2_plane_in = own([H], U8, "w2_plane_in")
+        w3_plane_in = own([H], U8, "w3_plane_in")
+        w2_s = own([H], U8, "w2_s")
         v_s = own([S], U8, "v_s")
 
-        def fill_plane(queue, plane, first, rows):
+        def fill_plane(queue, plane, rows):
             for r in range(QUADS):
-                queue.dma_start(out=plane[first + r : P : 32, :].bitcast(I32), in_=rows(r).bitcast(I32))
+                queue.dma_start(out=plane[r:P:32, :].bitcast(I32), in_=rows(r).bitcast(I32))
 
-        for plane in (tab_s, planes_in, v_s):
-            nc.vector.memset(plane[:].bitcast(I32), 0)
-        nc.gpsimd.dma_start(out=tab_w[:].bitcast(I32), in_=tab_words[0].rearrange("p e t -> p (e t)").bitcast(I32))
-        nc.gpsimd.dma_start(out=w3_in[:].bitcast(I32), in_=w3_words[0].rearrange("p c t -> p (c t)").bitcast(I32))
-        w1_rows = w1.rearrange("(p j) c -> p j c", j=PACK)
-        w1_early = placed([2, PACK, HALF], F32, "w1_early", AT_W1_EARLY)
-        for half in range(2):
-            nc.gpsimd.dma_start(out=w1_early[:, half], in_=w1_rows[:, :, HALF * half : HALF * (half + 1)])
-        w1_late = placed([PACK, GROUP], F32, "w1_late", AT_W1_LATE)
-        nc.gpsimd.dma_start(out=w1_late[:], in_=w1_rows[:, :, GROUP:])
+        nc.vector.memset(tab_s[:SCALE_ROWS, :].bitcast(I32), 0)
+        nc.vector.memset(w3_plane_in[:].bitcast(I32), 0)
+        nc.vector.memset(w2_s[:].bitcast(I32), 0)
+        nc.vector.memset(v_s[:].bitcast(I32), 0)
         nc.sync.dma_start(offs_sb[:], offs)
-        nc.sync.dma_start(out=w2_in[:].bitcast(I32), in_=w2_words[0].bitcast(I32))
+        nc.sync.dma_start(out=tab_s[SCALE_ROWS:, :].bitcast(I32), in_=tab_scales[0].bitcast(I32))
+        fill_plane(nc.sync, w2_plane_in, lambda r: w2_scales[0, r:BLOCKS:QUADS, :])
         nc.sync.dma_start(pos1_sb[:], pos1)
+        nc.sync.dma_start(out=tab_w[:].bitcast(I32), in_=tab_words[0].rearrange("p e t -> p (e t)").bitcast(I32))
         nc.sync.dma_start(pos2_sb[:], pos2)
-        nc.scalar.dma_start(out=tab_s[0:P:RUN, :].bitcast(I32), in_=tab_scales[0].bitcast(I32))
-        fill_plane(nc.sync, planes_in, 0, lambda r: w2_scales[0, r:BLOCKS:QUADS, :])
-        fill_plane(nc.scalar, planes_in, W3_PLANE, lambda r: w3_scales[0, r:BLOCKS:QUADS, :])
+        nc.sync.dma_start(out=w2_in[:].bitcast(I32), in_=w2_words[0].bitcast(I32))
+        fill_plane(nc.gpsimd, w3_plane_in, lambda r: w3_scales[0, r:BLOCKS:QUADS, :])
 
-        def deal_columns(copy, dst, src):
+        def deal_columns(copy, dst, src, rows=slice(0, P)):
             copy(
-                out=dst[:].bitcast(U32).rearrange("p (g t b w) -> p g t b w", g=GROUPS, t=PACK, b=BLOCKS),
-                in_=src[:].bitcast(U32).rearrange("p (g b t w) -> p g t b w", g=GROUPS, t=PACK, b=BLOCKS),
+                out=dst[rows, :].bitcast(U32).rearrange("p (g t b w) -> p g t b w", g=GROUPS, t=PACK, b=BLOCKS),
+                in_=src[rows, :].bitcast(U32).rearrange("p (g b t w) -> p g t b w", g=GROUPS, t=PACK, b=BLOCKS),
             )
 
-        w2_w = own([2 * H], U8, "w2_w")
-        deal_columns(nc.vector.tensor_copy, w2_w, w2_in)
-
-        picked_s = own([S], U8, "picked_s")
+        picked_s = placed([S], U8, "picked_s", AT_PICKED_SCALES)
         nc.vector.tensor_copy(picked_s[:], tab_s[:].indirect(offs_sb[:]))
-        fill_plane(nc.sync, v_s, 0, lambda r: picked_s[RUN * r : P : 32, :])
-        w_s = placed([H], U8, "w_s", AT_PLANES)
-        deal_columns(nc.vector.tensor_copy, w_s, planes_in)
+        fill_plane(nc.sync, v_s, lambda r: picked_s[SCALE_ROWS + r : P : QUADS, :])
+        nc.sync.dma_start(out=w3_in[:].bitcast(I32), in_=w3_words[0].rearrange("p c t -> p (c t)").bitcast(I32))
+        w1_rows = w1.rearrange("(p j) c -> p j c", j=PACK)
+        w1_early = placed([PACK, GROUP], F32, "w1_early", AT_W1_EARLY)
+        w1_late = placed([PACK, GROUP], F32, "w1_late", AT_W1_LATE)
+        nc.sync.dma_start(out=w1_early[:], in_=w1_rows[:, :, :GROUP])
+        nc.sync.dma_start(out=w1_late[:], in_=w1_rows[:, :, GROUP:])
+        for quad in range(QUADS):
+            deal_columns(nc.vector.tensor_copy, w2_s, w2_plane_in, slice(32 * quad, 32 * quad + QUADS))
+        w2_w = own([2 * H], U8, "w2_w")
+        deal_columns(nc.scalar.copy, w2_w, w2_in)
 
         v_w = own([S], U32, "v_w")
         for lo in range(0, S, BANK):
@@ -146,6 +148,8 @@ def tile_list_triple_pair_rerank_kernel(
             nc.vector.tensor_copy(v_w[:, lo : lo + BANK], tab_w[:].indirect(entries))
         w3_w = placed([4 * H], U8, "w3_w", AT_W3_WORDS)
         deal_columns(nc.vector.tensor_copy, w3_w, w3_in)
+        w3_s = placed([H], U8, "w3_s", AT_W3_PLANE)
+        deal_columns(nc.vector.tensor_copy, w3_s, w3_plane_in)
 
         w4_blocks = [(c_group, g) for g in range(GROUPS) for c_group in range(GROUPS)]
         w4_stage, w4_q, w1_q = {}, {}, {}
@@ -158,7 +162,6 @@ def tile_list_triple_pair_rerank_kernel(
             for j in range(PACK):
                 nc.sync.dma_start(out=w4_stage[number][:, j, :], in_=by_place[j])
 
-        load_w4(0)
         rel_sb = placed([GROUPS, PACK, RUN], F32, "rel_sb", AT_REL)
         by_tile = rel.rearrange("(g b t e) -> g t b e", g=GROUPS, t=PACK, e=RUN)
         for a in range(TILES):
@@ -171,14 +174,8 @@ def tile_list_triple_pair_rerank_kernel(
             nc.vector.quantize_mx(out=codes[:].bitcast(FP8X4), scales=scales[:], in_=woven)
             return codes, scales
 
-        def round_w1(halves):
-            rounded = placed([PACK * GROUP], BF16, "w1_rounded0", AT_W1_ROUNDED[0])
-            into = rounded[:].rearrange("p (t half b e j) -> p half t b e j", t=PACK, half=2, e=RUN, j=PACK)
-            for half in range(2):
-                by_place = halves[:, half].rearrange("p j (b t e) -> p t b e j", t=PACK, e=RUN)
-                for t in range(PACK):
-                    nc.gpsimd.tensor_scalar(into[:, half, t], by_place[:, t], 1.0, 0.0, MULT, ADD)
-            return rounded
+        def w1_rounded(g):
+            return placed([PACK * GROUP], BF16, "w1_rounded%d" % g, AT_W1_ROUNDED[g])
 
         def round_w4(number, copy):
             rounded = placed([PACK * GROUP], BF16, "w4_rounded%d" % number, AT_W4_ROUNDED[number])
@@ -207,15 +204,15 @@ def tile_list_triple_pair_rerank_kernel(
         def make_q(tiles):
             jobs = []
             for a in tiles:
-                q[a] = placed([S], F32, "q%d" % a, AT_Q + ROW * (a % PACK))
+                q[a] = placed([S], F32, "q%d" % a, AT_Q_THIRD if a == 2 else AT_Q + ROW * (a % PACK))
                 codes = w2_w[:, 2 * P * a : 2 * P * (a + 1)].bitcast(FP4X4)
-                jobs.append((q[a], codes, w_s[:, P * a : P * (a + 1)]))
+                jobs.append((q[a], codes, w2_s[:, P * a : P * (a + 1)]))
             first_stage(jobs)
 
         def make_r(a):
             r[a] = placed([S], F32, "r%d" % a, AT_R + ROW * (a % PACK))
             codes = w3_w[:, 4 * P * a : 4 * P * (a + 1)].bitcast(FP8X4)
-            first_stage([(r[a], codes, w_s[W3_PLANE:, P * a : P * (a + 1)])])
+            first_stage([(r[a], codes, w3_s[:, P * a : P * (a + 1)])])
 
         def make_h(a):
             g, t = divmod(a, PACK)
@@ -224,13 +221,13 @@ def tile_list_triple_pair_rerank_kernel(
             first_stage([(h[a], codes[:, P * t : P * (t + 1)].bitcast(FP8X4), scales[:, P * t : P * (t + 1)])])
 
         def pick_heads(g):
-            heads = placed([PACK, PAIRS], F32, "heads%d" % g, AT_HEADS)
+            heads = placed([PACK, PAIRS], F32, "heads%d" % g, AT_HEADS[g])
             for t in range(PACK):
                 nc.vector.tensor_copy(heads[:, t, :], q[PACK * g + t][:].indirect(pos1_sb[:]))
             return heads
 
         def differences(g, heads):
-            diff = placed([PACK, PAIRS], F32, "diff%d" % g, AT_DIFF[g])
+            diff = placed([PACK, PAIRS], F32, "diff%d" % g, AT_DIFF)
             for t in range(PACK):
                 nc.vector.tensor_tensor(diff[:, t, :], r[PACK * g + t][:].indirect(pos2_sb[:]), heads[:, t, :], SUBTRACT)
             return diff
@@ -282,20 +279,26 @@ def tile_list_triple_pair_rerank_kernel(
                 )
             return acc
 
-        rounded = round_w1(w1_early)
+        rounded = [w1_rounded(g) for g in range(GROUPS)]
+        nc.vector.tensor_copy(
+            out=rounded[0][:].rearrange("p (t b e j) -> p b t j e", t=PACK, e=RUN, j=PACK),
+            in_=w1_early[:].rearrange("p j (b t e) -> p b t j e", t=PACK, e=RUN),
+        )
+        w1_q[0] = quantised(GROUP, "w1_0", rounded[0][:])
+        nc.gpsimd.tensor_scalar(
+            rounded[1][:].rearrange("p (t b e j) -> p b t e j", t=PACK, e=RUN, j=PACK),
+            w1_late[:].rearrange("p j (b t e) -> p b t e j", t=PACK, e=RUN),
+            1.0, 0.0, MULT, ADD,
+        )
+        load_w4(0)
         make_q(range(EARLY_Q))
         for a in range(EARLY_Q, PACK):
             make_q((a,))
         heads = pick_heads(0)
-        w1_q[0] = quantised(GROUP, "w1_0", rounded[:], AT_W1_CODES[0])
+        w1_q[1] = quantised(GROUP, "w1_1", rounded[1][:], AT_W1_CODES)
         for a in range(PACK):
             make_r(a)
         diff = differences(0, heads)
-        rounded = placed([PACK * GROUP], BF16, "w1_rounded1", AT_W1_ROUNDED[1])
-        nc.vector.tensor_copy(
-            out=rounded[:].rearrange("p (t b e j) -> p b t j e", t=PACK, e=RUN, j=PACK),
-            in_=w1_late[:].rearrange("p j (b t e) -> p b t j e", t=PACK, e=RUN),
-        )
         load_w4(1)
         gated_first = [placed([PAIRS], F32, "gated_first%d" % k, AT_GATED + 4 * PAIRS * k) for k in range(2)]
         z_first = placed([PACK, PAIRS], F32, "z_first", AT_Z)
@@ -305,12 +308,10 @@ def tile_list_triple_pair_rerank_kernel(
             gates_of_pair(0, pair, diff)
             gated_heads(0, pair, 0, PAIRS, lambda t: gated_first[t % 2][:])
             times_tails(0, pair, 0, PAIRS, lambda t: gated_first[t % 2][:], lambda t: z_first[:, t, :])
-            if pair == 0:
-                w1_q[1] = quantised(GROUP, "w1_1", rounded[:], AT_W1_CODES[1])
-        load_w4(2)
         weighed = placed([PACK, PAIRS], F32, "weighed", AT_WEIGHED)
         for t in range(PACK):
             nc.gpsimd.tensor_scalar(weighed[:, t, :], z_first[:, t, :], rel_sb[:, 0, t, 0:1], 0.0, MULT, ADD)
+        load_w4(2)
 
         for a in range(PACK, TILES):
             make_q((a,))
@@ -340,20 +341,17 @@ def tile_list_triple_pair_rerank_kernel(
         spans = list(zip(edges[:-1], edges[1:]))
         last = len(PIECES) - 1
         y_scales = own([GROUPS * PAIRS], U8, "y_scales")
-        y_woven, gated = {}, {}
+        y_codes = own([GROUPS * PAIRS], U32, "y_codes")
+        y_woven = {}
 
         def second_group_z(piece):
             lo, hi = spans[piece]
-            half, at = divmod(lo, HALF)
-            if at == 0:
-                gated[half] = placed([PACK, HALF], F32, "gated_half%d" % half, (AT_GATED, AT_GATED_LATE)[half])
+            gated = placed([PACK, hi - lo], F32, "gated_piece%d" % piece, AT_GATED_PIECE[piece])
             z = placed([PACK, hi - lo], F32, "z_piece%d" % piece, AT_Z_PIECE[piece])
             for pair in range(2):
-                if at == 0:
-                    gated_heads(1, pair, lo, lo + HALF, lambda t: gated[half][:, t, :])
-                times_tails(1, pair, lo, hi, lambda t: gated[half][:, t, at : at + hi - lo], lambda t: z[:, t, :])
-            name = "z_woven%d" % piece
-            woven = placed([PACK * (hi - lo)], BF16, name, AT_Z_WOVEN_LAST) if piece == last else own([PACK * (hi - lo)], BF16, name)
+                gated_heads(1, pair, lo, hi, lambda t: gated[:, t, :])
+                times_tails(1, pair, lo, hi, lambda t: gated[:, t, :], lambda t: z[:, t, :])
+            woven = own([PACK * (hi - lo)], BF16, "z_woven%d" % piece)
             weigh_and_weave(1, z[:], woven)
             quantise_z(1, lo, hi, woven)
 
@@ -361,8 +359,11 @@ def tile_list_triple_pair_rerank_kernel(
             lo, hi = spans[piece]
             for g in range(GROUPS):
                 place = GROUPS * lo + g * (hi - lo)
-                y = placed([PACK, hi - lo], F32, "y%d_%d" % (piece, g), AT_R + 4 * PACK * place)
-                y_woven[piece, g] = placed([PACK * (hi - lo)], BF16, "y_woven%d_%d" % (piece, g), AT_HEADS + 2 * PACK * place)
+                at = AT_R + 4 * PACK * place
+                if piece == last and g == GROUPS - 1:
+                    at = AT_HEADS[1] + 2 * PACK * GROUPS * edges[last - 1]
+                y = placed([PACK, hi - lo], F32, "y%d_%d" % (piece, g), at)
+                y_woven[piece, g] = placed([PACK * (hi - lo)], BF16, "y_woven%d_%d" % (piece, g), AT_HEADS[1] + 2 * PACK * place)
                 for col in range(lo, hi, P):
                     second_passes(0, g, col)
                     acc = second_passes(1, g, col)
@@ -375,27 +376,22 @@ def tile_list_triple_pair_rerank_kernel(
                         nc.scalar.copy(out=y[:, :, at : at + P], in_=acc)
                         nc.scalar.copy(*weaving(into, acc))
                 rows = out_0[GROUP * g : GROUP * (g + 1), lo:hi].rearrange("(p t) i -> p t i", t=PACK)
-                queue = nc.scalar if piece == last and g == GROUPS - 1 else nc.sync
-                queue.dma_start(out=rows, in_=y[:])
-
-        for piece in range(len(PIECES)):
-            second_group_z(piece)
-            results(piece)
-
-        y_codes = placed([GROUPS * PAIRS], U32, "y_codes", AT_Y_CODES)
-        words = out_1.rearrange("g p i t -> p g (i t)").bitcast(I32)
-        codes = y_codes[:].bitcast(I32).rearrange("p (g i) -> p g i", g=GROUPS)
-        for piece, (lo, hi) in enumerate(spans):
-            for g in range(GROUPS):
+                nc.sync.dma_start(out=rows, in_=y[:])
                 nc.vector.quantize_mx(
                     out=y_codes[:, PAIRS * g + lo : PAIRS * g + hi].bitcast(FP8X4),
                     scales=y_scales[:, PAIRS * g + lo : PAIRS * g + hi],
                     in_=y_woven[piece, g][:],
                 )
-            if piece in (0, last):
-                begin = 0 if piece == 0 else edges[1]
-                queue = nc.gpsimd if piece == 0 else nc.sync
-                queue.dma_start(out=words[:, :, begin:hi], in_=codes[:, :, begin:hi])
+
+        words = out_1.rearrange("g p i t -> p g (i t)").bitcast(I32)
+        codes = y_codes[:].bitcast(I32).rearrange("p (g i) -> p g i", g=GROUPS)
+        for piece in range(len(PIECES)):
+            second_group_z(piece)
+            if piece > 0:
+                results(piece - 1)
+        nc.sync.dma_start(out=words[:, :, : edges[last]], in_=codes[:, :, : edges[last]])
+        results(last)
+        nc.sync.dma_start(out=words[:, :, edges[last] :], in_=codes[:, :, edges[last] :])
         plane = y_scales[:].rearrange("p (g i) -> p g i", g=GROUPS)
         for k in range(QUADS):
             rows = out_2[:, k:BLOCKS:QUADS, :].rearrange("g row i -> row g i")

@@ -56,9 +56,12 @@ AT_HEADS = (AT_W1_EARLY, AT_DIFF + 2 * ROW)
 AT_H_LATE = AT_HEADS[1] + 2 * ROW - ALIGN
 AT_WEIGHED = AT_H_LATE + ALIGN
 AT_H_EARLY = AT_WEIGHED + 2 * ROW
-AT_H = (AT_H_EARLY, AT_H_EARLY + ROW, AT_H_LATE, AT_H_LATE + ROW)
+AT_H_SECOND = AT_H_EARLY + 2 * ROW
+AT_H = (AT_H_EARLY, AT_H_EARLY + ROW, AT_H_LATE, AT_H_LATE + ROW) + tuple(AT_H_SECOND + ROW * t for t in range(PACK))
+AT_Y_CODES = AT_H[6]
+AT_Z_CODES_LAST = AT_H[4]
 AT_W4_ROUNDED = (AT_H[0], AT_H[1], AT_HEADS[1], AT_HEADS[1] + ROW)
-AT_GATED = AT_H_EARLY + 2 * ROW
+AT_GATED = AT_H_SECOND + PACK * ROW
 AT_GATES = (AT_GATED + 2 * ROW, AT_GATED + ROW)
 AT_Z = AT_GATES[0] + ROW
 AT_W1_ROUNDED = (AT_Z, AT_Z + ROW)
@@ -66,6 +69,7 @@ AT_Z_PIECE = (AT_Z, AT_W1_LATE, AT_W1_LATE + ROW // 2)
 AT_W4_THIRD = AT_Z + 2 * ROW - ALIGN
 AT_W4_STAGE = (AT_W1_LATE, AT_W1_EARLY, AT_W4_THIRD, AT_W1_LATE)
 AT_GATED_PIECE = (AT_GATED, AT_W4_THIRD + ALIGN, AT_W1_LATE + ROW)
+AT_Z_CODES_MIDDLE = AT_GATED_PIECE[0]
 AT_Q_THIRD = AT_W4_THIRD + STAGE
 AT_W1_CODES = AT_Q_THIRD
 
@@ -185,8 +189,8 @@ def tile_list_triple_pair_rerank_kernel(
             )
             return rounded
 
-        def quantise_w4(number, rounded):
-            w4_q[w4_blocks[number]] = quantised(GROUP, "w4_%d" % number, rounded[:])
+        def quantise_w4(number, rounded, at=None):
+            w4_q[w4_blocks[number]] = quantised(GROUP, "w4_%d" % number, rounded[:], at)
 
         def first_stage(jobs):
             for lo in range(0, S, BANK):
@@ -217,7 +221,7 @@ def tile_list_triple_pair_rerank_kernel(
         def make_h(a):
             g, t = divmod(a, PACK)
             codes, scales = w1_q[g]
-            h[a] = placed([S], F32, "h%d" % a, AT_H[t]) if g == 0 else own([S], F32, "h%d" % a)
+            h[a] = placed([S], F32, "h%d" % a, AT_H[a])
             first_stage([(h[a], codes[:, P * t : P * (t + 1)].bitcast(FP8X4), scales[:, P * t : P * (t + 1)])])
 
         def pick_heads(g):
@@ -227,14 +231,15 @@ def tile_list_triple_pair_rerank_kernel(
             return heads
 
         def differences(g, heads):
-            diff = placed([PACK, PAIRS], F32, "diff%d" % g, AT_DIFF)
+            diff = [placed([2, PAIRS], F32, "diff%d_%d" % (g, pair), AT_DIFF + ROW * pair) for pair in range(2)]
             for t in range(PACK):
-                nc.vector.tensor_tensor(diff[:, t, :], r[PACK * g + t][:].indirect(pos2_sb[:]), heads[:, t, :], SUBTRACT)
+                into = diff[t // 2][:, t % 2, :]
+                nc.vector.tensor_tensor(into, r[PACK * g + t][:].indirect(pos2_sb[:]), heads[:, t, :], SUBTRACT)
             return diff
 
         def gates_of_pair(g, pair, diff):
             both = placed([2, PAIRS], F32, "gate%d_%d" % (g, pair), AT_GATES[pair])
-            nc.scalar.activation(out=both[:], in_=diff[:, 2 * pair : 2 * pair + 2, :], func=SIGMOID, scale=-1.0)
+            nc.scalar.activation(out=both[:], in_=diff[pair][:], func=SIGMOID, scale=-1.0)
             for k in range(2):
                 gate[PACK * g + 2 * pair + k] = both[:, k, :]
 
@@ -244,8 +249,8 @@ def tile_list_triple_pair_rerank_kernel(
                 entries = pos1_sb[:, lo // LIST_ROWS : hi // LIST_ROWS]
                 nc.vector.tensor_tensor(gated(t), h[a][:].indirect(entries), gate[a][:, lo:hi], MULT)
 
-        def times_tails(g, pair, lo, hi, gated, z):
-            for t in (2 * pair, 2 * pair + 1):
+        def times_tails(g, places, lo, hi, gated, z):
+            for t in places:
                 entries = pos2_sb[:, lo // LIST_ROWS : hi // LIST_ROWS]
                 nc.vector.tensor_tensor(z(t), h[PACK * g + t][:].indirect(entries), gated(t), MULT)
 
@@ -262,8 +267,8 @@ def tile_list_triple_pair_rerank_kernel(
 
         z_q = {}
 
-        def quantise_z(g, lo, hi, woven):
-            codes, scales = quantised(hi - lo, "z%d_%d" % (g, lo), woven[:])
+        def quantise_z(g, lo, hi, woven, at=None):
+            codes, scales = quantised(hi - lo, "z%d_%d" % (g, lo), woven, at)
             for col in range(lo, hi, P):
                 z_q[g, col] = (codes[:, col - lo : col - lo + P].bitcast(FP8X4), scales[:, col - lo : col - lo + P])
 
@@ -307,7 +312,7 @@ def tile_list_triple_pair_rerank_kernel(
             make_h(2 * pair + 1)
             gates_of_pair(0, pair, diff)
             gated_heads(0, pair, 0, PAIRS, lambda t: gated_first[t % 2][:])
-            times_tails(0, pair, 0, PAIRS, lambda t: gated_first[t % 2][:], lambda t: z_first[:, t, :])
+            times_tails(0, (2 * pair, 2 * pair + 1), 0, PAIRS, lambda t: gated_first[t % 2][:], lambda t: z_first[:, t, :])
         weighed = placed([PACK, PAIRS], F32, "weighed", AT_WEIGHED)
         for t in range(PACK):
             nc.gpsimd.tensor_scalar(weighed[:, t, :], z_first[:, t, :], rel_sb[:, 0, t, 0:1], 0.0, MULT, ADD)
@@ -325,35 +330,52 @@ def tile_list_triple_pair_rerank_kernel(
             copy(*weaving(woven[:], weighed[:, :, HALF * half : HALF * (half + 1)]))
             return woven
 
-        woven = weave_first_z(0, nc.vector.tensor_copy)
-        quantise_w4(0, round_w4(0, nc.scalar.copy))
+        first_woven = [weave_first_z(0, nc.vector.tensor_copy)]
+        first_block = round_w4(0, nc.scalar.copy)
         load_w4(3)
         for pair in range(2):
             make_h(PACK + 2 * pair)
             make_h(PACK + 2 * pair + 1)
             gates_of_pair(1, pair, diff)
-        quantise_z(0, 0, HALF, woven)
-        for number in range(1, len(w4_blocks)):
-            quantise_w4(number, round_w4(number, nc.scalar.copy))
-        quantise_z(0, HALF, PAIRS, weave_first_z(1, nc.scalar.copy))
+        later_blocks = [round_w4(number, nc.scalar.copy) for number in range(1, len(w4_blocks))]
+        first_woven.append(weave_first_z(1, nc.scalar.copy))
 
         edges = [sum(PIECES[:k]) for k in range(len(PIECES) + 1)]
         spans = list(zip(edges[:-1], edges[1:]))
         last = len(PIECES) - 1
         y_scales = own([GROUPS * PAIRS], U8, "y_scales")
-        y_codes = own([GROUPS * PAIRS], U32, "y_codes")
-        y_woven = {}
+        y_codes = placed([GROUPS * PAIRS], U32, "y_codes", AT_Y_CODES)
+        y_woven, gated, z, z_woven = {}, {}, {}, {}
 
-        def second_group_z(piece):
+        def piece_tails(piece, places):
+            times_tails(1, places, *spans[piece], lambda t: gated[piece][:, t, :], lambda t: z[piece][:, t, :])
+
+        def piece_heads(piece, pair):
             lo, hi = spans[piece]
-            gated = placed([PACK, hi - lo], F32, "gated_piece%d" % piece, AT_GATED_PIECE[piece])
-            z = placed([PACK, hi - lo], F32, "z_piece%d" % piece, AT_Z_PIECE[piece])
-            for pair in range(2):
-                gated_heads(1, pair, lo, hi, lambda t: gated[:, t, :])
-                times_tails(1, pair, lo, hi, lambda t: gated[:, t, :], lambda t: z[:, t, :])
-            woven = own([PACK * (hi - lo)], BF16, "z_woven%d" % piece)
-            weigh_and_weave(1, z[:], woven)
-            quantise_z(1, lo, hi, woven)
+            if pair == 0:
+                gated[piece] = placed([PACK, hi - lo], F32, "gated_piece%d" % piece, AT_GATED_PIECE[piece])
+                z[piece] = placed([PACK, hi - lo], F32, "z_piece%d" % piece, AT_Z_PIECE[piece])
+            gated_heads(1, pair, lo, hi, lambda t: gated[piece][:, t, :])
+
+        def piece_products(piece, pair):
+            piece_heads(piece, pair)
+            piece_tails(piece, (2 * pair, 2 * pair + 1))
+
+        def weave_piece(piece):
+            lo, hi = spans[piece]
+            z_woven[piece] = own([PACK * (hi - lo)], BF16, "z_woven%d" % piece)
+            weigh_and_weave(1, z[piece][:], z_woven[piece])
+
+        def quantise_piece(piece):
+            quantise_z(1, *spans[piece], z_woven[piece][:])
+
+        def quantise_results(piece, g):
+            lo, hi = spans[piece]
+            nc.vector.quantize_mx(
+                out=y_codes[:, PAIRS * g + lo : PAIRS * g + hi].bitcast(FP8X4),
+                scales=y_scales[:, PAIRS * g + lo : PAIRS * g + hi],
+                in_=y_woven[piece, g][:],
+            )
 
         def results(piece):
             lo, hi = spans[piece]
@@ -377,20 +399,40 @@ def tile_list_triple_pair_rerank_kernel(
                         nc.scalar.copy(*weaving(into, acc))
                 rows = out_0[GROUP * g : GROUP * (g + 1), lo:hi].rearrange("(p t) i -> p t i", t=PACK)
                 nc.sync.dma_start(out=rows, in_=y[:])
-                nc.vector.quantize_mx(
-                    out=y_codes[:, PAIRS * g + lo : PAIRS * g + hi].bitcast(FP8X4),
-                    scales=y_scales[:, PAIRS * g + lo : PAIRS * g + hi],
-                    in_=y_woven[piece, g][:],
-                )
 
         words = out_1.rearrange("g p i t -> p g (i t)").bitcast(I32)
         codes = y_codes[:].bitcast(I32).rearrange("p (g i) -> p g i", g=GROUPS)
-        for piece in range(len(PIECES)):
-            second_group_z(piece)
-            if piece > 0:
-                results(piece - 1)
+        piece_products(0, 0)
+        quantise_z(0, 0, HALF, first_woven[0][:], AT_DIFF)
+        piece_products(0, 1)
+        quantise_w4(0, first_block, AT_DIFF + ROW)
+        weave_piece(0)
+        quantise_w4(1, later_blocks[0])
+        quantise_piece(0)
+        quantise_w4(2, later_blocks[1])
+        quantise_w4(3, later_blocks[2])
+        piece_products(1, 0)
+        piece_products(1, 1)
+        quantise_z(0, edges[1], edges[2], first_woven[1][:, : PACK * P], AT_Z_CODES_MIDDLE)
+        weave_piece(1)
+        quantise_piece(1)
+        results(0)
+        piece_products(2, 0)
+        piece_heads(2, 1)
+        piece_tails(2, (2,))
+        quantise_z(0, edges[2], PAIRS, first_woven[1][:, PACK * P :], AT_Z_CODES_LAST)
+        piece_tails(2, (3,))
+        quantise_results(0, 0)
+        weave_piece(2)
+        quantise_results(0, 1)
+        quantise_piece(2)
+        results(1)
+        for g in range(GROUPS):
+            quantise_results(1, g)
         nc.sync.dma_start(out=words[:, :, : edges[last]], in_=codes[:, :, : edges[last]])
         results(last)
+        for g in range(GROUPS):
+            quantise_results(last, g)
         nc.sync.dma_start(out=words[:, :, edges[last] :], in_=codes[:, :, edges[last] :])
         plane = y_scales[:].rearrange("p (g i) -> p g i", g=GROUPS)
         for k in range(QUADS):

@@ -37,15 +37,17 @@ ALIGN = 64
 PIECES = (256, 128, 128)
 HALF = GROUP // 2
 EARLY_Q = 2
+EMPTIED_BY_VECTOR = ("q1", BANK)
 
 ROW = 4 * S
 STAGE = 2 * ROW
 AT_TABLE = 0
 AT_W3_PLANE = AT_TABLE
 AT_W3_WORDS = AT_W3_PLANE + H
-AT_W3_IN = AT_TABLE + 4 * T
-AT_REL = AT_W3_IN
-AT_W1_EARLY = AT_W3_IN + 4 * H
+AT_W3_IN = (AT_TABLE + 4 * T + 2 * H, AT_TABLE + 4 * T + ALIGN)
+AT_W2_IN_LATE = AT_W3_IN[0] + ALIGN
+AT_REL = AT_W2_IN_LATE + H
+AT_W1_EARLY = AT_W3_IN[0] + 2 * H
 AT_TABLE_SCALES = AT_W1_EARLY - ALIGN
 AT_W1_LATE = AT_W1_EARLY + STAGE
 AT_PICKED_SCALES = AT_W1_LATE
@@ -64,13 +66,15 @@ AT_W4_ROUNDED = (AT_H[0], AT_H[1], AT_HEADS[1], AT_HEADS[1] + ROW)
 AT_GATED = AT_H_SECOND + PACK * ROW
 AT_GATES = (AT_GATED + 2 * ROW, AT_GATED + ROW)
 AT_Z = AT_GATES[0] + ROW
-AT_W1_ROUNDED = (AT_Z, AT_Z + ROW)
+AT_W1_ROUNDED = (AT_Z, AT_Z + ROW - ALIGN)
 AT_Z_PIECE = (AT_Z, AT_W1_LATE, AT_W1_LATE + ROW // 2)
-AT_W4_THIRD = AT_Z + 2 * ROW - ALIGN
-AT_W4_STAGE = (AT_W1_LATE, AT_W1_EARLY, AT_W4_THIRD, AT_W1_LATE)
-AT_GATED_PIECE = (AT_GATED, AT_W4_THIRD + ALIGN, AT_W1_LATE + ROW)
+AT_W4_SECOND = AT_Z + 2 * ROW - ALIGN
+AT_W4_THIRD = AT_W3_WORDS + 2 * H
+AT_W4_STAGE = (AT_W1_LATE, AT_W4_SECOND, AT_W4_THIRD, AT_W1_LATE)
+AT_GATED_PIECE = (AT_GATED, AT_W4_THIRD, AT_W1_LATE + ROW)
 AT_Z_CODES_MIDDLE = AT_GATED_PIECE[0]
-AT_Q_THIRD = AT_W4_THIRD + STAGE
+AT_DEALT_LATE = AT_W1_EARLY + ROW
+AT_Q_THIRD = AT_W4_SECOND + STAGE
 AT_W1_CODES = AT_Q_THIRD
 
 
@@ -102,8 +106,8 @@ def tile_list_triple_pair_rerank_kernel(
         pos2_sb = keep.tile([P, PAIRS // LIST_ROWS], U16, name="pos2_sb")
         tab_w = placed([T], U32, "tab_w", AT_TABLE)
         tab_s = placed([T], U8, "tab_s", AT_TABLE_SCALES)
-        w2_in = own([2 * H], U8, "w2_in")
-        w3_in = placed([4 * H], U8, "w3_in", AT_W3_IN)
+        w2_in = [own([H], U8, "w2_in0"), placed([H], U8, "w2_in1", AT_W2_IN_LATE)]
+        w3_in = [placed([2 * H], U8, "w3_in%d" % g, AT_W3_IN[g]) for g in range(GROUPS)]
         w2_plane_in = own([H], U8, "w2_plane_in")
         w3_plane_in = own([H], U8, "w3_plane_in")
         w2_s = own([H], U8, "w2_s")
@@ -123,19 +127,20 @@ def tile_list_triple_pair_rerank_kernel(
         nc.sync.dma_start(pos1_sb[:], pos1)
         nc.sync.dma_start(out=tab_w[:].bitcast(I32), in_=tab_words[0].rearrange("p e t -> p (e t)").bitcast(I32))
         nc.sync.dma_start(pos2_sb[:], pos2)
-        nc.sync.dma_start(out=w2_in[:].bitcast(I32), in_=w2_words[0].bitcast(I32))
+        nc.sync.dma_start(out=w2_in[0][:].bitcast(I32), in_=w2_words[0][:, :H].bitcast(I32))
         fill_plane(nc.gpsimd, w3_plane_in, lambda r: w3_scales[0, r:BLOCKS:QUADS, :])
 
-        def deal_columns(copy, dst, src, rows=slice(0, P)):
+        def deal_columns(copy, dst, src, rows=slice(0, P), groups=GROUPS):
             copy(
-                out=dst[rows, :].bitcast(U32).rearrange("p (g t b w) -> p g t b w", g=GROUPS, t=PACK, b=BLOCKS),
-                in_=src[rows, :].bitcast(U32).rearrange("p (g b t w) -> p g t b w", g=GROUPS, t=PACK, b=BLOCKS),
+                out=dst[rows, :].bitcast(U32).rearrange("p (g t b w) -> p g t b w", g=groups, t=PACK, b=BLOCKS),
+                in_=src[rows, :].bitcast(U32).rearrange("p (g b t w) -> p g t b w", g=groups, t=PACK, b=BLOCKS),
             )
 
         picked_s = placed([S], U8, "picked_s", AT_PICKED_SCALES)
         nc.vector.tensor_copy(picked_s[:], tab_s[:].indirect(offs_sb[:]))
         fill_plane(nc.sync, v_s, lambda r: picked_s[SCALE_ROWS + r : P : QUADS, :])
-        nc.sync.dma_start(out=w3_in[:].bitcast(I32), in_=w3_words[0].rearrange("p c t -> p (c t)").bitcast(I32))
+        w3_bytes = w3_words[0].rearrange("p c t -> p (c t)")
+        nc.sync.dma_start(out=w3_in[0][:].bitcast(I32), in_=w3_bytes[:, : 2 * H].bitcast(I32))
         w1_rows = w1.rearrange("(p j) c -> p j c", j=PACK)
         w1_early = placed([PACK, GROUP], F32, "w1_early", AT_W1_EARLY)
         w1_late = placed([PACK, GROUP], F32, "w1_late", AT_W1_LATE)
@@ -143,15 +148,17 @@ def tile_list_triple_pair_rerank_kernel(
         nc.sync.dma_start(out=w1_late[:], in_=w1_rows[:, :, GROUP:])
         for quad in range(QUADS):
             deal_columns(nc.vector.tensor_copy, w2_s, w2_plane_in, slice(32 * quad, 32 * quad + QUADS))
-        w2_w = own([2 * H], U8, "w2_w")
-        deal_columns(nc.scalar.copy, w2_w, w2_in)
+        w2_w = [own([H], U8, "w2_w0"), placed([H], U8, "w2_w1", AT_DEALT_LATE)]
+        deal_columns(nc.scalar.copy, w2_w[0], w2_in[0], groups=1)
 
         v_w = own([S], U32, "v_w")
         for lo in range(0, S, BANK):
             entries = offs_sb[:, lo // LIST_ROWS : (lo + BANK) // LIST_ROWS]
             nc.vector.tensor_copy(v_w[:, lo : lo + BANK], tab_w[:].indirect(entries))
-        w3_w = placed([4 * H], U8, "w3_w", AT_W3_WORDS)
-        deal_columns(nc.vector.tensor_copy, w3_w, w3_in)
+        w3_w = [placed([2 * H], U8, "w3_w0", AT_W3_WORDS), placed([2 * H], U8, "w3_w1", AT_DEALT_LATE + H)]
+        deal_columns(nc.vector.tensor_copy, w3_w[0], w3_in[0], groups=1)
+        nc.sync.dma_start(out=w2_in[1][:].bitcast(I32), in_=w2_words[0][:, H:].bitcast(I32))
+        nc.sync.dma_start(out=w3_in[1][:].bitcast(I32), in_=w3_bytes[:, 2 * H :].bitcast(I32))
         w3_s = placed([H], U8, "w3_s", AT_W3_PLANE)
         deal_columns(nc.vector.tensor_copy, w3_s, w3_plane_in)
 
@@ -194,14 +201,15 @@ def tile_list_triple_pair_rerank_kernel(
 
         def first_stage(jobs):
             for lo in range(0, S, BANK):
-                for rows, codes, scales in jobs:
+                for name, rows, codes, scales in jobs:
                     acc = next_bank()
                     nc.tensor.matmul_mx(
                         out=acc[:], lhsT=codes, lhsT_scale=scales,
                         rhs=v_w[:, lo : lo + BANK].bitcast(FP8X4), rhs_scale=v_s[:, lo : lo + BANK],
                         start=True, stop=True,
                     )
-                    nc.scalar.copy(out=rows[:, lo : lo + BANK], in_=acc[:])
+                    copy = nc.vector.tensor_copy if (name, lo) == EMPTIED_BY_VECTOR else nc.scalar.copy
+                    copy(out=rows[:, lo : lo + BANK], in_=acc[:])
 
         q, r, h, gate = {}, {}, {}, {}
 
@@ -209,20 +217,20 @@ def tile_list_triple_pair_rerank_kernel(
             jobs = []
             for a in tiles:
                 q[a] = placed([S], F32, "q%d" % a, AT_Q_THIRD if a == 2 else AT_Q + ROW * (a % PACK))
-                codes = w2_w[:, 2 * P * a : 2 * P * (a + 1)].bitcast(FP4X4)
-                jobs.append((q[a], codes, w2_s[:, P * a : P * (a + 1)]))
+                codes = w2_w[a // PACK][:, 2 * P * (a % PACK) : 2 * P * (a % PACK + 1)].bitcast(FP4X4)
+                jobs.append(("q%d" % a, q[a], codes, w2_s[:, P * a : P * (a + 1)]))
             first_stage(jobs)
 
         def make_r(a):
             r[a] = placed([S], F32, "r%d" % a, AT_R + ROW * (a % PACK))
-            codes = w3_w[:, 4 * P * a : 4 * P * (a + 1)].bitcast(FP8X4)
-            first_stage([(r[a], codes, w3_s[:, P * a : P * (a + 1)])])
+            codes = w3_w[a // PACK][:, 4 * P * (a % PACK) : 4 * P * (a % PACK + 1)].bitcast(FP8X4)
+            first_stage([("r%d" % a, r[a], codes, w3_s[:, P * a : P * (a + 1)])])
 
         def make_h(a):
             g, t = divmod(a, PACK)
             codes, scales = w1_q[g]
             h[a] = placed([S], F32, "h%d" % a, AT_H[a])
-            first_stage([(h[a], codes[:, P * t : P * (t + 1)].bitcast(FP8X4), scales[:, P * t : P * (t + 1)])])
+            first_stage([("h%d" % a, h[a], codes[:, P * t : P * (t + 1)].bitcast(FP8X4), scales[:, P * t : P * (t + 1)])])
 
         def pick_heads(g):
             heads = placed([PACK, PAIRS], F32, "heads%d" % g, AT_HEADS[g])
@@ -304,11 +312,14 @@ def tile_list_triple_pair_rerank_kernel(
         for a in range(PACK):
             make_r(a)
         diff = differences(0, heads)
-        load_w4(1)
+        load_w4(2)
         gated_first = [placed([PAIRS], F32, "gated_first%d" % k, AT_GATED + 4 * PAIRS * k) for k in range(2)]
         z_first = placed([PACK, PAIRS], F32, "z_first", AT_Z)
         for pair in range(2):
             make_h(2 * pair)
+            if pair == 1:
+                deal_columns(nc.scalar.copy, w2_w[1], w2_in[1], groups=1)
+                deal_columns(nc.scalar.copy, w3_w[1], w3_in[1], groups=1)
             make_h(2 * pair + 1)
             gates_of_pair(0, pair, diff)
             gated_heads(0, pair, 0, PAIRS, lambda t: gated_first[t % 2][:])
@@ -316,7 +327,7 @@ def tile_list_triple_pair_rerank_kernel(
         weighed = placed([PACK, PAIRS], F32, "weighed", AT_WEIGHED)
         for t in range(PACK):
             nc.gpsimd.tensor_scalar(weighed[:, t, :], z_first[:, t, :], rel_sb[:, 0, t, 0:1], 0.0, MULT, ADD)
-        load_w4(2)
+        load_w4(1)
 
         for a in range(PACK, TILES):
             make_q((a,))

@@ -36,25 +36,24 @@ ALIGN = 64
 
 PIECES = (256, 128, 128)
 HALF = GROUP // 2
-EARLY_Q = 2
-EMPTIED_BY_VECTOR = ("q1", BANK)
+ENTITY_CUTS = ((0, 256), (256, 512), (512, 1024))
 
 ROW = 4 * S
 STAGE = 2 * ROW
 AT_TABLE = 0
-AT_W3_PLANE = AT_TABLE
-AT_W3_WORDS = AT_W3_PLANE + H
+AT_W3_WORDS = AT_TABLE
 AT_W3_IN = (AT_TABLE + 4 * T + 2 * H, AT_TABLE + 4 * T + ALIGN)
 AT_W2_IN_LATE = AT_W3_IN[0] + ALIGN
 AT_REL = AT_W2_IN_LATE + H
 AT_W1_EARLY = AT_W3_IN[0] + 2 * H
 AT_TABLE_SCALES = AT_W1_EARLY - ALIGN
-AT_W1_LATE = AT_W1_EARLY + STAGE
+AT_W3_PLANE = AT_W1_EARLY + STAGE - ALIGN
+AT_W1_LATE = AT_W3_PLANE + H
 AT_PICKED_SCALES = AT_W1_LATE
 AT_Q = AT_W1_LATE + STAGE
 AT_R = AT_Q + PACK * ROW
 AT_DIFF = AT_R + PACK * ROW
-AT_HEADS = (AT_W1_EARLY, AT_DIFF + 2 * ROW)
+AT_HEADS = (AT_W1_EARLY - ALIGN, AT_DIFF + 2 * ROW)
 AT_H_LATE = AT_HEADS[1] + 2 * ROW - ALIGN
 AT_WEIGHED = AT_H_LATE + ALIGN
 AT_H_EARLY = AT_WEIGHED + 2 * ROW
@@ -73,7 +72,7 @@ AT_W4_THIRD = AT_W3_WORDS + 2 * H
 AT_W4_STAGE = (AT_W1_LATE, AT_W4_SECOND, AT_W4_THIRD, AT_W1_LATE)
 AT_GATED_PIECE = (AT_GATED, AT_W4_THIRD, AT_W1_LATE + ROW)
 AT_Z_CODES_MIDDLE = AT_GATED_PIECE[0]
-AT_DEALT_LATE = AT_W1_EARLY + ROW
+AT_DEALT_LATE = AT_W1_EARLY + ROW - ALIGN
 AT_Q_THIRD = AT_W4_SECOND + STAGE
 AT_W1_CODES = AT_Q_THIRD
 
@@ -140,11 +139,11 @@ def tile_list_triple_pair_rerank_kernel(
         nc.vector.tensor_copy(picked_s[:], tab_s[:].indirect(offs_sb[:]))
         fill_plane(nc.sync, v_s, lambda r: picked_s[SCALE_ROWS + r : P : QUADS, :])
         w3_bytes = w3_words[0].rearrange("p c t -> p (c t)")
-        nc.sync.dma_start(out=w3_in[0][:].bitcast(I32), in_=w3_bytes[:, : 2 * H].bitcast(I32))
         w1_rows = w1.rearrange("(p j) c -> p j c", j=PACK)
         w1_early = placed([PACK, GROUP], F32, "w1_early", AT_W1_EARLY)
         w1_late = placed([PACK, GROUP], F32, "w1_late", AT_W1_LATE)
         nc.sync.dma_start(out=w1_early[:], in_=w1_rows[:, :, :GROUP])
+        nc.sync.dma_start(out=w3_in[0][:].bitcast(I32), in_=w3_bytes[:, : 2 * H].bitcast(I32))
         nc.sync.dma_start(out=w1_late[:], in_=w1_rows[:, :, GROUP:])
         for quad in range(QUADS):
             deal_columns(nc.vector.tensor_copy, w2_s, w2_plane_in, slice(32 * quad, 32 * quad + QUADS))
@@ -152,15 +151,8 @@ def tile_list_triple_pair_rerank_kernel(
         deal_columns(nc.scalar.copy, w2_w[0], w2_in[0], groups=1)
 
         v_w = own([S], U32, "v_w")
-        for lo in range(0, S, BANK):
-            entries = offs_sb[:, lo // LIST_ROWS : (lo + BANK) // LIST_ROWS]
-            nc.vector.tensor_copy(v_w[:, lo : lo + BANK], tab_w[:].indirect(entries))
-        w3_w = [placed([2 * H], U8, "w3_w0", AT_W3_WORDS), placed([2 * H], U8, "w3_w1", AT_DEALT_LATE + H)]
-        deal_columns(nc.vector.tensor_copy, w3_w[0], w3_in[0], groups=1)
-        nc.sync.dma_start(out=w2_in[1][:].bitcast(I32), in_=w2_words[0][:, H:].bitcast(I32))
-        nc.sync.dma_start(out=w3_in[1][:].bitcast(I32), in_=w3_bytes[:, 2 * H :].bitcast(I32))
-        w3_s = placed([H], U8, "w3_s", AT_W3_PLANE)
-        deal_columns(nc.vector.tensor_copy, w3_s, w3_plane_in)
+        for lo, hi in ENTITY_CUTS:
+            nc.vector.tensor_copy(v_w[:, lo:hi], tab_w[:].indirect(offs_sb[:, lo // LIST_ROWS : hi // LIST_ROWS]))
 
         w4_blocks = [(c_group, g) for g in range(GROUPS) for c_group in range(GROUPS)]
         w4_stage, w4_q, w1_q = {}, {}, {}
@@ -172,12 +164,6 @@ def tile_list_triple_pair_rerank_kernel(
             by_place = rows.rearrange("(b j e) n -> j b e n", j=PACK, e=RUN)
             for j in range(PACK):
                 nc.sync.dma_start(out=w4_stage[number][:, j, :], in_=by_place[j])
-
-        rel_sb = placed([GROUPS, PACK, RUN], F32, "rel_sb", AT_REL)
-        by_tile = rel.rearrange("(g b t e) -> g t b e", g=GROUPS, t=PACK, e=RUN)
-        for a in range(TILES):
-            g, t = divmod(a, PACK)
-            nc.sync.dma_start(out=rel_sb[:, g, t, 0:1], in_=by_tile[g, t])
 
         def quantised(width, name, woven, at=None):
             codes = own([width], U32, name + "_codes") if at is None else placed([width], U32, name + "_codes", at)
@@ -199,38 +185,35 @@ def tile_list_triple_pair_rerank_kernel(
         def quantise_w4(number, rounded, at=None):
             w4_q[w4_blocks[number]] = quantised(GROUP, "w4_%d" % number, rounded[:], at)
 
-        def first_stage(jobs):
-            for lo in range(0, S, BANK):
-                for name, rows, codes, scales in jobs:
-                    acc = next_bank()
-                    nc.tensor.matmul_mx(
-                        out=acc[:], lhsT=codes, lhsT_scale=scales,
-                        rhs=v_w[:, lo : lo + BANK].bitcast(FP8X4), rhs_scale=v_s[:, lo : lo + BANK],
-                        start=True, stop=True,
-                    )
-                    copy = nc.vector.tensor_copy if (name, lo) == EMPTIED_BY_VECTOR else nc.scalar.copy
-                    copy(out=rows[:, lo : lo + BANK], in_=acc[:])
+        def first_stage(rows, codes, scales, cuts=((0, BANK), (BANK, S)), copy=nc.scalar.copy):
+            for lo, hi in cuts:
+                acc = next_bank()[:, : hi - lo]
+                nc.tensor.matmul_mx(
+                    out=acc, lhsT=codes, lhsT_scale=scales,
+                    rhs=v_w[:, lo:hi].bitcast(FP8X4), rhs_scale=v_s[:, lo:hi],
+                    start=True, stop=True,
+                )
+                copy(out=rows[:, lo:hi], in_=acc)
 
         q, r, h, gate = {}, {}, {}, {}
 
-        def make_q(tiles):
-            jobs = []
-            for a in tiles:
-                q[a] = placed([S], F32, "q%d" % a, AT_Q_THIRD if a == 2 else AT_Q + ROW * (a % PACK))
-                codes = w2_w[a // PACK][:, 2 * P * (a % PACK) : 2 * P * (a % PACK + 1)].bitcast(FP4X4)
-                jobs.append(("q%d" % a, q[a], codes, w2_s[:, P * a : P * (a + 1)]))
-            first_stage(jobs)
+        def make_q(a, *how):
+            g, t = divmod(a, PACK)
+            if a not in q:
+                q[a] = placed([S], F32, "q%d" % a, AT_Q_THIRD if a == 2 else AT_Q + ROW * t)
+            codes = w2_w[g][:, 2 * P * t : 2 * P * (t + 1)].bitcast(FP4X4)
+            first_stage(q[a], codes, w2_s[:, P * a : P * (a + 1)], *how)
 
         def make_r(a):
             r[a] = placed([S], F32, "r%d" % a, AT_R + ROW * (a % PACK))
             codes = w3_w[a // PACK][:, 4 * P * (a % PACK) : 4 * P * (a % PACK + 1)].bitcast(FP8X4)
-            first_stage([("r%d" % a, r[a], codes, w3_s[:, P * a : P * (a + 1)])])
+            first_stage(r[a], codes, w3_s[:, P * a : P * (a + 1)])
 
         def make_h(a):
             g, t = divmod(a, PACK)
             codes, scales = w1_q[g]
             h[a] = placed([S], F32, "h%d" % a, AT_H[a])
-            first_stage([("h%d" % a, h[a], codes[:, P * t : P * (t + 1)].bitcast(FP8X4), scales[:, P * t : P * (t + 1)])])
+            first_stage(h[a], codes[:, P * t : P * (t + 1)].bitcast(FP8X4), scales[:, P * t : P * (t + 1)])
 
         def pick_heads(g):
             heads = placed([PACK, PAIRS], F32, "heads%d" % g, AT_HEADS[g])
@@ -297,6 +280,17 @@ def tile_list_triple_pair_rerank_kernel(
             out=rounded[0][:].rearrange("p (t b e j) -> p b t j e", t=PACK, e=RUN, j=PACK),
             in_=w1_early[:].rearrange("p j (b t e) -> p b t j e", t=PACK, e=RUN),
         )
+        w3_w = [placed([2 * H], U8, "w3_w0", AT_W3_WORDS), placed([2 * H], U8, "w3_w1", AT_DEALT_LATE + H)]
+        deal_columns(nc.vector.tensor_copy, w3_w[0], w3_in[0], groups=1)
+        nc.sync.dma_start(out=w2_in[1][:].bitcast(I32), in_=w2_words[0][:, H:].bitcast(I32))
+        nc.sync.dma_start(out=w3_in[1][:].bitcast(I32), in_=w3_bytes[:, 2 * H :].bitcast(I32))
+        rel_sb = placed([GROUPS, PACK, RUN], F32, "rel_sb", AT_REL)
+        by_tile = rel.rearrange("(g b t e) -> g t b e", g=GROUPS, t=PACK, e=RUN)
+        for a in range(TILES):
+            g, t = divmod(a, PACK)
+            nc.sync.dma_start(out=rel_sb[:, g, t, 0:1], in_=by_tile[g, t])
+        w3_s = placed([H], U8, "w3_s", AT_W3_PLANE)
+        deal_columns(nc.vector.tensor_copy, w3_s, w3_plane_in)
         w1_q[0] = quantised(GROUP, "w1_0", rounded[0][:])
         nc.gpsimd.tensor_scalar(
             rounded[1][:].rearrange("p (t b e j) -> p b t e j", t=PACK, e=RUN, j=PACK),
@@ -304,9 +298,14 @@ def tile_list_triple_pair_rerank_kernel(
             1.0, 0.0, MULT, ADD,
         )
         load_w4(0)
-        make_q(range(EARLY_Q))
-        for a in range(EARLY_Q, PACK):
-            make_q((a,))
+        make_q(0, ENTITY_CUTS[:1])
+        make_q(1, ENTITY_CUTS[:1])
+        make_q(0, ENTITY_CUTS[1:2])
+        make_q(1, ENTITY_CUTS[1:2])
+        make_q(2, [(0, BANK)], nc.vector.tensor_copy)
+        make_q(3, [(0, BANK)])
+        for a in range(PACK):
+            make_q(a, [(BANK, S)])
         heads = pick_heads(0)
         w1_q[1] = quantised(GROUP, "w1_1", rounded[1][:], AT_W1_CODES)
         for a in range(PACK):
@@ -330,7 +329,7 @@ def tile_list_triple_pair_rerank_kernel(
         load_w4(1)
 
         for a in range(PACK, TILES):
-            make_q((a,))
+            make_q(a)
         heads = pick_heads(1)
         for a in range(PACK, TILES):
             make_r(a)

@@ -112,8 +112,8 @@ def tile_list_triple_pair_rerank_kernel(
         w2_s = own([H], U8, "w2_s")
         v_s = own([S], U8, "v_s")
 
-        def fill_plane(queue, plane, rows):
-            for r in range(QUADS):
+        def fill_plane(queues, plane, rows):
+            for r, queue in enumerate(queues):
                 queue.dma_start(out=plane[r:P:32, :].bitcast(I32), in_=rows(r).bitcast(I32))
 
         nc.vector.memset(tab_s[:SCALE_ROWS, :].bitcast(I32), 0)
@@ -122,12 +122,12 @@ def tile_list_triple_pair_rerank_kernel(
         nc.vector.memset(v_s[:].bitcast(I32), 0)
         nc.sync.dma_start(offs_sb[:], offs)
         nc.sync.dma_start(out=tab_s[SCALE_ROWS:, :].bitcast(I32), in_=tab_scales[0].bitcast(I32))
-        fill_plane(nc.sync, w2_plane_in, lambda r: w2_scales[0, r:BLOCKS:QUADS, :])
+        fill_plane([nc.scalar, nc.scalar, nc.scalar, nc.sync], w2_plane_in, lambda r: w2_scales[0, r:BLOCKS:QUADS, :])
         nc.sync.dma_start(pos1_sb[:], pos1)
         nc.sync.dma_start(out=tab_w[:].bitcast(I32), in_=tab_words[0].rearrange("p e t -> p (e t)").bitcast(I32))
         nc.sync.dma_start(pos2_sb[:], pos2)
         nc.sync.dma_start(out=w2_in[0][:].bitcast(I32), in_=w2_words[0][:, :H].bitcast(I32))
-        fill_plane(nc.gpsimd, w3_plane_in, lambda r: w3_scales[0, r:BLOCKS:QUADS, :])
+        fill_plane([nc.gpsimd] * QUADS, w3_plane_in, lambda r: w3_scales[0, r:BLOCKS:QUADS, :])
 
         def deal_columns(copy, dst, src, rows=slice(0, P), groups=GROUPS):
             copy(
@@ -137,7 +137,7 @@ def tile_list_triple_pair_rerank_kernel(
 
         picked_s = placed([S], U8, "picked_s", AT_PICKED_SCALES)
         nc.vector.tensor_copy(picked_s[:], tab_s[:].indirect(offs_sb[:]))
-        fill_plane(nc.sync, v_s, lambda r: picked_s[SCALE_ROWS + r : P : QUADS, :])
+        fill_plane([nc.sync] * QUADS, v_s, lambda r: picked_s[SCALE_ROWS + r : P : QUADS, :])
         w3_bytes = w3_words[0].rearrange("p c t -> p (c t)")
         w1_rows = w1.rearrange("(p j) c -> p j c", j=PACK)
         w1_early = placed([PACK, GROUP], F32, "w1_early", AT_W1_EARLY)

@@ -120,6 +120,10 @@ def tile_list_triple_pair_rerank_kernel(
         nc.vector.memset(w3_plane_in[:].bitcast(I32), 0)
         nc.vector.memset(w2_s[:].bitcast(I32), 0)
         nc.vector.memset(v_s[:].bitcast(I32), 0)
+        zeros = own([LINE], F32, "zeros")
+        warm = own([LINE], F32, "warm")
+        nc.vector.memset(zeros[:], 0.0)
+        nc.scalar.activation(out=warm[:], in_=zeros[:], func=SIGMOID)
         nc.sync.dma_start(offs_sb[:], offs)
         nc.sync.dma_start(out=tab_s[SCALE_ROWS:, :].bitcast(I32), in_=tab_scales[0].bitcast(I32))
         fill_plane([nc.scalar, nc.scalar, nc.scalar, nc.sync], w2_plane_in, lambda r: w2_scales[0, r:BLOCKS:QUADS, :])

@@ -1,6 +1,7 @@
 from contextlib import ExitStack
 
 import concourse.mybir as mybir
+from concourse.masks import make_identity
 
 K, T, S, PAIRS, H, N = 512, 4096, 1024, 512, 1024, 1024
 FLOPS = 3 * 2 * K * H * S + 2 * H * N * PAIRS
@@ -14,10 +15,9 @@ U8 = mybir.dt.uint8
 FP8X4 = mybir.dt.float8_e4m3fn_x4
 FP4X4 = mybir.dt.float4_e2m1fn_x4
 COPY = mybir.ActivationFunctionType.Copy
+SIGMOID = mybir.ActivationFunctionType.Sigmoid
 MULT = mybir.AluOpType.mult
 ADD = mybir.AluOpType.add
-SUBTRACT = mybir.AluOpType.subtract
-SIGMOID = mybir.ActivationFunctionType.Sigmoid
 
 P = 128
 PACK = 4
@@ -26,6 +26,7 @@ GROUPS = 2
 TILES = H // P
 BANK = 512
 BANKS = 8
+RING = 4
 LIST_ROWS = 16
 SCALE_ROWS = 112
 RUN = 8
@@ -33,48 +34,46 @@ BLOCKS = P // RUN
 QUADS = 4
 LINE = 4
 ALIGN = 64
-
 PIECES = (256, 128, 128)
 HALF = GROUP // 2
 ENTITY_CUTS = ((0, 256), (256, 512), (512, 1024))
 
 ROW = 4 * S
 STAGE = 2 * ROW
-AT_TABLE = 0
-AT_W3_WORDS = AT_TABLE
-AT_W3_IN = (AT_TABLE + 4 * T + 2 * H, AT_TABLE + 4 * T + ALIGN)
-AT_W2_IN_LATE = AT_W3_IN[0] + ALIGN
-AT_REL = AT_W2_IN_LATE + H
-AT_W1_EARLY = AT_W3_IN[0] + 2 * H
-AT_TABLE_SCALES = AT_W1_EARLY - ALIGN
-AT_W3_PLANE = AT_W1_EARLY + STAGE - ALIGN
-AT_W1_LATE = AT_W3_PLANE + H
-AT_PICKED_SCALES = AT_W1_LATE
-AT_Q = AT_W1_LATE + STAGE
-AT_R = AT_Q + PACK * ROW
-AT_DIFF = AT_R + PACK * ROW
-AT_HEADS = (AT_W1_EARLY - ALIGN, AT_DIFF + 2 * ROW)
-AT_H_LATE = AT_HEADS[1] + 2 * ROW - ALIGN
-AT_WEIGHED = AT_H_LATE + ALIGN
-AT_H_EARLY = AT_WEIGHED + 2 * ROW
-AT_H_SECOND = AT_H_EARLY + 2 * ROW
-AT_H = (AT_H_EARLY, AT_H_EARLY + ROW, AT_H_LATE, AT_H_LATE + ROW) + tuple(AT_H_SECOND + ROW * t for t in range(PACK))
-AT_Y_CODES = AT_H[6]
-AT_Z_CODES_LAST = AT_H[4]
-AT_W4_ROUNDED = (AT_H[0], AT_H[1], AT_HEADS[1], AT_HEADS[1] + ROW)
-AT_GATED = AT_H_SECOND + PACK * ROW
-AT_GATES = (AT_GATED + 2 * ROW, AT_GATED + ROW)
-AT_Z = AT_GATES[0] + ROW
-AT_W1_ROUNDED = (AT_Z, AT_Z + ROW - ALIGN)
-AT_Z_PIECE = (AT_Z, AT_W1_LATE, AT_W1_LATE + ROW // 2)
-AT_W4_SECOND = AT_Z + 2 * ROW - ALIGN
-AT_W4_THIRD = AT_W3_WORDS + 2 * H
-AT_W4_STAGE = (AT_W1_LATE, AT_W4_SECOND, AT_W4_THIRD, AT_W1_LATE)
-AT_GATED_PIECE = (AT_GATED, AT_W4_THIRD, AT_W1_LATE + ROW)
-AT_Z_CODES_MIDDLE = AT_GATED_PIECE[0]
-AT_DEALT_LATE = AT_W1_EARLY + ROW - ALIGN
-AT_Q_THIRD = AT_W4_SECOND + STAGE
-AT_W1_CODES = AT_Q_THIRD
+AT_TABLE = ALIGN
+AT_W4_FIRST = AT_TABLE
+AT_TAILS_LATE = AT_W4_FIRST + STAGE - ALIGN
+AT_W4_THIRD = 0
+AT_TAILS_EARLY = AT_TABLE + 4 * T
+AT_W1_EARLY = AT_TAILS_EARLY + STAGE - ALIGN
+AT_W3_LATE = AT_W1_EARLY + ALIGN
+AT_REL_ROW = AT_W3_LATE + 2 * H
+AT_GATED_PAIR = (AT_REL_ROW + TILES * ALIGN, AT_REL_ROW + TILES * ALIGN + ROW // 2)
+AT_REL = tuple({5: AT_GATED_PAIR[0], 7: AT_GATED_PAIR[1]}.get(a, AT_REL_ROW + ALIGN * a) for a in range(TILES))
+AT_TABLE_SCALES = AT_W1_EARLY + STAGE - ALIGN
+AT_W3_EARLY = AT_W1_EARLY + STAGE
+AT_W2_LATE = AT_W3_EARLY + 2 * H
+AT_GATED_FIRST = AT_TABLE_SCALES + T
+AT_W1_LATE = AT_GATED_FIRST + ROW
+AT_PICKED_SCALES = AT_W1_LATE - S + ALIGN
+AT_W4_SECOND = AT_W1_LATE - ALIGN
+AT_W4_FOURTH = AT_W1_LATE
+AT_HEADS_LATE = AT_W1_LATE + STAGE - ALIGN
+AT_ROUNDED = AT_HEADS_LATE + STAGE
+AT_QR = AT_ROUNDED + PACK * ROW
+AT_H = AT_QR
+AT_Y = AT_QR + PACK * STAGE
+AT_Y_WOVEN = AT_Y + 2 * STAGE
+AT_TURNED = AT_QR + TILES * STAGE
+AT_Z = AT_TURNED + STAGE
+AT_W4_STAGE = (AT_W4_FIRST, AT_W4_SECOND, AT_W4_THIRD, AT_W4_FOURTH)
+AT_W4_ROUNDED = (AT_ROUNDED + 2 * (ROW - ALIGN), AT_ROUNDED + 3 * (ROW - ALIGN), AT_H + 3 * ROW, AT_H + 2 * ROW)
+AT_GATED_PIECE = (AT_GATED_PAIR, (AT_W4_THIRD, AT_W4_THIRD + ROW // 4), (AT_W4_FOURTH + ROW, AT_W4_FOURTH + ROW + ROW // 4))
+AT_Z_PIECE = (AT_H, AT_H + ROW, AT_Z)
+AT_Z_WOVEN = (AT_W4_THIRD + ROW // 2, AT_W4_FOURTH, AT_TURNED)
+AT_FIRST_WOVEN = AT_W4_FOURTH + ROW // 4
+AT_Z_CODES = (AT_TURNED + ROW, AT_GATED_PAIR[1], AT_H + 6 * ROW)
+AT_Y_CODES = AT_H + 7 * ROW
 
 
 def tile_list_triple_pair_rerank_kernel(
@@ -94,7 +93,7 @@ def tile_list_triple_pair_rerank_kernel(
             return shared.tile([P] + shape, dtype, name=name, align_bytes=ALIGN, offset=at)
 
         banks = [psum.tile([P, BANK], F32, name="bank%d" % k) for k in range(BANKS)]
-        bank_ring = list(banks)
+        bank_ring = banks[:RING]
 
         def next_bank():
             bank_ring.append(bank_ring.pop(0))
@@ -105,11 +104,11 @@ def tile_list_triple_pair_rerank_kernel(
         pos2_sb = keep.tile([P, PAIRS // LIST_ROWS], U16, name="pos2_sb")
         tab_w = placed([T], U32, "tab_w", AT_TABLE)
         tab_s = placed([T], U8, "tab_s", AT_TABLE_SCALES)
-        w2_in = [own([H], U8, "w2_in0"), placed([H], U8, "w2_in1", AT_W2_IN_LATE)]
-        w3_in = [placed([2 * H], U8, "w3_in%d" % g, AT_W3_IN[g]) for g in range(GROUPS)]
+        w2_w = [own([H], U8, "w2_w0"), placed([H], U8, "w2_w1", AT_W2_LATE)]
+        w3_w = [placed([2 * H], U8, "w3_w0", AT_W3_EARLY), placed([2 * H], U8, "w3_w1", AT_W3_LATE)]
         w2_plane_in = own([H], U8, "w2_plane_in")
-        w3_plane_in = own([H], U8, "w3_plane_in")
         w2_s = own([H], U8, "w2_s")
+        w3_s = own([H], U8, "w3_s")
         v_s = own([S], U8, "v_s")
 
         def fill_plane(queues, plane, rows):
@@ -117,7 +116,7 @@ def tile_list_triple_pair_rerank_kernel(
                 queue.dma_start(out=plane[r:P:32, :].bitcast(I32), in_=rows(r).bitcast(I32))
 
         nc.vector.memset(tab_s[:SCALE_ROWS, :].bitcast(I32), 0)
-        nc.vector.memset(w3_plane_in[:].bitcast(I32), 0)
+        nc.vector.memset(w3_s[:].bitcast(I32), 0)
         nc.vector.memset(w2_s[:].bitcast(I32), 0)
         nc.vector.memset(v_s[:].bitcast(I32), 0)
         zeros = own([LINE], F32, "zeros")
@@ -130,36 +129,31 @@ def tile_list_triple_pair_rerank_kernel(
         nc.sync.dma_start(pos1_sb[:], pos1)
         nc.sync.dma_start(out=tab_w[:].bitcast(I32), in_=tab_words[0].rearrange("p e t -> p (e t)").bitcast(I32))
         nc.sync.dma_start(pos2_sb[:], pos2)
-        nc.sync.dma_start(out=w2_in[0][:].bitcast(I32), in_=w2_words[0][:, :H].bitcast(I32))
-        fill_plane([nc.gpsimd] * QUADS, w3_plane_in, lambda r: w3_scales[0, r:BLOCKS:QUADS, :])
-
-        def deal_columns(copy, dst, src, rows=slice(0, P), groups=GROUPS):
-            copy(
-                out=dst[rows, :].bitcast(U32).rearrange("p (g t b w) -> p g t b w", g=groups, t=PACK, b=BLOCKS),
-                in_=src[rows, :].bitcast(U32).rearrange("p (g b t w) -> p g t b w", g=groups, t=PACK, b=BLOCKS),
-            )
+        nc.sync.dma_start(out=w2_w[0][:].bitcast(I32), in_=w2_words[0][:, :H].bitcast(I32))
+        fill_plane([nc.gpsimd] * QUADS, w3_s, lambda r: w3_scales[0, r:BLOCKS:QUADS, :])
+        ident = own([P], F32, "ident")
+        make_identity(nc, ident[:])
 
         picked_s = placed([S], U8, "picked_s", AT_PICKED_SCALES)
         nc.vector.tensor_copy(picked_s[:], tab_s[:].indirect(offs_sb[:]))
         fill_plane([nc.sync] * QUADS, v_s, lambda r: picked_s[SCALE_ROWS + r : P : QUADS, :])
         w3_bytes = w3_words[0].rearrange("p c t -> p (c t)")
         w1_rows = w1.rearrange("(p j) c -> p j c", j=PACK)
-        w1_early = placed([PACK, GROUP], F32, "w1_early", AT_W1_EARLY)
-        w1_late = placed([PACK, GROUP], F32, "w1_late", AT_W1_LATE)
-        nc.sync.dma_start(out=w1_early[:], in_=w1_rows[:, :, :GROUP])
-        nc.sync.dma_start(out=w3_in[0][:].bitcast(I32), in_=w3_bytes[:, : 2 * H].bitcast(I32))
-        nc.sync.dma_start(out=w1_late[:], in_=w1_rows[:, :, GROUP:])
+        w1_stage = [placed([PACK, GROUP], F32, "w1_stage%d" % g, at) for g, at in enumerate((AT_W1_EARLY, AT_W1_LATE))]
+        nc.sync.dma_start(out=w1_stage[0][:], in_=w1_rows[:, :, :GROUP])
+        nc.sync.dma_start(out=w3_w[0][:].bitcast(I32), in_=w3_bytes[:, : 2 * H].bitcast(I32))
+        nc.sync.dma_start(out=w2_w[1][:].bitcast(I32), in_=w2_words[0][:, H:].bitcast(I32))
+        nc.sync.dma_start(out=w1_stage[1][:], in_=w1_rows[:, :, GROUP:])
         for quad in range(QUADS):
-            deal_columns(nc.vector.tensor_copy, w2_s, w2_plane_in, slice(32 * quad, 32 * quad + QUADS))
-        w2_w = [own([H], U8, "w2_w0"), placed([H], U8, "w2_w1", AT_DEALT_LATE)]
-        deal_columns(nc.scalar.copy, w2_w[0], w2_in[0], groups=1)
+            rows = slice(32 * quad, 32 * quad + QUADS)
+            nc.vector.tensor_copy(out=w2_s[rows, :].bitcast(I32), in_=w2_plane_in[rows, :].bitcast(I32))
 
         v_w = own([S], U32, "v_w")
         for lo, hi in ENTITY_CUTS:
             nc.vector.tensor_copy(v_w[:, lo:hi], tab_w[:].indirect(offs_sb[:, lo // LIST_ROWS : hi // LIST_ROWS]))
 
         w4_blocks = [(c_group, g) for g in range(GROUPS) for c_group in range(GROUPS)]
-        w4_stage, w4_q, w1_q = {}, {}, {}
+        w4_stage, w4_rounded, w4_q, w1_rounded, w1_q = {}, {}, {}, {}, {}
 
         def load_w4(number):
             c_group, g = w4_blocks[number]
@@ -175,19 +169,30 @@ def tile_list_triple_pair_rerank_kernel(
             nc.vector.quantize_mx(out=codes[:].bitcast(FP8X4), scales=scales[:], in_=woven)
             return codes, scales
 
-        def w1_rounded(g):
-            return placed([PACK * GROUP], BF16, "w1_rounded%d" % g, AT_W1_ROUNDED[g])
-
-        def round_w4(number, copy):
-            rounded = placed([PACK * GROUP], BF16, "w4_rounded%d" % number, AT_W4_ROUNDED[number])
-            copy(
-                out=rounded[:].rearrange("p (t m j) -> p m j t", t=PACK, j=PACK),
-                in_=w4_stage[number][:].rearrange("p j (m t) -> p m j t", t=PACK),
+        def round_w1(g):
+            w1_rounded[g] = placed([PACK * GROUP], BF16, "w1_rounded%d" % g, AT_ROUNDED + g * (ROW - ALIGN))
+            nc.gpsimd.tensor_scalar(
+                w1_rounded[g][:].rearrange("p (t b e j) -> p b t e j", t=PACK, e=RUN, j=PACK),
+                w1_stage[g][:].rearrange("p j (b t e) -> p b t e j", t=PACK, e=RUN),
+                1.0, 0.0, MULT, ADD,
             )
-            return rounded
 
-        def quantise_w4(number, rounded, at=None):
-            w4_q[w4_blocks[number]] = quantised(GROUP, "w4_%d" % number, rounded[:], at)
+        def round_w4(number):
+            w4_rounded[number] = placed([PACK * GROUP], BF16, "w4_rounded%d" % number, AT_W4_ROUNDED[number])
+            if number < GROUPS:
+                nc.gpsimd.tensor_scalar(
+                    w4_rounded[number][:].rearrange("p (t m j) -> p m t j", t=PACK, j=PACK),
+                    w4_stage[number][:].rearrange("p j (m t) -> p m t j", t=PACK),
+                    1.0, 0.0, MULT, ADD,
+                )
+            else:
+                nc.scalar.copy(
+                    out=w4_rounded[number][:].rearrange("p (t m j) -> p m j t", t=PACK, j=PACK),
+                    in_=w4_stage[number][:].rearrange("p j (m t) -> p m j t", t=PACK),
+                )
+
+        def quantise_w4(number):
+            w4_q[w4_blocks[number]] = quantised(GROUP, "w4_%d" % number, w4_rounded[number][:])
 
         def first_stage(rows, codes, scales, cuts=((0, BANK), (BANK, S)), copy=nc.scalar.copy):
             for lo, hi in cuts:
@@ -199,66 +204,73 @@ def tile_list_triple_pair_rerank_kernel(
                 )
                 copy(out=rows[:, lo:hi], in_=acc)
 
-        q, r, h, gate = {}, {}, {}, {}
+        qr = [placed([2 * S], F32, "qr%d" % a, AT_QR + STAGE * a) for a in range(TILES)]
+        h, gate = {}, {}
 
         def make_q(a, *how):
             g, t = divmod(a, PACK)
-            if a not in q:
-                q[a] = placed([S], F32, "q%d" % a, AT_Q_THIRD if a == 2 else AT_Q + ROW * t)
             codes = w2_w[g][:, 2 * P * t : 2 * P * (t + 1)].bitcast(FP4X4)
-            first_stage(q[a], codes, w2_s[:, P * a : P * (a + 1)], *how)
+            first_stage(qr[a][:, S:], codes, w2_s[:, P * a : P * (a + 1)], *how)
 
         def make_r(a):
-            r[a] = placed([S], F32, "r%d" % a, AT_R + ROW * (a % PACK))
-            codes = w3_w[a // PACK][:, 4 * P * (a % PACK) : 4 * P * (a % PACK + 1)].bitcast(FP8X4)
-            first_stage(r[a], codes, w3_s[:, P * a : P * (a + 1)])
+            g, t = divmod(a, PACK)
+            codes = w3_w[g][:, 4 * P * t : 4 * P * (t + 1)].bitcast(FP8X4)
+            first_stage(qr[a][:, :S], codes, w3_s[:, P * a : P * (a + 1)])
 
         def make_h(a):
             g, t = divmod(a, PACK)
             codes, scales = w1_q[g]
-            h[a] = placed([S], F32, "h%d" % a, AT_H[a])
+            h[a] = placed([S], F32, "h%d" % a, AT_H + ROW * a)
             first_stage(h[a], codes[:, P * t : P * (t + 1)].bitcast(FP8X4), scales[:, P * t : P * (t + 1)])
 
+        heads = [own([PACK, PAIRS], F32, "heads0"), placed([PACK, PAIRS], F32, "heads1", AT_HEADS_LATE)]
+        tails = [placed([PACK, PAIRS], F32, "tails%d" % g, at) for g, at in enumerate((AT_TAILS_EARLY, AT_TAILS_LATE))]
+        turned = [placed([PACK, GROUP], F32, "turned%d" % g, AT_TURNED) for g in range(GROUPS)]
+
         def pick_heads(g):
-            heads = placed([PACK, PAIRS], F32, "heads%d" % g, AT_HEADS[g])
             for t in range(PACK):
-                nc.vector.tensor_copy(heads[:, t, :], q[PACK * g + t][:].indirect(pos1_sb[:]))
-            return heads
+                nc.vector.tensor_copy(heads[g][:, t, :], qr[PACK * g + t][:, S:].indirect(pos1_sb[:]))
 
-        def differences(g, heads):
-            diff = [placed([2, PAIRS], F32, "diff%d_%d" % (g, pair), AT_DIFF + ROW * pair) for pair in range(2)]
+        def pick_tails(g):
             for t in range(PACK):
-                into = diff[t // 2][:, t % 2, :]
-                nc.vector.tensor_tensor(into, r[PACK * g + t][:].indirect(pos2_sb[:]), heads[:, t, :], SUBTRACT)
-            return diff
+                nc.vector.tensor_scalar(tails[g][:, t, :], qr[PACK * g + t][:].indirect(pos2_sb[:]), -1.0, 0.0, MULT, ADD)
 
-        def gates_of_pair(g, pair, diff):
-            both = placed([2, PAIRS], F32, "gate%d_%d" % (g, pair), AT_GATES[pair])
-            nc.scalar.activation(out=both[:], in_=diff[pair][:], func=SIGMOID, scale=-1.0)
-            for k in range(2):
-                gate[PACK * g + 2 * pair + k] = both[:, k, :]
+        def turned_gates(a):
+            g, t = divmod(a, PACK)
+            acc = next_bank()
+            for run in range(PACK):
+                cols = slice(P * run, P * (run + 1))
+                nc.tensor.matmul(acc[:, cols], heads[g][:, t, cols], ident[:], start=True, stop=False, is_transpose=True)
+                nc.tensor.matmul(acc[:, cols], tails[g][:, t, cols], ident[:], start=False, stop=True, is_transpose=True)
+            nc.scalar.activation(
+                out=turned[g][:].rearrange("p run (t a b e) -> p a t run b e", t=PACK, a=PACK, e=RUN)[:, t],
+                in_=acc[:].rearrange("p (run b t e) -> p t run b e", run=PACK, t=PACK, e=RUN),
+                func=SIGMOID,
+            )
 
-        def gated_heads(g, pair, lo, hi, gated):
+        def turn_back(g, pair):
             for t in (2 * pair, 2 * pair + 1):
-                a = PACK * g + t
-                entries = pos1_sb[:, lo // LIST_ROWS : hi // LIST_ROWS]
-                nc.vector.tensor_tensor(gated(t), h[a][:].indirect(entries), gate[a][:, lo:hi], MULT)
+                for run in range(PACK):
+                    nc.tensor.transpose(banks[RING + t][:, P * run : P * (run + 1)], turned[g][:, run, P * t : P * (t + 1)], ident[:])
 
-        def times_tails(g, places, lo, hi, gated, z):
-            for t in places:
-                entries = pos2_sb[:, lo // LIST_ROWS : hi // LIST_ROWS]
-                nc.vector.tensor_tensor(z(t), h[PACK * g + t][:].indirect(entries), gated(t), MULT)
+        def weighed_gate(a):
+            g, t = divmod(a, PACK)
+            gate[a] = own([PAIRS], F32, "gate%d" % a)
+            nc.scalar.activation(out=gate[a][:], in_=banks[RING + t][:], func=COPY, scale=rel_sb[a][:, 0:1])
+
+        def gated_heads(a, lo, hi, into):
+            entries = pos1_sb[:, lo // LIST_ROWS : hi // LIST_ROWS]
+            nc.vector.tensor_tensor(into, h[a][:].indirect(entries), gate[a][:, lo:hi], MULT)
+
+        def times_tails(a, lo, hi, gated, into):
+            entries = pos2_sb[:, lo // LIST_ROWS : hi // LIST_ROWS]
+            nc.vector.tensor_tensor(into, h[a][:].indirect(entries), gated, MULT)
 
         def weaving(woven, rows):
             return (
                 woven.rearrange("p (run i t) -> p run t i", i=LINE, t=PACK),
                 rows.rearrange("p t (run i) -> p run t i", i=LINE),
             )
-
-        def weigh_and_weave(g, z, woven):
-            into, by_runs = weaving(woven[:], z)
-            runs = z.shape[2] // LINE
-            nc.vector.tensor_tensor(into, by_runs, rel_sb[:, g, :, 0:1].unsqueeze(1).broadcast_to([P, runs, PACK, LINE]), MULT)
 
         z_q = {}
 
@@ -279,106 +291,112 @@ def tile_list_triple_pair_rerank_kernel(
                 )
             return acc
 
-        rounded = [w1_rounded(g) for g in range(GROUPS)]
-        nc.vector.tensor_copy(
-            out=rounded[0][:].rearrange("p (t b e j) -> p b t j e", t=PACK, e=RUN, j=PACK),
-            in_=w1_early[:].rearrange("p j (b t e) -> p b t j e", t=PACK, e=RUN),
-        )
-        w3_w = [placed([2 * H], U8, "w3_w0", AT_W3_WORDS), placed([2 * H], U8, "w3_w1", AT_DEALT_LATE + H)]
-        deal_columns(nc.vector.tensor_copy, w3_w[0], w3_in[0], groups=1)
-        nc.sync.dma_start(out=w2_in[1][:].bitcast(I32), in_=w2_words[0][:, H:].bitcast(I32))
-        nc.sync.dma_start(out=w3_in[1][:].bitcast(I32), in_=w3_bytes[:, 2 * H :].bitcast(I32))
-        rel_sb = placed([GROUPS, PACK, RUN], F32, "rel_sb", AT_REL)
+        round_w1(0)
+        nc.sync.dma_start(out=w3_w[1][:].bitcast(I32), in_=w3_bytes[:, 2 * H :].bitcast(I32))
+        load_w4(0)
+        rel_sb = [placed([RUN], F32, "rel%d" % a, AT_REL[a]) for a in range(TILES)]
         by_tile = rel.rearrange("(g b t e) -> g t b e", g=GROUPS, t=PACK, e=RUN)
         for a in range(TILES):
             g, t = divmod(a, PACK)
-            nc.sync.dma_start(out=rel_sb[:, g, t, 0:1], in_=by_tile[g, t])
-        w3_s = placed([H], U8, "w3_s", AT_W3_PLANE)
-        deal_columns(nc.vector.tensor_copy, w3_s, w3_plane_in)
-        w1_q[0] = quantised(GROUP, "w1_0", rounded[0][:])
-        nc.gpsimd.tensor_scalar(
-            rounded[1][:].rearrange("p (t b e j) -> p b t e j", t=PACK, e=RUN, j=PACK),
-            w1_late[:].rearrange("p j (b t e) -> p b t e j", t=PACK, e=RUN),
-            1.0, 0.0, MULT, ADD,
-        )
-        load_w4(0)
-        make_q(0, ENTITY_CUTS[:1])
-        make_q(1, ENTITY_CUTS[:1])
-        make_q(0, ENTITY_CUTS[1:2])
-        make_q(1, ENTITY_CUTS[1:2])
+            nc.sync.dma_start(out=rel_sb[a][:, 0:1], in_=by_tile[g, t])
+        make_q(0, ENTITY_CUTS[:2])
+        make_q(1, [(0, BANK)])
         make_q(2, [(0, BANK)], nc.vector.tensor_copy)
-        make_q(3, [(0, BANK)])
-        for a in range(PACK):
+        make_q(0, [(BANK, S)])
+        make_q(3, [(0, BANK)], nc.vector.tensor_copy)
+        for a in range(1, PACK):
             make_q(a, [(BANK, S)])
-        heads = pick_heads(0)
-        w1_q[1] = quantised(GROUP, "w1_1", rounded[1][:], AT_W1_CODES)
+        pick_heads(0)
         for a in range(PACK):
             make_r(a)
-        diff = differences(0, heads)
-        load_w4(2)
-        gated_first = [placed([PAIRS], F32, "gated_first%d" % k, AT_GATED + 4 * PAIRS * k) for k in range(2)]
-        z_first = placed([PACK, PAIRS], F32, "z_first", AT_Z)
-        for pair in range(2):
-            make_h(2 * pair)
-            if pair == 1:
-                deal_columns(nc.scalar.copy, w2_w[1], w2_in[1], groups=1)
-                deal_columns(nc.scalar.copy, w3_w[1], w3_in[1], groups=1)
-            make_h(2 * pair + 1)
-            gates_of_pair(0, pair, diff)
-            gated_heads(0, pair, 0, PAIRS, lambda t: gated_first[t % 2][:])
-            times_tails(0, (2 * pair, 2 * pair + 1), 0, PAIRS, lambda t: gated_first[t % 2][:], lambda t: z_first[:, t, :])
-        weighed = placed([PACK, PAIRS], F32, "weighed", AT_WEIGHED)
-        for t in range(PACK):
-            nc.gpsimd.tensor_scalar(weighed[:, t, :], z_first[:, t, :], rel_sb[:, 0, t, 0:1], 0.0, MULT, ADD)
-        load_w4(1)
-
+        w1_q[0] = quantised(GROUP, "w1_0", w1_rounded[0][:])
+        round_w1(1)
+        pick_tails(0)
         for a in range(PACK, TILES):
             make_q(a)
-        heads = pick_heads(1)
-        for a in range(PACK, TILES):
-            make_r(a)
-        diff = differences(1, heads)
-
-        def weave_first_z(half, copy):
-            woven = own([PACK * HALF], BF16, "z_woven_half%d" % half)
-            copy(*weaving(woven[:], weighed[:, :, HALF * half : HALF * (half + 1)]))
-            return woven
-
-        first_woven = [weave_first_z(0, nc.vector.tensor_copy)]
-        first_block = round_w4(0, nc.scalar.copy)
+        w1_q[1] = quantised(GROUP, "w1_1", w1_rounded[1][:])
+        round_w4(0)
+        load_w4(1)
+        pick_heads(1)
+        for t in range(PACK):
+            turned_gates(t)
+            make_r(PACK + t)
+        quantise_w4(0)
+        round_w4(1)
+        load_w4(2)
+        pick_tails(1)
+        quantise_w4(1)
         load_w4(3)
+        make_h(0)
+        make_h(1)
+        turn_back(0, 0)
+        weighed_gate(0)
+        weighed_gate(1)
+        for t in (0, 1):
+            turned_gates(PACK + t)
+            make_h(2 + t)
+        turn_back(0, 1)
+        weighed_gate(2)
+        weighed_gate(3)
+        gated_first = [placed([PAIRS], F32, "gated_first%d" % k, AT_GATED_FIRST + 4 * PAIRS * (1 - k)) for k in range(2)]
+        z_first = placed([PACK, PAIRS], F32, "z_first", AT_Z)
         for pair in range(2):
-            make_h(PACK + 2 * pair)
-            make_h(PACK + 2 * pair + 1)
-            gates_of_pair(1, pair, diff)
-        later_blocks = [round_w4(number, nc.scalar.copy) for number in range(1, len(w4_blocks))]
-        first_woven.append(weave_first_z(1, nc.scalar.copy))
+            for t in (2 * pair, 2 * pair + 1):
+                gated_heads(t, 0, PAIRS, gated_first[t % 2][:])
+            for t in (2 * pair, 2 * pair + 1):
+                times_tails(t, 0, PAIRS, gated_first[t % 2][:], z_first[:, t, :])
+        turned_gates(6)
+        turned_gates(7)
+        make_h(4)
+        make_h(5)
+        turn_back(1, 0)
+        weighed_gate(4)
+        weighed_gate(5)
+        make_h(6)
+        make_h(7)
+        turn_back(1, 1)
+        weighed_gate(6)
+        weighed_gate(7)
+
+        first_woven = [
+            own([PACK * HALF], BF16, "first_woven0"),
+            placed([PACK * P], BF16, "first_woven1", AT_FIRST_WOVEN),
+            own([PACK * P], BF16, "first_woven2"),
+        ]
+
+        def weave_first_z(piece, copy):
+            lo = sum(PIECES[:piece])
+            copy(*weaving(first_woven[piece][:], z_first[:, :, lo : lo + PIECES[piece]]))
+
+        round_w4(2)
+        weave_first_z(0, nc.scalar.copy)
+        round_w4(3)
 
         edges = [sum(PIECES[:k]) for k in range(len(PIECES) + 1)]
         spans = list(zip(edges[:-1], edges[1:]))
         last = len(PIECES) - 1
         y_scales = own([GROUPS * PAIRS], U8, "y_scales")
         y_codes = placed([GROUPS * PAIRS], U32, "y_codes", AT_Y_CODES)
-        y_woven, gated, z, z_woven = {}, {}, {}, {}
+        y_woven, gated, z, z_woven, sums, y = {}, {}, {}, {}, {}, {}
+
+        def piece_heads(piece, places):
+            lo, hi = spans[piece]
+            if piece not in gated:
+                gated[piece] = [
+                    placed([2, hi - lo], F32, "gated%d_%d" % (piece, pair), at) for pair, at in enumerate(AT_GATED_PIECE[piece])
+                ]
+                z[piece] = placed([PACK, hi - lo], F32, "z_piece%d" % piece, AT_Z_PIECE[piece])
+            for t in places:
+                gated_heads(PACK + t, lo, hi, gated[piece][t // 2][:, t % 2, :])
 
         def piece_tails(piece, places):
-            times_tails(1, places, *spans[piece], lambda t: gated[piece][:, t, :], lambda t: z[piece][:, t, :])
-
-        def piece_heads(piece, pair):
-            lo, hi = spans[piece]
-            if pair == 0:
-                gated[piece] = placed([PACK, hi - lo], F32, "gated_piece%d" % piece, AT_GATED_PIECE[piece])
-                z[piece] = placed([PACK, hi - lo], F32, "z_piece%d" % piece, AT_Z_PIECE[piece])
-            gated_heads(1, pair, lo, hi, lambda t: gated[piece][:, t, :])
-
-        def piece_products(piece, pair):
-            piece_heads(piece, pair)
-            piece_tails(piece, (2 * pair, 2 * pair + 1))
+            for t in places:
+                times_tails(PACK + t, *spans[piece], gated[piece][t // 2][:, t % 2, :], z[piece][:, t, :])
 
         def weave_piece(piece):
             lo, hi = spans[piece]
-            z_woven[piece] = own([PACK * (hi - lo)], BF16, "z_woven%d" % piece)
-            weigh_and_weave(1, z[piece][:], z_woven[piece])
+            z_woven[piece] = placed([PACK * (hi - lo)], BF16, "z_woven%d" % piece, AT_Z_WOVEN[piece])
+            nc.vector.tensor_copy(*weaving(z_woven[piece][:], z[piece][:]))
 
         def quantise_piece(piece):
             quantise_z(1, *spans[piece], z_woven[piece][:])
@@ -391,62 +409,77 @@ def tile_list_triple_pair_rerank_kernel(
                 in_=y_woven[piece, g][:],
             )
 
-        def results(piece):
+        def close_sums(piece):
             lo, hi = spans[piece]
             for g in range(GROUPS):
-                place = GROUPS * lo + g * (hi - lo)
-                at = AT_R + 4 * PACK * place
-                if piece == last and g == GROUPS - 1:
-                    at = AT_HEADS[1] + 2 * PACK * GROUPS * edges[last - 1]
-                y = placed([PACK, hi - lo], F32, "y%d_%d" % (piece, g), at)
-                y_woven[piece, g] = placed([PACK * (hi - lo)], BF16, "y_woven%d_%d" % (piece, g), AT_HEADS[1] + 2 * PACK * place)
                 for col in range(lo, hi, P):
                     second_passes(0, g, col)
-                    acc = second_passes(1, g, col)
-                    at = col - lo
-                    into = y_woven[piece, g][:, PACK * at : PACK * (at + P)]
-                    if piece == last and g == GROUPS - 1:
-                        nc.vector.tensor_copy(out=y[:], in_=acc)
-                        nc.vector.tensor_copy(*weaving(into, y[:]))
-                    else:
-                        nc.scalar.copy(out=y[:, :, at : at + P], in_=acc)
-                        nc.scalar.copy(*weaving(into, acc))
-                rows = out_0[GROUP * g : GROUP * (g + 1), lo:hi].rearrange("(p t) i -> p t i", t=PACK)
-                nc.sync.dma_start(out=rows, in_=y[:])
+                    sums[g, col] = second_passes(1, g, col)
+
+        def store_values(piece, g, copy=nc.scalar.copy, at=None):
+            lo, hi = spans[piece]
+            place = GROUPS * lo + g * (hi - lo)
+            at = AT_Y + 4 * PACK * place if at is None else at
+            y[piece, g] = placed([PACK, hi - lo], F32, "y%d_%d" % (piece, g), at)
+            for col in range(lo, hi, P):
+                copy(out=y[piece, g][:, :, col - lo : col - lo + P], in_=sums[g, col])
+            rows = out_0[GROUP * g : GROUP * (g + 1), lo:hi].rearrange("(p t) i -> p t i", t=PACK)
+            nc.sync.dma_start(out=rows, in_=y[piece, g][:])
+
+        def weave_results(piece, g, copy, from_bank, cols=None):
+            lo, hi = spans[piece]
+            if (piece, g) not in y_woven:
+                at = AT_Y_WOVEN + 2 * PACK * (GROUPS * lo + g * (hi - lo))
+                y_woven[piece, g] = placed([PACK * (hi - lo)], BF16, "y_woven%d_%d" % (piece, g), at)
+            for col in cols or range(lo, hi, P):
+                rows = sums[g, col] if from_bank else y[piece, g][:, :, col - lo : col - lo + P]
+                copy(*weaving(y_woven[piece, g][:, PACK * (col - lo) : PACK * (col - lo + P)], rows))
 
         words = out_1.rearrange("g p i t -> p g (i t)").bitcast(I32)
         codes = y_codes[:].bitcast(I32).rearrange("p (g i) -> p g i", g=GROUPS)
-        piece_products(0, 0)
-        quantise_z(0, 0, HALF, first_woven[0][:], AT_DIFF)
-        piece_products(0, 1)
-        quantise_w4(0, first_block, AT_DIFF + ROW)
+        piece_heads(0, (0, 1))
+        piece_tails(0, (0, 1))
+        piece_heads(0, (2, 3))
+        piece_tails(0, (2, 3))
+        quantise_w4(2)
         weave_piece(0)
-        quantise_w4(1, later_blocks[0])
+        quantise_z(0, 0, HALF, first_woven[0][:], AT_Z_CODES[0])
         quantise_piece(0)
-        quantise_w4(2, later_blocks[1])
-        quantise_w4(3, later_blocks[2])
-        piece_products(1, 0)
-        piece_products(1, 1)
-        quantise_z(0, edges[1], edges[2], first_woven[1][:, : PACK * P], AT_Z_CODES_MIDDLE)
+        piece_heads(1, range(PACK))
+        piece_tails(1, range(PACK))
+        quantise_w4(3)
         weave_piece(1)
+        weave_first_z(1, nc.vector.tensor_copy)
         quantise_piece(1)
-        results(0)
-        piece_products(2, 0)
-        piece_heads(2, 1)
-        piece_tails(2, (2,))
-        quantise_z(0, edges[2], PAIRS, first_woven[1][:, PACK * P :], AT_Z_CODES_LAST)
-        piece_tails(2, (3,))
-        quantise_results(0, 0)
+        quantise_z(0, edges[1], edges[2], first_woven[1][:])
+        close_sums(0)
+        store_values(0, 0)
+        weave_first_z(2, nc.scalar.copy)
+        weave_results(0, 0, nc.scalar.copy, True)
+        store_values(0, 1)
+        weave_results(0, 1, nc.scalar.copy, True)
+        piece_heads(2, range(PACK))
+        piece_tails(2, range(PACK))
+        quantise_z(0, edges[2], PAIRS, first_woven[2][:], AT_Z_CODES[2])
         weave_piece(2)
-        quantise_results(0, 1)
+        quantise_results(0, 0)
         quantise_piece(2)
-        results(1)
+        close_sums(1)
         for g in range(GROUPS):
-            quantise_results(1, g)
+            store_values(1, g)
+        quantise_results(0, 1)
+        weave_results(1, 0, nc.scalar.copy, True)
+        weave_results(1, 1, nc.vector.tensor_copy, False)
+        quantise_results(1, 0)
+        quantise_results(1, 1)
         nc.sync.dma_start(out=words[:, :, : edges[last]], in_=codes[:, :, : edges[last]])
-        results(last)
-        for g in range(GROUPS):
-            quantise_results(last, g)
+        close_sums(last)
+        store_values(last, 0)
+        weave_results(last, 0, nc.scalar.copy, True)
+        store_values(last, 1, nc.vector.tensor_copy, AT_Y_WOVEN + 2 * PACK * (GROUPS * edges[1] - P))
+        weave_results(last, 1, nc.vector.tensor_copy, False)
+        quantise_results(last, 0)
+        quantise_results(last, 1)
         nc.sync.dma_start(out=words[:, :, edges[last] :], in_=codes[:, :, edges[last] :])
         plane = y_scales[:].rearrange("p (g i) -> p g i", g=GROUPS)
         for k in range(QUADS):

@@ -26,7 +26,7 @@ GROUPS = 2
 TILES = H // P
 BANK = 512
 BANKS = 8
-RING = 4
+RING = 6
 LIST_ROWS = 16
 SCALE_ROWS = 112
 RUN = 8
@@ -40,39 +40,48 @@ ENTITY_CUTS = ((0, 256), (256, 512), (512, 1024))
 
 ROW = 4 * S
 STAGE = 2 * ROW
-AT_TABLE = ALIGN
-AT_W4_FIRST = AT_TABLE
-AT_TAILS_LATE = AT_W4_FIRST + STAGE - ALIGN
-AT_W4_THIRD = 0
-AT_TAILS_EARLY = AT_TABLE + 4 * T
-AT_W1_EARLY = AT_TAILS_EARLY + STAGE - ALIGN
+AT_TABLE = 0
+AT_W1_EARLY = AT_TABLE + 4 * T
+AT_W4_FIRST = AT_W1_EARLY + ALIGN - STAGE
 AT_W3_LATE = AT_W1_EARLY + ALIGN
 AT_REL_ROW = AT_W3_LATE + 2 * H
-AT_GATED_PAIR = (AT_REL_ROW + TILES * ALIGN, AT_REL_ROW + TILES * ALIGN + ROW // 2)
-AT_REL = tuple({5: AT_GATED_PAIR[0], 7: AT_GATED_PAIR[1]}.get(a, AT_REL_ROW + ALIGN * a) for a in range(TILES))
+REL_BYTES = 2 * ALIGN
+AT_GATED_PAIR = (AT_REL_ROW + TILES * REL_BYTES, AT_REL_ROW + TILES * REL_BYTES + ROW // 2)
+AT_REL = tuple(
+    {5: AT_GATED_PAIR[0], 7: AT_GATED_PAIR[1] + ROW // 2 - ALIGN}.get(a, AT_REL_ROW + REL_BYTES * a)
+    for a in range(TILES)
+)
 AT_TABLE_SCALES = AT_W1_EARLY + STAGE - ALIGN
 AT_W3_EARLY = AT_W1_EARLY + STAGE
-AT_W2_LATE = AT_W3_EARLY + 2 * H
-AT_GATED_FIRST = AT_TABLE_SCALES + T
-AT_W1_LATE = AT_GATED_FIRST + ROW
-AT_PICKED_SCALES = AT_W1_LATE - S + ALIGN
-AT_W4_SECOND = AT_W1_LATE - ALIGN
-AT_W4_FOURTH = AT_W1_LATE
-AT_HEADS_LATE = AT_W1_LATE + STAGE - ALIGN
-AT_ROUNDED = AT_HEADS_LATE + STAGE
-AT_QR = AT_ROUNDED + PACK * ROW
+AT_W4_SECOND = AT_W3_EARLY + 2 * H - ALIGN
+AT_W2_LATE = AT_W4_SECOND + STAGE
+AT_PICKED_SCALES = AT_W2_LATE + H - ALIGN
+AT_W1_LATE = AT_PICKED_SCALES + S - ALIGN
+AT_W1_SCALES = AT_W1_LATE
+AT_TAILS_HELD = AT_W1_SCALES + GROUP
+AT_W4_THIRD = AT_W1_LATE + STAGE - ALIGN
+AT_W1_ROUNDED = AT_W4_THIRD + STAGE
+AT_QR = AT_W1_ROUNDED + 3 * ROW
 AT_H = AT_QR
 AT_Y = AT_QR + PACK * STAGE
 AT_Y_WOVEN = AT_Y + 2 * STAGE
 AT_TURNED = AT_QR + TILES * STAGE
-AT_Z = AT_TURNED + STAGE
+AT_Z = AT_TURNED + GROUPS * STAGE
+AT_W4_FOURTH = AT_W4_THIRD
 AT_W4_STAGE = (AT_W4_FIRST, AT_W4_SECOND, AT_W4_THIRD, AT_W4_FOURTH)
-AT_W4_ROUNDED = (AT_ROUNDED + 2 * (ROW - ALIGN), AT_ROUNDED + 3 * (ROW - ALIGN), AT_H + 3 * ROW, AT_H + 2 * ROW)
-AT_GATED_PIECE = (AT_GATED_PAIR, (AT_W4_THIRD, AT_W4_THIRD + ROW // 4), (AT_W4_FOURTH + ROW, AT_W4_FOURTH + ROW + ROW // 4))
-AT_Z_PIECE = (AT_H, AT_H + ROW, AT_Z)
-AT_Z_WOVEN = (AT_W4_THIRD + ROW // 2, AT_W4_FOURTH, AT_TURNED)
-AT_FIRST_WOVEN = AT_W4_FOURTH + ROW // 4
-AT_Z_CODES = (AT_TURNED + ROW, AT_GATED_PAIR[1], AT_H + 6 * ROW)
+AT_W4_ROUNDED = (AT_W1_ROUNDED + 2 * ROW - ALIGN, AT_W4_FIRST, AT_W4_SECOND, AT_TURNED + STAGE)
+QUARTER = ROW // 4
+AT_GATED_PIECE = (
+    AT_GATED_PAIR,
+    (AT_GATED_PAIR[1], AT_GATED_PAIR[1] + QUARTER),
+    (AT_W4_FOURTH + ROW, AT_W4_FOURTH + ROW + QUARTER),
+)
+AT_Z_PIECE = (AT_H, AT_W4_FOURTH, AT_Z)
+AT_W4_CODES = (AT_QR + 7 * STAGE, AT_QR + 7 * STAGE + 4 * GROUP, AT_Z_PIECE[0], None)
+AT_Z_WOVEN = (AT_TURNED + ROW // 2, AT_TURNED + ROW, AT_TURNED)
+AT_FIRST_WOVEN = tuple(AT_TURNED + STAGE + ROW + QUARTER * k for k in (0, 2, 3))
+AT_Z_CODES_SECOND = AT_GATED_PAIR[1]
+AT_Z_CODES_LAST = AT_H + 6 * ROW
 AT_Y_CODES = AT_H + 7 * ROW
 
 
@@ -142,8 +151,8 @@ def tile_list_triple_pair_rerank_kernel(
         w1_stage = [placed([PACK, GROUP], F32, "w1_stage%d" % g, at) for g, at in enumerate((AT_W1_EARLY, AT_W1_LATE))]
         nc.sync.dma_start(out=w1_stage[0][:], in_=w1_rows[:, :, :GROUP])
         nc.sync.dma_start(out=w3_w[0][:].bitcast(I32), in_=w3_bytes[:, : 2 * H].bitcast(I32))
-        nc.sync.dma_start(out=w2_w[1][:].bitcast(I32), in_=w2_words[0][:, H:].bitcast(I32))
         nc.sync.dma_start(out=w1_stage[1][:], in_=w1_rows[:, :, GROUP:])
+        nc.sync.dma_start(out=w2_w[1][:].bitcast(I32), in_=w2_words[0][:, H:].bitcast(I32))
         for quad in range(QUADS):
             rows = slice(32 * quad, 32 * quad + QUADS)
             nc.vector.tensor_copy(out=w2_s[rows, :].bitcast(I32), in_=w2_plane_in[rows, :].bitcast(I32))
@@ -163,14 +172,14 @@ def tile_list_triple_pair_rerank_kernel(
             for j in range(PACK):
                 nc.sync.dma_start(out=w4_stage[number][:, j, :], in_=by_place[j])
 
-        def quantised(width, name, woven, at=None):
+        def quantised(width, name, woven, at=None, scales_at=None):
             codes = own([width], U32, name + "_codes") if at is None else placed([width], U32, name + "_codes", at)
-            scales = own([width], U8, name + "_scales")
+            scales = own([width], U8, name + "_scales") if scales_at is None else placed([width], U8, name + "_scales", scales_at)
             nc.vector.quantize_mx(out=codes[:].bitcast(FP8X4), scales=scales[:], in_=woven)
             return codes, scales
 
         def round_w1(g):
-            w1_rounded[g] = placed([PACK * GROUP], BF16, "w1_rounded%d" % g, AT_ROUNDED + g * (ROW - ALIGN))
+            w1_rounded[g] = placed([PACK * GROUP], BF16, "w1_rounded%d" % g, AT_W1_ROUNDED + g * ROW)
             nc.gpsimd.tensor_scalar(
                 w1_rounded[g][:].rearrange("p (t b e j) -> p b t e j", t=PACK, e=RUN, j=PACK),
                 w1_stage[g][:].rearrange("p j (b t e) -> p b t e j", t=PACK, e=RUN),
@@ -179,7 +188,7 @@ def tile_list_triple_pair_rerank_kernel(
 
         def round_w4(number):
             w4_rounded[number] = placed([PACK * GROUP], BF16, "w4_rounded%d" % number, AT_W4_ROUNDED[number])
-            if number < GROUPS:
+            if number < len(w4_blocks) - 1:
                 nc.gpsimd.tensor_scalar(
                     w4_rounded[number][:].rearrange("p (t m j) -> p m t j", t=PACK, j=PACK),
                     w4_stage[number][:].rearrange("p j (m t) -> p m t j", t=PACK),
@@ -192,7 +201,8 @@ def tile_list_triple_pair_rerank_kernel(
                 )
 
         def quantise_w4(number):
-            w4_q[w4_blocks[number]] = quantised(GROUP, "w4_%d" % number, w4_rounded[number][:])
+            at = AT_W4_CODES[number]
+            w4_q[w4_blocks[number]] = quantised(GROUP, "w4_%d" % number, w4_rounded[number][:], at)
 
         def first_stage(rows, codes, scales, cuts=((0, BANK), (BANK, S)), copy=nc.scalar.copy):
             for lo, hi in cuts:
@@ -223,40 +233,44 @@ def tile_list_triple_pair_rerank_kernel(
             h[a] = placed([S], F32, "h%d" % a, AT_H + ROW * a)
             first_stage(h[a], codes[:, P * t : P * (t + 1)].bitcast(FP8X4), scales[:, P * t : P * (t + 1)])
 
-        heads = [own([PACK, PAIRS], F32, "heads0"), placed([PACK, PAIRS], F32, "heads1", AT_HEADS_LATE)]
-        tails = [placed([PACK, PAIRS], F32, "tails%d" % g, at) for g, at in enumerate((AT_TAILS_EARLY, AT_TAILS_LATE))]
-        turned = [placed([PACK, GROUP], F32, "turned%d" % g, AT_TURNED) for g in range(GROUPS)]
+        heads = [
+            placed([PAIRS], F32, "heads%d" % a, AT_TAILS_HELD + ROW) if a == PACK else own([PAIRS], F32, "heads%d" % a)
+            for a in range(TILES)
+        ]
+        tails = [
+            placed([PAIRS], F32, "tails%d" % a, AT_TAILS_HELD + 4 * PAIRS * (a - 2)) if a in (2, 3) else own([PAIRS], F32, "tails%d" % a)
+            for a in range(TILES)
+        ]
+        turned = [placed([PACK, GROUP], F32, "turned%d" % g, AT_TURNED + STAGE * g) for g in range(GROUPS)]
 
-        def pick_heads(g):
-            for t in range(PACK):
-                nc.vector.tensor_copy(heads[g][:, t, :], qr[PACK * g + t][:, S:].indirect(pos1_sb[:]))
+        def pick_heads(tiles):
+            for a in tiles:
+                nc.vector.tensor_copy(heads[a][:], qr[a][:, S:].indirect(pos1_sb[:]))
 
-        def pick_tails(g):
-            for t in range(PACK):
-                nc.vector.tensor_scalar(tails[g][:, t, :], qr[PACK * g + t][:].indirect(pos2_sb[:]), -1.0, 0.0, MULT, ADD)
+        def pick_tails(tiles):
+            for a in tiles:
+                nc.vector.tensor_scalar(tails[a][:], qr[a][:].indirect(pos2_sb[:]), -1.0, 0.0, MULT, ADD)
 
         def turned_gates(a):
             g, t = divmod(a, PACK)
             acc = next_bank()
             for run in range(PACK):
                 cols = slice(P * run, P * (run + 1))
-                nc.tensor.matmul(acc[:, cols], heads[g][:, t, cols], ident[:], start=True, stop=False, is_transpose=True)
-                nc.tensor.matmul(acc[:, cols], tails[g][:, t, cols], ident[:], start=False, stop=True, is_transpose=True)
+                nc.tensor.matmul(acc[:, cols], heads[a][:, cols], ident[:], start=True, stop=False, is_transpose=True)
+                nc.tensor.matmul(acc[:, cols], tails[a][:, cols], ident[:], start=False, stop=True, is_transpose=True)
             nc.scalar.activation(
                 out=turned[g][:].rearrange("p run (t a b e) -> p a t run b e", t=PACK, a=PACK, e=RUN)[:, t],
                 in_=acc[:].rearrange("p (run b t e) -> p t run b e", run=PACK, t=PACK, e=RUN),
                 func=SIGMOID,
             )
 
-        def turn_back(g, pair):
-            for t in (2 * pair, 2 * pair + 1):
-                for run in range(PACK):
-                    nc.tensor.transpose(banks[RING + t][:, P * run : P * (run + 1)], turned[g][:, run, P * t : P * (t + 1)], ident[:])
-
         def weighed_gate(a):
             g, t = divmod(a, PACK)
+            acc = next_bank()
+            for run in range(PACK):
+                nc.tensor.transpose(acc[:, P * run : P * (run + 1)], turned[g][:, run, P * t : P * (t + 1)], ident[:])
             gate[a] = own([PAIRS], F32, "gate%d" % a)
-            nc.scalar.activation(out=gate[a][:], in_=banks[RING + t][:], func=COPY, scale=rel_sb[a][:, 0:1])
+            nc.scalar.activation(out=gate[a][:], in_=acc[:], func=COPY, scale=rel_sb[a][:, 0:1])
 
         def gated_heads(a, lo, hi, into):
             entries = pos1_sb[:, lo // LIST_ROWS : hi // LIST_ROWS]
@@ -292,9 +306,11 @@ def tile_list_triple_pair_rerank_kernel(
             return acc
 
         round_w1(0)
-        nc.sync.dma_start(out=w3_w[1][:].bitcast(I32), in_=w3_bytes[:, 2 * H :].bitcast(I32))
+        round_w1(1)
         load_w4(0)
-        rel_sb = [placed([RUN], F32, "rel%d" % a, AT_REL[a]) for a in range(TILES)]
+        nc.sync.dma_start(out=w3_w[1][:].bitcast(I32), in_=w3_bytes[:, 2 * H :].bitcast(I32))
+        load_w4(1)
+        rel_sb = [placed([REL_BYTES // 4], F32, "rel%d" % a, AT_REL[a]) for a in range(TILES)]
         by_tile = rel.rearrange("(g b t e) -> g t b e", g=GROUPS, t=PACK, e=RUN)
         for a in range(TILES):
             g, t = divmod(a, PACK)
@@ -306,71 +322,59 @@ def tile_list_triple_pair_rerank_kernel(
         make_q(3, [(0, BANK)], nc.vector.tensor_copy)
         for a in range(1, PACK):
             make_q(a, [(BANK, S)])
-        pick_heads(0)
+        pick_heads(range(PACK))
         for a in range(PACK):
             make_r(a)
-        w1_q[0] = quantised(GROUP, "w1_0", w1_rounded[0][:])
-        round_w1(1)
-        pick_tails(0)
+        pick_tails((0, 1))
+        w1_q[0] = quantised(GROUP, "w1_0", w1_rounded[0][:], None, AT_W1_SCALES)
+        w1_q[1] = quantised(GROUP, "w1_1", w1_rounded[1][:])
+        load_w4(2)
+        for number in range(len(w4_blocks) - 1):
+            round_w4(number)
+        load_w4(3)
+        pick_tails((2, 3))
         for a in range(PACK, TILES):
             make_q(a)
-        w1_q[1] = quantised(GROUP, "w1_1", w1_rounded[1][:])
-        round_w4(0)
-        load_w4(1)
-        pick_heads(1)
+        pick_heads(range(PACK, TILES))
         for t in range(PACK):
             turned_gates(t)
             make_r(PACK + t)
-        quantise_w4(0)
-        round_w4(1)
-        load_w4(2)
-        pick_tails(1)
-        quantise_w4(1)
-        load_w4(3)
-        make_h(0)
-        make_h(1)
-        turn_back(0, 0)
-        weighed_gate(0)
-        weighed_gate(1)
-        for t in (0, 1):
-            turned_gates(PACK + t)
-            make_h(2 + t)
-        turn_back(0, 1)
-        weighed_gate(2)
-        weighed_gate(3)
-        gated_first = [placed([PAIRS], F32, "gated_first%d" % k, AT_GATED_FIRST + 4 * PAIRS * (1 - k)) for k in range(2)]
+        pick_tails(range(PACK, TILES))
+        for number in range(GROUPS):
+            quantise_w4(number)
+
+        def rows_and_gates(pair, turned_before=(None, None)):
+            for a, other in zip((2 * pair, 2 * pair + 1), turned_before):
+                if other is not None:
+                    turned_gates(other)
+                make_h(a)
+            for a in (2 * pair, 2 * pair + 1):
+                weighed_gate(a)
+
+        rows_and_gates(0)
+        rows_and_gates(1, (4, 5))
+        gated_first = [own([PAIRS], F32, "gated_first%d" % k) for k in range(2)]
         z_first = placed([PACK, PAIRS], F32, "z_first", AT_Z)
         for pair in range(2):
             for t in (2 * pair, 2 * pair + 1):
                 gated_heads(t, 0, PAIRS, gated_first[t % 2][:])
             for t in (2 * pair, 2 * pair + 1):
                 times_tails(t, 0, PAIRS, gated_first[t % 2][:], z_first[:, t, :])
-        turned_gates(6)
-        turned_gates(7)
-        make_h(4)
-        make_h(5)
-        turn_back(1, 0)
-        weighed_gate(4)
-        weighed_gate(5)
-        make_h(6)
-        make_h(7)
-        turn_back(1, 1)
-        weighed_gate(6)
-        weighed_gate(7)
+        rows_and_gates(2, (6, 7))
+        rows_and_gates(3)
 
         first_woven = [
-            own([PACK * HALF], BF16, "first_woven0"),
-            placed([PACK * P], BF16, "first_woven1", AT_FIRST_WOVEN),
-            own([PACK * P], BF16, "first_woven2"),
+            placed([PACK * width], BF16, "first_woven%d" % piece, AT_FIRST_WOVEN[piece]) for piece, width in enumerate(PIECES)
         ]
 
-        def weave_first_z(piece, copy):
+        def weave_first_z(piece):
             lo = sum(PIECES[:piece])
-            copy(*weaving(first_woven[piece][:], z_first[:, :, lo : lo + PIECES[piece]]))
+            nc.scalar.copy(*weaving(first_woven[piece][:], z_first[:, :, lo : lo + PIECES[piece]]))
 
-        round_w4(2)
-        weave_first_z(0, nc.scalar.copy)
+        weave_first_z(0)
         round_w4(3)
+        weave_first_z(1)
+        weave_first_z(2)
 
         edges = [sum(PIECES[:k]) for k in range(len(PIECES) + 1)]
         spans = list(zip(edges[:-1], edges[1:]))
@@ -396,10 +400,13 @@ def tile_list_triple_pair_rerank_kernel(
         def weave_piece(piece):
             lo, hi = spans[piece]
             z_woven[piece] = placed([PACK * (hi - lo)], BF16, "z_woven%d" % piece, AT_Z_WOVEN[piece])
-            nc.vector.tensor_copy(*weaving(z_woven[piece][:], z[piece][:]))
+            for at in range(0, hi - lo, P):
+                nc.vector.tensor_copy(*weaving(z_woven[piece][:, PACK * at : PACK * (at + P)], z[piece][:, :, at : at + P]))
 
         def quantise_piece(piece):
-            quantise_z(1, *spans[piece], z_woven[piece][:])
+            lo, hi = spans[piece]
+            for at in range(0, hi - lo, P):
+                quantise_z(1, lo + at, lo + at + P, z_woven[piece][:, PACK * at : PACK * (at + P)])
 
         def quantise_results(piece, g):
             lo, hi = spans[piece]
@@ -435,32 +442,32 @@ def tile_list_triple_pair_rerank_kernel(
                 rows = sums[g, col] if from_bank else y[piece, g][:, :, col - lo : col - lo + P]
                 copy(*weaving(y_woven[piece, g][:, PACK * (col - lo) : PACK * (col - lo + P)], rows))
 
-        words = out_1.rearrange("g p i t -> p g (i t)").bitcast(I32)
-        codes = y_codes[:].bitcast(I32).rearrange("p (g i) -> p g i", g=GROUPS)
+        def store_codes(g, lo, hi):
+            words = out_1[g].rearrange("p i t -> p (i t)").bitcast(I32)
+            nc.sync.dma_start(out=words[:, lo:hi], in_=y_codes[:, PAIRS * g + lo : PAIRS * g + hi].bitcast(I32))
+
         piece_heads(0, (0, 1))
         piece_tails(0, (0, 1))
         piece_heads(0, (2, 3))
         piece_tails(0, (2, 3))
-        quantise_w4(2)
+        quantise_z(0, 0, HALF, first_woven[0][:])
         weave_piece(0)
-        quantise_z(0, 0, HALF, first_woven[0][:], AT_Z_CODES[0])
         quantise_piece(0)
+        quantise_w4(2)
         piece_heads(1, range(PACK))
-        piece_tails(1, range(PACK))
         quantise_w4(3)
+        piece_tails(1, range(PACK))
+        quantise_z(0, edges[1], edges[2], first_woven[1][:], AT_Z_CODES_SECOND)
         weave_piece(1)
-        weave_first_z(1, nc.vector.tensor_copy)
         quantise_piece(1)
-        quantise_z(0, edges[1], edges[2], first_woven[1][:])
         close_sums(0)
         store_values(0, 0)
-        weave_first_z(2, nc.scalar.copy)
         weave_results(0, 0, nc.scalar.copy, True)
         store_values(0, 1)
         weave_results(0, 1, nc.scalar.copy, True)
         piece_heads(2, range(PACK))
         piece_tails(2, range(PACK))
-        quantise_z(0, edges[2], PAIRS, first_woven[2][:], AT_Z_CODES[2])
+        quantise_z(0, edges[2], PAIRS, first_woven[2][:], AT_Z_CODES_LAST)
         weave_piece(2)
         quantise_results(0, 0)
         quantise_piece(2)
@@ -468,11 +475,11 @@ def tile_list_triple_pair_rerank_kernel(
         for g in range(GROUPS):
             store_values(1, g)
         quantise_results(0, 1)
-        weave_results(1, 0, nc.scalar.copy, True)
-        weave_results(1, 1, nc.vector.tensor_copy, False)
-        quantise_results(1, 0)
-        quantise_results(1, 1)
-        nc.sync.dma_start(out=words[:, :, : edges[last]], in_=codes[:, :, : edges[last]])
+        store_codes(1, 0, edges[1])
+        for g in range(GROUPS):
+            weave_results(1, g, nc.scalar.copy, True)
+            quantise_results(1, g)
+        store_codes(0, 0, edges[last])
         close_sums(last)
         store_values(last, 0)
         weave_results(last, 0, nc.scalar.copy, True)
@@ -480,7 +487,8 @@ def tile_list_triple_pair_rerank_kernel(
         weave_results(last, 1, nc.vector.tensor_copy, False)
         quantise_results(last, 0)
         quantise_results(last, 1)
-        nc.sync.dma_start(out=words[:, :, edges[last] :], in_=codes[:, :, edges[last] :])
+        store_codes(0, edges[last], PAIRS)
+        store_codes(1, edges[1], PAIRS)
         plane = y_scales[:].rearrange("p (g i) -> p g i", g=GROUPS)
         for k in range(QUADS):
             rows = out_2[:, k:BLOCKS:QUADS, :].rearrange("g row i -> row g i")

@@ -46,10 +46,11 @@ AT_W4_FIRST = AT_W1_EARLY + ALIGN - STAGE
 AT_W3_LATE = AT_W1_EARLY + ALIGN
 AT_REL_ROW = AT_W3_LATE + 2 * H
 REL_BYTES = 2 * ALIGN
-AT_GATED_PAIR = (AT_REL_ROW + TILES * REL_BYTES, AT_REL_ROW + TILES * REL_BYTES + ROW // 2)
-AT_REL = tuple(
-    {5: AT_GATED_PAIR[0], 7: AT_GATED_PAIR[1] + ROW // 2 - ALIGN}.get(a, AT_REL_ROW + REL_BYTES * a)
-    for a in range(TILES)
+AT_FIRST_WOVEN = AT_REL_ROW + 6 * REL_BYTES
+AT_GATED_PAIR = (AT_FIRST_WOVEN + ROW // 2, AT_FIRST_WOVEN + ROW)
+AT_Z_CODES_FIRST = AT_GATED_PAIR[1] + ROW // 2
+AT_REL = tuple(AT_REL_ROW + REL_BYTES * a for a in range(5)) + (
+    AT_GATED_PAIR[0] - ALIGN, AT_REL_ROW + 5 * REL_BYTES, AT_Z_CODES_FIRST - ALIGN,
 )
 AT_TABLE_SCALES = AT_W1_EARLY + STAGE - ALIGN
 AT_W3_EARLY = AT_W1_EARLY + STAGE
@@ -58,7 +59,7 @@ AT_W2_LATE = AT_W4_SECOND + STAGE
 AT_PICKED_SCALES = AT_W2_LATE + H - ALIGN
 AT_W1_LATE = AT_PICKED_SCALES + S - ALIGN
 AT_W1_SCALES = AT_W1_LATE
-AT_TAILS_HELD = AT_W1_SCALES + GROUP
+AT_HEADS_HELD = AT_W1_SCALES + GROUP
 AT_W4_THIRD = AT_W1_LATE + STAGE - ALIGN
 AT_W1_ROUNDED = AT_W4_THIRD + STAGE
 AT_QR = AT_W1_ROUNDED + 3 * ROW
@@ -66,10 +67,11 @@ AT_H = AT_QR
 AT_Y = AT_QR + PACK * STAGE
 AT_Y_WOVEN = AT_Y + 2 * STAGE
 AT_TURNED = AT_QR + TILES * STAGE
-AT_Z = AT_TURNED + GROUPS * STAGE
-AT_W4_FOURTH = AT_W4_THIRD
+AT_LATE = AT_TURNED + STAGE
+AT_Z = AT_LATE + STAGE
+AT_W4_FOURTH = AT_W4_SECOND
 AT_W4_STAGE = (AT_W4_FIRST, AT_W4_SECOND, AT_W4_THIRD, AT_W4_FOURTH)
-AT_W4_ROUNDED = (AT_W1_ROUNDED + 2 * ROW - ALIGN, AT_W4_FIRST, AT_W4_SECOND, AT_TURNED + STAGE)
+AT_W4_ROUNDED = (AT_W1_ROUNDED + 2 * ROW - ALIGN, AT_W4_FIRST, AT_LATE, AT_LATE + ROW)
 QUARTER = ROW // 4
 AT_GATED_PIECE = (
     AT_GATED_PAIR,
@@ -79,8 +81,8 @@ AT_GATED_PIECE = (
 AT_Z_PIECE = (AT_H, AT_W4_FOURTH, AT_Z)
 AT_W4_CODES = (AT_QR + 7 * STAGE, AT_QR + 7 * STAGE + 4 * GROUP, AT_Z_PIECE[0], None)
 AT_Z_WOVEN = (AT_TURNED + ROW // 2, AT_TURNED + ROW, AT_TURNED)
-AT_FIRST_WOVEN = tuple(AT_TURNED + STAGE + ROW + QUARTER * k for k in (0, 2, 3))
-AT_Z_CODES_SECOND = AT_GATED_PAIR[1]
+AT_FIRST_WOVEN_BY_PIECE = (AT_FIRST_WOVEN, AT_W4_THIRD, AT_W4_THIRD + QUARTER)
+AT_Z_CODES_SECOND = AT_GATED_PIECE[1][0]
 AT_Z_CODES_LAST = AT_H + 6 * ROW
 AT_Y_CODES = AT_H + 7 * ROW
 
@@ -188,7 +190,7 @@ def tile_list_triple_pair_rerank_kernel(
 
         def round_w4(number):
             w4_rounded[number] = placed([PACK * GROUP], BF16, "w4_rounded%d" % number, AT_W4_ROUNDED[number])
-            if number < len(w4_blocks) - 1:
+            if number < GROUPS:
                 nc.gpsimd.tensor_scalar(
                     w4_rounded[number][:].rearrange("p (t m j) -> p m t j", t=PACK, j=PACK),
                     w4_stage[number][:].rearrange("p j (m t) -> p m t j", t=PACK),
@@ -234,13 +236,10 @@ def tile_list_triple_pair_rerank_kernel(
             first_stage(h[a], codes[:, P * t : P * (t + 1)].bitcast(FP8X4), scales[:, P * t : P * (t + 1)])
 
         heads = [
-            placed([PAIRS], F32, "heads%d" % a, AT_TAILS_HELD + ROW) if a == PACK else own([PAIRS], F32, "heads%d" % a)
+            placed([PAIRS], F32, "heads%d" % a, AT_HEADS_HELD + 4 * PAIRS * (a - PACK)) if a in (PACK, PACK + 1) else own([PAIRS], F32, "heads%d" % a)
             for a in range(TILES)
         ]
-        tails = [
-            placed([PAIRS], F32, "tails%d" % a, AT_TAILS_HELD + 4 * PAIRS * (a - 2)) if a in (2, 3) else own([PAIRS], F32, "tails%d" % a)
-            for a in range(TILES)
-        ]
+        tails = [own([PAIRS], F32, "tails%d" % a) for a in range(TILES)]
         turned = [placed([PACK, GROUP], F32, "turned%d" % g, AT_TURNED + STAGE * g) for g in range(GROUPS)]
 
         def pick_heads(tiles):
@@ -325,14 +324,13 @@ def tile_list_triple_pair_rerank_kernel(
         pick_heads(range(PACK))
         for a in range(PACK):
             make_r(a)
-        pick_tails((0, 1))
+        pick_tails(range(PACK))
         w1_q[0] = quantised(GROUP, "w1_0", w1_rounded[0][:], None, AT_W1_SCALES)
         w1_q[1] = quantised(GROUP, "w1_1", w1_rounded[1][:])
         load_w4(2)
-        for number in range(len(w4_blocks) - 1):
+        for number in range(GROUPS):
             round_w4(number)
         load_w4(3)
-        pick_tails((2, 3))
         for a in range(PACK, TILES):
             make_q(a)
         pick_heads(range(PACK, TILES))
@@ -364,14 +362,14 @@ def tile_list_triple_pair_rerank_kernel(
         rows_and_gates(3)
 
         first_woven = [
-            placed([PACK * width], BF16, "first_woven%d" % piece, AT_FIRST_WOVEN[piece]) for piece, width in enumerate(PIECES)
+            placed([PACK * width], BF16, "first_woven%d" % piece, AT_FIRST_WOVEN_BY_PIECE[piece]) for piece, width in enumerate(PIECES)
         ]
 
-        def weave_first_z(piece):
+        def weave_first_z(piece, copy=nc.scalar.copy):
             lo = sum(PIECES[:piece])
-            nc.scalar.copy(*weaving(first_woven[piece][:], z_first[:, :, lo : lo + PIECES[piece]]))
+            copy(*weaving(first_woven[piece][:], z_first[:, :, lo : lo + PIECES[piece]]))
 
-        weave_first_z(0)
+        round_w4(2)
         round_w4(3)
         weave_first_z(1)
         weave_first_z(2)
@@ -442,15 +440,17 @@ def tile_list_triple_pair_rerank_kernel(
                 rows = sums[g, col] if from_bank else y[piece, g][:, :, col - lo : col - lo + P]
                 copy(*weaving(y_woven[piece, g][:, PACK * (col - lo) : PACK * (col - lo + P)], rows))
 
-        def store_codes(g, lo, hi):
-            words = out_1[g].rearrange("p i t -> p (i t)").bitcast(I32)
-            nc.sync.dma_start(out=words[:, lo:hi], in_=y_codes[:, PAIRS * g + lo : PAIRS * g + hi].bitcast(I32))
+        def store_codes(lo, hi):
+            words = out_1.rearrange("g p i t -> p g (i t)").bitcast(I32)
+            codes = y_codes[:].bitcast(I32).rearrange("p (g i) -> p g i", g=GROUPS)
+            nc.sync.dma_start(out=words[:, :, lo:hi], in_=codes[:, :, lo:hi])
 
         piece_heads(0, (0, 1))
         piece_tails(0, (0, 1))
+        weave_first_z(0, nc.vector.tensor_copy)
         piece_heads(0, (2, 3))
         piece_tails(0, (2, 3))
-        quantise_z(0, 0, HALF, first_woven[0][:])
+        quantise_z(0, 0, HALF, first_woven[0][:], AT_Z_CODES_FIRST)
         weave_piece(0)
         quantise_piece(0)
         quantise_w4(2)
@@ -464,7 +464,7 @@ def tile_list_triple_pair_rerank_kernel(
         store_values(0, 0)
         weave_results(0, 0, nc.scalar.copy, True)
         store_values(0, 1)
-        weave_results(0, 1, nc.scalar.copy, True)
+        weave_results(0, 1, nc.scalar.copy, True, [0])
         piece_heads(2, range(PACK))
         piece_tails(2, range(PACK))
         quantise_z(0, edges[2], PAIRS, first_woven[2][:], AT_Z_CODES_LAST)
@@ -474,12 +474,12 @@ def tile_list_triple_pair_rerank_kernel(
         close_sums(1)
         for g in range(GROUPS):
             store_values(1, g)
+        weave_results(0, 1, nc.scalar.copy, True, [P])
         quantise_results(0, 1)
-        store_codes(1, 0, edges[1])
+        store_codes(0, edges[1])
         for g in range(GROUPS):
             weave_results(1, g, nc.scalar.copy, True)
             quantise_results(1, g)
-        store_codes(0, 0, edges[last])
         close_sums(last)
         store_values(last, 0)
         weave_results(last, 0, nc.scalar.copy, True)
@@ -487,8 +487,7 @@ def tile_list_triple_pair_rerank_kernel(
         weave_results(last, 1, nc.vector.tensor_copy, False)
         quantise_results(last, 0)
         quantise_results(last, 1)
-        store_codes(0, edges[last], PAIRS)
-        store_codes(1, edges[1], PAIRS)
+        store_codes(edges[1], PAIRS)
         plane = y_scales[:].rearrange("p (g i) -> p g i", g=GROUPS)
         for k in range(QUADS):
             rows = out_2[:, k:BLOCKS:QUADS, :].rearrange("g row i -> row g i")

@@ -43,25 +43,24 @@ STAGE = 2 * ROW
 AT_TABLE = 0
 AT_W1_EARLY = AT_TABLE + 4 * T
 AT_W4_FIRST = AT_W1_EARLY + ALIGN - STAGE
-AT_W3_LATE = AT_W1_EARLY + ALIGN
-AT_REL_ROW = AT_W3_LATE + 2 * H
-REL_BYTES = 2 * ALIGN
-AT_FIRST_WOVEN = AT_REL_ROW + 6 * REL_BYTES
-AT_GATED_PAIR = (AT_FIRST_WOVEN + ROW // 2, AT_FIRST_WOVEN + ROW)
-AT_Z_CODES_FIRST = AT_GATED_PAIR[1] + ROW // 2
-AT_REL = tuple(AT_REL_ROW + REL_BYTES * a for a in range(5)) + (
-    AT_GATED_PAIR[0] - ALIGN, AT_REL_ROW + 5 * REL_BYTES, AT_Z_CODES_FIRST - ALIGN,
-)
+AT_W4_THIRD = AT_W4_FIRST + ROW
 AT_TABLE_SCALES = AT_W1_EARLY + STAGE - ALIGN
 AT_W3_EARLY = AT_W1_EARLY + STAGE
-AT_W4_SECOND = AT_W3_EARLY + 2 * H - ALIGN
-AT_W2_LATE = AT_W4_SECOND + STAGE
-AT_PICKED_SCALES = AT_W2_LATE + H - ALIGN
-AT_W1_LATE = AT_PICKED_SCALES + S - ALIGN
-AT_W1_SCALES = AT_W1_LATE
+AT_W3_LATE = AT_W3_EARLY + 2 * H
+AT_W4_SECOND = AT_W3_LATE + 2 * H
+AT_W1_LATE = AT_W4_SECOND + STAGE - ALIGN
+AT_PICKED_SCALES = AT_W1_LATE - S + ALIGN
+AT_W2_LATE = AT_PICKED_SCALES - H + ALIGN
+AT_W1_SCALES = AT_W1_LATE + ALIGN
 AT_HEADS_HELD = AT_W1_SCALES + GROUP
-AT_W4_THIRD = AT_W1_LATE + STAGE - ALIGN
-AT_W1_ROUNDED = AT_W4_THIRD + STAGE
+AT_GATED_PAIR = (AT_HEADS_HELD + ROW, AT_W1_LATE + STAGE - ALIGN)
+AT_FIRST_WOVEN = AT_GATED_PAIR[0] - ROW // 2
+AT_Z_CODES_FIRST = AT_GATED_PAIR[1] - ROW // 4
+AT_REL_ROW = AT_GATED_PAIR[0] + ROW // 2
+AT_REL = tuple(AT_REL_ROW + ALIGN * a for a in range(5)) + (
+    AT_GATED_PAIR[0] - ALIGN, AT_REL_ROW + 5 * ALIGN, AT_GATED_PAIR[1] - ALIGN,
+)
+AT_W1_ROUNDED = AT_GATED_PAIR[1] + ROW // 2
 AT_QR = AT_W1_ROUNDED + 3 * ROW
 AT_H = AT_QR
 AT_Y = AT_QR + PACK * STAGE
@@ -71,7 +70,7 @@ AT_LATE = AT_TURNED + STAGE
 AT_Z = AT_LATE + STAGE
 AT_W4_FOURTH = AT_W4_SECOND
 AT_W4_STAGE = (AT_W4_FIRST, AT_W4_SECOND, AT_W4_THIRD, AT_W4_FOURTH)
-AT_W4_ROUNDED = (AT_W1_ROUNDED + 2 * ROW - ALIGN, AT_W4_FIRST, AT_LATE, AT_LATE + ROW)
+AT_W4_ROUNDED = (AT_W1_ROUNDED + 2 * ROW - ALIGN, AT_W1_ROUNDED + ALIGN, AT_LATE, AT_LATE + ROW)
 QUARTER = ROW // 4
 AT_GATED_PIECE = (
     AT_GATED_PAIR,
@@ -153,6 +152,7 @@ def tile_list_triple_pair_rerank_kernel(
         w1_stage = [placed([PACK, GROUP], F32, "w1_stage%d" % g, at) for g, at in enumerate((AT_W1_EARLY, AT_W1_LATE))]
         nc.sync.dma_start(out=w1_stage[0][:], in_=w1_rows[:, :, :GROUP])
         nc.sync.dma_start(out=w3_w[0][:].bitcast(I32), in_=w3_bytes[:, : 2 * H].bitcast(I32))
+        nc.sync.dma_start(out=w3_w[1][:].bitcast(I32), in_=w3_bytes[:, 2 * H :].bitcast(I32))
         nc.sync.dma_start(out=w1_stage[1][:], in_=w1_rows[:, :, GROUP:])
         nc.sync.dma_start(out=w2_w[1][:].bitcast(I32), in_=w2_words[0][:, H:].bitcast(I32))
         for quad in range(QUADS):
@@ -307,13 +307,7 @@ def tile_list_triple_pair_rerank_kernel(
         round_w1(0)
         round_w1(1)
         load_w4(0)
-        nc.sync.dma_start(out=w3_w[1][:].bitcast(I32), in_=w3_bytes[:, 2 * H :].bitcast(I32))
         load_w4(1)
-        rel_sb = [placed([REL_BYTES // 4], F32, "rel%d" % a, AT_REL[a]) for a in range(TILES)]
-        by_tile = rel.rearrange("(g b t e) -> g t b e", g=GROUPS, t=PACK, e=RUN)
-        for a in range(TILES):
-            g, t = divmod(a, PACK)
-            nc.sync.dma_start(out=rel_sb[a][:, 0:1], in_=by_tile[g, t])
         make_q(0, ENTITY_CUTS[:2])
         make_q(1, [(0, BANK)])
         make_q(2, [(0, BANK)], nc.vector.tensor_copy)
@@ -334,6 +328,11 @@ def tile_list_triple_pair_rerank_kernel(
         for a in range(PACK, TILES):
             make_q(a)
         pick_heads(range(PACK, TILES))
+        rel_sb = [placed([ALIGN // (2 if a in (5, 7) else 4)], F32, "rel%d" % a, AT_REL[a]) for a in range(TILES)]
+        by_tile = rel.rearrange("(g b t e) -> g t b e", g=GROUPS, t=PACK, e=RUN)
+        for a in range(TILES):
+            g, t = divmod(a, PACK)
+            nc.sync.dma_start(out=rel_sb[a][:, 0:1], in_=by_tile[g, t])
         for t in range(PACK):
             turned_gates(t)
             make_r(PACK + t)

@@ -54,11 +54,14 @@ AT_W2_LATE = AT_PICKED_SCALES - H + ALIGN
 AT_W1_SCALES = AT_W1_LATE + ALIGN
 AT_HEADS_HELD = AT_W1_SCALES + GROUP
 AT_GATED_PAIR = (AT_HEADS_HELD + ROW, AT_W1_LATE + STAGE - ALIGN)
-AT_FIRST_WOVEN = AT_GATED_PAIR[0] - ROW // 2
 AT_Z_CODES_FIRST = AT_GATED_PAIR[1] - ROW // 4
 AT_REL_ROW = AT_GATED_PAIR[0] + ROW // 2
-AT_REL = tuple(AT_REL_ROW + ALIGN * a for a in range(5)) + (
-    AT_GATED_PAIR[0] - ALIGN, AT_REL_ROW + 5 * ALIGN, AT_GATED_PAIR[1] - ALIGN,
+AT_W4_CODES_EARLY = AT_W4_THIRD + STAGE
+AT_REL = tuple(
+    {1: AT_W4_CODES_EARLY + ROW // 2 - ALIGN, 5: AT_GATED_PAIR[0], 6: AT_REL_ROW + ALIGN, 7: AT_GATED_PAIR[1] - ALIGN}.get(
+        a, AT_REL_ROW + ALIGN * a
+    )
+    for a in range(TILES)
 )
 AT_W1_ROUNDED = AT_GATED_PAIR[1] + ROW // 2
 AT_QR = AT_W1_ROUNDED + 3 * ROW
@@ -66,7 +69,7 @@ AT_H = AT_QR
 AT_Y = AT_QR + PACK * STAGE
 AT_Y_WOVEN = AT_Y + 2 * STAGE
 AT_TURNED = AT_QR + TILES * STAGE
-AT_LATE = AT_TURNED + STAGE
+AT_LATE = AT_TURNED + STAGE + ALIGN
 AT_Z = AT_LATE + STAGE
 AT_W4_FOURTH = AT_W4_SECOND
 AT_W4_STAGE = (AT_W4_FIRST, AT_W4_SECOND, AT_W4_THIRD, AT_W4_FOURTH)
@@ -78,9 +81,9 @@ AT_GATED_PIECE = (
     (AT_W4_FOURTH + ROW, AT_W4_FOURTH + ROW + QUARTER),
 )
 AT_Z_PIECE = (AT_H, AT_W4_FOURTH, AT_Z)
-AT_W4_CODES = (AT_QR + 7 * STAGE, AT_QR + 7 * STAGE + 4 * GROUP, AT_Z_PIECE[0], None)
+AT_W4_CODES = (AT_W4_CODES_EARLY, AT_W4_CODES_EARLY + ROW // 2, AT_Z_PIECE[0], None)
 AT_Z_WOVEN = (AT_TURNED + ROW // 2, AT_TURNED + ROW, AT_TURNED)
-AT_FIRST_WOVEN_BY_PIECE = (AT_FIRST_WOVEN, AT_W4_THIRD, AT_W4_THIRD + QUARTER)
+AT_FIRST_WOVEN_BY_PIECE = (AT_LATE - ROW // 2, AT_W4_THIRD, AT_W4_THIRD + QUARTER)
 AT_Z_CODES_SECOND = AT_GATED_PIECE[1][0]
 AT_Z_CODES_LAST = AT_H + 6 * ROW
 AT_Y_CODES = AT_H + 7 * ROW
@@ -328,7 +331,7 @@ def tile_list_triple_pair_rerank_kernel(
         for a in range(PACK, TILES):
             make_q(a)
         pick_heads(range(PACK, TILES))
-        rel_sb = [placed([ALIGN // (2 if a in (5, 7) else 4)], F32, "rel%d" % a, AT_REL[a]) for a in range(TILES)]
+        rel_sb = [placed([ALIGN // (2 if a in (1, 7) else 4)], F32, "rel%d" % a, AT_REL[a]) for a in range(TILES)]
         by_tile = rel.rearrange("(g b t e) -> g t b e", g=GROUPS, t=PACK, e=RUN)
         for a in range(TILES):
             g, t = divmod(a, PACK)
@@ -337,8 +340,6 @@ def tile_list_triple_pair_rerank_kernel(
             turned_gates(t)
             make_r(PACK + t)
         pick_tails(range(PACK, TILES))
-        for number in range(GROUPS):
-            quantise_w4(number)
 
         def rows_and_gates(pair, turned_before=(None, None)):
             for a, other in zip((2 * pair, 2 * pair + 1), turned_before):
@@ -357,6 +358,8 @@ def tile_list_triple_pair_rerank_kernel(
                 gated_heads(t, 0, PAIRS, gated_first[t % 2][:])
             for t in (2 * pair, 2 * pair + 1):
                 times_tails(t, 0, PAIRS, gated_first[t % 2][:], z_first[:, t, :])
+        for number in range(GROUPS):
+            quantise_w4(number)
         rows_and_gates(2, (6, 7))
         rows_and_gates(3)
 
@@ -364,10 +367,11 @@ def tile_list_triple_pair_rerank_kernel(
             placed([PACK * width], BF16, "first_woven%d" % piece, AT_FIRST_WOVEN_BY_PIECE[piece]) for piece, width in enumerate(PIECES)
         ]
 
-        def weave_first_z(piece, copy=nc.scalar.copy):
+        def weave_first_z(piece):
             lo = sum(PIECES[:piece])
-            copy(*weaving(first_woven[piece][:], z_first[:, :, lo : lo + PIECES[piece]]))
+            nc.scalar.copy(*weaving(first_woven[piece][:], z_first[:, :, lo : lo + PIECES[piece]]))
 
+        weave_first_z(0)
         round_w4(2)
         round_w4(3)
         weave_first_z(1)
@@ -446,7 +450,6 @@ def tile_list_triple_pair_rerank_kernel(
 
         piece_heads(0, (0, 1))
         piece_tails(0, (0, 1))
-        weave_first_z(0, nc.vector.tensor_copy)
         piece_heads(0, (2, 3))
         piece_tails(0, (2, 3))
         quantise_z(0, 0, HALF, first_woven[0][:], AT_Z_CODES_FIRST)

@@ -36,6 +36,7 @@ LINE = 4
 ALIGN = 64
 PIECES = (256, 128, 128)
 HALF = GROUP // 2
+WARM_PASSES = 6
 ENTITY_CUTS = ((0, 256), (256, 512), (512, 1024))
 
 ROW = 4 * S
@@ -136,6 +137,11 @@ def tile_list_triple_pair_rerank_kernel(
         warm = own([LINE], F32, "warm")
         nc.vector.memset(zeros[:], 0.0)
         nc.scalar.activation(out=warm[:], in_=zeros[:], func=SIGMOID)
+        idle = own([PACK * HALF], BF16, "idle")
+        idle_codes = own([HALF], U32, "idle_codes")
+        idle_scales = own([HALF], U8, "idle_scales")
+        nc.vector.memset(idle[:].bitcast(I32), 0)
+        nc.vector.quantize_mx(out=idle_codes[:].bitcast(FP8X4), scales=idle_scales[:], in_=idle[:])
         nc.sync.dma_start(offs_sb[:], offs)
         nc.sync.dma_start(out=tab_s[SCALE_ROWS:, :].bitcast(I32), in_=tab_scales[0].bitcast(I32))
         fill_plane([nc.scalar, nc.scalar, nc.scalar, nc.sync], w2_plane_in, lambda r: w2_scales[0, r:BLOCKS:QUADS, :])
@@ -161,6 +167,12 @@ def tile_list_triple_pair_rerank_kernel(
         for quad in range(QUADS):
             rows = slice(32 * quad, 32 * quad + QUADS)
             nc.vector.tensor_copy(out=w2_s[rows, :].bitcast(I32), in_=w2_plane_in[rows, :].bitcast(I32))
+
+        for _ in range(WARM_PASSES):
+            nc.tensor.matmul_mx(
+                out=banks[BANKS - 1][:, :HALF], lhsT=idle_codes[:, :P].bitcast(FP8X4), lhsT_scale=w2_s[:, :P],
+                rhs=idle_codes[:].bitcast(FP8X4), rhs_scale=idle_scales[:], start=True, stop=True,
+            )
 
         v_w = own([S], U32, "v_w")
         for lo, hi in ENTITY_CUTS:

@@ -37,7 +37,7 @@ ALIGN = 64
 PIECES = (256, 128, 128)
 HALF = GROUP // 2
 WARM_PASSES = 6
-ENTITY_CUTS = ((0, 256), (256, 512), (512, 1024))
+ENTITY_CUTS = ((0, 256), (256, 512), (512, 768), (768, 1024))
 
 ROW = 4 * S
 STAGE = 2 * ROW
@@ -59,7 +59,7 @@ AT_Z_CODES_FIRST = AT_GATED_PAIR[1] - ROW // 4
 AT_REL_ROW = AT_GATED_PAIR[0] + ROW // 2
 AT_W4_CODES_EARLY = AT_W4_THIRD + STAGE
 AT_REL = tuple(
-    {1: AT_W4_CODES_EARLY + ROW // 2 - ALIGN, 5: AT_GATED_PAIR[0], 6: AT_REL_ROW + ALIGN, 7: AT_GATED_PAIR[1] - ALIGN}.get(
+    {0: AT_W4_CODES_EARLY, 1: AT_W4_CODES_EARLY + ROW // 2, 5: AT_GATED_PAIR[0], 6: AT_REL_ROW + ALIGN, 7: AT_GATED_PAIR[1] - ALIGN}.get(
         a, AT_REL_ROW + ALIGN * a
     )
     for a in range(TILES)
@@ -326,8 +326,8 @@ def tile_list_triple_pair_rerank_kernel(
         make_q(0, ENTITY_CUTS[:2])
         make_q(1, [(0, BANK)])
         make_q(2, [(0, BANK)], nc.vector.tensor_copy)
-        make_q(0, [(BANK, S)])
         make_q(3, [(0, BANK)], nc.vector.tensor_copy)
+        make_q(0, ENTITY_CUTS[2:])
         for a in range(1, PACK):
             make_q(a, [(BANK, S)])
         pick_heads(range(PACK))
@@ -343,7 +343,7 @@ def tile_list_triple_pair_rerank_kernel(
         for a in range(PACK, TILES):
             make_q(a)
         pick_heads(range(PACK, TILES))
-        rel_sb = [placed([ALIGN // (2 if a in (1, 7) else 4)], F32, "rel%d" % a, AT_REL[a]) for a in range(TILES)]
+        rel_sb = [placed([ALIGN // (2 if a == TILES - 1 else 4)], F32, "rel%d" % a, AT_REL[a]) for a in range(TILES)]
         by_tile = rel.rearrange("(g b t e) -> g t b e", g=GROUPS, t=PACK, e=RUN)
         for a in range(TILES):
             g, t = divmod(a, PACK)
@@ -361,7 +361,9 @@ def tile_list_triple_pair_rerank_kernel(
             for a in (2 * pair, 2 * pair + 1):
                 weighed_gate(a)
 
-        rows_and_gates(0)
+        for a in range(2):
+            make_h(a)
+            weighed_gate(a)
         rows_and_gates(1, (4, 5))
         gated_first = [own([PAIRS], F32, "gated_first%d" % k) for k in range(2)]
         z_first = placed([PACK, PAIRS], F32, "z_first", AT_Z)

@@ -415,13 +415,10 @@ def tile_list_triple_pair_rerank_kernel(
         def weave_piece(piece):
             lo, hi = spans[piece]
             z_woven[piece] = placed([PACK * (hi - lo)], BF16, "z_woven%d" % piece, AT_Z_WOVEN[piece])
-            for at in range(0, hi - lo, P):
-                nc.vector.tensor_copy(*weaving(z_woven[piece][:, PACK * at : PACK * (at + P)], z[piece][:, :, at : at + P]))
+            nc.vector.tensor_copy(*weaving(z_woven[piece][:], z[piece][:]))
 
         def quantise_piece(piece):
-            lo, hi = spans[piece]
-            for at in range(0, hi - lo, P):
-                quantise_z(1, lo + at, lo + at + P, z_woven[piece][:, PACK * at : PACK * (at + P)])
+            quantise_z(1, *spans[piece], z_woven[piece][:])
 
         def quantise_results(piece, g):
             lo, hi = spans[piece]
@@ -431,9 +428,9 @@ def tile_list_triple_pair_rerank_kernel(
                 in_=y_woven[piece, g][:],
             )
 
-        def close_sums(piece):
+        def close_sums(piece, groups=range(GROUPS)):
             lo, hi = spans[piece]
-            for g in range(GROUPS):
+            for g in groups:
                 for col in range(lo, hi, P):
                     second_passes(0, g, col)
                     sums[g, col] = second_passes(1, g, col)
@@ -496,13 +493,13 @@ def tile_list_triple_pair_rerank_kernel(
         for g in range(GROUPS):
             weave_results(1, g, nc.scalar.copy, True)
             quantise_results(1, g)
-        close_sums(last)
-        store_values(last, 0)
-        weave_results(last, 0, nc.scalar.copy, True)
+        close_sums(last, (1, 0))
         store_values(last, 1, nc.vector.tensor_copy, AT_Y_WOVEN + 2 * PACK * (GROUPS * edges[1] - P))
         weave_results(last, 1, nc.vector.tensor_copy, False)
-        quantise_results(last, 0)
         quantise_results(last, 1)
+        store_values(last, 0)
+        weave_results(last, 0, nc.scalar.copy, True)
+        quantise_results(last, 0)
         store_codes(edges[1], PAIRS)
         plane = y_scales[:].rearrange("p (g i) -> p g i", g=GROUPS)
         for k in range(QUADS):

from contextlib import ExitStack

import concourse.mybir as mybir
from concourse.masks import make_identity

K, T, S, PAIRS, H, N = 512, 4096, 1024, 512, 1024, 1024
FLOPS = 3 * 2 * K * H * S + 2 * H * N * PAIRS

F32 = mybir.dt.float32
BF16 = mybir.dt.bfloat16
I32 = mybir.dt.int32
U32 = mybir.dt.uint32
U16 = mybir.dt.uint16
U8 = mybir.dt.uint8
FP8X4 = mybir.dt.float8_e4m3fn_x4
FP4X4 = mybir.dt.float4_e2m1fn_x4
COPY = mybir.ActivationFunctionType.Copy
SIGMOID = mybir.ActivationFunctionType.Sigmoid
MULT = mybir.AluOpType.mult
ADD = mybir.AluOpType.add

P = 128
PACK = 4
GROUP = P * PACK
GROUPS = 2
TILES = H // P
BANK = 512
BANKS = 8
RING = 6
LIST_ROWS = 16
SCALE_ROWS = 112
RUN = 8
BLOCKS = P // RUN
QUADS = 4
LINE = 4
ALIGN = 64
PIECES = (256, 128, 128)
HALF = GROUP // 2
WARM_PASSES = 6
ENTITY_CUTS = ((0, 256), (256, 512), (512, 768), (768, 1024))

ROW = 4 * S
STAGE = 2 * ROW
AT_TABLE = 0
AT_W1_EARLY = AT_TABLE + 4 * T
AT_W4_FIRST = AT_W1_EARLY + ALIGN - STAGE
AT_W4_THIRD = AT_W4_FIRST + ROW
AT_TABLE_SCALES = AT_W1_EARLY + STAGE - ALIGN
AT_W3_EARLY = AT_W1_EARLY + STAGE
AT_W3_LATE = AT_W3_EARLY + 2 * H
AT_W4_SECOND = AT_W3_LATE + 2 * H
AT_W1_LATE = AT_W4_SECOND + STAGE - ALIGN
AT_PICKED_SCALES = AT_W1_LATE - S + ALIGN
AT_W2_LATE = AT_PICKED_SCALES - H + ALIGN
AT_W1_SCALES = AT_W1_LATE + ALIGN
AT_HEADS_HELD = AT_W1_SCALES + GROUP
AT_GATED_PAIR = (AT_HEADS_HELD + ROW, AT_W1_LATE + STAGE - ALIGN)
AT_Z_CODES_FIRST = AT_GATED_PAIR[1] - ROW // 4
AT_REL_ROW = AT_GATED_PAIR[0] + ROW // 2
AT_W4_CODES_EARLY = AT_W4_THIRD + STAGE
AT_REL = tuple(
    {0: AT_W4_CODES_EARLY, 1: AT_W4_CODES_EARLY + ROW // 2, 5: AT_GATED_PAIR[0], 6: AT_REL_ROW + ALIGN, 7: AT_GATED_PAIR[1] - ALIGN}.get(
        a, AT_REL_ROW + ALIGN * a
    )
    for a in range(TILES)
)
AT_W1_ROUNDED = AT_GATED_PAIR[1] + ROW // 2
AT_QR = AT_W1_ROUNDED + 3 * ROW
AT_H = AT_QR
AT_Y = AT_QR + PACK * STAGE
AT_Y_WOVEN = AT_Y + 2 * STAGE
AT_TURNED = AT_QR + TILES * STAGE
AT_LATE = AT_TURNED + STAGE + ALIGN
AT_Z = AT_LATE + STAGE
AT_W4_FOURTH = AT_W4_SECOND
AT_W4_STAGE = (AT_W4_FIRST, AT_W4_SECOND, AT_W4_THIRD, AT_W4_FOURTH)
AT_W4_ROUNDED = (AT_W1_ROUNDED + 2 * ROW - ALIGN, AT_W1_ROUNDED + ALIGN, AT_LATE, AT_LATE + ROW)
QUARTER = ROW // 4
AT_GATED_PIECE = (
    AT_GATED_PAIR,
    (AT_GATED_PAIR[1], AT_GATED_PAIR[1] + QUARTER),
    (AT_W4_FOURTH + ROW, AT_W4_FOURTH + ROW + QUARTER),
)
AT_Z_PIECE = (AT_H, AT_W4_FOURTH, AT_Z)
AT_W4_CODES = (AT_W4_CODES_EARLY, AT_W4_CODES_EARLY + ROW // 2, AT_Z_PIECE[0], None)
AT_Z_WOVEN = (AT_TURNED + ROW // 2, AT_TURNED + ROW, AT_TURNED)
AT_FIRST_WOVEN_BY_PIECE = (AT_LATE - ROW // 2, AT_W4_THIRD, AT_W4_THIRD + QUARTER)
AT_Z_CODES_SECOND = AT_GATED_PIECE[1][0]
AT_Z_CODES_LAST = AT_H + 6 * ROW
AT_Y_CODES = AT_H + 7 * ROW


def tile_list_triple_pair_rerank_kernel(
    tc, tab_words, tab_scales, offs, pos1, pos2, w1, w2_words, w2_scales, w3_words, w3_scales, rel, w4,
    out_0, out_1, out_2,
):
    nc = tc.nc
    with ExitStack() as ctx:
        keep = ctx.enter_context(tc.tile_pool(name="keep", bufs=1))
        shared = ctx.enter_context(tc.tile_pool(name="shared", bufs=1))
        psum = ctx.enter_context(tc.psum_pool(name="psum", bufs=1))

        def own(shape, dtype, name):
            return keep.tile([P] + shape, dtype, name=name, align_bytes=ALIGN)

        def placed(shape, dtype, name, at):
            return shared.tile([P] + shape, dtype, name=name, align_bytes=ALIGN, offset=at)

        banks = [psum.tile([P, BANK], F32, name="bank%d" % k) for k in range(BANKS)]
        bank_ring = banks[:RING]

        def next_bank():
            bank_ring.append(bank_ring.pop(0))
            return bank_ring[-1]

        offs_sb = keep.tile([P, S // LIST_ROWS], U16, name="offs_sb")
        pos1_sb = keep.tile([P, PAIRS // LIST_ROWS], U16, name="pos1_sb")
        pos2_sb = keep.tile([P, PAIRS // LIST_ROWS], U16, name="pos2_sb")
        tab_w = placed([T], U32, "tab_w", AT_TABLE)
        tab_s = placed([T], U8, "tab_s", AT_TABLE_SCALES)
        w2_w = [own([H], U8, "w2_w0"), placed([H], U8, "w2_w1", AT_W2_LATE)]
        w3_w = [placed([2 * H], U8, "w3_w0", AT_W3_EARLY), placed([2 * H], U8, "w3_w1", AT_W3_LATE)]
        w2_plane_in = own([H], U8, "w2_plane_in")
        w2_s = own([H], U8, "w2_s")
        w3_s = own([H], U8, "w3_s")
        v_s = own([S], U8, "v_s")

        def fill_plane(queues, plane, rows):
            for r, queue in enumerate(queues):
                queue.dma_start(out=plane[r:P:32, :].bitcast(I32), in_=rows(r).bitcast(I32))

        nc.vector.memset(tab_s[:SCALE_ROWS, :].bitcast(I32), 0)
        nc.vector.memset(w3_s[:].bitcast(I32), 0)
        nc.vector.memset(w2_s[:].bitcast(I32), 0)
        nc.vector.memset(v_s[:].bitcast(I32), 0)
        zeros = own([LINE], F32, "zeros")
        warm = own([LINE], F32, "warm")
        nc.vector.memset(zeros[:], 0.0)
        nc.scalar.activation(out=warm[:], in_=zeros[:], func=SIGMOID)
        idle = own([PACK * HALF], BF16, "idle")
        idle_codes = own([HALF], U32, "idle_codes")
        idle_scales = own([HALF], U8, "idle_scales")
        nc.vector.memset(idle[:].bitcast(I32), 0)
        nc.vector.quantize_mx(out=idle_codes[:].bitcast(FP8X4), scales=idle_scales[:], in_=idle[:])
        nc.sync.dma_start(offs_sb[:], offs)
        nc.sync.dma_start(out=tab_s[SCALE_ROWS:, :].bitcast(I32), in_=tab_scales[0].bitcast(I32))
        fill_plane([nc.scalar, nc.scalar, nc.scalar, nc.sync], w2_plane_in, lambda r: w2_scales[0, r:BLOCKS:QUADS, :])
        nc.sync.dma_start(pos1_sb[:], pos1)
        nc.sync.dma_start(out=tab_w[:].bitcast(I32), in_=tab_words[0].rearrange("p e t -> p (e t)").bitcast(I32))
        nc.sync.dma_start(pos2_sb[:], pos2)
        nc.sync.dma_start(out=w2_w[0][:].bitcast(I32), in_=w2_words[0][:, :H].bitcast(I32))
        fill_plane([nc.gpsimd] * QUADS, w3_s, lambda r: w3_scales[0, r:BLOCKS:QUADS, :])
        ident = own([P], F32, "ident")
        make_identity(nc, ident[:])

        picked_s = placed([S], U8, "picked_s", AT_PICKED_SCALES)
        nc.vector.tensor_copy(picked_s[:], tab_s[:].indirect(offs_sb[:]))
        fill_plane([nc.sync] * QUADS, v_s, lambda r: picked_s[SCALE_ROWS + r : P : QUADS, :])
        w3_bytes = w3_words[0].rearrange("p c t -> p (c t)")
        w1_rows = w1.rearrange("(p j) c -> p j c", j=PACK)
        w1_stage = [placed([PACK, GROUP], F32, "w1_stage%d" % g, at) for g, at in enumerate((AT_W1_EARLY, AT_W1_LATE))]
        nc.sync.dma_start(out=w1_stage[0][:], in_=w1_rows[:, :, :GROUP])
        nc.sync.dma_start(out=w3_w[0][:].bitcast(I32), in_=w3_bytes[:, : 2 * H].bitcast(I32))
        nc.sync.dma_start(out=w3_w[1][:].bitcast(I32), in_=w3_bytes[:, 2 * H :].bitcast(I32))
        nc.sync.dma_start(out=w1_stage[1][:], in_=w1_rows[:, :, GROUP:])
        nc.sync.dma_start(out=w2_w[1][:].bitcast(I32), in_=w2_words[0][:, H:].bitcast(I32))
        for quad in range(QUADS):
            rows = slice(32 * quad, 32 * quad + QUADS)
            nc.vector.tensor_copy(out=w2_s[rows, :].bitcast(I32), in_=w2_plane_in[rows, :].bitcast(I32))

        for _ in range(WARM_PASSES):
            nc.tensor.matmul_mx(
                out=banks[BANKS - 1][:, :HALF], lhsT=idle_codes[:, :P].bitcast(FP8X4), lhsT_scale=w2_s[:, :P],
                rhs=idle_codes[:].bitcast(FP8X4), rhs_scale=idle_scales[:], start=True, stop=True,
            )

        v_w = own([S], U32, "v_w")
        for lo, hi in ENTITY_CUTS:
            nc.vector.tensor_copy(v_w[:, lo:hi], tab_w[:].indirect(offs_sb[:, lo // LIST_ROWS : hi // LIST_ROWS]))

        w4_blocks = [(c_group, g) for g in range(GROUPS) for c_group in range(GROUPS)]
        w4_stage, w4_rounded, w4_q, w1_rounded, w1_q = {}, {}, {}, {}, {}

        def load_w4(number):
            c_group, g = w4_blocks[number]
            w4_stage[number] = placed([PACK, GROUP], F32, "w4_stage%d" % number, AT_W4_STAGE[number])
            rows = w4[GROUP * c_group : GROUP * (c_group + 1), GROUP * g : GROUP * (g + 1)]
            by_place = rows.rearrange("(b j e) n -> j b e n", j=PACK, e=RUN)
            for j in range(PACK):
                nc.sync.dma_start(out=w4_stage[number][:, j, :], in_=by_place[j])

        def quantised(width, name, woven, at=None, scales_at=None):
            codes = own([width], U32, name + "_codes") if at is None else placed([width], U32, name + "_codes", at)
            scales = own([width], U8, name + "_scales") if scales_at is None else placed([width], U8, name + "_scales", scales_at)
            nc.vector.quantize_mx(out=codes[:].bitcast(FP8X4), scales=scales[:], in_=woven)
            return codes, scales

        def round_w1(g):
            w1_rounded[g] = placed([PACK * GROUP], BF16, "w1_rounded%d" % g, AT_W1_ROUNDED + g * ROW)
            nc.gpsimd.tensor_scalar(
                w1_rounded[g][:].rearrange("p (t b e j) -> p b t e j", t=PACK, e=RUN, j=PACK),
                w1_stage[g][:].rearrange("p j (b t e) -> p b t e j", t=PACK, e=RUN),
                1.0, 0.0, MULT, ADD,
            )

        def round_w4(number):
            w4_rounded[number] = placed([PACK * GROUP], BF16, "w4_rounded%d" % number, AT_W4_ROUNDED[number])
            if number < GROUPS:
                nc.gpsimd.tensor_scalar(
                    w4_rounded[number][:].rearrange("p (t m j) -> p m t j", t=PACK, j=PACK),
                    w4_stage[number][:].rearrange("p j (m t) -> p m t j", t=PACK),
                    1.0, 0.0, MULT, ADD,
                )
            else:
                nc.scalar.copy(
                    out=w4_rounded[number][:].rearrange("p (t m j) -> p m j t", t=PACK, j=PACK),
                    in_=w4_stage[number][:].rearrange("p j (m t) -> p m j t", t=PACK),
                )

        def quantise_w4(number):
            at = AT_W4_CODES[number]
            w4_q[w4_blocks[number]] = quantised(GROUP, "w4_%d" % number, w4_rounded[number][:], at)

        def first_stage(rows, codes, scales, cuts=((0, BANK), (BANK, S)), copy=nc.scalar.copy):
            for lo, hi in cuts:
                acc = next_bank()[:, : hi - lo]
                nc.tensor.matmul_mx(
                    out=acc, lhsT=codes, lhsT_scale=scales,
                    rhs=v_w[:, lo:hi].bitcast(FP8X4), rhs_scale=v_s[:, lo:hi],
                    start=True, stop=True,
                )
                copy(out=rows[:, lo:hi], in_=acc)

        qr = [placed([2 * S], F32, "qr%d" % a, AT_QR + STAGE * a) for a in range(TILES)]
        h, gate = {}, {}

        def make_q(a, *how):
            g, t = divmod(a, PACK)
            codes = w2_w[g][:, 2 * P * t : 2 * P * (t + 1)].bitcast(FP4X4)
            first_stage(qr[a][:, S:], codes, w2_s[:, P * a : P * (a + 1)], *how)

        def make_r(a):
            g, t = divmod(a, PACK)
            codes = w3_w[g][:, 4 * P * t : 4 * P * (t + 1)].bitcast(FP8X4)
            first_stage(qr[a][:, :S], codes, w3_s[:, P * a : P * (a + 1)])

        def make_h(a):
            g, t = divmod(a, PACK)
            codes, scales = w1_q[g]
            h[a] = placed([S], F32, "h%d" % a, AT_H + ROW * a)
            first_stage(h[a], codes[:, P * t : P * (t + 1)].bitcast(FP8X4), scales[:, P * t : P * (t + 1)])

        heads = [
            placed([PAIRS], F32, "heads%d" % a, AT_HEADS_HELD + 4 * PAIRS * (a - PACK)) if a in (PACK, PACK + 1) else own([PAIRS], F32, "heads%d" % a)
            for a in range(TILES)
        ]
        tails = [own([PAIRS], F32, "tails%d" % a) for a in range(TILES)]
        turned = [placed([PACK, GROUP], F32, "turned%d" % g, AT_TURNED + STAGE * g) for g in range(GROUPS)]

        def pick_heads(tiles):
            for a in tiles:
                nc.vector.tensor_copy(heads[a][:], qr[a][:, S:].indirect(pos1_sb[:]))

        def pick_tails(tiles):
            for a in tiles:
                nc.vector.tensor_scalar(tails[a][:], qr[a][:].indirect(pos2_sb[:]), -1.0, 0.0, MULT, ADD)

        def turned_gates(a):
            g, t = divmod(a, PACK)
            acc = next_bank()
            for run in range(PACK):
                cols = slice(P * run, P * (run + 1))
                nc.tensor.matmul(acc[:, cols], heads[a][:, cols], ident[:], start=True, stop=False, is_transpose=True)
                nc.tensor.matmul(acc[:, cols], tails[a][:, cols], ident[:], start=False, stop=True, is_transpose=True)
            nc.scalar.activation(
                out=turned[g][:].rearrange("p run (t a b e) -> p a t run b e", t=PACK, a=PACK, e=RUN)[:, t],
                in_=acc[:].rearrange("p (run b t e) -> p t run b e", run=PACK, t=PACK, e=RUN),
                func=SIGMOID,
            )

        def weighed_gate(a):
            g, t = divmod(a, PACK)
            acc = next_bank()
            for run in range(PACK):
                nc.tensor.transpose(acc[:, P * run : P * (run + 1)], turned[g][:, run, P * t : P * (t + 1)], ident[:])
            gate[a] = own([PAIRS], F32, "gate%d" % a)
            nc.scalar.activation(out=gate[a][:], in_=acc[:], func=COPY, scale=rel_sb[a][:, 0:1])

        def gated_heads(a, lo, hi, into):
            entries = pos1_sb[:, lo // LIST_ROWS : hi // LIST_ROWS]
            nc.vector.tensor_tensor(into, h[a][:].indirect(entries), gate[a][:, lo:hi], MULT)

        def times_tails(a, lo, hi, gated, into):
            entries = pos2_sb[:, lo // LIST_ROWS : hi // LIST_ROWS]
            nc.vector.tensor_tensor(into, h[a][:].indirect(entries), gated, MULT)

        def weaving(woven, rows):
            return (
                woven.rearrange("p (run i t) -> p run t i", i=LINE, t=PACK),
                rows.rearrange("p t (run i) -> p run t i", i=LINE),
            )

        z_q = {}

        def quantise_z(g, lo, hi, woven, at=None):
            codes, scales = quantised(hi - lo, "z%d_%d" % (g, lo), woven, at)
            for col in range(lo, hi, P):
                z_q[g, col] = (codes[:, col - lo : col - lo + P].bitcast(FP8X4), scales[:, col - lo : col - lo + P])

        def second_passes(c_group, g, col):
            acc = banks[GROUPS * (col // P) + g][:].rearrange("p (t i) -> p t i", t=PACK)
            codes, scales = w4_q[c_group, g]
            for t in range(PACK):
                nc.tensor.matmul_mx(
                    out=acc[:, t, :],
                    lhsT=codes[:, P * t : P * (t + 1)].bitcast(FP8X4), lhsT_scale=scales[:, P * t : P * (t + 1)],
                    rhs=z_q[c_group, col][0], rhs_scale=z_q[c_group, col][1],
                    start=(c_group == 0 and t == 0), stop=(c_group == GROUPS - 1 and t == PACK - 1),
                )
            return acc

        round_w1(0)
        round_w1(1)
        load_w4(0)
        load_w4(1)
        make_q(0, ENTITY_CUTS[:2])
        make_q(1, [(0, BANK)])
        make_q(2, [(0, BANK)], nc.vector.tensor_copy)
        make_q(3, [(0, BANK)], nc.vector.tensor_copy)
        make_q(0, ENTITY_CUTS[2:])
        for a in range(1, PACK):
            make_q(a, [(BANK, S)])
        pick_heads(range(PACK))
        for a in range(PACK):
            make_r(a)
        pick_tails(range(PACK))
        w1_q[0] = quantised(GROUP, "w1_0", w1_rounded[0][:], None, AT_W1_SCALES)
        w1_q[1] = quantised(GROUP, "w1_1", w1_rounded[1][:])
        load_w4(2)
        for number in range(GROUPS):
            round_w4(number)
        load_w4(3)
        for a in range(PACK, TILES):
            make_q(a)
        pick_heads(range(PACK, TILES))
        rel_sb = [placed([ALIGN // (2 if a == TILES - 1 else 4)], F32, "rel%d" % a, AT_REL[a]) for a in range(TILES)]
        by_tile = rel.rearrange("(g b t e) -> g t b e", g=GROUPS, t=PACK, e=RUN)
        for a in range(TILES):
            g, t = divmod(a, PACK)
            nc.sync.dma_start(out=rel_sb[a][:, 0:1], in_=by_tile[g, t])
        for t in range(PACK):
            turned_gates(t)
            make_r(PACK + t)
        pick_tails(range(PACK, TILES))

        def rows_and_gates(pair, turned_before=(None, None)):
            for a, other in zip((2 * pair, 2 * pair + 1), turned_before):
                if other is not None:
                    turned_gates(other)
                make_h(a)
            for a in (2 * pair, 2 * pair + 1):
                weighed_gate(a)

        for a in range(2):
            make_h(a)
            weighed_gate(a)
        rows_and_gates(1, (4, 5))
        gated_first = [own([PAIRS], F32, "gated_first%d" % k) for k in range(2)]
        z_first = placed([PACK, PAIRS], F32, "z_first", AT_Z)
        for pair in range(2):
            for t in (2 * pair, 2 * pair + 1):
                gated_heads(t, 0, PAIRS, gated_first[t % 2][:])
            for t in (2 * pair, 2 * pair + 1):
                times_tails(t, 0, PAIRS, gated_first[t % 2][:], z_first[:, t, :])
        for number in range(GROUPS):
            quantise_w4(number)
        rows_and_gates(2, (6, 7))
        rows_and_gates(3)

        first_woven = [
            placed([PACK * width], BF16, "first_woven%d" % piece, AT_FIRST_WOVEN_BY_PIECE[piece]) for piece, width in enumerate(PIECES)
        ]

        def weave_first_z(piece):
            lo = sum(PIECES[:piece])
            nc.scalar.copy(*weaving(first_woven[piece][:], z_first[:, :, lo : lo + PIECES[piece]]))

        weave_first_z(0)
        round_w4(2)
        round_w4(3)
        weave_first_z(1)
        weave_first_z(2)

        edges = [sum(PIECES[:k]) for k in range(len(PIECES) + 1)]
        spans = list(zip(edges[:-1], edges[1:]))
        last = len(PIECES) - 1
        y_scales = own([GROUPS * PAIRS], U8, "y_scales")
        y_codes = placed([GROUPS * PAIRS], U32, "y_codes", AT_Y_CODES)
        y_woven, gated, z, z_woven, sums, y = {}, {}, {}, {}, {}, {}

        def piece_heads(piece, places):
            lo, hi = spans[piece]
            if piece not in gated:
                gated[piece] = [
                    placed([2, hi - lo], F32, "gated%d_%d" % (piece, pair), at) for pair, at in enumerate(AT_GATED_PIECE[piece])
                ]
                z[piece] = placed([PACK, hi - lo], F32, "z_piece%d" % piece, AT_Z_PIECE[piece])
            for t in places:
                gated_heads(PACK + t, lo, hi, gated[piece][t // 2][:, t % 2, :])

        def piece_tails(piece, places):
            for t in places:
                times_tails(PACK + t, *spans[piece], gated[piece][t // 2][:, t % 2, :], z[piece][:, t, :])

        def weave_piece(piece):
            lo, hi = spans[piece]
            z_woven[piece] = placed([PACK * (hi - lo)], BF16, "z_woven%d" % piece, AT_Z_WOVEN[piece])
            nc.vector.tensor_copy(*weaving(z_woven[piece][:], z[piece][:]))

        def quantise_piece(piece):
            quantise_z(1, *spans[piece], z_woven[piece][:])

        def quantise_results(piece, g):
            lo, hi = spans[piece]
            nc.vector.quantize_mx(
                out=y_codes[:, PAIRS * g + lo : PAIRS * g + hi].bitcast(FP8X4),
                scales=y_scales[:, PAIRS * g + lo : PAIRS * g + hi],
                in_=y_woven[piece, g][:],
            )

        def close_sums(piece, groups=range(GROUPS)):
            lo, hi = spans[piece]
            for g in groups:
                for col in range(lo, hi, P):
                    second_passes(0, g, col)
                    sums[g, col] = second_passes(1, g, col)

        def store_values(piece, g, copy=nc.scalar.copy, at=None):
            lo, hi = spans[piece]
            place = GROUPS * lo + g * (hi - lo)
            at = AT_Y + 4 * PACK * place if at is None else at
            y[piece, g] = placed([PACK, hi - lo], F32, "y%d_%d" % (piece, g), at)
            for col in range(lo, hi, P):
                copy(out=y[piece, g][:, :, col - lo : col - lo + P], in_=sums[g, col])
            rows = out_0[GROUP * g : GROUP * (g + 1), lo:hi].rearrange("(p t) i -> p t i", t=PACK)
            nc.sync.dma_start(out=rows, in_=y[piece, g][:])

        def weave_results(piece, g, copy, from_bank, cols=None):
            lo, hi = spans[piece]
            if (piece, g) not in y_woven:
                at = AT_Y_WOVEN + 2 * PACK * (GROUPS * lo + g * (hi - lo))
                y_woven[piece, g] = placed([PACK * (hi - lo)], BF16, "y_woven%d_%d" % (piece, g), at)
            for col in cols or range(lo, hi, P):
                rows = sums[g, col] if from_bank else y[piece, g][:, :, col - lo : col - lo + P]
                copy(*weaving(y_woven[piece, g][:, PACK * (col - lo) : PACK * (col - lo + P)], rows))

        def store_codes(lo, hi):
            words = out_1.rearrange("g p i t -> p g (i t)").bitcast(I32)
            codes = y_codes[:].bitcast(I32).rearrange("p (g i) -> p g i", g=GROUPS)
            nc.sync.dma_start(out=words[:, :, lo:hi], in_=codes[:, :, lo:hi])

        piece_heads(0, (0, 1))
        piece_tails(0, (0, 1))
        piece_heads(0, (2, 3))
        piece_tails(0, (2, 3))
        quantise_z(0, 0, HALF, first_woven[0][:], AT_Z_CODES_FIRST)
        weave_piece(0)
        quantise_piece(0)
        quantise_w4(2)
        piece_heads(1, range(PACK))
        quantise_w4(3)
        piece_tails(1, range(PACK))
        quantise_z(0, edges[1], edges[2], first_woven[1][:], AT_Z_CODES_SECOND)
        weave_piece(1)
        quantise_piece(1)
        close_sums(0)
        store_values(0, 0)
        weave_results(0, 0, nc.scalar.copy, True)
        store_values(0, 1)
        weave_results(0, 1, nc.scalar.copy, True, [0])
        piece_heads(2, range(PACK))
        piece_tails(2, range(PACK))
        quantise_z(0, edges[2], PAIRS, first_woven[2][:], AT_Z_CODES_LAST)
        weave_piece(2)
        quantise_results(0, 0)
        quantise_piece(2)
        close_sums(1)
        for g in range(GROUPS):
            store_values(1, g)
        weave_results(0, 1, nc.scalar.copy, True, [P])
        quantise_results(0, 1)
        store_codes(0, edges[1])
        for g in range(GROUPS):
            weave_results(1, g, nc.scalar.copy, True)
            quantise_results(1, g)
        close_sums(last, (1, 0))
        store_values(last, 1, nc.vector.tensor_copy, AT_Y_WOVEN + 2 * PACK * (GROUPS * edges[1] - P))
        weave_results(last, 1, nc.vector.tensor_copy, False)
        quantise_results(last, 1)
        store_values(last, 0)
        weave_results(last, 0, nc.scalar.copy, True)
        quantise_results(last, 0)
        store_codes(edges[1], PAIRS)
        plane = y_scales[:].rearrange("p (g i) -> p g i", g=GROUPS)
        for k in range(QUADS):
            rows = out_2[:, k:BLOCKS:QUADS, :].rearrange("g row i -> row g i")
            nc.scalar.dma_start(out=rows.bitcast(I32), in_=plane[k:P:32].bitcast(I32))
